import numpy as np
import ml_dtypes


def mxq(x, axis, fmt="e4m3"):
    dtype, down = {"e4m3": (ml_dtypes.float8_e4m3fn, 7), "e5m2": (ml_dtypes.float8_e5m2, 14)}[fmt]
    v = np.moveaxis(np.asarray(x, np.float32).astype(ml_dtypes.bfloat16).astype(np.float64), axis, -1)
    blocks = v.reshape(v.shape[:-1] + (-1, 32))
    amax = np.abs(blocks).max(-1, keepdims=True)
    byte = np.maximum(np.where(amax > 0, np.frexp(amax)[1] - 1 + 127, 0) - down, 1)
    scale = np.exp2(byte - 127.0)
    codes = (blocks / scale).astype(np.float32).astype(dtype).astype(np.float64)
    return np.moveaxis((codes * scale).reshape(v.shape), -1, axis)


WIDE = False


def mx_kscale(k):
    if not WIDE:
        return np.ones(k)
    levels = np.array([10, -10, 5, -5, 0])
    if k % 512:
        return np.exp2(np.random.permutation(np.resize(levels, k // 32))).repeat(32)
    a = np.empty((k // 512, 16))
    for p in range(k // 512):
        a[p, :8] = np.random.permutation(np.resize(levels, 8))
        for g in range(8):
            far = levels[np.abs(levels - a[p, g]) >= 10]
            a[p, g + 8] = far[np.random.randint(len(far))]
    return np.exp2(a.ravel()).repeat(32)


BF16 = ml_dtypes.bfloat16


def bf(x):
    return np.asarray(x, np.float32).astype(BF16)


def f64(x):
    return np.asarray(x).astype(np.float64)


N, D, C, O = 8192, 512, 512, 256


def centre_logits(x, a, m, p, lp):
    h = x * a
    k = (x * x - 1.0) * a
    hm = mxq(h, 1, "e4m3") @ mxq(m, 0, "e4m3")
    kp = mxq(k, 1, "e4m3") @ mxq(p, 0, "e4m3")
    return hm - kp + lp


def draw0():
    s, t = mx_kscale(D), mx_kscale(C)
    return {
        "x": bf(np.random.standard_normal((N, D))),
        "a": bf((1.0 + 0.1 * np.random.standard_normal(D)) * s),
        "m": bf(np.random.standard_normal((D, C)) * (0.7 / np.sqrt(D)) / s[:, None]),
        "p": bf(np.random.standard_normal((D, C)) * (0.5 / np.sqrt(D)) / s[:, None]),
        "lp": bf(0.3 * np.random.standard_normal(C)),
        "gc": bf((1.0 + 0.1 * np.random.standard_normal(C)) * t),
        "w": bf(np.random.standard_normal((C, O)) / np.sqrt(C) / t[:, None]),
    }


def core(x, a, m, p, lp, gc, w):
    q = centre_logits(f64(x), f64(a), f64(m), f64(p), f64(lp))
    e = np.exp(q - q.max(-1, keepdims=True))
    phi = e / e.sum(-1, keepdims=True)
    num_centres = phi.shape[-1]
    r = (num_centres * phi - 1.0) * f64(gc)
    return mxq(r, 1, "e4m3") @ mxq(f64(w), 0, "e4m3")


def e4m3fn_bytes(y):
    return np.clip(np.asarray(y, np.float64), -448.0, 448.0).astype(np.float32).astype(ml_dtypes.float8_e4m3fn).view(np.uint8)


def e4m3fn_values(b):
    return np.asarray(b, np.uint8).view(ml_dtypes.float8_e4m3fn).astype(np.float64)


def setup_inputs():
    d = draw0()
    x0 = np.asarray(d['p']).astype(np.float64)
    s = (np.max(np.abs(x0), axis=(1,), keepdims=True) / 448.0).astype(np.float32)
    out = {}
    for k, v in d.items():
        if k == 'p':
            out['p_bytes'] = e4m3fn_bytes(x0 / s.astype(np.float64))
            out['p_scale'] = s
        else:
            out[k] = v
    return out


def reference(x, a, m, p_bytes, p_scale, lp, gc, w):
    return core(x, a, m, e4m3fn_values(p_bytes) * p_scale.astype(np.float64), lp, gc, w)

@@ -1,0 +1,288 @@
+from contextlib import ExitStack
+
+import concourse.mybir as mybir
+from concourse.masks import make_identity
+
+N, D, C, O = 8192, 512, 512, 256
+FLOPS = 2 * N * D * C * 2 + 2 * N * C * O
+
+F32 = mybir.dt.float32
+BF16 = mybir.dt.bfloat16
+U32 = mybir.dt.uint32
+U8 = mybir.dt.uint8
+FP8 = mybir.dt.float8_e4m3fn
+FP8X4 = mybir.dt.float8_e4m3fn_x4
+ACT = mybir.ActivationFunctionType
+ALU = mybir.AluOpType
+AX = mybir.AxisListType
+
+P = 128
+PACK = 4
+J = 2
+TOK = J * P
+PAIRS = N // TOK
+
+ORDER = [
+    ("QZ", 2), ("TX", 0), ("TU1", 5), ("TQ0", 3), ("K", 1), ("I1", 6), ("SQ", 0), ("C", 4),
+    ("TQ1", 3), ("M0", 3), ("TU0", 5), ("R1", 5), ("QR", 6), ("E0", 3), ("QA", 2), ("LA", 2),
+    ("QB", 2), ("M1", 3), ("OU", 6), ("U1", 4), ("LB", 2), ("E1", 3), ("CO", 6), ("H", 0),
+    ("U0", 4), ("R0", 5),
+]
+
+
+def tile_ellipticalnormalizedrbfnet_t_kernel(tc, x, a, m, p_bytes, p_scale, lp, gc, w, out):
+    nc = tc.nc
+    x_v = x.rearrange("(g p j) d -> g p j d", p=P, j=J)
+    out_v = out.rearrange("(g p j) o -> g p j o", p=P, j=J)
+
+    with ExitStack() as ctx:
+        keep = ctx.enter_context(tc.tile_pool(name="keep", bufs=1))
+        xin = ctx.enter_context(tc.tile_pool(name="xin", bufs=6))
+        work = ctx.enter_context(tc.tile_pool(name="work", bufs=5))
+        psum = ctx.enter_context(tc.psum_pool(name="psum", bufs=2))
+
+        x_tiles = {}
+
+        def load(i):
+            x_sb = xin.tile([P, J, D], BF16, name="x_sb")
+            nc.sync.dma_start(out=x_sb[:], in_=x_v[i])
+            x_tiles[i] = x_sb
+
+        ident = keep.tile([P, P], F32, name="ident")
+        make_identity(nc, ident[:])
+        warm = keep.tile([P, 1], F32, name="warm")
+        nc.gpsimd.memset(warm[:], 0.0)
+        warm2 = keep.tile([P, 1], F32, name="warm2")
+        nc.scalar.activation(out=warm2[:], in_=warm[:], func=ACT.Exp, bias=0.0, scale=1.0)
+
+        load(0)
+        a_sb = keep.tile([P, PACK], BF16, name="a_sb")
+        nc.sync.dma_start(out=a_sb[:], in_=a.rearrange("(p t) -> p t", t=PACK))
+        ps_sb = keep.tile([P, PACK], F32, name="ps_sb")
+        nc.sync.dma_start(out=ps_sb[:], in_=p_scale.rearrange("(p t) o -> p (t o)", t=PACK))
+        pb_sb = keep.tile([P, PACK, C], U8, name="pb_sb")
+        nc.sync.dma_start(out=pb_sb[:], in_=p_bytes.rearrange("(p t) c -> p t c", t=PACK))
+        m_sb = keep.tile([P, PACK, C], BF16, name="m_sb")
+        nc.sync.dma_start(out=m_sb[:], in_=m.rearrange("(p t) c -> p t c", t=PACK))
+        lp_sb = keep.tile([P, PACK], BF16, name="lp_sb")
+        nc.sync.dma_start(out=lp_sb[:], in_=lp.rearrange("(p t) -> p t", t=PACK))
+        gc_sb = keep.tile([P, PACK], BF16, name="gc_sb")
+        nc.sync.dma_start(out=gc_sb[:], in_=gc.rearrange("(p t) -> p t", t=PACK))
+        load(1)
+        w_sb = keep.tile([P, PACK, O], BF16, name="w_sb")
+        nc.sync.dma_start(out=w_sb[:], in_=w.rearrange("(p t) o -> p t o", t=PACK))
+        load(2)
+        load(3)
+
+        a_rep = keep.tile([P, TOK, PACK], BF16, name="a_rep", align_bytes=64)
+        nc.gpsimd.tensor_scalar(
+            out=a_rep[:], in0=a_sb[:].unsqueeze(1).to_broadcast([P, TOK, PACK]), scalar1=1.0, scalar2=0.0, op0=ALU.mult, op1=ALU.add
+        )
+        gc_rep = keep.tile([P, P, PACK], F32, name="gc_rep", align_bytes=64)
+        nc.gpsimd.tensor_scalar(
+            out=gc_rep[:], in0=gc_sb[:].unsqueeze(1).to_broadcast([P, P, PACK]), scalar1=float(C), scalar2=0.0, op0=ALU.mult, op1=ALU.add
+        )
+        gc_f = keep.tile([P, PACK], F32, name="gc_f")
+        nc.gpsimd.tensor_scalar(out=gc_f[:], in0=gc_sb[:], scalar1=float(C), scalar2=0.0, op0=ALU.mult, op1=ALU.add)
+        lp_f = keep.tile([P, PACK], F32, name="lp_f")
+        nc.gpsimd.tensor_copy(out=lp_f[:], in_=lp_sb[:])
+
+        m_codes = keep.tile([P, C], U32, name="m_codes", align_bytes=64)
+        m_scales = keep.tile([P, C], U8, name="m_scales", align_bytes=64)
+        p_codes = keep.tile([P, C], U32, name="p_codes", align_bytes=64)
+        p_scales = keep.tile([P, C], U8, name="p_scales", align_bytes=64)
+        w_codes = keep.tile([P, O], U32, name="w_codes", align_bytes=64)
+        w_scales = keep.tile([P, O], U8, name="w_scales", align_bytes=64)
+        m_g = keep.tile([P, PACK * C], BF16, name="m_g", align_bytes=64)
+        p_g = keep.tile([P, PACK * C], BF16, name="p_g", align_bytes=64)
+        w_g = keep.tile([P, PACK * O], BF16, name="w_g", align_bytes=64)
+        p_w = keep.tile([P, PACK, C], BF16, name="p_w")
+        nps = keep.tile([P, PACK], F32, name="nps")
+        nc.vector.tensor_scalar(out=nps[:], in0=ps_sb[:], scalar1=-1.0, scalar2=None, op0=ALU.mult)
+        for t in range(PACK):
+            nc.vector.tensor_scalar(out=p_w[:, t, :], in0=pb_sb[:, t, :].bitcast(FP8), scalar1=nps[:, t : t + 1], scalar2=None, op0=ALU.mult)
+        nc.scalar.copy(
+            out=m_g[:].rearrange("p (s i t) -> p s i t", s=PACK, t=PACK),
+            in_=m_sb[:].rearrange("p t (i s) -> p s i t", s=PACK),
+        )
+        nc.vector.tensor_copy(
+            out=p_g[:].rearrange("p (s i t) -> p s i t", s=PACK, t=PACK),
+            in_=p_w[:].rearrange("p t (i s) -> p s i t", s=PACK),
+        )
+        nc.vector.quantize_mx(out=m_codes[:].bitcast(FP8X4), scales=m_scales[:], in_=m_g[:])
+        nc.vector.quantize_mx(out=p_codes[:].bitcast(FP8X4), scales=p_scales[:], in_=p_g[:])
+        nc.gpsimd.tensor_scalar(
+            out=w_g[:].rearrange("p (o t) -> p o t", t=PACK), in0=w_sb[:].rearrange("p t o -> p o t"), scalar1=1.0, scalar2=0.0, op0=ALU.mult, op1=ALU.add
+        )
+        nc.vector.quantize_mx(out=w_codes[:].bitcast(FP8X4), scales=w_scales[:], in_=w_g[:])
+
+        st = {}
+
+        def put(kind, i, t):
+            st[(kind, i)] = t
+            return t
+
+        def get(kind, i):
+            return st[(kind, i)]
+
+        def tx(i):
+            if i + 4 < PAIRS:
+                load(i + 4)
+            words = x_tiles[i][:].rearrange("p j d -> p (j d)").bitcast(F32)
+            xt = put("xt", i, psum.tile([P, TOK, 2], F32, name="xt"))
+            half = D // 2
+            for j in range(J):
+                for u in range(2):
+                    nc.tensor.transpose(xt[:, j * P : (j + 1) * P, u], words[:, j * half + u : (j + 1) * half : 2], ident[:])
+
+        def sq(i):
+            x2 = put("x2", i, work.tile([P, TOK * PACK], F32, name="x2"))
+            xb = get("xt", i)[:].rearrange("p r u -> p (r u)").bitcast(BF16)
+            nc.scalar.activation(out=x2[:], in_=xb, func=ACT.Square)
+
+        def hk_tile(i):
+            if ("hk", i) not in st:
+                put("hk", i, work.tile([P, 2, TOK * PACK], BF16, name="hk", align_bytes=64))
+            return get("hk", i)
+
+        def h(i):
+            hk = hk_tile(i)
+            xb = get("xt", i)[:].rearrange("p r u -> p (r u)").bitcast(BF16)
+            nc.vector.tensor_tensor(out=hk[:, 0, :], in0=xb, in1=a_rep[:].rearrange("p r t -> p (r t)"), op=ALU.mult)
+
+        def k(i):
+            nc.vector.scalar_tensor_tensor(
+                out=hk_tile(i)[:, 1, :], in0=get("x2", i)[:], scalar=-1.0, in1=a_rep[:].rearrange("p r t -> p (r t)"), op0=ALU.add, op1=ALU.mult
+            )
+
+        def qz(i):
+            codes = put("codes", i, work.tile([P, 2, TOK], U32, name="codes", align_bytes=64))
+            scales = put("scales", i, work.tile([P, 2, TOK], U8, name="scales", align_bytes=64))
+            nc.vector.quantize_mx(
+                out=codes[:].rearrange("p b r -> p (b r)").bitcast(FP8X4),
+                scales=scales[:].rearrange("p b r -> p (b r)"),
+                in_=get("hk", i)[:].rearrange("p b r -> p (b r)"),
+            )
+
+        def q_half(i, b):
+            qt = put(("qt", b), i, psum.tile([P, 2, TOK], F32, name="qt"))
+            codes, scales = get("codes", i), get("scales", i)
+            for s2 in range(2):
+                s = 2 * b + s2
+                cols = slice(s * P, (s + 1) * P)
+                for b2, (wc, ws) in enumerate(((m_codes, m_scales), (p_codes, p_scales))):
+                    nc.tensor.matmul_mx(
+                        out=qt[:, s2, :],
+                        lhsT=wc[:, cols].bitcast(FP8X4),
+                        lhsT_scale=ws[:, cols],
+                        rhs=codes[:, b2, :].bitcast(FP8X4),
+                        rhs_scale=scales[:, b2, :],
+                        start=(b2 == 0),
+                        stop=(b2 == 1),
+                    )
+
+        def lp_half(i, b):
+            if ("ql", i) not in st:
+                put("ql", i, work.tile([P, PACK, TOK], F32, name="ql"))
+            ql = get("ql", i)
+            qt = get(("qt", b), i)
+            for s2 in range(2):
+                s = 2 * b + s2
+                nc.scalar.activation(out=ql[:, s, :], in_=qt[:, s2, :], func=ACT.Identity, bias=lp_f[:, s : s + 1], scale=1.0)
+
+        def tq(i, j):
+            q = put(("q", j), i, psum.tile([P, C], F32, name="q"))
+            ql = get("ql", i)
+            for s in range(PACK):
+                nc.tensor.transpose(q[:, s * P : (s + 1) * P], ql[:, s, j * P : (j + 1) * P], ident[:])
+
+        def mx(i, j):
+            nm = put(("nm", j), i, work.tile([P, 1], F32, name="nm" + str(j)))
+            nc.vector.tensor_reduce(out=nm[:], in_=get(("q", j), i)[:], axis=AX.X, op=ALU.max, negate=True)
+
+        def ex(i, j):
+            e = put(("e", j), i, work.tile([P, C], F32, name="e" + str(j)))
+            if ("ssum", i) not in st:
+                put("ssum", i, work.tile([P, J], F32, name="ssum"))
+            ssum = get("ssum", i)
+            nc.scalar.activation(out=e[:], in_=get(("q", j), i)[:], func=ACT.Exp, bias=get(("nm", j), i)[:], scale=1.0, accum_out=ssum[:, j : j + 1])
+
+        def rc(i):
+            rs = put("rs", i, work.tile([P, J], F32, name="rs"))
+            nc.vector.reciprocal(out=rs[:], in_=get("ssum", i)[:])
+
+        def us(i, j):
+            u = put(("u", j), i, work.tile([P, C], F32, name="u" + str(j)))
+            nc.gpsimd.tensor_scalar(
+                out=u[:], in0=get(("e", j), i)[:], scalar1=get("rs", i)[:, j : j + 1], scalar2=-1.0 / C, op0=ALU.mult, op1=ALU.add
+            )
+
+        def tu(i, j):
+            ut = put(("ut", j), i, psum.tile([P, PACK, P], F32, name="ut"))
+            u = get(("u", j), i)
+            for s in range(PACK):
+                nc.tensor.transpose(ut[:, s, :], u[:, s * P : (s + 1) * P], ident[:])
+
+        def rr(i, j):
+            if ("r", i) not in st:
+                put("r", i, work.tile([P, TOK, PACK], BF16, name="r", align_bytes=64))
+            nc.vector.tensor_tensor(
+                out=get("r", i)[:, j * P : (j + 1) * P, :], in0=get(("ut", j), i)[:].rearrange("p s n -> p n s"), in1=gc_rep[:], op=ALU.mult
+            )
+
+        def ra(i, j):
+            rp = put("rp", i, work.tile([P, PACK, P], BF16, name="rp"))
+            ut = get(("ut", j), i)
+            for s in range(PACK):
+                nc.scalar.activation(out=rp[:, s, :], in_=ut[:, s, :], func=ACT.Copy, scale=gc_f[:, s : s + 1])
+
+        def il(i, j):
+            if ("r", i) not in st:
+                put("r", i, work.tile([P, TOK, PACK], BF16, name="r", align_bytes=64))
+            o_v = get("r", i)[:, j * P : (j + 1) * P, :]
+            i_v = get("rp", i)[:].rearrange("p s n -> p n s")
+            nc.gpsimd.tensor_scalar(out=o_v, in0=i_v, scalar1=1.0, scalar2=0.0, op0=ALU.mult, op1=ALU.add)
+
+        def qr(i):
+            rcodes = put("rcodes", i, work.tile([P, TOK], U32, name="rcodes", align_bytes=64))
+            rscales = put("rscales", i, work.tile([P, TOK], U8, name="rscales", align_bytes=64))
+            nc.vector.quantize_mx(out=rcodes[:].bitcast(FP8X4), scales=rscales[:], in_=get("r", i)[:].rearrange("p n s -> p (n s)"))
+
+        def ou(i):
+            o_ps = put("o_ps", i, psum.tile([P, J, O], F32, name="ut"))
+            for j in range(J):
+                cols = slice(j * P, (j + 1) * P)
+                nc.tensor.matmul_mx(
+                    out=o_ps[:, j, :],
+                    lhsT=get("rcodes", i)[:, cols].bitcast(FP8X4),
+                    lhsT_scale=get("rscales", i)[:, cols],
+                    rhs=w_codes[:].bitcast(FP8X4),
+                    rhs_scale=w_scales[:],
+                    start=True,
+                    stop=True,
+                )
+
+        def co(i):
+            o_sb = work.tile([P, J, O], F32, name="o_sb")
+            nc.scalar.copy(out=o_sb[:], in_=get("o_ps", i)[:])
+            nc.sync.dma_start(out=out_v[i], in_=o_sb[:])
+
+        steps = {
+            "TX": tx, "SQ": sq, "H": h, "K": k, "QZ": qz,
+            "QA": lambda i: q_half(i, 0), "QB": lambda i: q_half(i, 1),
+            "LA": lambda i: lp_half(i, 0), "LB": lambda i: lp_half(i, 1),
+            "TQ0": lambda i: tq(i, 0), "TQ1": lambda i: tq(i, 1),
+            "M0": lambda i: mx(i, 0), "M1": lambda i: mx(i, 1),
+            "E0": lambda i: ex(i, 0), "E1": lambda i: ex(i, 1),
+            "C": rc,
+            "U0": lambda i: us(i, 0), "U1": lambda i: us(i, 1),
+            "TU0": lambda i: tu(i, 0), "TU1": lambda i: tu(i, 1),
+            "R0": lambda i: rr(i, 0), "R1": lambda i: rr(i, 1) if i % 4 == 3 else ra(i, 1), "I1": lambda i: None if i % 4 == 3 else il(i, 1),
+            "QR": qr, "OU": ou, "CO": co,
+        }
+        with tc.manual_schedule():
+            for step in range(PAIRS + 6):
+                for name, off in ORDER:
+                    i = step - off
+                    if 0 <= i < PAIRS:
+                        steps[name](i)

@@ -23,11 +23,12 @@ TOK = J * P
 PAIRS = N // TOK
 
 ORDER = [
-    ("QZ", 2), ("TX", 0), ("TU1", 5), ("TQ0", 3), ("K", 1), ("I1", 6), ("SQ", 0), ("C", 4),
-    ("TQ1", 3), ("M0", 3), ("TU0", 5), ("R1", 5), ("QR", 6), ("E0", 3), ("QA", 2), ("LA", 2),
-    ("QB", 2), ("M1", 3), ("OU", 6), ("U1", 4), ("LB", 2), ("E1", 3), ("CO", 6), ("H", 0),
-    ("U0", 4), ("R0", 5),
+    ("C", 5), ("M0", 4), ("QA", 2), ("OU0", 7), ("U0", 5), ("U1", 5), ("R0", 6), ("CW", 6), ("TQ1", 4),
+    ("LA", 2), ("H", 1), ("TU0", 5), ("CO0", 7), ("GT", 5), ("M1", 4), ("E0", 4), ("QB", 2), ("K", 1),
+    ("E1", 4), ("OU1", 7), ("TX", 0), ("LB", 2), ("QR", 6), ("TQ0", 3), ("QZ", 1), ("CO1", 7), ("TW", 5),
+    ("SQ", 0),
 ]
+DEPTH = 7
 
 
 def tile_ellipticalnormalizedrbfnet_t_kernel(tc, x, a, m, p_bytes, p_scale, lp, gc, w, out):
@@ -39,7 +40,7 @@ def tile_ellipticalnormalizedrbfnet_t_kernel(tc, x, a, m, p_bytes, p_scale, lp, 
         keep = ctx.enter_context(tc.tile_pool(name="keep", bufs=1))
         xin = ctx.enter_context(tc.tile_pool(name="xin", bufs=6))
         work = ctx.enter_context(tc.tile_pool(name="work", bufs=5))
-        psum = ctx.enter_context(tc.psum_pool(name="psum", bufs=2))
+        psum = ctx.enter_context(tc.psum_pool(name="psum", bufs=1))
 
         x_tiles = {}
 
@@ -78,12 +79,21 @@ def tile_ellipticalnormalizedrbfnet_t_kernel(tc, x, a, m, p_bytes, p_scale, lp, 
         nc.gpsimd.tensor_scalar(
             out=a_rep[:], in0=a_sb[:].unsqueeze(1).to_broadcast([P, TOK, PACK]), scalar1=1.0, scalar2=0.0, op0=ALU.mult, op1=ALU.add
         )
+        a_f = keep.tile([P, PACK], F32, name="a_f")
+        nc.gpsimd.tensor_copy(out=a_f[:], in_=a_sb[:])
+        a_ps = psum.tile([P, PACK], F32, name="a_ps")
+        nc.tensor.matmul(a_ps[:], lhsT=ident[:], rhs=a_f[:], start=True, stop=True)
         gc_rep = keep.tile([P, P, PACK], F32, name="gc_rep", align_bytes=64)
         nc.gpsimd.tensor_scalar(
             out=gc_rep[:], in0=gc_sb[:].unsqueeze(1).to_broadcast([P, P, PACK]), scalar1=float(C), scalar2=0.0, op0=ALU.mult, op1=ALU.add
         )
         gc_f = keep.tile([P, PACK], F32, name="gc_f")
         nc.gpsimd.tensor_scalar(out=gc_f[:], in0=gc_sb[:], scalar1=float(C), scalar2=0.0, op0=ALU.mult, op1=ALU.add)
+        gc_ps = psum.tile([P, PACK, P], F32, name="ut1")
+        for t in range(PACK):
+            nc.tensor.transpose(gc_ps[:, t, :], gc_f[:, t : t + 1].to_broadcast([P, P]), ident[:])
+        gc_tok = keep.tile([P, C], F32, name="gc_tok")
+        nc.scalar.copy(out=gc_tok[:].rearrange("n (u p e) -> n u p e", u=2, e=2), in_=gc_ps[:].rearrange("n (u e) p -> n u p e", u=2))
         lp_f = keep.tile([P, PACK], F32, name="lp_f")
         nc.gpsimd.tensor_copy(out=lp_f[:], in_=lp_sb[:])
 
@@ -98,12 +108,16 @@ def tile_ellipticalnormalizedrbfnet_t_kernel(tc, x, a, m, p_bytes, p_scale, lp, 
         w_g = keep.tile([P, PACK * O], BF16, name="w_g", align_bytes=64)
         p_w = keep.tile([P, PACK, C], BF16, name="p_w")
         nps = keep.tile([P, PACK], F32, name="nps")
-        nc.vector.tensor_scalar(out=nps[:], in0=ps_sb[:], scalar1=-1.0, scalar2=None, op0=ALU.mult)
+        nc.gpsimd.tensor_scalar(out=nps[:], in0=ps_sb[:], scalar1=-1.0, scalar2=0.0, op0=ALU.mult, op1=ALU.add)
         for t in range(PACK):
-            nc.vector.tensor_scalar(out=p_w[:, t, :], in0=pb_sb[:, t, :].bitcast(FP8), scalar1=nps[:, t : t + 1], scalar2=None, op0=ALU.mult)
-        nc.scalar.copy(
+            nc.scalar.activation(out=p_w[:, t, :], in_=pb_sb[:, t, :].bitcast(FP8), func=ACT.Copy, scale=nps[:, t : t + 1])
+        nc.gpsimd.tensor_scalar(
             out=m_g[:].rearrange("p (s i t) -> p s i t", s=PACK, t=PACK),
-            in_=m_sb[:].rearrange("p t (i s) -> p s i t", s=PACK),
+            in0=m_sb[:].rearrange("p t (i s) -> p s i t", s=PACK),
+            scalar1=1.0,
+            scalar2=0.0,
+            op0=ALU.mult,
+            op1=ALU.add,
         )
         nc.vector.tensor_copy(
             out=p_g[:].rearrange("p (s i t) -> p s i t", s=PACK, t=PACK),
@@ -129,16 +143,19 @@ def tile_ellipticalnormalizedrbfnet_t_kernel(tc, x, a, m, p_bytes, p_scale, lp, 
             if i + 4 < PAIRS:
                 load(i + 4)
             words = x_tiles[i][:].rearrange("p j d -> p (j d)").bitcast(F32)
-            xt = put("xt", i, psum.tile([P, TOK, 2], F32, name="xt"))
+            xt = put("xt", i, psum.tile([P, 2, TOK], F32, name="xt"))
             half = D // 2
             for j in range(J):
                 for u in range(2):
-                    nc.tensor.transpose(xt[:, j * P : (j + 1) * P, u], words[:, j * half + u : (j + 1) * half : 2], ident[:])
+                    nc.tensor.transpose(xt[:, u, j * P : (j + 1) * P], words[:, j * half + u : (j + 1) * half : 2], ident[:])
+
+        def x_turned(i):
+            halves = get("xt", i)[:].rearrange("p u r -> p (u r)").bitcast(BF16)
+            return halves.rearrange("p (u r e) -> p r u e", u=2, e=2)
 
         def sq(i):
             x2 = put("x2", i, work.tile([P, TOK * PACK], F32, name="x2"))
-            xb = get("xt", i)[:].rearrange("p r u -> p (r u)").bitcast(BF16)
-            nc.scalar.activation(out=x2[:], in_=xb, func=ACT.Square)
+            nc.scalar.activation(out=x2[:].rearrange("p (r u e) -> p r u e", u=2, e=2), in_=x_turned(i), func=ACT.Square)
 
         def hk_tile(i):
             if ("hk", i) not in st:
@@ -147,12 +164,21 @@ def tile_ellipticalnormalizedrbfnet_t_kernel(tc, x, a, m, p_bytes, p_scale, lp, 
 
         def h(i):
             hk = hk_tile(i)
-            xb = get("xt", i)[:].rearrange("p r u -> p (r u)").bitcast(BF16)
-            nc.vector.tensor_tensor(out=hk[:, 0, :], in0=xb, in1=a_rep[:].rearrange("p r t -> p (r t)"), op=ALU.mult)
+            nc.vector.tensor_tensor(
+                out=hk[:, 0, :].rearrange("p (r u e) -> p r u e", u=2, e=2),
+                in0=x_turned(i),
+                in1=a_rep[:].rearrange("p r (u e) -> p r u e", e=2),
+                op=ALU.mult,
+            )
 
         def k(i):
             nc.vector.scalar_tensor_tensor(
-                out=hk_tile(i)[:, 1, :], in0=get("x2", i)[:], scalar=-1.0, in1=a_rep[:].rearrange("p r t -> p (r t)"), op0=ALU.add, op1=ALU.mult
+                out=hk_tile(i)[:, 1, :].rearrange("p (r t) -> p r t", t=PACK),
+                in0=get("x2", i)[:].rearrange("p (r t) -> p r t", t=PACK),
+                scalar=-1.0,
+                in1=a_ps[:].unsqueeze(1).to_broadcast([P, TOK, PACK]),
+                op0=ALU.add,
+                op1=ALU.mult,
             )
 
         def qz(i):
@@ -165,7 +191,7 @@ def tile_ellipticalnormalizedrbfnet_t_kernel(tc, x, a, m, p_bytes, p_scale, lp, 
             )
 
         def q_half(i, b):
-            qt = put(("qt", b), i, psum.tile([P, 2, TOK], F32, name="qt"))
+            qt = put(("qt", b), i, psum.tile([P, 2, TOK], F32, name="mx" + str(b)))
             codes, scales = get("codes", i), get("scales", i)
             for s2 in range(2):
                 s = 2 * b + s2
@@ -191,7 +217,7 @@ def tile_ellipticalnormalizedrbfnet_t_kernel(tc, x, a, m, p_bytes, p_scale, lp, 
                 nc.scalar.activation(out=ql[:, s, :], in_=qt[:, s2, :], func=ACT.Identity, bias=lp_f[:, s : s + 1], scale=1.0)
 
         def tq(i, j):
-            q = put(("q", j), i, psum.tile([P, C], F32, name="q"))
+            q = put(("q", j), i, psum.tile([P, C], F32, name="q" + str(j)))
             ql = get("ql", i)
             for s in range(PACK):
                 nc.tensor.transpose(q[:, s * P : (s + 1) * P], ql[:, s, j * P : (j + 1) * P], ident[:])
@@ -205,7 +231,11 @@ def tile_ellipticalnormalizedrbfnet_t_kernel(tc, x, a, m, p_bytes, p_scale, lp, 
             if ("ssum", i) not in st:
                 put("ssum", i, work.tile([P, J], F32, name="ssum"))
             ssum = get("ssum", i)
-            nc.scalar.activation(out=e[:], in_=get(("q", j), i)[:], func=ACT.Exp, bias=get(("nm", j), i)[:], scale=1.0, accum_out=ssum[:, j : j + 1])
+            e_v, q_v = e[:], get(("q", j), i)[:]
+            if j == 1:
+                e_v = e_v.rearrange("n (u p e) -> n u p e", u=2, e=2)
+                q_v = q_v.rearrange("n (u e p) -> n u p e", u=2, e=2)
+            nc.scalar.activation(out=e_v, in_=q_v, func=ACT.Exp, bias=get(("nm", j), i)[:], scale=1.0, accum_out=ssum[:, j : j + 1])
 
         def rc(i):
             rs = put("rs", i, work.tile([P, J], F32, name="rs"))
@@ -218,7 +248,7 @@ def tile_ellipticalnormalizedrbfnet_t_kernel(tc, x, a, m, p_bytes, p_scale, lp, 
             )
 
         def tu(i, j):
-            ut = put(("ut", j), i, psum.tile([P, PACK, P], F32, name="ut"))
+            ut = put(("ut", j), i, psum.tile([P, PACK, P], F32, name="ut" + str(j)))
             u = get(("u", j), i)
             for s in range(PACK):
                 nc.tensor.transpose(ut[:, s, :], u[:, s * P : (s + 1) * P], ident[:])
@@ -230,41 +260,45 @@ def tile_ellipticalnormalizedrbfnet_t_kernel(tc, x, a, m, p_bytes, p_scale, lp, 
                 out=get("r", i)[:, j * P : (j + 1) * P, :], in0=get(("ut", j), i)[:].rearrange("p s n -> p n s"), in1=gc_rep[:], op=ALU.mult
             )
 
-        def ra(i, j):
-            rp = put("rp", i, work.tile([P, PACK, P], BF16, name="rp"))
-            ut = get(("ut", j), i)
-            for s in range(PACK):
-                nc.scalar.activation(out=rp[:, s, :], in_=ut[:, s, :], func=ACT.Copy, scale=gc_f[:, s : s + 1])
+        def gt(i):
+            r_tok = put("r_tok", i, work.tile([P, C], BF16, name="r_tok"))
+            nc.gpsimd.tensor_tensor(out=r_tok[:], in0=get(("u", 1), i)[:], in1=gc_tok[:], op=ALU.mult)
 
-        def il(i, j):
-            if ("r", i) not in st:
-                put("r", i, work.tile([P, TOK, PACK], BF16, name="r", align_bytes=64))
-            o_v = get("r", i)[:, j * P : (j + 1) * P, :]
-            i_v = get("rp", i)[:].rearrange("p s n -> p n s")
-            nc.gpsimd.tensor_scalar(out=o_v, in0=i_v, scalar1=1.0, scalar2=0.0, op0=ALU.mult, op1=ALU.add)
+        def tw(i):
+            rw = put("rw", i, psum.tile([P, 2, P], F32, name="ut1"))
+            words = get("r_tok", i)[:].bitcast(F32)
+            for u in range(2):
+                nc.tensor.transpose(rw[:, u, :], words[:, u * P : (u + 1) * P], ident[:])
+
+        def cw(i):
+            words = get("r", i)[:, P:TOK, :].rearrange("p n s -> p (n s)").bitcast(F32)
+            nc.scalar.copy(out=words.rearrange("p (n u) -> p n u", u=2), in_=get("rw", i)[:].rearrange("p u n -> p n u"))
 
         def qr(i):
             rcodes = put("rcodes", i, work.tile([P, TOK], U32, name="rcodes", align_bytes=64))
             rscales = put("rscales", i, work.tile([P, TOK], U8, name="rscales", align_bytes=64))
             nc.vector.quantize_mx(out=rcodes[:].bitcast(FP8X4), scales=rscales[:], in_=get("r", i)[:].rearrange("p n s -> p (n s)"))
 
-        def ou(i):
-            o_ps = put("o_ps", i, psum.tile([P, J, O], F32, name="ut"))
-            for j in range(J):
-                cols = slice(j * P, (j + 1) * P)
-                nc.tensor.matmul_mx(
-                    out=o_ps[:, j, :],
-                    lhsT=get("rcodes", i)[:, cols].bitcast(FP8X4),
-                    lhsT_scale=get("rscales", i)[:, cols],
-                    rhs=w_codes[:].bitcast(FP8X4),
-                    rhs_scale=w_scales[:],
-                    start=True,
-                    stop=True,
-                )
+        def ou(i, j):
+            o_ps = put(("o_ps", j), i, psum.tile([P, O], F32, name="mx" + str(1 - j)))
+            cols = slice(j * P, (j + 1) * P)
+            nc.tensor.matmul_mx(
+                out=o_ps[:],
+                lhsT=get("rcodes", i)[:, cols].bitcast(FP8X4),
+                lhsT_scale=get("rscales", i)[:, cols],
+                rhs=w_codes[:].bitcast(FP8X4),
+                rhs_scale=w_scales[:],
+                start=True,
+                stop=True,
+            )
 
-        def co(i):
-            o_sb = work.tile([P, J, O], F32, name="o_sb")
-            nc.scalar.copy(out=o_sb[:], in_=get("o_ps", i)[:])
+        def co0(i):
+            o_sb = put("o_sb", i, work.tile([P, J, O], F32, name="o_sb"))
+            nc.scalar.copy(out=o_sb[:, 0, :], in_=get(("o_ps", 0), i)[:])
+
+        def co1(i):
+            o_sb = get("o_sb", i)
+            nc.scalar.copy(out=o_sb[:, 1, :], in_=get(("o_ps", 1), i)[:])
             nc.sync.dma_start(out=out_v[i], in_=o_sb[:])
 
         steps = {
@@ -276,12 +310,12 @@ def tile_ellipticalnormalizedrbfnet_t_kernel(tc, x, a, m, p_bytes, p_scale, lp, 
             "E0": lambda i: ex(i, 0), "E1": lambda i: ex(i, 1),
             "C": rc,
             "U0": lambda i: us(i, 0), "U1": lambda i: us(i, 1),
-            "TU0": lambda i: tu(i, 0), "TU1": lambda i: tu(i, 1),
-            "R0": lambda i: rr(i, 0), "R1": lambda i: rr(i, 1) if i % 4 == 3 else ra(i, 1), "I1": lambda i: None if i % 4 == 3 else il(i, 1),
-            "QR": qr, "OU": ou, "CO": co,
+            "TU0": lambda i: tu(i, 0),
+            "R0": lambda i: rr(i, 0), "GT": gt, "TW": tw, "CW": cw,
+            "QR": qr, "OU0": lambda i: ou(i, 0), "OU1": lambda i: ou(i, 1), "CO0": co0, "CO1": co1,
         }
         with tc.manual_schedule():
-            for step in range(PAIRS + 6):
+            for step in range(PAIRS + DEPTH):
                 for name, off in ORDER:
                     i = step - off
                     if 0 <= i < PAIRS:

@@ -23,9 +23,9 @@ TOK = J * P
 PAIRS = N // TOK
 
 ORDER = [
-    ("C", 5), ("M0", 4), ("QA", 2), ("OU0", 7), ("U0", 5), ("U1", 5), ("R0", 6), ("CW", 6), ("TQ1", 4),
-    ("LA", 2), ("H", 1), ("TU0", 5), ("CO0", 7), ("GT", 5), ("M1", 4), ("E0", 4), ("QB", 2), ("K", 1),
-    ("E1", 4), ("OU1", 7), ("TX", 0), ("LB", 2), ("QR", 6), ("TQ0", 3), ("QZ", 1), ("CO1", 7), ("TW", 5),
+    ("M0", 4), ("QA", 2), ("OU0", 7), ("U0", 5), ("U1", 5), ("R0", 6), ("CW", 6), ("TQ1", 4), ("LA", 2),
+    ("H", 1), ("TU0", 5), ("CO0", 7), ("GT", 5), ("M1", 4), ("E0", 4), ("QB", 2), ("K", 1), ("E1", 4),
+    ("OU1", 7), ("TX", 0), ("LB", 2), ("QR", 6), ("TQ0", 3), ("C", 4), ("QZ", 1), ("CO1", 7), ("TW", 5),
     ("SQ", 0),
 ]
 DEPTH = 7

@@ -21,14 +21,8 @@ PACK = 4
 J = 2
 TOK = J * P
 PAIRS = N // TOK
-
-ORDER = [
-    ("M0", 4), ("QA", 2), ("OU0", 7), ("U0", 5), ("U1", 5), ("R0", 6), ("CW", 6), ("TQ1", 4), ("LA", 2),
-    ("H", 1), ("TU0", 5), ("CO0", 7), ("GT", 5), ("M1", 4), ("E0", 4), ("QB", 2), ("K", 1), ("E1", 4),
-    ("OU1", 7), ("TX", 0), ("LB", 2), ("QR", 6), ("TQ0", 3), ("C", 4), ("QZ", 1), ("CO1", 7), ("TW", 5),
-    ("SQ", 0),
-]
-DEPTH = 7
+HALF = C // 2
+AHEAD = 4
 
 
 def tile_ellipticalnormalizedrbfnet_t_kernel(tc, x, a, m, p_bytes, p_scale, lp, gc, w, out):
@@ -38,97 +32,10 @@ def tile_ellipticalnormalizedrbfnet_t_kernel(tc, x, a, m, p_bytes, p_scale, lp, 
 
     with ExitStack() as ctx:
         keep = ctx.enter_context(tc.tile_pool(name="keep", bufs=1))
-        xin = ctx.enter_context(tc.tile_pool(name="xin", bufs=6))
-        work = ctx.enter_context(tc.tile_pool(name="work", bufs=5))
+        xin = ctx.enter_context(tc.tile_pool(name="xin", bufs=AHEAD + 2))
+        work = ctx.enter_context(tc.tile_pool(name="work", bufs=4))
         psum = ctx.enter_context(tc.psum_pool(name="psum", bufs=1))
-
-        x_tiles = {}
-
-        def load(i):
-            x_sb = xin.tile([P, J, D], BF16, name="x_sb")
-            nc.sync.dma_start(out=x_sb[:], in_=x_v[i])
-            x_tiles[i] = x_sb
-
-        ident = keep.tile([P, P], F32, name="ident")
-        make_identity(nc, ident[:])
-        warm = keep.tile([P, 1], F32, name="warm")
-        nc.gpsimd.memset(warm[:], 0.0)
-        warm2 = keep.tile([P, 1], F32, name="warm2")
-        nc.scalar.activation(out=warm2[:], in_=warm[:], func=ACT.Exp, bias=0.0, scale=1.0)
-
-        load(0)
-        a_sb = keep.tile([P, PACK], BF16, name="a_sb")
-        nc.sync.dma_start(out=a_sb[:], in_=a.rearrange("(p t) -> p t", t=PACK))
-        ps_sb = keep.tile([P, PACK], F32, name="ps_sb")
-        nc.sync.dma_start(out=ps_sb[:], in_=p_scale.rearrange("(p t) o -> p (t o)", t=PACK))
-        pb_sb = keep.tile([P, PACK, C], U8, name="pb_sb")
-        nc.sync.dma_start(out=pb_sb[:], in_=p_bytes.rearrange("(p t) c -> p t c", t=PACK))
-        m_sb = keep.tile([P, PACK, C], BF16, name="m_sb")
-        nc.sync.dma_start(out=m_sb[:], in_=m.rearrange("(p t) c -> p t c", t=PACK))
-        lp_sb = keep.tile([P, PACK], BF16, name="lp_sb")
-        nc.sync.dma_start(out=lp_sb[:], in_=lp.rearrange("(p t) -> p t", t=PACK))
-        gc_sb = keep.tile([P, PACK], BF16, name="gc_sb")
-        nc.sync.dma_start(out=gc_sb[:], in_=gc.rearrange("(p t) -> p t", t=PACK))
-        load(1)
-        w_sb = keep.tile([P, PACK, O], BF16, name="w_sb")
-        nc.sync.dma_start(out=w_sb[:], in_=w.rearrange("(p t) o -> p t o", t=PACK))
-        load(2)
-        load(3)
-
-        a_rep = keep.tile([P, TOK, PACK], BF16, name="a_rep", align_bytes=64)
-        nc.gpsimd.tensor_scalar(
-            out=a_rep[:], in0=a_sb[:].unsqueeze(1).to_broadcast([P, TOK, PACK]), scalar1=1.0, scalar2=0.0, op0=ALU.mult, op1=ALU.add
-        )
-        a_f = keep.tile([P, PACK], F32, name="a_f")
-        nc.gpsimd.tensor_copy(out=a_f[:], in_=a_sb[:])
-        a_ps = psum.tile([P, PACK], F32, name="a_ps")
-        nc.tensor.matmul(a_ps[:], lhsT=ident[:], rhs=a_f[:], start=True, stop=True)
-        gc_rep = keep.tile([P, P, PACK], F32, name="gc_rep", align_bytes=64)
-        nc.gpsimd.tensor_scalar(
-            out=gc_rep[:], in0=gc_sb[:].unsqueeze(1).to_broadcast([P, P, PACK]), scalar1=float(C), scalar2=0.0, op0=ALU.mult, op1=ALU.add
-        )
-        gc_f = keep.tile([P, PACK], F32, name="gc_f")
-        nc.gpsimd.tensor_scalar(out=gc_f[:], in0=gc_sb[:], scalar1=float(C), scalar2=0.0, op0=ALU.mult, op1=ALU.add)
-        gc_ps = psum.tile([P, PACK, P], F32, name="ut1")
-        for t in range(PACK):
-            nc.tensor.transpose(gc_ps[:, t, :], gc_f[:, t : t + 1].to_broadcast([P, P]), ident[:])
-        gc_tok = keep.tile([P, C], F32, name="gc_tok")
-        nc.scalar.copy(out=gc_tok[:].rearrange("n (u p e) -> n u p e", u=2, e=2), in_=gc_ps[:].rearrange("n (u e) p -> n u p e", u=2))
-        lp_f = keep.tile([P, PACK], F32, name="lp_f")
-        nc.gpsimd.tensor_copy(out=lp_f[:], in_=lp_sb[:])
-
-        m_codes = keep.tile([P, C], U32, name="m_codes", align_bytes=64)
-        m_scales = keep.tile([P, C], U8, name="m_scales", align_bytes=64)
-        p_codes = keep.tile([P, C], U32, name="p_codes", align_bytes=64)
-        p_scales = keep.tile([P, C], U8, name="p_scales", align_bytes=64)
-        w_codes = keep.tile([P, O], U32, name="w_codes", align_bytes=64)
-        w_scales = keep.tile([P, O], U8, name="w_scales", align_bytes=64)
-        m_g = keep.tile([P, PACK * C], BF16, name="m_g", align_bytes=64)
-        p_g = keep.tile([P, PACK * C], BF16, name="p_g", align_bytes=64)
-        w_g = keep.tile([P, PACK * O], BF16, name="w_g", align_bytes=64)
-        p_w = keep.tile([P, PACK, C], BF16, name="p_w")
-        nps = keep.tile([P, PACK], F32, name="nps")
-        nc.gpsimd.tensor_scalar(out=nps[:], in0=ps_sb[:], scalar1=-1.0, scalar2=0.0, op0=ALU.mult, op1=ALU.add)
-        for t in range(PACK):
-            nc.scalar.activation(out=p_w[:, t, :], in_=pb_sb[:, t, :].bitcast(FP8), func=ACT.Copy, scale=nps[:, t : t + 1])
-        nc.gpsimd.tensor_scalar(
-            out=m_g[:].rearrange("p (s i t) -> p s i t", s=PACK, t=PACK),
-            in0=m_sb[:].rearrange("p t (i s) -> p s i t", s=PACK),
-            scalar1=1.0,
-            scalar2=0.0,
-            op0=ALU.mult,
-            op1=ALU.add,
-        )
-        nc.vector.tensor_copy(
-            out=p_g[:].rearrange("p (s i t) -> p s i t", s=PACK, t=PACK),
-            in_=p_w[:].rearrange("p t (i s) -> p s i t", s=PACK),
-        )
-        nc.vector.quantize_mx(out=m_codes[:].bitcast(FP8X4), scales=m_scales[:], in_=m_g[:])
-        nc.vector.quantize_mx(out=p_codes[:].bitcast(FP8X4), scales=p_scales[:], in_=p_g[:])
-        nc.gpsimd.tensor_scalar(
-            out=w_g[:].rearrange("p (o t) -> p o t", t=PACK), in0=w_sb[:].rearrange("p t o -> p o t"), scalar1=1.0, scalar2=0.0, op0=ALU.mult, op1=ALU.add
-        )
-        nc.vector.quantize_mx(out=w_codes[:].bitcast(FP8X4), scales=w_scales[:], in_=w_g[:])
+        ctx.enter_context(tc.manual_schedule())
 
         st = {}
 
@@ -139,11 +46,81 @@ def tile_ellipticalnormalizedrbfnet_t_kernel(tc, x, a, m, p_bytes, p_scale, lp, 
         def get(kind, i):
             return st[(kind, i)]
 
-        def tx(i):
-            if i + 4 < PAIRS:
-                load(i + 4)
-            words = x_tiles[i][:].rearrange("p j d -> p (j d)").bitcast(F32)
-            xt = put("xt", i, psum.tile([P, 2, TOK], F32, name="xt"))
+        def load(i):
+            x_sb = put("x", i, xin.tile([P, J, D], BF16, name="x_sb"))
+            nc.sync.dma_start(out=x_sb[:], in_=x_v[i])
+
+        load(0)
+        ps_sb = keep.tile([P, PACK], F32, name="ps_sb")
+        nc.sync.dma_start(out=ps_sb[:], in_=p_scale.rearrange("(p t) o -> p (t o)", t=PACK))
+        pb_sb = keep.tile([P, PACK, C], U8, name="pb_sb")
+        nc.sync.dma_start(out=pb_sb[:], in_=p_bytes.rearrange("(p t) c -> p t c", t=PACK))
+        a_sb = keep.tile([P, PACK], BF16, name="a_sb")
+        nc.sync.dma_start(out=a_sb[:], in_=a.rearrange("(p t) -> p t", t=PACK))
+        for b in range(2):
+            m_sb = put("m_sb", b, keep.tile([P, PACK, HALF], BF16, name="m_sb" + str(b)))
+            nc.sync.dma_start(out=m_sb[:], in_=m.rearrange("(p t) c -> p t c", t=PACK)[:, :, b * HALF : (b + 1) * HALF])
+        load(1)
+        load(2)
+        lp_sb = keep.tile([P, PACK, 2], BF16, name="lp_sb")
+        with nc.allow_non_contiguous_dma("512 values, one to a partition and slice"):
+            nc.sync.dma_start(out=lp_sb[:, :, 0:1], in_=lp.rearrange("(s p o) -> p s o", p=P, o=1))
+        gc_sb = keep.tile([P, PACK], BF16, name="gc_sb")
+        nc.sync.dma_start(out=gc_sb[:], in_=gc.rearrange("(p t) -> p t", t=PACK))
+        w_sb = keep.tile([P, PACK, O], BF16, name="w_sb")
+        nc.sync.dma_start(out=w_sb[:], in_=w.rearrange("(p t) o -> p t o", t=PACK))
+        load(3)
+
+        ident = keep.tile([P, P], F32, name="ident")
+        make_identity(nc, ident[:])
+        warm = keep.tile([P, 1], F32, name="warm")
+        nc.gpsimd.memset(warm[:], 0.0)
+        warm2 = keep.tile([P, 1], F32, name="warm2")
+        nc.scalar.activation(out=warm2[:], in_=warm[:], func=ACT.Exp, bias=0.0, scale=1.0)
+
+        def gp_copy(dst, src, factor=1.0):
+            nc.gpsimd.tensor_scalar(out=dst, in0=src, scalar1=factor, scalar2=0.0, op0=ALU.mult, op1=ALU.add)
+
+        def planes(name, width):
+            codes = keep.tile([P, width], U32, name=name + "_codes", align_bytes=64)
+            scales = keep.tile([P, width], U8, name=name + "_scales", align_bytes=64)
+            return codes, scales
+
+        def quantise(name, b, width):
+            codes, scales = put(name, b, planes(name + str(b), width))
+            nc.vector.quantize_mx(out=codes[:].bitcast(FP8X4), scales=scales[:], in_=get(name + "_g", b)[:])
+
+        def interleaved(name, b, width):
+            g = put(name + "_g", b, keep.tile([P, PACK * width], BF16, name=name + "_g" + str(b), align_bytes=64))
+            return g[:].rearrange("p (c i t) -> p c t i", i=4, t=PACK)
+
+        def by_fours(rows):
+            return rows.rearrange("p t (c i) -> p c t i", i=4)
+
+        nps = keep.tile([P, PACK], F32, name="nps")
+
+        def p_half(b):
+            p_w = keep.tile([P, PACK, HALF], BF16, name="p_w" + str(b))
+            for t in range(PACK):
+                nc.vector.tensor_scalar(
+                    out=p_w[:, t, :], in0=pb_sb[:, t, b * HALF : (b + 1) * HALF].bitcast(FP8), scalar1=nps[:, t : t + 1], scalar2=None, op0=ALU.mult
+                )
+            nc.vector.tensor_copy(out=interleaved("p", b, HALF), in_=by_fours(p_w[:]))
+
+        def m_half(b):
+            nc.scalar.copy(out=interleaved("m", b, HALF), in_=by_fours(get("m_sb", b)[:]))
+
+        def turn(dst, src, plain):
+            if plain:
+                nc.tensor.matmul(dst, lhsT=src, rhs=ident[:], start=True, stop=True)
+            else:
+                nc.tensor.transpose(dst, src, ident[:])
+
+        def tx(i, bank="xt"):
+            if i + AHEAD < PAIRS:
+                load(i + AHEAD)
+            words = get("x", i)[:].rearrange("p j d -> p (j d)").bitcast(F32)
+            xt = put("xt", i, psum.tile([P, 2, TOK], F32, name=bank))
             half = D // 2
             for j in range(J):
                 for u in range(2):
@@ -157,13 +134,8 @@ def tile_ellipticalnormalizedrbfnet_t_kernel(tc, x, a, m, p_bytes, p_scale, lp, 
             x2 = put("x2", i, work.tile([P, TOK * PACK], F32, name="x2"))
             nc.scalar.activation(out=x2[:].rearrange("p (r u e) -> p r u e", u=2, e=2), in_=x_turned(i), func=ACT.Square)
 
-        def hk_tile(i):
-            if ("hk", i) not in st:
-                put("hk", i, work.tile([P, 2, TOK * PACK], BF16, name="hk", align_bytes=64))
-            return get("hk", i)
-
         def h(i):
-            hk = hk_tile(i)
+            hk = put("hk", i, work.tile([P, 2, TOK * PACK], BF16, name="hk", align_bytes=64))
             nc.vector.tensor_tensor(
                 out=hk[:, 0, :].rearrange("p (r u e) -> p r u e", u=2, e=2),
                 in0=x_turned(i),
@@ -173,7 +145,7 @@ def tile_ellipticalnormalizedrbfnet_t_kernel(tc, x, a, m, p_bytes, p_scale, lp, 
 
         def k(i):
             nc.vector.scalar_tensor_tensor(
-                out=hk_tile(i)[:, 1, :].rearrange("p (r t) -> p r t", t=PACK),
+                out=get("hk", i)[:, 1, :].rearrange("p (r t) -> p r t", t=PACK),
                 in0=get("x2", i)[:].rearrange("p (r t) -> p r t", t=PACK),
                 scalar=-1.0,
                 in1=a_ps[:].unsqueeze(1).to_broadcast([P, TOK, PACK]),
@@ -194,9 +166,9 @@ def tile_ellipticalnormalizedrbfnet_t_kernel(tc, x, a, m, p_bytes, p_scale, lp, 
             qt = put(("qt", b), i, psum.tile([P, 2, TOK], F32, name="mx" + str(b)))
             codes, scales = get("codes", i), get("scales", i)
             for s2 in range(2):
-                s = 2 * b + s2
-                cols = slice(s * P, (s + 1) * P)
-                for b2, (wc, ws) in enumerate(((m_codes, m_scales), (p_codes, p_scales))):
+                cols = slice(s2 * P, (s2 + 1) * P)
+                for b2, name in enumerate(("m", "p")):
+                    wc, ws = get(name, b)
                     nc.tensor.matmul_mx(
                         out=qt[:, s2, :],
                         lhsT=wc[:, cols].bitcast(FP8X4),
@@ -208,7 +180,7 @@ def tile_ellipticalnormalizedrbfnet_t_kernel(tc, x, a, m, p_bytes, p_scale, lp, 
                     )
 
         def lp_half(i, b):
-            if ("ql", i) not in st:
+            if b == 0:
                 put("ql", i, work.tile([P, PACK, TOK], F32, name="ql"))
             ql = get("ql", i)
             qt = get(("qt", b), i)
@@ -220,7 +192,7 @@ def tile_ellipticalnormalizedrbfnet_t_kernel(tc, x, a, m, p_bytes, p_scale, lp, 
             q = put(("q", j), i, psum.tile([P, C], F32, name="q" + str(j)))
             ql = get("ql", i)
             for s in range(PACK):
-                nc.tensor.transpose(q[:, s * P : (s + 1) * P], ql[:, s, j * P : (j + 1) * P], ident[:])
+                turn(q[:, s * P : (s + 1) * P], ql[:, s, j * P : (j + 1) * P], plain=(j == 0 and s == PACK - 1))
 
         def mx(i, j):
             nm = put(("nm", j), i, work.tile([P, 1], F32, name="nm" + str(j)))
@@ -228,14 +200,14 @@ def tile_ellipticalnormalizedrbfnet_t_kernel(tc, x, a, m, p_bytes, p_scale, lp, 
 
         def ex(i, j):
             e = put(("e", j), i, work.tile([P, C], F32, name="e" + str(j)))
-            if ("ssum", i) not in st:
+            if j == 0:
                 put("ssum", i, work.tile([P, J], F32, name="ssum"))
-            ssum = get("ssum", i)
-            e_v, q_v = e[:], get(("q", j), i)[:]
-            if j == 1:
-                e_v = e_v.rearrange("n (u p e) -> n u p e", u=2, e=2)
-                q_v = q_v.rearrange("n (u e p) -> n u p e", u=2, e=2)
-            nc.scalar.activation(out=e_v, in_=q_v, func=ACT.Exp, bias=get(("nm", j), i)[:], scale=1.0, accum_out=ssum[:, j : j + 1])
+                e_v = e[:].rearrange("n (t p) -> n t p", t=PACK)
+                q_v = get(("q", j), i)[:].rearrange("n (p t) -> n t p", t=PACK)
+            else:
+                e_v = e[:].rearrange("n (u p e) -> n u p e", u=2, e=2)
+                q_v = get(("q", j), i)[:].rearrange("n (p u e) -> n u p e", u=2, e=2)
+            nc.scalar.activation(out=e_v, in_=q_v, func=ACT.Exp, bias=get(("nm", j), i)[:], scale=1.0, accum_out=get("ssum", i)[:, j : j + 1])
 
         def rc(i):
             rs = put("rs", i, work.tile([P, J], F32, name="rs"))
@@ -247,18 +219,15 @@ def tile_ellipticalnormalizedrbfnet_t_kernel(tc, x, a, m, p_bytes, p_scale, lp, 
                 out=u[:], in0=get(("e", j), i)[:], scalar1=get("rs", i)[:, j : j + 1], scalar2=-1.0 / C, op0=ALU.mult, op1=ALU.add
             )
 
-        def tu(i, j):
-            ut = put(("ut", j), i, psum.tile([P, PACK, P], F32, name="ut" + str(j)))
-            u = get(("u", j), i)
+        def tu(i):
+            ut = put("ut", i, psum.tile([P, PACK, P], F32, name="ut0"))
+            u = get(("u", 0), i)
             for s in range(PACK):
-                nc.tensor.transpose(ut[:, s, :], u[:, s * P : (s + 1) * P], ident[:])
+                turn(ut[:, s, :], u[:, s * P : (s + 1) * P], plain=(s == PACK - 1))
 
-        def rr(i, j):
-            if ("r", i) not in st:
-                put("r", i, work.tile([P, TOK, PACK], BF16, name="r", align_bytes=64))
-            nc.vector.tensor_tensor(
-                out=get("r", i)[:, j * P : (j + 1) * P, :], in0=get(("ut", j), i)[:].rearrange("p s n -> p n s"), in1=gc_rep[:], op=ALU.mult
-            )
+        def rr(i):
+            r = put("r", i, work.tile([P, TOK, PACK], BF16, name="r", align_bytes=64))
+            nc.vector.tensor_tensor(out=r[:, 0:P, :], in0=get("ut", i)[:].rearrange("p s n -> p n s"), in1=gc_rep[:], op=ALU.mult)
 
         def gt(i):
             r_tok = put("r_tok", i, work.tile([P, C], BF16, name="r_tok"))
@@ -282,6 +251,7 @@ def tile_ellipticalnormalizedrbfnet_t_kernel(tc, x, a, m, p_bytes, p_scale, lp, 
         def ou(i, j):
             o_ps = put(("o_ps", j), i, psum.tile([P, O], F32, name="mx" + str(1 - j)))
             cols = slice(j * P, (j + 1) * P)
+            w_codes, w_scales = get("w", 0)
             nc.tensor.matmul_mx(
                 out=o_ps[:],
                 lhsT=get("rcodes", i)[:, cols].bitcast(FP8X4),
@@ -292,31 +262,87 @@ def tile_ellipticalnormalizedrbfnet_t_kernel(tc, x, a, m, p_bytes, p_scale, lp, 
                 stop=True,
             )
 
-        def co0(i):
-            o_sb = put("o_sb", i, work.tile([P, J, O], F32, name="o_sb"))
-            nc.scalar.copy(out=o_sb[:, 0, :], in_=get(("o_ps", 0), i)[:])
-
-        def co1(i):
+        def co(i, j):
+            if j == 0:
+                put("o_sb", i, work.tile([P, J, O], F32, name="o_sb"))
             o_sb = get("o_sb", i)
-            nc.scalar.copy(out=o_sb[:, 1, :], in_=get(("o_ps", 1), i)[:])
-            nc.sync.dma_start(out=out_v[i], in_=o_sb[:])
+            nc.scalar.copy(out=o_sb[:, j, :], in_=get(("o_ps", j), i)[:])
+            if j == 1:
+                nc.sync.dma_start(out=out_v[i], in_=o_sb[:])
 
-        steps = {
-            "TX": tx, "SQ": sq, "H": h, "K": k, "QZ": qz,
-            "QA": lambda i: q_half(i, 0), "QB": lambda i: q_half(i, 1),
-            "LA": lambda i: lp_half(i, 0), "LB": lambda i: lp_half(i, 1),
-            "TQ0": lambda i: tq(i, 0), "TQ1": lambda i: tq(i, 1),
-            "M0": lambda i: mx(i, 0), "M1": lambda i: mx(i, 1),
-            "E0": lambda i: ex(i, 0), "E1": lambda i: ex(i, 1),
-            "C": rc,
-            "U0": lambda i: us(i, 0), "U1": lambda i: us(i, 1),
-            "TU0": lambda i: tu(i, 0),
-            "R0": lambda i: rr(i, 0), "GT": gt, "TW": tw, "CW": cw,
-            "QR": qr, "OU0": lambda i: ou(i, 0), "OU1": lambda i: ou(i, 1), "CO0": co0, "CO1": co1,
-        }
-        with tc.manual_schedule():
-            for step in range(PAIRS + DEPTH):
-                for name, off in ORDER:
-                    i = step - off
-                    if 0 <= i < PAIRS:
-                        steps[name](i)
+        nc.vector.tensor_scalar(out=nps[:], in0=ps_sb[:], scalar1=-1.0, scalar2=None, op0=ALU.mult)
+        a_f = keep.tile([P, PACK], F32, name="a_f")
+        gp_copy(a_f[:], a_sb[:])
+        a_rep = keep.tile([P, TOK, PACK], BF16, name="a_rep", align_bytes=64)
+        gp_copy(a_rep[:], a_sb[:].unsqueeze(1).to_broadcast([P, TOK, PACK]))
+        tx(0, "q1")
+        a_ps = psum.tile([P, PACK], F32, name="a_ps")
+        nc.tensor.matmul(a_ps[:], lhsT=ident[:], rhs=a_f[:], start=True, stop=True)
+        tx(1, "ut0")
+        tx(2)
+        p_half(0)
+        sq(0)
+        m_half(0)
+        p_half(1)
+        h(0)
+        k(0)
+        m_half(1)
+        quantise("p", 0, HALF)
+        quantise("m", 0, HALF)
+        qz(0)
+        sq(1)
+        quantise("p", 1, HALF)
+        quantise("m", 1, HALF)
+        lp_f = keep.tile([P, PACK], F32, name="lp_f")
+        gp_copy(lp_f[:], lp_sb[:, :, 0])
+        gc_f = keep.tile([P, PACK], F32, name="gc_f")
+        gp_copy(gc_f[:], gc_sb[:], float(C))
+        gc_rep = keep.tile([P, P, PACK], F32, name="gc_rep", align_bytes=64)
+        gp_copy(gc_rep[:], gc_sb[:].unsqueeze(1).to_broadcast([P, P, PACK]), float(C))
+        gc_tok = keep.tile([P, C], F32, name="gc_tok")
+
+        def late_constants():
+            gc_ps = psum.tile([P, PACK, P], F32, name="ut1")
+            for t in range(PACK):
+                nc.tensor.transpose(gc_ps[:, t, :], gc_f[:, t : t + 1].to_broadcast([P, P]), ident[:])
+            nc.scalar.copy(out=gc_tok[:].rearrange("n (u p e) -> n u p e", u=2, e=2), in_=gc_ps[:].rearrange("n (u e) p -> n u p e", u=2))
+            gp_copy(interleaved("w", 0, O), by_fours(w_sb[:]))
+            quantise("w", 0, O)
+
+        order = [
+            (5, rr, 0),
+            (2, lambda i: q_half(i, 0), 0),
+            (6, lambda i: ou(i, 0), 0),
+            (4, lambda i: us(i, 0), 0),
+            (4, lambda i: us(i, 1), 0),
+            (3, lambda i: mx(i, 0), 0),
+            (5, cw, 0),
+            (3, lambda i: tq(i, 1), 0),
+            (2, lambda i: lp_half(i, 0), 0),
+            (1, h, 0),
+            (4, tu, 0),
+            (6, lambda i: co(i, 0), 0),
+            (4, gt, 0),
+            (3, lambda i: mx(i, 1), 0),
+            (3, lambda i: ex(i, 0), 0),
+            (2, lambda i: q_half(i, 1), 0),
+            (1, k, 0),
+            (3, lambda i: ex(i, 1), 0),
+            (6, lambda i: ou(i, 1), 0),
+            (0, tx, 3),
+            (2, lambda i: lp_half(i, 1), 0),
+            (5, qr, 0),
+            (3, rc, 0),
+            (1, qz, 0),
+            (6, lambda i: co(i, 1), 0),
+            (4, tw, 0),
+            (2, lambda i: tq(i, 0), 0),
+            (0, sq, 0),
+        ]
+        depth = max(lag for lag, stage, first in order)
+        for step in range(2, PAIRS + depth):
+            for lag, stage, first in order:
+                if first <= step - lag < PAIRS:
+                    stage(step - lag)
+            if step == 2:
+                late_constants()

@@ -22,6 +22,8 @@ J = 2
 TOK = J * P
 PAIRS = N // TOK
 HALF = C // 2
+OUT_V = 144
+DRAIN = PAIRS - 2
 AHEAD = 4
 
 
@@ -33,7 +35,7 @@ def tile_ellipticalnormalizedrbfnet_t_kernel(tc, x, a, m, p_bytes, p_scale, lp, 
     with ExitStack() as ctx:
         keep = ctx.enter_context(tc.tile_pool(name="keep", bufs=1))
         xin = ctx.enter_context(tc.tile_pool(name="xin", bufs=AHEAD + 2))
-        work = ctx.enter_context(tc.tile_pool(name="work", bufs=4))
+        work = ctx.enter_context(tc.tile_pool(name="work", bufs=5))
         psum = ctx.enter_context(tc.psum_pool(name="psum", bufs=1))
         ctx.enter_context(tc.manual_schedule())
 
@@ -148,7 +150,7 @@ def tile_ellipticalnormalizedrbfnet_t_kernel(tc, x, a, m, p_bytes, p_scale, lp, 
                 out=get("hk", i)[:, 1, :].rearrange("p (r t) -> p r t", t=PACK),
                 in0=get("x2", i)[:].rearrange("p (r t) -> p r t", t=PACK),
                 scalar=-1.0,
-                in1=a_ps[:].unsqueeze(1).to_broadcast([P, TOK, PACK]),
+                in1=a_ps.unsqueeze(1).to_broadcast([P, TOK, PACK]),
                 op0=ALU.add,
                 op1=ALU.mult,
             )
@@ -188,11 +190,11 @@ def tile_ellipticalnormalizedrbfnet_t_kernel(tc, x, a, m, p_bytes, p_scale, lp, 
                 s = 2 * b + s2
                 nc.scalar.activation(out=ql[:, s, :], in_=qt[:, s2, :], func=ACT.Identity, bias=lp_f[:, s : s + 1], scale=1.0)
 
-        def tq(i, j):
-            q = put(("q", j), i, psum.tile([P, C], F32, name="q" + str(j)))
+        def tq(i, j, bank=None):
+            q = put(("q", j), i, psum.tile([P, C], F32, name=bank or "q" + str(j)))
             ql = get("ql", i)
             for s in range(PACK):
-                turn(q[:, s * P : (s + 1) * P], ql[:, s, j * P : (j + 1) * P], plain=(j == 0 and s == PACK - 1))
+                turn(q[:, s * P : (s + 1) * P], ql[:, s, j * P : (j + 1) * P], plain=(j == 0 and s == 0))
 
         def mx(i, j):
             nm = put(("nm", j), i, work.tile([P, 1], F32, name="nm" + str(j)))
@@ -200,84 +202,106 @@ def tile_ellipticalnormalizedrbfnet_t_kernel(tc, x, a, m, p_bytes, p_scale, lp, 
 
         def ex(i, j):
             e = put(("e", j), i, work.tile([P, C], F32, name="e" + str(j)))
-            if j == 0:
-                put("ssum", i, work.tile([P, J], F32, name="ssum"))
+            g = i + 1 - j
+            if j == 0 or g == 0:
+                put("ssum", g, work.tile([P, J], F32, name="ssum"))
+            if j == 0 or i >= DRAIN:
                 e_v = e[:].rearrange("n (t p) -> n t p", t=PACK)
                 q_v = get(("q", j), i)[:].rearrange("n (p t) -> n t p", t=PACK)
             else:
                 e_v = e[:].rearrange("n (u p e) -> n u p e", u=2, e=2)
                 q_v = get(("q", j), i)[:].rearrange("n (p u e) -> n u p e", u=2, e=2)
-            nc.scalar.activation(out=e_v, in_=q_v, func=ACT.Exp, bias=get(("nm", j), i)[:], scale=1.0, accum_out=get("ssum", i)[:, j : j + 1])
+            nc.scalar.activation(out=e_v, in_=q_v, func=ACT.Exp, bias=get(("nm", j), i)[:], scale=1.0, accum_out=get("ssum", g)[:, j : j + 1])
 
-        def rc(i):
-            rs = put("rs", i, work.tile([P, J], F32, name="rs"))
-            nc.vector.reciprocal(out=rs[:], in_=get("ssum", i)[:])
+        def rc(g):
+            cols = slice(1 if g == 0 else 0, 1 if g == PAIRS else J)
+            rs = put("rs", g, work.tile([P, J], F32, name="rs"))
+            nc.vector.reciprocal(out=rs[:, cols], in_=get("ssum", g)[:, cols])
 
         def us(i, j):
             u = put(("u", j), i, work.tile([P, C], F32, name="u" + str(j)))
             nc.gpsimd.tensor_scalar(
-                out=u[:], in0=get(("e", j), i)[:], scalar1=get("rs", i)[:, j : j + 1], scalar2=-1.0 / C, op0=ALU.mult, op1=ALU.add
+                out=u[:], in0=get(("e", j), i)[:], scalar1=get("rs", i + 1 - j)[:, j : j + 1], scalar2=-1.0 / C, op0=ALU.mult, op1=ALU.add
             )
 
-        def tu(i):
-            ut = put("ut", i, psum.tile([P, PACK, P], F32, name="ut0"))
-            u = get(("u", 0), i)
-            for s in range(PACK):
-                turn(ut[:, s, :], u[:, s * P : (s + 1) * P], plain=(s == PACK - 1))
+        def uv(i, j):
+            u = put(("u", j), i, work.tile([P, C], F32, name="u" + str(j)))
+            nc.vector.tensor_scalar(
+                out=u[:], in0=get(("e", j), i)[:], scalar1=get("rs", i + 1 - j)[:, j : j + 1], scalar2=-1.0 / C, op0=ALU.mult, op1=ALU.add
+            )
 
-        def rr(i):
-            r = put("r", i, work.tile([P, TOK, PACK], BF16, name="r", align_bytes=64))
-            nc.vector.tensor_tensor(out=r[:, 0:P, :], in0=get("ut", i)[:].rearrange("p s n -> p n s"), in1=gc_rep[:], op=ALU.mult)
+        def tu(i, j=0, bank="ut0"):
+            ut = put(("ut", j), i, psum.tile([P, PACK, P], F32, name=bank))
+            u = get(("u", j), i)
+            for s in range(PACK):
+                nc.tensor.transpose(ut[:, s, :], u[:, s * P : (s + 1) * P], ident[:])
+
+        def rr(i, j=0):
+            if ("r", i) not in st:
+                put("r", i, work.tile([P, TOK, PACK], BF16, name="r", align_bytes=64))
+            nc.vector.tensor_tensor(
+                out=get("r", i)[:, j * P : (j + 1) * P, :], in0=get(("ut", j), i)[:].rearrange("p s n -> p n s"), in1=gc_rep[:], op=ALU.mult
+            )
 
         def gt(i):
             r_tok = put("r_tok", i, work.tile([P, C], BF16, name="r_tok"))
             nc.gpsimd.tensor_tensor(out=r_tok[:], in0=get(("u", 1), i)[:], in1=gc_tok[:], op=ALU.mult)
 
         def tw(i):
-            rw = put("rw", i, psum.tile([P, 2, P], F32, name="ut1"))
             words = get("r_tok", i)[:].bitcast(F32)
             for u in range(2):
                 nc.tensor.transpose(rw[:, u, :], words[:, u * P : (u + 1) * P], ident[:])
 
         def cw(i):
+            if ("r", i) not in st:
+                put("r", i, work.tile([P, TOK, PACK], BF16, name="r", align_bytes=64))
             words = get("r", i)[:, P:TOK, :].rearrange("p n s -> p (n s)").bitcast(F32)
-            nc.scalar.copy(out=words.rearrange("p (n u) -> p n u", u=2), in_=get("rw", i)[:].rearrange("p u n -> p n u"))
+            nc.scalar.copy(out=words.rearrange("p (n u) -> p n u", u=2), in_=rw.rearrange("p u n -> p n u"))
 
         def qr(i):
             rcodes = put("rcodes", i, work.tile([P, TOK], U32, name="rcodes", align_bytes=64))
             rscales = put("rscales", i, work.tile([P, TOK], U8, name="rscales", align_bytes=64))
             nc.vector.quantize_mx(out=rcodes[:].bitcast(FP8X4), scales=rscales[:], in_=get("r", i)[:].rearrange("p n s -> p (n s)"))
 
-        def ou(i, j):
-            o_ps = put(("o_ps", j), i, psum.tile([P, O], F32, name="mx" + str(1 - j)))
-            cols = slice(j * P, (j + 1) * P)
+        def ou(i, bank="o_ps"):
+            o_ps = put("o_ps", i, psum.tile([P, J * O], F32, name=bank))
             w_codes, w_scales = get("w", 0)
-            nc.tensor.matmul_mx(
-                out=o_ps[:],
-                lhsT=get("rcodes", i)[:, cols].bitcast(FP8X4),
-                lhsT_scale=get("rscales", i)[:, cols],
-                rhs=w_codes[:].bitcast(FP8X4),
-                rhs_scale=w_scales[:],
-                start=True,
-                stop=True,
-            )
+            for j in range(J):
+                cols = slice(j * P, (j + 1) * P)
+                nc.tensor.matmul_mx(
+                    out=o_ps[:, j * O : (j + 1) * O],
+                    lhsT=get("rcodes", i)[:, cols].bitcast(FP8X4),
+                    lhsT_scale=get("rscales", i)[:, cols],
+                    rhs=w_codes[:].bitcast(FP8X4),
+                    rhs_scale=w_scales[:],
+                    start=True,
+                    stop=True,
+                )
 
-        def co(i, j):
-            if j == 0:
-                put("o_sb", i, work.tile([P, J, O], F32, name="o_sb"))
+        def ov(i):
+            o_sb = put("o_sb", i, work.tile([P, J * O], F32, name="o_sb"))
+            nc.vector.tensor_copy(out=o_sb[:, 0:OUT_V], in_=get("o_ps", i)[:, 0:OUT_V])
+
+        def oscal(i):
             o_sb = get("o_sb", i)
-            nc.scalar.copy(out=o_sb[:, j, :], in_=get(("o_ps", j), i)[:])
-            if j == 1:
-                nc.sync.dma_start(out=out_v[i], in_=o_sb[:])
+            nc.scalar.copy(out=o_sb[:, OUT_V:], in_=get("o_ps", i)[:, OUT_V:])
+            nc.sync.dma_start(out=out_v[i], in_=o_sb[:].rearrange("p (j o) -> p j o", j=J))
+
+        def out_scalar(i):
+            o_sb = work.tile([P, J * O], F32, name="o_sb")
+            nc.scalar.copy(out=o_sb[:], in_=get("o_ps", i)[:])
+            nc.sync.dma_start(out=out_v[i], in_=o_sb[:].rearrange("p (j o) -> p j o", j=J))
 
         nc.vector.tensor_scalar(out=nps[:], in0=ps_sb[:], scalar1=-1.0, scalar2=None, op0=ALU.mult)
         a_f = keep.tile([P, PACK], F32, name="a_f")
         gp_copy(a_f[:], a_sb[:])
         a_rep = keep.tile([P, TOK, PACK], BF16, name="a_rep", align_bytes=64)
         gp_copy(a_rep[:], a_sb[:].unsqueeze(1).to_broadcast([P, TOK, PACK]))
-        tx(0, "q1")
-        a_ps = psum.tile([P, PACK], F32, name="a_ps")
-        nc.tensor.matmul(a_ps[:], lhsT=ident[:], rhs=a_f[:], start=True, stop=True)
+        tx(0, "q0")
+        side = psum.tile([P, C], F32, name="side")
+        rw = side[:, 0:TOK].rearrange("p (u n) -> p u n", u=2)
+        a_ps = side[:, TOK : TOK + PACK]
+        nc.tensor.matmul(a_ps, lhsT=ident[:], rhs=a_f[:], start=True, stop=True)
         tx(1, "ut0")
         tx(2)
         p_half(0)
@@ -302,7 +326,7 @@ def tile_ellipticalnormalizedrbfnet_t_kernel(tc, x, a, m, p_bytes, p_scale, lp, 
         gc_tok = keep.tile([P, C], F32, name="gc_tok")
 
         def late_constants():
-            gc_ps = psum.tile([P, PACK, P], F32, name="ut1")
+            gc_ps = psum.tile([P, PACK, P], F32, name="o_ps")
             for t in range(PACK):
                 nc.tensor.transpose(gc_ps[:, t, :], gc_f[:, t : t + 1].to_broadcast([P, P]), ident[:])
             nc.scalar.copy(out=gc_tok[:].rearrange("n (u p e) -> n u p e", u=2, e=2), in_=gc_ps[:].rearrange("n (u e) p -> n u p e", u=2))
@@ -310,39 +334,99 @@ def tile_ellipticalnormalizedrbfnet_t_kernel(tc, x, a, m, p_bytes, p_scale, lp, 
             quantise("w", 0, O)
 
         order = [
-            (5, rr, 0),
-            (2, lambda i: q_half(i, 0), 0),
-            (6, lambda i: ou(i, 0), 0),
-            (4, lambda i: us(i, 0), 0),
-            (4, lambda i: us(i, 1), 0),
-            (3, lambda i: mx(i, 0), 0),
-            (5, cw, 0),
-            (3, lambda i: tq(i, 1), 0),
-            (2, lambda i: lp_half(i, 0), 0),
-            (1, h, 0),
-            (4, tu, 0),
-            (6, lambda i: co(i, 0), 0),
-            (4, gt, 0),
-            (3, lambda i: mx(i, 1), 0),
-            (3, lambda i: ex(i, 0), 0),
-            (2, lambda i: q_half(i, 1), 0),
-            (1, k, 0),
-            (3, lambda i: ex(i, 1), 0),
-            (6, lambda i: ou(i, 1), 0),
-            (0, tx, 3),
-            (2, lambda i: lp_half(i, 1), 0),
-            (5, qr, 0),
-            (3, rc, 0),
-            (1, qz, 0),
-            (6, lambda i: co(i, 1), 0),
-            (4, tw, 0),
-            (2, lambda i: tq(i, 0), 0),
-            (0, sq, 0),
+            (7, ov, 0, PAIRS),
+            (5, lambda i: us(i, 0), 0, PAIRS),
+            (4, lambda i: us(i, 1), 0, PAIRS),
+            (4, gt, 0, PAIRS),
+            (2, lambda i: q_half(i, 0), 0, PAIRS),
+            (4, lambda i: mx(i, 0), 0, PAIRS),
+            (5, cw, 0, PAIRS),
+            (7, oscal, 0, PAIRS),
+            (1, h, 0, PAIRS),
+            (5, tu, 0, PAIRS),
+            (2, lambda i: lp_half(i, 0), 0, PAIRS),
+            (3, lambda i: mx(i, 1), 0, PAIRS),
+            (0, tx, 3, PAIRS),
+            (4, lambda i: ex(i, 0), 0, PAIRS),
+            (5, rr, 0, PAIRS),
+            (2, lambda i: q_half(i, 1), 0, PAIRS),
+            (1, k, 0, PAIRS),
+            (3, lambda i: ex(i, 1), 0, PAIRS),
+            (6, ou, 0, PAIRS),
+            (3, lambda i: tq(i, 0), 0, PAIRS),
+            (2, lambda i: lp_half(i, 1), 0, PAIRS),
+            (5, qr, 0, PAIRS),
+            (0, sq, 0, PAIRS),
+            (3, rc, 0, PAIRS + 1),
+            (2, lambda i: tq(i, 1), 0, PAIRS),
+            (1, qz, 0, PAIRS),
+            (4, tw, 0, PAIRS),
         ]
-        depth = max(lag for lag, stage, first in order)
-        for step in range(2, PAIRS + depth):
-            for lag, stage, first in order:
-                if first <= step - lag < PAIRS:
+        for step in range(2, PAIRS + 1):
+            for lag, stage, first, last in order:
+                if first <= step - lag < last:
                     stage(step - lag)
             if step == 2:
                 late_constants()
+
+        z = PAIRS - 1
+        ov(z - 5)
+        us(z - 3, 0)
+        us(z - 2, 1)
+        gt(z - 2)
+        q_half(z, 0)
+        q_half(z, 1)
+        cw(z - 3)
+        oscal(z - 5)
+        mx(z - 2, 0)
+        mx(z - 1, 1)
+        tq(z - 1, 0, "xt")
+        tu(z - 3)
+        lp_half(z, 0)
+        lp_half(z, 1)
+        ou(z - 4)
+        mx(z - 1, 0)
+        rr(z - 3)
+        ex(z - 2, 0)
+        ex(z - 1, 1)
+        tq(z, 1, "mx0")
+        tq(z, 0, "mx1")
+        tw(z - 2)
+        qr(z - 3)
+        mx(z, 1)
+        rc(z - 1)
+        mx(z, 0)
+        ex(z - 1, 0)
+        ex(z, 1)
+        ex(z, 0)
+        uv(z - 2, 0)
+        uv(z - 1, 1)
+        tu(z - 2, 0, "ut0")
+        tu(z - 1, 1, "q0")
+        rc(z)
+        rr(z - 2)
+        uv(z - 1, 0)
+        uv(z, 1)
+        tu(z - 1, 0, "q1")
+        tu(z, 1, "xt")
+        cw(z - 2)
+        out_scalar(z - 4)
+        ou(z - 3)
+        rc(z + 1)
+        rr(z - 1, 1)
+        uv(z, 0)
+        tu(z, 0, "mx0")
+        qr(z - 2)
+        ou(z - 2, "mx1")
+        out_scalar(z - 3)
+        rr(z - 1, 0)
+        rr(z, 1)
+        qr(z - 1)
+        ou(z - 1, "ut0")
+        rr(z, 0)
+        out_scalar(z - 2)
+        qr(z)
+        out_scalar(z - 1)
+        ou(z, "q0")
+        ov(z)
+        oscal(z)

@@ -155,14 +155,11 @@ def tile_ellipticalnormalizedrbfnet_t_kernel(tc, x, a, m, p_bytes, p_scale, lp, 
                 op1=ALU.mult,
             )
 
-        def qz(i):
-            codes = put("codes", i, work.tile([P, 2, TOK], U32, name="codes", align_bytes=64))
-            scales = put("scales", i, work.tile([P, 2, TOK], U8, name="scales", align_bytes=64))
-            nc.vector.quantize_mx(
-                out=codes[:].rearrange("p b r -> p (b r)").bitcast(FP8X4),
-                scales=scales[:].rearrange("p b r -> p (b r)"),
-                in_=get("hk", i)[:].rearrange("p b r -> p (b r)"),
-            )
+        def qz(i, b):
+            if b == 0:
+                put("codes", i, work.tile([P, 2, TOK], U32, name="codes", align_bytes=64))
+                put("scales", i, work.tile([P, 2, TOK], U8, name="scales", align_bytes=64))
+            nc.vector.quantize_mx(out=get("codes", i)[:, b, :].bitcast(FP8X4), scales=get("scales", i)[:, b, :], in_=get("hk", i)[:, b, :])
 
         def q_half(i, b):
             qt = put(("qt", b), i, psum.tile([P, 2, TOK], F32, name="mx" + str(b)))
@@ -194,7 +191,7 @@ def tile_ellipticalnormalizedrbfnet_t_kernel(tc, x, a, m, p_bytes, p_scale, lp, 
             q = put(("q", j), i, psum.tile([P, C], F32, name=bank or "q" + str(j)))
             ql = get("ql", i)
             for s in range(PACK):
-                turn(q[:, s * P : (s + 1) * P], ql[:, s, j * P : (j + 1) * P], plain=(j == 0 and s == 0))
+                turn(q[:, s * P : (s + 1) * P], ql[:, s, j * P : (j + 1) * P], plain=False)
 
         def mx(i, j):
             nm = put(("nm", j), i, work.tile([P, 1], F32, name="nm" + str(j)))
@@ -241,6 +238,26 @@ def tile_ellipticalnormalizedrbfnet_t_kernel(tc, x, a, m, p_bytes, p_scale, lp, 
                 put("r", i, work.tile([P, TOK, PACK], BF16, name="r", align_bytes=64))
             nc.vector.tensor_tensor(
                 out=get("r", i)[:, j * P : (j + 1) * P, :], in0=get(("ut", j), i)[:].rearrange("p s n -> p n s"), in1=gc_rep[:], op=ALU.mult
+            )
+
+        def dg(i):
+            diag = put("diag", i, work.tile([P, P], F32, name="diag"))
+            nc.vector.tensor_scalar(out=diag[:], in0=ident_ps, scalar1=get("rs", i + 1)[:, 0:1], scalar2=None, op0=ALU.mult)
+
+        def dm(i):
+            ut = put(("ut", 0), i, psum.tile([P, PACK, P], F32, name="ut0"))
+            e = get(("e", 0), i)
+            for s in range(PACK):
+                nc.tensor.matmul(ut[:, s, :], lhsT=e[:, s * P : (s + 1) * P], rhs=get("diag", i)[:], start=True, stop=True)
+
+        def rd(i):
+            nc.vector.scalar_tensor_tensor(
+                out=get("r", i)[:, 0:P, :],
+                in0=get(("ut", 0), i)[:].rearrange("p s n -> p n s"),
+                scalar=-1.0 / C,
+                in1=gc_rep[:],
+                op0=ALU.add,
+                op1=ALU.mult,
             )
 
         def gt(i):
@@ -300,8 +317,10 @@ def tile_ellipticalnormalizedrbfnet_t_kernel(tc, x, a, m, p_bytes, p_scale, lp, 
         tx(0, "q0")
         side = psum.tile([P, C], F32, name="side")
         rw = side[:, 0:TOK].rearrange("p (u n) -> p u n", u=2)
-        a_ps = side[:, TOK : TOK + PACK]
+        ident_ps = side[:, TOK : TOK + P]
+        a_ps = side[:, TOK + P : TOK + P + PACK]
         nc.tensor.matmul(a_ps, lhsT=ident[:], rhs=a_f[:], start=True, stop=True)
+        nc.tensor.transpose(ident_ps, ident[:], ident[:])
         tx(1, "ut0")
         tx(2)
         p_half(0)
@@ -313,7 +332,8 @@ def tile_ellipticalnormalizedrbfnet_t_kernel(tc, x, a, m, p_bytes, p_scale, lp, 
         m_half(1)
         quantise("p", 0, HALF)
         quantise("m", 0, HALF)
-        qz(0)
+        qz(0, 0)
+        qz(0, 1)
         sq(1)
         quantise("p", 1, HALF)
         quantise("m", 1, HALF)
@@ -334,33 +354,33 @@ def tile_ellipticalnormalizedrbfnet_t_kernel(tc, x, a, m, p_bytes, p_scale, lp, 
             quantise("w", 0, O)
 
         order = [
-            (7, ov, 0, PAIRS),
-            (5, lambda i: us(i, 0), 0, PAIRS),
+            (5, dg, 0, PAIRS),
             (4, lambda i: us(i, 1), 0, PAIRS),
             (4, gt, 0, PAIRS),
             (2, lambda i: q_half(i, 0), 0, PAIRS),
             (4, lambda i: mx(i, 0), 0, PAIRS),
             (5, cw, 0, PAIRS),
-            (7, oscal, 0, PAIRS),
+            (5, dm, 0, PAIRS),
+            (7, out_scalar, 0, PAIRS),
             (1, h, 0, PAIRS),
-            (5, tu, 0, PAIRS),
             (2, lambda i: lp_half(i, 0), 0, PAIRS),
             (3, lambda i: mx(i, 1), 0, PAIRS),
-            (0, tx, 3, PAIRS),
             (4, lambda i: ex(i, 0), 0, PAIRS),
-            (5, rr, 0, PAIRS),
-            (2, lambda i: q_half(i, 1), 0, PAIRS),
             (1, k, 0, PAIRS),
+            (2, lambda i: q_half(i, 1), 0, PAIRS),
             (3, lambda i: ex(i, 1), 0, PAIRS),
             (6, ou, 0, PAIRS),
-            (3, lambda i: tq(i, 0), 0, PAIRS),
+            (0, tx, 3, PAIRS),
+            (5, rd, 0, PAIRS),
             (2, lambda i: lp_half(i, 1), 0, PAIRS),
-            (5, qr, 0, PAIRS),
-            (0, sq, 0, PAIRS),
-            (3, rc, 0, PAIRS + 1),
-            (2, lambda i: tq(i, 1), 0, PAIRS),
-            (1, qz, 0, PAIRS),
+            (3, lambda i: tq(i, 0), 0, PAIRS),
+            (1, lambda i: qz(i, 0), 0, PAIRS),
             (4, tw, 0, PAIRS),
+            (0, sq, 0, PAIRS),
+            (5, qr, 0, PAIRS),
+            (2, lambda i: tq(i, 1), 0, PAIRS),
+            (3, rc, 0, PAIRS + 1),
+            (1, lambda i: qz(i, 1), 0, PAIRS),
         ]
         for step in range(2, PAIRS + 1):
             for lag, stage, first, last in order:
@@ -370,23 +390,22 @@ def tile_ellipticalnormalizedrbfnet_t_kernel(tc, x, a, m, p_bytes, p_scale, lp, 
                 late_constants()
 
         z = PAIRS - 1
-        ov(z - 5)
-        us(z - 3, 0)
+        dg(z - 3)
         us(z - 2, 1)
         gt(z - 2)
         q_half(z, 0)
         q_half(z, 1)
         cw(z - 3)
-        oscal(z - 5)
+        out_scalar(z - 5)
         mx(z - 2, 0)
         mx(z - 1, 1)
         tq(z - 1, 0, "xt")
-        tu(z - 3)
+        dm(z - 3)
         lp_half(z, 0)
         lp_half(z, 1)
         ou(z - 4)
         mx(z - 1, 0)
-        rr(z - 3)
+        rd(z - 3)
         ex(z - 2, 0)
         ex(z - 1, 1)
         tq(z, 1, "mx0")

@@ -155,11 +155,14 @@ def tile_ellipticalnormalizedrbfnet_t_kernel(tc, x, a, m, p_bytes, p_scale, lp, 
                 op1=ALU.mult,
             )
 
-        def qz(i, b):
-            if b == 0:
-                put("codes", i, work.tile([P, 2, TOK], U32, name="codes", align_bytes=64))
-                put("scales", i, work.tile([P, 2, TOK], U8, name="scales", align_bytes=64))
-            nc.vector.quantize_mx(out=get("codes", i)[:, b, :].bitcast(FP8X4), scales=get("scales", i)[:, b, :], in_=get("hk", i)[:, b, :])
+        def qz(i):
+            codes = put("codes", i, work.tile([P, 2, TOK], U32, name="codes", align_bytes=64))
+            scales = put("scales", i, work.tile([P, 2, TOK], U8, name="scales", align_bytes=64))
+            nc.vector.quantize_mx(
+                out=codes[:].rearrange("p b r -> p (b r)").bitcast(FP8X4),
+                scales=scales[:].rearrange("p b r -> p (b r)"),
+                in_=get("hk", i)[:].rearrange("p b r -> p (b r)"),
+            )
 
         def q_half(i, b):
             qt = put(("qt", b), i, psum.tile([P, 2, TOK], F32, name="mx" + str(b)))
@@ -242,7 +245,7 @@ def tile_ellipticalnormalizedrbfnet_t_kernel(tc, x, a, m, p_bytes, p_scale, lp, 
 
         def dg(i):
             diag = put("diag", i, work.tile([P, P], F32, name="diag"))
-            nc.vector.tensor_scalar(out=diag[:], in0=ident_ps, scalar1=get("rs", i + 1)[:, 0:1], scalar2=None, op0=ALU.mult)
+            gp_copy(diag[:], ident[:], get("rs", i + 1)[:, 0:1])
 
         def dm(i):
             ut = put(("ut", 0), i, psum.tile([P, PACK, P], F32, name="ut0"))
@@ -317,10 +320,8 @@ def tile_ellipticalnormalizedrbfnet_t_kernel(tc, x, a, m, p_bytes, p_scale, lp, 
         tx(0, "q0")
         side = psum.tile([P, C], F32, name="side")
         rw = side[:, 0:TOK].rearrange("p (u n) -> p u n", u=2)
-        ident_ps = side[:, TOK : TOK + P]
-        a_ps = side[:, TOK + P : TOK + P + PACK]
+        a_ps = side[:, TOK : TOK + PACK]
         nc.tensor.matmul(a_ps, lhsT=ident[:], rhs=a_f[:], start=True, stop=True)
-        nc.tensor.transpose(ident_ps, ident[:], ident[:])
         tx(1, "ut0")
         tx(2)
         p_half(0)
@@ -332,9 +333,9 @@ def tile_ellipticalnormalizedrbfnet_t_kernel(tc, x, a, m, p_bytes, p_scale, lp, 
         m_half(1)
         quantise("p", 0, HALF)
         quantise("m", 0, HALF)
-        qz(0, 0)
-        qz(0, 1)
+        qz(0)
         sq(1)
+        q_half(0, 0)
         quantise("p", 1, HALF)
         quantise("m", 1, HALF)
         lp_f = keep.tile([P, PACK], F32, name="lp_f")
@@ -357,7 +358,6 @@ def tile_ellipticalnormalizedrbfnet_t_kernel(tc, x, a, m, p_bytes, p_scale, lp, 
             (5, dg, 0, PAIRS),
             (4, lambda i: us(i, 1), 0, PAIRS),
             (4, gt, 0, PAIRS),
-            (2, lambda i: q_half(i, 0), 0, PAIRS),
             (4, lambda i: mx(i, 0), 0, PAIRS),
             (5, cw, 0, PAIRS),
             (5, dm, 0, PAIRS),
@@ -374,13 +374,13 @@ def tile_ellipticalnormalizedrbfnet_t_kernel(tc, x, a, m, p_bytes, p_scale, lp, 
             (5, rd, 0, PAIRS),
             (2, lambda i: lp_half(i, 1), 0, PAIRS),
             (3, lambda i: tq(i, 0), 0, PAIRS),
-            (1, lambda i: qz(i, 0), 0, PAIRS),
+            (1, qz, 0, PAIRS),
             (4, tw, 0, PAIRS),
             (0, sq, 0, PAIRS),
-            (5, qr, 0, PAIRS),
             (2, lambda i: tq(i, 1), 0, PAIRS),
             (3, rc, 0, PAIRS + 1),
-            (1, lambda i: qz(i, 1), 0, PAIRS),
+            (5, qr, 0, PAIRS),
+            (1, lambda i: q_half(i, 0), 0, PAIRS),
         ]
         for step in range(2, PAIRS + 1):
             for lag, stage, first, last in order:
@@ -393,7 +393,6 @@ def tile_ellipticalnormalizedrbfnet_t_kernel(tc, x, a, m, p_bytes, p_scale, lp, 
         dg(z - 3)
         us(z - 2, 1)
         gt(z - 2)
-        q_half(z, 0)
         q_half(z, 1)
         cw(z - 3)
         out_scalar(z - 5)

@@ -22,7 +22,7 @@ J = 2
 TOK = J * P
 PAIRS = N // TOK
 HALF = C // 2
-OUT_V = 144
+WORDS_V = 3
 DRAIN = PAIRS - 2
 AHEAD = 4
 
@@ -75,10 +75,6 @@ def tile_ellipticalnormalizedrbfnet_t_kernel(tc, x, a, m, p_bytes, p_scale, lp, 
 
         ident = keep.tile([P, P], F32, name="ident")
         make_identity(nc, ident[:])
-        warm = keep.tile([P, 1], F32, name="warm")
-        nc.gpsimd.memset(warm[:], 0.0)
-        warm2 = keep.tile([P, 1], F32, name="warm2")
-        nc.scalar.activation(out=warm2[:], in_=warm[:], func=ACT.Exp, bias=0.0, scale=1.0)
 
         def gp_copy(dst, src, factor=1.0):
             nc.gpsimd.tensor_scalar(out=dst, in0=src, scalar1=factor, scalar2=0.0, op0=ALU.mult, op1=ALU.add)
@@ -230,6 +226,32 @@ def tile_ellipticalnormalizedrbfnet_t_kernel(tc, x, a, m, p_bytes, p_scale, lp, 
                 out=u[:], in0=get(("e", j), i)[:], scalar1=get("rs", i + 1 - j)[:, j : j + 1], scalar2=-1.0 / C, op0=ALU.mult, op1=ALU.add
             )
 
+        def ua(i, j):
+            u = put(("u", j), i, work.tile([P, C], F32, name="u" + str(j)))
+            nc.scalar.activation(
+                out=u[:], in_=get(("e", j), i)[:], func=ACT.Identity, scale=get("rs", i + 1 - j)[:, j : j + 1], bias=minus_mean[:]
+            )
+
+        def last_out(i):
+            w_codes, w_scales = get("w", 0)
+            for j, bank in enumerate(("q0", "q1")):
+                o_ps = put(("o_last", j), i, psum.tile([P, O], F32, name=bank))
+                cols = slice(j * P, (j + 1) * P)
+                nc.tensor.matmul_mx(
+                    out=o_ps[:],
+                    lhsT=get("rcodes", i)[:, cols].bitcast(FP8X4),
+                    lhsT_scale=get("rscales", i)[:, cols],
+                    rhs=w_codes[:].bitcast(FP8X4),
+                    rhs_scale=w_scales[:],
+                    start=True,
+                    stop=True,
+                )
+            o_sb = work.tile([P, J * O], F32, name="o_sb")
+            nc.vector.tensor_copy(out=o_sb[:, 0:O], in_=get(("o_last", 0), i)[:])
+            nc.sync.dma_start(out=out_v[i][:, 0, :], in_=o_sb[:, 0:O])
+            nc.scalar.copy(out=o_sb[:, O:], in_=get(("o_last", 1), i)[:])
+            nc.scalar.dma_start(out=out_v[i][:, 1, :], in_=o_sb[:, O:])
+
         def tu(i, j=0, bank="ut0"):
             ut = put(("ut", j), i, psum.tile([P, PACK, P], F32, name=bank))
             u = get(("u", j), i)
@@ -276,7 +298,8 @@ def tile_ellipticalnormalizedrbfnet_t_kernel(tc, x, a, m, p_bytes, p_scale, lp, 
             if ("r", i) not in st:
                 put("r", i, work.tile([P, TOK, PACK], BF16, name="r", align_bytes=64))
             words = get("r", i)[:, P:TOK, :].rearrange("p n s -> p (n s)").bitcast(F32)
-            nc.scalar.copy(out=words.rearrange("p (n u) -> p n u", u=2), in_=rw.rearrange("p u n -> p n u"))
+            copy = nc.vector.tensor_copy if i % WORDS_V == 0 else nc.scalar.copy
+            copy(out=words.rearrange("p (n u) -> p n u", u=2), in_=rw.rearrange("p u n -> p n u"))
 
         def qr(i):
             rcodes = put("rcodes", i, work.tile([P, TOK], U32, name="rcodes", align_bytes=64))
@@ -297,15 +320,6 @@ def tile_ellipticalnormalizedrbfnet_t_kernel(tc, x, a, m, p_bytes, p_scale, lp, 
                     start=True,
                     stop=True,
                 )
-
-        def ov(i):
-            o_sb = put("o_sb", i, work.tile([P, J * O], F32, name="o_sb"))
-            nc.vector.tensor_copy(out=o_sb[:, 0:OUT_V], in_=get("o_ps", i)[:, 0:OUT_V])
-
-        def oscal(i):
-            o_sb = get("o_sb", i)
-            nc.scalar.copy(out=o_sb[:, OUT_V:], in_=get("o_ps", i)[:, OUT_V:])
-            nc.sync.dma_start(out=out_v[i], in_=o_sb[:].rearrange("p (j o) -> p j o", j=J))
 
         def out_scalar(i):
             o_sb = work.tile([P, J * O], F32, name="o_sb")
@@ -345,6 +359,8 @@ def tile_ellipticalnormalizedrbfnet_t_kernel(tc, x, a, m, p_bytes, p_scale, lp, 
         gc_rep = keep.tile([P, P, PACK], F32, name="gc_rep", align_bytes=64)
         gp_copy(gc_rep[:], gc_sb[:].unsqueeze(1).to_broadcast([P, P, PACK]), float(C))
         gc_tok = keep.tile([P, C], F32, name="gc_tok")
+        minus_mean = keep.tile([P, 1], F32, name="minus_mean")
+        nc.gpsimd.memset(minus_mean[:], -1.0 / C)
 
         def late_constants():
             gc_ps = psum.tile([P, PACK, P], F32, name="o_ps")
@@ -400,39 +416,39 @@ def tile_ellipticalnormalizedrbfnet_t_kernel(tc, x, a, m, p_bytes, p_scale, lp, 
         mx(z - 1, 1)
         tq(z - 1, 0, "xt")
         dm(z - 3)
+        ex(z - 2, 0)
         lp_half(z, 0)
         lp_half(z, 1)
         ou(z - 4)
         mx(z - 1, 0)
         rd(z - 3)
-        ex(z - 2, 0)
         ex(z - 1, 1)
         tq(z, 1, "mx0")
         tq(z, 0, "mx1")
         tw(z - 2)
         qr(z - 3)
-        mx(z, 1)
         rc(z - 1)
+        us(z - 2, 0)
+        us(z - 1, 1)
+        mx(z, 1)
         mx(z, 0)
         ex(z - 1, 0)
         ex(z, 1)
         ex(z, 0)
-        uv(z - 2, 0)
-        uv(z - 1, 1)
         tu(z - 2, 0, "ut0")
         tu(z - 1, 1, "q0")
         rc(z)
-        rr(z - 2)
-        uv(z - 1, 0)
-        uv(z, 1)
+        us(z - 1, 0)
+        ua(z, 1)
+        rr(z - 2, 0)
+        cw(z - 2)
         tu(z - 1, 0, "q1")
         tu(z, 1, "xt")
-        cw(z - 2)
+        rc(z + 1)
+        uv(z, 0)
+        rr(z - 1, 1)
         out_scalar(z - 4)
         ou(z - 3)
-        rc(z + 1)
-        rr(z - 1, 1)
-        uv(z, 0)
         tu(z, 0, "mx0")
         qr(z - 2)
         ou(z - 2, "mx1")
@@ -445,6 +461,4 @@ def tile_ellipticalnormalizedrbfnet_t_kernel(tc, x, a, m, p_bytes, p_scale, lp, 
         out_scalar(z - 2)
         qr(z)
         out_scalar(z - 1)
-        ou(z, "q0")
-        ov(z)
-        oscal(z)
+        last_out(z)

@@ -64,11 +64,11 @@ def tile_ellipticalnormalizedrbfnet_t_kernel(tc, x, a, m, p_bytes, p_scale, lp, 
             nc.sync.dma_start(out=m_sb[:], in_=m.rearrange("(p t) c -> p t c", t=PACK)[:, :, b * HALF : (b + 1) * HALF])
         load(1)
         load(2)
+        gc_sb = keep.tile([P, PACK], BF16, name="gc_sb")
+        nc.sync.dma_start(out=gc_sb[:], in_=gc.rearrange("(p t) -> p t", t=PACK))
         lp_sb = keep.tile([P, PACK, 2], BF16, name="lp_sb")
         with nc.allow_non_contiguous_dma("512 values, one to a partition and slice"):
             nc.sync.dma_start(out=lp_sb[:, :, 0:1], in_=lp.rearrange("(s p o) -> p s o", p=P, o=1))
-        gc_sb = keep.tile([P, PACK], BF16, name="gc_sb")
-        nc.sync.dma_start(out=gc_sb[:], in_=gc.rearrange("(p t) -> p t", t=PACK))
         w_sb = keep.tile([P, PACK, O], BF16, name="w_sb")
         nc.sync.dma_start(out=w_sb[:], in_=w.rearrange("(p t) o -> p t o", t=PACK))
         load(3)
@@ -190,7 +190,7 @@ def tile_ellipticalnormalizedrbfnet_t_kernel(tc, x, a, m, p_bytes, p_scale, lp, 
             q = put(("q", j), i, psum.tile([P, C], F32, name=bank or "q" + str(j)))
             ql = get("ql", i)
             for s in range(PACK):
-                turn(q[:, s * P : (s + 1) * P], ql[:, s, j * P : (j + 1) * P], plain=False)
+                turn(q[:, s * P : (s + 1) * P], ql[:, s, j * P : (j + 1) * P], plain=(j == 0 and s == PACK - 1))
 
         def mx(i, j):
             nm = put(("nm", j), i, work.tile([P, 1], F32, name="nm" + str(j)))
@@ -349,13 +349,17 @@ def tile_ellipticalnormalizedrbfnet_t_kernel(tc, x, a, m, p_bytes, p_scale, lp, 
         quantise("m", 0, HALF)
         qz(0)
         sq(1)
+        gc_f = keep.tile([P, PACK], F32, name="gc_f")
+        gp_copy(gc_f[:], gc_sb[:], float(C))
+        gc_ps = psum.tile([P, PACK, P], F32, name="o_ps")
+        for t in range(PACK):
+            nc.tensor.matmul(gc_ps[:, t, :], lhsT=gc_f[:, t : t + 1].to_broadcast([P, P]), rhs=ident[:], start=True, stop=True)
         q_half(0, 0)
         quantise("p", 1, HALF)
         quantise("m", 1, HALF)
+        sq(2)
         lp_f = keep.tile([P, PACK], F32, name="lp_f")
         gp_copy(lp_f[:], lp_sb[:, :, 0])
-        gc_f = keep.tile([P, PACK], F32, name="gc_f")
-        gp_copy(gc_f[:], gc_sb[:], float(C))
         gc_rep = keep.tile([P, P, PACK], F32, name="gc_rep", align_bytes=64)
         gp_copy(gc_rep[:], gc_sb[:].unsqueeze(1).to_broadcast([P, P, PACK]), float(C))
         gc_tok = keep.tile([P, C], F32, name="gc_tok")
@@ -363,9 +367,6 @@ def tile_ellipticalnormalizedrbfnet_t_kernel(tc, x, a, m, p_bytes, p_scale, lp, 
         nc.gpsimd.memset(minus_mean[:], -1.0 / C)
 
         def late_constants():
-            gc_ps = psum.tile([P, PACK, P], F32, name="o_ps")
-            for t in range(PACK):
-                nc.tensor.transpose(gc_ps[:, t, :], gc_f[:, t : t + 1].to_broadcast([P, P]), ident[:])
             nc.scalar.copy(out=gc_tok[:].rearrange("n (u p e) -> n u p e", u=2, e=2), in_=gc_ps[:].rearrange("n (u e) p -> n u p e", u=2))
             gp_copy(interleaved("w", 0, O), by_fours(w_sb[:]))
             quantise("w", 0, O)
@@ -385,14 +386,14 @@ def tile_ellipticalnormalizedrbfnet_t_kernel(tc, x, a, m, p_bytes, p_scale, lp, 
             (1, k, 0, PAIRS),
             (2, lambda i: q_half(i, 1), 0, PAIRS),
             (3, lambda i: ex(i, 1), 0, PAIRS),
-            (6, ou, 0, PAIRS),
             (0, tx, 3, PAIRS),
             (5, rd, 0, PAIRS),
             (2, lambda i: lp_half(i, 1), 0, PAIRS),
             (3, lambda i: tq(i, 0), 0, PAIRS),
+            (6, ou, 0, PAIRS),
             (1, qz, 0, PAIRS),
             (4, tw, 0, PAIRS),
-            (0, sq, 0, PAIRS),
+            (0, sq, 3, PAIRS),
             (2, lambda i: tq(i, 1), 0, PAIRS),
             (3, rc, 0, PAIRS + 1),
             (5, qr, 0, PAIRS),

@@ -186,11 +186,11 @@ def tile_ellipticalnormalizedrbfnet_t_kernel(tc, x, a, m, p_bytes, p_scale, lp, 
                 s = 2 * b + s2
                 nc.scalar.activation(out=ql[:, s, :], in_=qt[:, s2, :], func=ACT.Identity, bias=lp_f[:, s : s + 1], scale=1.0)
 
-        def tq(i, j, bank=None):
+        def tq(i, j, bank=None, plain=0):
             q = put(("q", j), i, psum.tile([P, C], F32, name=bank or "q" + str(j)))
             ql = get("ql", i)
             for s in range(PACK):
-                turn(q[:, s * P : (s + 1) * P], ql[:, s, j * P : (j + 1) * P], plain=(j == 0 and s == PACK - 1))
+                turn(q[:, s * P : (s + 1) * P], ql[:, s, j * P : (j + 1) * P], plain=(s >= PACK - plain))
 
         def mx(i, j):
             nm = put(("nm", j), i, work.tile([P, 1], F32, name="nm" + str(j)))
@@ -209,10 +209,10 @@ def tile_ellipticalnormalizedrbfnet_t_kernel(tc, x, a, m, p_bytes, p_scale, lp, 
                 q_v = get(("q", j), i)[:].rearrange("n (p u e) -> n u p e", u=2, e=2)
             nc.scalar.activation(out=e_v, in_=q_v, func=ACT.Exp, bias=get(("nm", j), i)[:], scale=1.0, accum_out=get("ssum", g)[:, j : j + 1])
 
-        def rc(g):
-            cols = slice(1 if g == 0 else 0, 1 if g == PAIRS else J)
-            rs = put("rs", g, work.tile([P, J], F32, name="rs"))
-            nc.vector.reciprocal(out=rs[:, cols], in_=get("ssum", g)[:, cols])
+        def rc(g, first=0, last=J):
+            if ("rs", g) not in st:
+                put("rs", g, work.tile([P, J], F32, name="rs"))
+            nc.vector.reciprocal(out=get("rs", g)[:, first:last], in_=get("ssum", g)[:, first:last])
 
         def us(i, j):
             u = put(("u", j), i, work.tile([P, C], F32, name="u" + str(j)))
@@ -232,25 +232,33 @@ def tile_ellipticalnormalizedrbfnet_t_kernel(tc, x, a, m, p_bytes, p_scale, lp, 
                 out=u[:], in_=get(("e", j), i)[:], func=ACT.Identity, scale=get("rs", i + 1 - j)[:, j : j + 1], bias=minus_mean[:]
             )
 
-        def last_out(i):
+        def qr_tile(i, j):
+            if j == 1:
+                put("rcodes", i, work.tile([P, TOK], U32, name="rcodes", align_bytes=64))
+                put("rscales", i, work.tile([P, TOK], U8, name="rscales", align_bytes=64))
+            cols = slice(j * P, (j + 1) * P)
+            nc.vector.quantize_mx(
+                out=get("rcodes", i)[:, cols].bitcast(FP8X4),
+                scales=get("rscales", i)[:, cols],
+                in_=get("r", i)[:, cols, :].rearrange("p n s -> p (n s)"),
+            )
+
+        def out_tile(i, j, bank, copy, queue):
             w_codes, w_scales = get("w", 0)
-            for j, bank in enumerate(("q0", "q1")):
-                o_ps = put(("o_last", j), i, psum.tile([P, O], F32, name=bank))
-                cols = slice(j * P, (j + 1) * P)
-                nc.tensor.matmul_mx(
-                    out=o_ps[:],
-                    lhsT=get("rcodes", i)[:, cols].bitcast(FP8X4),
-                    lhsT_scale=get("rscales", i)[:, cols],
-                    rhs=w_codes[:].bitcast(FP8X4),
-                    rhs_scale=w_scales[:],
-                    start=True,
-                    stop=True,
-                )
-            o_sb = work.tile([P, J * O], F32, name="o_sb")
-            nc.vector.tensor_copy(out=o_sb[:, 0:O], in_=get(("o_last", 0), i)[:])
-            nc.sync.dma_start(out=out_v[i][:, 0, :], in_=o_sb[:, 0:O])
-            nc.scalar.copy(out=o_sb[:, O:], in_=get(("o_last", 1), i)[:])
-            nc.scalar.dma_start(out=out_v[i][:, 1, :], in_=o_sb[:, O:])
+            o_ps = psum.tile([P, O], F32, name=bank)
+            cols = slice(j * P, (j + 1) * P)
+            nc.tensor.matmul_mx(
+                out=o_ps[:],
+                lhsT=get("rcodes", i)[:, cols].bitcast(FP8X4),
+                lhsT_scale=get("rscales", i)[:, cols],
+                rhs=w_codes[:].bitcast(FP8X4),
+                rhs_scale=w_scales[:],
+                start=True,
+                stop=True,
+            )
+            o_sb = work.tile([P, O], F32, name="o_last")
+            copy(out=o_sb[:], in_=o_ps[:])
+            queue.dma_start(out=out_v[i][:, j, :], in_=o_sb[:])
 
         def tu(i, j=0, bank="ut0"):
             ut = put(("ut", j), i, psum.tile([P, PACK, P], F32, name=bank))
@@ -258,26 +266,29 @@ def tile_ellipticalnormalizedrbfnet_t_kernel(tc, x, a, m, p_bytes, p_scale, lp, 
             for s in range(PACK):
                 nc.tensor.transpose(ut[:, s, :], u[:, s * P : (s + 1) * P], ident[:])
 
-        def rr(i, j=0):
+        def r_tile(i):
             if ("r", i) not in st:
                 put("r", i, work.tile([P, TOK, PACK], BF16, name="r", align_bytes=64))
+            return get("r", i)
+
+        def rr(i, j=0):
             nc.vector.tensor_tensor(
-                out=get("r", i)[:, j * P : (j + 1) * P, :], in0=get(("ut", j), i)[:].rearrange("p s n -> p n s"), in1=gc_rep[:], op=ALU.mult
+                out=r_tile(i)[:, j * P : (j + 1) * P, :], in0=get(("ut", j), i)[:].rearrange("p s n -> p n s"), in1=gc_rep[:], op=ALU.mult
             )
 
         def dg(i):
             diag = put("diag", i, work.tile([P, P], F32, name="diag"))
             gp_copy(diag[:], ident[:], get("rs", i + 1)[:, 0:1])
 
-        def dm(i):
-            ut = put(("ut", 0), i, psum.tile([P, PACK, P], F32, name="ut0"))
+        def dm(i, bank="ut0"):
+            ut = put(("ut", 0), i, psum.tile([P, PACK, P], F32, name=bank))
             e = get(("e", 0), i)
             for s in range(PACK):
                 nc.tensor.matmul(ut[:, s, :], lhsT=e[:, s * P : (s + 1) * P], rhs=get("diag", i)[:], start=True, stop=True)
 
         def rd(i):
             nc.vector.scalar_tensor_tensor(
-                out=get("r", i)[:, 0:P, :],
+                out=r_tile(i)[:, 0:P, :],
                 in0=get(("ut", 0), i)[:].rearrange("p s n -> p n s"),
                 scalar=-1.0 / C,
                 in1=gc_rep[:],
@@ -295,9 +306,7 @@ def tile_ellipticalnormalizedrbfnet_t_kernel(tc, x, a, m, p_bytes, p_scale, lp, 
                 nc.tensor.transpose(rw[:, u, :], words[:, u * P : (u + 1) * P], ident[:])
 
         def cw(i):
-            if ("r", i) not in st:
-                put("r", i, work.tile([P, TOK, PACK], BF16, name="r", align_bytes=64))
-            words = get("r", i)[:, P:TOK, :].rearrange("p n s -> p (n s)").bitcast(F32)
+            words = r_tile(i)[:, P:TOK, :].rearrange("p n s -> p (n s)").bitcast(F32)
             copy = nc.vector.tensor_copy if i % WORDS_V == 0 else nc.scalar.copy
             copy(out=words.rearrange("p (n u) -> p n u", u=2), in_=rw.rearrange("p u n -> p n u"))
 
@@ -389,17 +398,17 @@ def tile_ellipticalnormalizedrbfnet_t_kernel(tc, x, a, m, p_bytes, p_scale, lp, 
             (0, tx, 3, PAIRS),
             (5, rd, 0, PAIRS),
             (2, lambda i: lp_half(i, 1), 0, PAIRS),
-            (3, lambda i: tq(i, 0), 0, PAIRS),
+            (3, lambda i: tq(i, 0, plain=2 if i < 3 else 1), 0, PAIRS),
             (6, ou, 0, PAIRS),
             (1, qz, 0, PAIRS),
             (4, tw, 0, PAIRS),
             (0, sq, 3, PAIRS),
             (2, lambda i: tq(i, 1), 0, PAIRS),
-            (3, rc, 0, PAIRS + 1),
+            (3, lambda g: rc(g, first=1 if g == 0 else 0), 0, PAIRS),
             (5, qr, 0, PAIRS),
             (1, lambda i: q_half(i, 0), 0, PAIRS),
         ]
-        for step in range(2, PAIRS + 1):
+        for step in range(2, PAIRS):
             for lag, stage, first, last in order:
                 if first <= step - lag < last:
                     stage(step - lag)
@@ -407,59 +416,86 @@ def tile_ellipticalnormalizedrbfnet_t_kernel(tc, x, a, m, p_bytes, p_scale, lp, 
                 late_constants()
 
         z = PAIRS - 1
-        dg(z - 3)
-        us(z - 2, 1)
-        gt(z - 2)
+        dg(z - 4)
+        us(z - 3, 1)
+        gt(z - 3)
+        cw(z - 4)
+        h(z)
+        mx(z - 3, 0)
+        dm(z - 4)
+        lp_half(z - 1, 0)
+        k(z)
+        ex(z - 3, 0)
+        q_half(z - 1, 1)
+        out_scalar(z - 6)
+        mx(z - 2, 1)
+        tq(z - 2, 0)
+        lp_half(z - 1, 1)
+        ou(z - 5)
+        qz(z)
+        tw(z - 3)
+        ex(z - 2, 1)
+        tq(z - 1, 1, "xt")
+        rd(z - 4)
+        q_half(z, 0)
         q_half(z, 1)
-        cw(z - 3)
         out_scalar(z - 5)
         mx(z - 2, 0)
-        mx(z - 1, 1)
-        tq(z - 1, 0, "xt")
-        dm(z - 3)
+        rc(z - 2)
+        qr(z - 4)
+        dg(z - 3)
+        us(z - 2, 1)
+        tq(z - 1, 0, "q1")
+        ou(z - 4)
         ex(z - 2, 0)
         lp_half(z, 0)
+        mx(z - 1, 1)
+        rc(z - 1, 0, 1)
+        dg(z - 2)
+        gt(z - 2)
+        dm(z - 3)
         lp_half(z, 1)
-        ou(z - 4)
         mx(z - 1, 0)
-        rd(z - 3)
         ex(z - 1, 1)
-        tq(z, 1, "mx0")
-        tq(z, 0, "mx1")
-        tw(z - 2)
-        qr(z - 3)
-        rc(z - 1)
-        us(z - 2, 0)
-        us(z - 1, 1)
-        mx(z, 1)
-        mx(z, 0)
+        cw(z - 3)
+        tq(z, 1, "q0")
+        tq(z, 0, "xt")
+        rd(z - 3)
+        dm(z - 2, "mx0")
         ex(z - 1, 0)
+        mx(z, 1)
+        qr(z - 3)
+        rc(z - 1, 1, 2)
+        us(z - 1, 1)
+        mx(z, 0)
         ex(z, 1)
         ex(z, 0)
-        tu(z - 2, 0, "ut0")
-        tu(z - 1, 1, "q0")
+        tw(z - 2)
+        ou(z - 3, "ut0")
+        rd(z - 2)
         rc(z)
-        us(z - 1, 0)
+        uv(z - 1, 0)
         ua(z, 1)
-        rr(z - 2, 0)
-        cw(z - 2)
+        tu(z - 1, 1, "mx1")
         tu(z - 1, 0, "q1")
-        tu(z, 1, "xt")
-        rc(z + 1)
+        rc(z + 1, 0, 1)
         uv(z, 0)
+        cw(z - 2)
+        tu(z, 1, "q0")
+        tu(z, 0, "xt")
         rr(z - 1, 1)
         out_scalar(z - 4)
-        ou(z - 3)
-        tu(z, 0, "mx0")
         qr(z - 2)
-        ou(z - 2, "mx1")
-        out_scalar(z - 3)
         rr(z - 1, 0)
+        ou(z - 2)
+        out_scalar(z - 3)
         rr(z, 1)
         qr(z - 1)
-        ou(z - 1, "ut0")
         rr(z, 0)
+        ou(z - 1, "mx0")
         out_scalar(z - 2)
-        qr(z)
+        qr_tile(z, 1)
         out_scalar(z - 1)
-        last_out(z)
+        out_tile(z, 1, "q1", nc.scalar.copy, nc.scalar)
+        qr_tile(z, 0)
+        out_tile(z, 0, "mx1", nc.vector.tensor_copy, nc.sync)

@@ -22,7 +22,6 @@ J = 2
 TOK = J * P
 PAIRS = N // TOK
 HALF = C // 2
-WORDS_V = 3
 DRAIN = PAIRS - 2
 AHEAD = 4
 
@@ -307,8 +306,7 @@ def tile_ellipticalnormalizedrbfnet_t_kernel(tc, x, a, m, p_bytes, p_scale, lp, 
 
         def cw(i):
             words = r_tile(i)[:, P:TOK, :].rearrange("p n s -> p (n s)").bitcast(F32)
-            copy = nc.vector.tensor_copy if i % WORDS_V == 0 else nc.scalar.copy
-            copy(out=words.rearrange("p (n u) -> p n u", u=2), in_=rw.rearrange("p u n -> p n u"))
+            nc.scalar.copy(out=words.rearrange("p (n u) -> p n u", u=2), in_=rw.rearrange("p u n -> p n u"))
 
         def qr(i):
             rcodes = put("rcodes", i, work.tile([P, TOK], U32, name="rcodes", align_bytes=64))

@@ -94,15 +94,10 @@ def tile_ellipticalnormalizedrbfnet_t_kernel(tc, x, a, m, p_bytes, p_scale, lp, 
         def by_fours(rows):
             return rows.rearrange("p t (c i) -> p c t i", i=4)
 
-        nps = keep.tile([P, PACK], F32, name="nps")
+        p_w = keep.tile([P, PACK, C], BF16, name="p_w")
 
         def p_half(b):
-            p_w = keep.tile([P, PACK, HALF], BF16, name="p_w" + str(b))
-            for t in range(PACK):
-                nc.vector.tensor_scalar(
-                    out=p_w[:, t, :], in0=pb_sb[:, t, b * HALF : (b + 1) * HALF].bitcast(FP8), scalar1=nps[:, t : t + 1], scalar2=None, op0=ALU.mult
-                )
-            nc.vector.tensor_copy(out=interleaved("p", b, HALF), in_=by_fours(p_w[:]))
+            nc.vector.tensor_copy(out=interleaved("p", b, HALF), in_=by_fours(p_w[:, :, b * HALF : (b + 1) * HALF]))
 
         def m_half(b):
             nc.scalar.copy(out=interleaved("m", b, HALF), in_=by_fours(get("m_sb", b)[:]))
@@ -333,9 +328,10 @@ def tile_ellipticalnormalizedrbfnet_t_kernel(tc, x, a, m, p_bytes, p_scale, lp, 
             nc.scalar.copy(out=o_sb[:], in_=get("o_ps", i)[:])
             nc.sync.dma_start(out=out_v[i], in_=o_sb[:].rearrange("p (j o) -> p j o", j=J))
 
-        nc.vector.tensor_scalar(out=nps[:], in0=ps_sb[:], scalar1=-1.0, scalar2=None, op0=ALU.mult)
+        for t in range(PACK):
+            nc.vector.tensor_scalar(out=p_w[:, t, :], in0=pb_sb[:, t, :].bitcast(FP8), scalar1=ps_sb[:, t : t + 1], scalar2=None, op0=ALU.mult)
         a_f = keep.tile([P, PACK], F32, name="a_f")
-        gp_copy(a_f[:], a_sb[:])
+        gp_copy(a_f[:], a_sb[:], -1.0)
         a_rep = keep.tile([P, TOK, PACK], BF16, name="a_rep", align_bytes=64)
         gp_copy(a_rep[:], a_sb[:].unsqueeze(1).to_broadcast([P, TOK, PACK]))
         tx(0, "q0")
@@ -373,10 +369,12 @@ def tile_ellipticalnormalizedrbfnet_t_kernel(tc, x, a, m, p_bytes, p_scale, lp, 
         minus_mean = keep.tile([P, 1], F32, name="minus_mean")
         nc.gpsimd.memset(minus_mean[:], -1.0 / C)
 
-        def late_constants():
-            nc.scalar.copy(out=gc_tok[:].rearrange("n (u p e) -> n u p e", u=2, e=2), in_=gc_ps[:].rearrange("n (u e) p -> n u p e", u=2))
+        def w_operand(i):
             gp_copy(interleaved("w", 0, O), by_fours(w_sb[:]))
             quantise("w", 0, O)
+
+        def gc_rows(i):
+            nc.scalar.copy(out=gc_tok[:].rearrange("n (u p e) -> n u p e", u=2, e=2), in_=gc_ps[:].rearrange("n (u e) p -> n u p e", u=2))
 
         order = [
             (5, dg, 0, PAIRS),
@@ -395,6 +393,7 @@ def tile_ellipticalnormalizedrbfnet_t_kernel(tc, x, a, m, p_bytes, p_scale, lp, 
             (3, lambda i: ex(i, 1), 0, PAIRS),
             (0, tx, 3, PAIRS),
             (5, rd, 0, PAIRS),
+            (2, w_operand, 0, 1),
             (2, lambda i: lp_half(i, 1), 0, PAIRS),
             (3, lambda i: tq(i, 0, plain=2 if i < 3 else 1), 0, PAIRS),
             (6, ou, 0, PAIRS),
@@ -405,21 +404,20 @@ def tile_ellipticalnormalizedrbfnet_t_kernel(tc, x, a, m, p_bytes, p_scale, lp, 
             (3, lambda g: rc(g, first=1 if g == 0 else 0), 0, PAIRS),
             (5, qr, 0, PAIRS),
             (1, lambda i: q_half(i, 0), 0, PAIRS),
+            (2, gc_rows, 0, 1),
         ]
         for step in range(2, PAIRS):
             for lag, stage, first, last in order:
                 if first <= step - lag < last:
                     stage(step - lag)
-            if step == 2:
-                late_constants()
 
         z = PAIRS - 1
         dg(z - 4)
         us(z - 3, 1)
         gt(z - 3)
         cw(z - 4)
-        h(z)
         mx(z - 3, 0)
+        h(z)
         dm(z - 4)
         lp_half(z - 1, 0)
         k(z)

@@ -18,23 +18,23 @@ AX = mybir.AxisListType
 
 P = 128
 PACK = 4
-J = 2
-TOK = J * P
-PAIRS = N // TOK
-HALF = C // 2
-DRAIN = PAIRS - 2
+TOK = 2 * P
+GT = 4 * P
+GROUPS = N // GT
+DIRECT = GROUPS - 1
 AHEAD = 4
+PLAIN_Q = ((3, 3), (1, 3))
 
 
 def tile_ellipticalnormalizedrbfnet_t_kernel(tc, x, a, m, p_bytes, p_scale, lp, gc, w, out):
     nc = tc.nc
-    x_v = x.rearrange("(g p j) d -> g p j d", p=P, j=J)
-    out_v = out.rearrange("(g p j) o -> g p j o", p=P, j=J)
+    x_v = x.rearrange("(g p j) d -> g p j d", p=P, j=2)
+    out_v = out.rearrange("(g p j) o -> g p j o", p=P, j=2)
 
     with ExitStack() as ctx:
         keep = ctx.enter_context(tc.tile_pool(name="keep", bufs=1))
         xin = ctx.enter_context(tc.tile_pool(name="xin", bufs=AHEAD + 2))
-        work = ctx.enter_context(tc.tile_pool(name="work", bufs=5))
+        work = ctx.enter_context(tc.tile_pool(name="work", bufs=3))
         psum = ctx.enter_context(tc.psum_pool(name="psum", bufs=1))
         ctx.enter_context(tc.manual_schedule())
 
@@ -47,8 +47,11 @@ def tile_ellipticalnormalizedrbfnet_t_kernel(tc, x, a, m, p_bytes, p_scale, lp, 
         def get(kind, i):
             return st[(kind, i)]
 
+        def bank(shape, name):
+            return psum.tile(shape, F32, name=name)
+
         def load(i):
-            x_sb = put("x", i, xin.tile([P, J, D], BF16, name="x_sb"))
+            x_sb = put("x", i, xin.tile([P, 2, D], BF16, name="x_sb"))
             nc.sync.dma_start(out=x_sb[:], in_=x_v[i])
 
         load(0)
@@ -58,11 +61,11 @@ def tile_ellipticalnormalizedrbfnet_t_kernel(tc, x, a, m, p_bytes, p_scale, lp, 
         nc.sync.dma_start(out=pb_sb[:], in_=p_bytes.rearrange("(p t) c -> p t c", t=PACK))
         a_sb = keep.tile([P, PACK], BF16, name="a_sb")
         nc.sync.dma_start(out=a_sb[:], in_=a.rearrange("(p t) -> p t", t=PACK))
-        for b in range(2):
-            m_sb = put("m_sb", b, keep.tile([P, PACK, HALF], BF16, name="m_sb" + str(b)))
-            nc.sync.dma_start(out=m_sb[:], in_=m.rearrange("(p t) c -> p t c", t=PACK)[:, :, b * HALF : (b + 1) * HALF])
         load(1)
+        m_sb = keep.tile([P, PACK, C], BF16, name="m_sb")
+        nc.sync.dma_start(out=m_sb[:], in_=m.rearrange("(p t) c -> p t c", t=PACK))
         load(2)
+        load(3)
         gc_sb = keep.tile([P, PACK], BF16, name="gc_sb")
         nc.sync.dma_start(out=gc_sb[:], in_=gc.rearrange("(p t) -> p t", t=PACK))
         lp_sb = keep.tile([P, PACK, 2], BF16, name="lp_sb")
@@ -70,7 +73,6 @@ def tile_ellipticalnormalizedrbfnet_t_kernel(tc, x, a, m, p_bytes, p_scale, lp, 
             nc.sync.dma_start(out=lp_sb[:, :, 0:1], in_=lp.rearrange("(s p o) -> p s o", p=P, o=1))
         w_sb = keep.tile([P, PACK, O], BF16, name="w_sb")
         nc.sync.dma_start(out=w_sb[:], in_=w.rearrange("(p t) o -> p t o", t=PACK))
-        load(3)
 
         ident = keep.tile([P, P], F32, name="ident")
         make_identity(nc, ident[:])
@@ -78,29 +80,93 @@ def tile_ellipticalnormalizedrbfnet_t_kernel(tc, x, a, m, p_bytes, p_scale, lp, 
         def gp_copy(dst, src, factor=1.0):
             nc.gpsimd.tensor_scalar(out=dst, in0=src, scalar1=factor, scalar2=0.0, op0=ALU.mult, op1=ALU.add)
 
-        def planes(name, width):
+        def quantise(name, width):
             codes = keep.tile([P, width], U32, name=name + "_codes", align_bytes=64)
             scales = keep.tile([P, width], U8, name=name + "_scales", align_bytes=64)
-            return codes, scales
+            put(name, 0, (codes, scales))
+            nc.vector.quantize_mx(out=codes[:].bitcast(FP8X4), scales=scales[:], in_=get(name + "_g", 0)[:])
 
-        def quantise(name, b, width):
-            codes, scales = put(name, b, planes(name + str(b), width))
-            nc.vector.quantize_mx(out=codes[:].bitcast(FP8X4), scales=scales[:], in_=get(name + "_g", b)[:])
-
-        def interleaved(name, b, width):
-            g = put(name + "_g", b, keep.tile([P, PACK * width], BF16, name=name + "_g" + str(b), align_bytes=64))
+        def interleaved(name, width):
+            g = put(name + "_g", 0, keep.tile([P, PACK * width], BF16, name=name + "_g", align_bytes=64))
             return g[:].rearrange("p (c i t) -> p c t i", i=4, t=PACK)
 
         def by_fours(rows):
             return rows.rearrange("p t (c i) -> p c t i", i=4)
 
-        p_w = keep.tile([P, PACK, C], BF16, name="p_w")
+        def tx(g, b, name="xt"):
+            i = 2 * g + b
+            if i + AHEAD < 2 * GROUPS:
+                load(i + AHEAD)
+            words = get("x", i)[:].rearrange("p j d -> p (j d)").bitcast(F32)
+            xt = put(("xt", b), g, bank([P, 2, TOK], name))
+            half = D // 2
+            for j in range(2):
+                for u in range(2):
+                    nc.tensor.transpose(xt[:, u, j * P : (j + 1) * P], words[:, j * half + u : (j + 1) * half : 2], ident[:])
 
-        def p_half(b):
-            nc.vector.tensor_copy(out=interleaved("p", b, HALF), in_=by_fours(p_w[:, :, b * HALF : (b + 1) * HALF]))
+        def x_turned(g, b):
+            halves = get(("xt", b), g)[:].rearrange("p u r -> p (u r)").bitcast(BF16)
+            return halves.rearrange("p (u r e) -> p r u e", u=2, e=2)
 
-        def m_half(b):
-            nc.scalar.copy(out=interleaved("m", b, HALF), in_=by_fours(get("m_sb", b)[:]))
+        def sq(g, b):
+            x2 = put(("x2", b), g, work.tile([P, TOK * PACK], F32, name="x2", bufs=4))
+            nc.scalar.activation(out=x2[:].rearrange("p (r u e) -> p r u e", u=2, e=2), in_=x_turned(g, b), func=ACT.Square)
+
+        def hk_part(g, which, b):
+            if ("hk", g) not in st:
+                put("hk", g, work.tile([P, 2, GT * PACK], BF16, name="hk", align_bytes=64, bufs=2))
+            return get("hk", g)[:, which, b * TOK * PACK : (b + 1) * TOK * PACK]
+
+        def h(g, b):
+            nc.vector.tensor_tensor(
+                out=hk_part(g, 0, b).rearrange("p (r u e) -> p r u e", u=2, e=2),
+                in0=x_turned(g, b),
+                in1=a_sb[:].rearrange("p (u e) -> p u e", e=2).unsqueeze(1).to_broadcast([P, TOK, 2, 2]),
+                op=ALU.mult,
+            )
+
+        def k(g, b):
+            nc.vector.scalar_tensor_tensor(
+                out=hk_part(g, 1, b).rearrange("p (r t) -> p r t", t=PACK),
+                in0=get(("x2", b), g)[:].rearrange("p (r t) -> p r t", t=PACK),
+                scalar=-1.0,
+                in1=a_ps[:].unsqueeze(1).to_broadcast([P, TOK, PACK]),
+                op0=ALU.add,
+                op1=ALU.mult,
+            )
+
+        def qz(g):
+            codes = put("codes", g, work.tile([P, 2, GT], U32, name="codes", align_bytes=64))
+            scales = put("scales", g, work.tile([P, 2, GT], U8, name="scales", align_bytes=64))
+            nc.vector.quantize_mx(
+                out=codes[:].rearrange("p b r -> p (b r)").bitcast(FP8X4),
+                scales=scales[:].rearrange("p b r -> p (b r)"),
+                in_=get("hk", g)[:].rearrange("p b r -> p (b r)"),
+            )
+
+        def plane(g, s, name=None):
+            qt = put(("qt", s), g, bank([P, GT], name or ("pc", "pb", "pa", "pa")[s]))
+            codes, scales = get("codes", g), get("scales", g)
+            cols = slice(s * P, (s + 1) * P)
+            for b, name in enumerate(("m", "p")):
+                wc, ws = get(name, 0)
+                nc.tensor.matmul_mx(
+                    out=qt[:],
+                    lhsT=wc[:, cols].bitcast(FP8X4),
+                    lhsT_scale=ws[:, cols],
+                    rhs=codes[:, b, :].bitcast(FP8X4),
+                    rhs_scale=scales[:, b, :],
+                    start=(b == 0),
+                    stop=(b == 1),
+                )
+
+        def add_lp(g, s):
+            ql = put(("ql", s), g, work.tile([P, GT], F32, name="ql" + str(s)))
+            nc.scalar.activation(out=ql[:], in_=get(("qt", s), g)[:], func=ACT.Identity, bias=lp_sb[:, s, 0:1], scale=1.0)
+
+        def add_lp_vector(g, s):
+            ql = put(("ql", s), g, work.tile([P, GT], F32, name="ql" + str(s)))
+            nc.vector.tensor_scalar(out=ql[:], in0=get(("qt", s), g)[:], scalar1=lp_sb[:, s, 0:1], scalar2=None, op0=ALU.add)
 
         def turn(dst, src, plain):
             if plain:
@@ -108,390 +174,367 @@ def tile_ellipticalnormalizedrbfnet_t_kernel(tc, x, a, m, p_bytes, p_scale, lp, 
             else:
                 nc.tensor.transpose(dst, src, ident[:])
 
-        def tx(i, bank="xt"):
-            if i + AHEAD < PAIRS:
-                load(i + AHEAD)
-            words = get("x", i)[:].rearrange("p j d -> p (j d)").bitcast(F32)
-            xt = put("xt", i, psum.tile([P, 2, TOK], F32, name=bank))
-            half = D // 2
-            for j in range(J):
-                for u in range(2):
-                    nc.tensor.transpose(xt[:, u, j * P : (j + 1) * P], words[:, j * half + u : (j + 1) * half : 2], ident[:])
-
-        def x_turned(i):
-            halves = get("xt", i)[:].rearrange("p u r -> p (u r)").bitcast(BF16)
-            return halves.rearrange("p (u r e) -> p r u e", u=2, e=2)
-
-        def sq(i):
-            x2 = put("x2", i, work.tile([P, TOK * PACK], F32, name="x2"))
-            nc.scalar.activation(out=x2[:].rearrange("p (r u e) -> p r u e", u=2, e=2), in_=x_turned(i), func=ACT.Square)
-
-        def h(i):
-            hk = put("hk", i, work.tile([P, 2, TOK * PACK], BF16, name="hk", align_bytes=64))
-            nc.vector.tensor_tensor(
-                out=hk[:, 0, :].rearrange("p (r u e) -> p r u e", u=2, e=2),
-                in0=x_turned(i),
-                in1=a_rep[:].rearrange("p r (u e) -> p r u e", e=2),
-                op=ALU.mult,
-            )
-
-        def k(i):
-            nc.vector.scalar_tensor_tensor(
-                out=get("hk", i)[:, 1, :].rearrange("p (r t) -> p r t", t=PACK),
-                in0=get("x2", i)[:].rearrange("p (r t) -> p r t", t=PACK),
-                scalar=-1.0,
-                in1=a_ps.unsqueeze(1).to_broadcast([P, TOK, PACK]),
-                op0=ALU.add,
-                op1=ALU.mult,
-            )
-
-        def qz(i):
-            codes = put("codes", i, work.tile([P, 2, TOK], U32, name="codes", align_bytes=64))
-            scales = put("scales", i, work.tile([P, 2, TOK], U8, name="scales", align_bytes=64))
-            nc.vector.quantize_mx(
-                out=codes[:].rearrange("p b r -> p (b r)").bitcast(FP8X4),
-                scales=scales[:].rearrange("p b r -> p (b r)"),
-                in_=get("hk", i)[:].rearrange("p b r -> p (b r)"),
-            )
-
-        def q_half(i, b):
-            qt = put(("qt", b), i, psum.tile([P, 2, TOK], F32, name="mx" + str(b)))
-            codes, scales = get("codes", i), get("scales", i)
-            for s2 in range(2):
-                cols = slice(s2 * P, (s2 + 1) * P)
-                for b2, name in enumerate(("m", "p")):
-                    wc, ws = get(name, b)
-                    nc.tensor.matmul_mx(
-                        out=qt[:, s2, :],
-                        lhsT=wc[:, cols].bitcast(FP8X4),
-                        lhsT_scale=ws[:, cols],
-                        rhs=codes[:, b2, :].bitcast(FP8X4),
-                        rhs_scale=scales[:, b2, :],
-                        start=(b2 == 0),
-                        stop=(b2 == 1),
-                    )
-
-        def lp_half(i, b):
-            if b == 0:
-                put("ql", i, work.tile([P, PACK, TOK], F32, name="ql"))
-            ql = get("ql", i)
-            qt = get(("qt", b), i)
-            for s2 in range(2):
-                s = 2 * b + s2
-                nc.scalar.activation(out=ql[:, s, :], in_=qt[:, s2, :], func=ACT.Identity, bias=lp_f[:, s : s + 1], scale=1.0)
-
-        def tq(i, j, bank=None, plain=0):
-            q = put(("q", j), i, psum.tile([P, C], F32, name=bank or "q" + str(j)))
-            ql = get("ql", i)
+        def tq(g, j, name=None):
+            q = put(("q", j), g, bank([P, C], name or "q" + str(j % 2)))
             for s in range(PACK):
-                turn(q[:, s * P : (s + 1) * P], ql[:, s, j * P : (j + 1) * P], plain=(s >= PACK - plain))
+                turn(q[:, s * P : (s + 1) * P], get(("ql", s), g)[:, j * P : (j + 1) * P], (j, s) in PLAIN_Q)
 
-        def mx(i, j):
-            nm = put(("nm", j), i, work.tile([P, 1], F32, name="nm" + str(j)))
-            nc.vector.tensor_reduce(out=nm[:], in_=get(("q", j), i)[:], axis=AX.X, op=ALU.max, negate=True)
+        def mx(g, j):
+            nm = put(("nm", j), g, work.tile([P, 1], F32, name="nm" + str(j)))
+            nc.vector.tensor_reduce(out=nm[:], in_=get(("q", j), g)[:], axis=AX.X, op=ALU.max, negate=True)
 
-        def ex(i, j):
-            e = put(("e", j), i, work.tile([P, C], F32, name="e" + str(j)))
-            g = i + 1 - j
-            if j == 0 or g == 0:
-                put("ssum", g, work.tile([P, J], F32, name="ssum"))
-            if j == 0 or i >= DRAIN:
+        def ex(g, j):
+            e = put(("e", j), g, work.tile([P, C], F32, name="e" + str(j), bufs=2))
+            if j % 2 == 0:
+                put(("ssum", j // 2), g, work.tile([P, 2], F32, name="ssum" + str(j // 2)))
+            if j >= 2 or g >= DIRECT:
                 e_v = e[:].rearrange("n (t p) -> n t p", t=PACK)
-                q_v = get(("q", j), i)[:].rearrange("n (p t) -> n t p", t=PACK)
+                q_v = get(("q", j), g)[:].rearrange("n (p t) -> n t p", t=PACK)
             else:
                 e_v = e[:].rearrange("n (u p e) -> n u p e", u=2, e=2)
-                q_v = get(("q", j), i)[:].rearrange("n (p u e) -> n u p e", u=2, e=2)
-            nc.scalar.activation(out=e_v, in_=q_v, func=ACT.Exp, bias=get(("nm", j), i)[:], scale=1.0, accum_out=get("ssum", g)[:, j : j + 1])
+                q_v = get(("q", j), g)[:].rearrange("n (p u e) -> n u p e", u=2, e=2)
+            total = get(("ssum", j // 2), g)[:, j % 2 : j % 2 + 1]
+            nc.scalar.activation(out=e_v, in_=q_v, func=ACT.Exp, bias=get(("nm", j), g)[:], scale=1.0, accum_out=total)
 
-        def rc(g, first=0, last=J):
-            if ("rs", g) not in st:
-                put("rs", g, work.tile([P, J], F32, name="rs"))
-            nc.vector.reciprocal(out=get("rs", g)[:, first:last], in_=get("ssum", g)[:, first:last])
+        def rc(g, b):
+            rs = put(("rs", b), g, work.tile([P, 2], F32, name="rs" + str(b)))
+            nc.vector.reciprocal(out=rs[:], in_=get(("ssum", b), g)[:])
 
-        def us(i, j):
-            u = put(("u", j), i, work.tile([P, C], F32, name="u" + str(j)))
-            nc.gpsimd.tensor_scalar(
-                out=u[:], in0=get(("e", j), i)[:], scalar1=get("rs", i + 1 - j)[:, j : j + 1], scalar2=-1.0 / C, op0=ALU.mult, op1=ALU.add
+        def u_part(g, j):
+            if (("u", j // 2), g) not in st:
+                put(("u", j // 2), g, work.tile([P, 2, C], F32, name="u" + str(j // 2)))
+            return get(("u", j // 2), g)[:, j % 2, :]
+
+        def us(g, j, engine=nc.gpsimd):
+            engine.tensor_scalar(
+                out=u_part(g, j),
+                in0=get(("e", j), g)[:],
+                scalar1=get(("rs", j // 2), g)[:, j % 2 : j % 2 + 1],
+                scalar2=-1.0 / C,
+                op0=ALU.mult,
+                op1=ALU.add,
             )
 
-        def uv(i, j):
-            u = put(("u", j), i, work.tile([P, C], F32, name="u" + str(j)))
-            nc.vector.tensor_scalar(
-                out=u[:], in0=get(("e", j), i)[:], scalar1=get("rs", i + 1 - j)[:, j : j + 1], scalar2=-1.0 / C, op0=ALU.mult, op1=ALU.add
-            )
-
-        def ua(i, j):
-            u = put(("u", j), i, work.tile([P, C], F32, name="u" + str(j)))
+        def ua(g, j):
             nc.scalar.activation(
-                out=u[:], in_=get(("e", j), i)[:], func=ACT.Identity, scale=get("rs", i + 1 - j)[:, j : j + 1], bias=minus_mean[:]
+                out=u_part(g, j), in_=get(("e", j), g)[:], func=ACT.Identity, scale=get(("rs", j // 2), g)[:, j % 2 : j % 2 + 1], bias=minus_mean[:]
             )
 
-        def qr_tile(i, j):
-            if j == 1:
-                put("rcodes", i, work.tile([P, TOK], U32, name="rcodes", align_bytes=64))
-                put("rscales", i, work.tile([P, TOK], U8, name="rscales", align_bytes=64))
-            cols = slice(j * P, (j + 1) * P)
-            nc.vector.quantize_mx(
-                out=get("rcodes", i)[:, cols].bitcast(FP8X4),
-                scales=get("rscales", i)[:, cols],
-                in_=get("r", i)[:, cols, :].rearrange("p n s -> p (n s)"),
-            )
+        def gt(g):
+            r_tok = put("r_tok", g, work.tile([P, 2, C], BF16, name="r_tok", bufs=2))
+            nc.gpsimd.tensor_tensor(out=r_tok[:], in0=get(("u", 0), g)[:], in1=gc_tok[:].unsqueeze(1).to_broadcast([P, 2, C]), op=ALU.mult)
 
-        def out_tile(i, j, bank, copy, queue):
-            w_codes, w_scales = get("w", 0)
-            o_ps = psum.tile([P, O], F32, name=bank)
-            cols = slice(j * P, (j + 1) * P)
-            nc.tensor.matmul_mx(
-                out=o_ps[:],
-                lhsT=get("rcodes", i)[:, cols].bitcast(FP8X4),
-                lhsT_scale=get("rscales", i)[:, cols],
-                rhs=w_codes[:].bitcast(FP8X4),
-                rhs_scale=w_scales[:],
-                start=True,
-                stop=True,
-            )
-            o_sb = work.tile([P, O], F32, name="o_last")
-            copy(out=o_sb[:], in_=o_ps[:])
-            queue.dma_start(out=out_v[i][:, j, :], in_=o_sb[:])
+        def tw(g, name="pa"):
+            words = get("r_tok", g)[:].rearrange("n j c -> n (j c)").bitcast(F32)
+            rw = put("rw", g, bank([P, PACK, P], name))
+            for ju in range(4):
+                nc.tensor.transpose(rw[:, ju, :], words[:, ju * P : (ju + 1) * P], ident[:])
 
-        def tu(i, j=0, bank="ut0"):
-            ut = put(("ut", j), i, psum.tile([P, PACK, P], F32, name=bank))
-            u = get(("u", j), i)
+        def r_tile(g):
+            if ("r", g) not in st:
+                put("r", g, work.tile([P, GT, PACK], BF16, name="r", align_bytes=64))
+            return get("r", g)
+
+        def cw(g):
+            words = r_tile(g)[:, 0:TOK, :].rearrange("p n s -> p (n s)").bitcast(F32)
+            nc.scalar.copy(out=words.rearrange("p (j n u) -> p j n u", j=2, u=2), in_=get("rw", g)[:].rearrange("p (j u) n -> p j n u", u=2))
+
+        def tu(g, j, name=None, plain=0):
+            ut = put(("ut", j), g, bank([P, PACK, P], name or ("pb" if j == 2 else "q0")))
+            u = get(("u", j // 2), g)
             for s in range(PACK):
-                nc.tensor.transpose(ut[:, s, :], u[:, s * P : (s + 1) * P], ident[:])
+                turn(ut[:, s, :], u[:, j % 2, s * P : (s + 1) * P], s >= PACK - plain)
 
-        def r_tile(i):
-            if ("r", i) not in st:
-                put("r", i, work.tile([P, TOK, PACK], BF16, name="r", align_bytes=64))
-            return get("r", i)
-
-        def rr(i, j=0):
+        def rr(g, j):
             nc.vector.tensor_tensor(
-                out=r_tile(i)[:, j * P : (j + 1) * P, :], in0=get(("ut", j), i)[:].rearrange("p s n -> p n s"), in1=gc_rep[:], op=ALU.mult
+                out=r_tile(g)[:, j * P : (j + 1) * P, :], in0=get(("ut", j), g)[:].rearrange("p s n -> p n s"), in1=gc_f[:].unsqueeze(1).to_broadcast([P, P, PACK]), op=ALU.mult
             )
 
-        def dg(i):
-            diag = put("diag", i, work.tile([P, P], F32, name="diag"))
-            gp_copy(diag[:], ident[:], get("rs", i + 1)[:, 0:1])
-
-        def dm(i, bank="ut0"):
-            ut = put(("ut", 0), i, psum.tile([P, PACK, P], F32, name=bank))
-            e = get(("e", 0), i)
+        def dm(g, j, name):
+            diag = work.tile([P, P], F32, name="diag")
+            nc.scalar.activation(out=diag[:], in_=ident[:], func=ACT.Copy, scale=get(("rs", j // 2), g)[:, j % 2 : j % 2 + 1])
+            ut = put(("ut", j), g, bank([P, PACK, P], name))
+            e = get(("e", j), g)
             for s in range(PACK):
-                nc.tensor.matmul(ut[:, s, :], lhsT=e[:, s * P : (s + 1) * P], rhs=get("diag", i)[:], start=True, stop=True)
+                nc.tensor.matmul(ut[:, s, :], lhsT=e[:, s * P : (s + 1) * P], rhs=diag[:], start=True, stop=True)
 
-        def rd(i):
+        def rd(g, j):
             nc.vector.scalar_tensor_tensor(
-                out=r_tile(i)[:, 0:P, :],
-                in0=get(("ut", 0), i)[:].rearrange("p s n -> p n s"),
+                out=r_tile(g)[:, j * P : (j + 1) * P, :],
+                in0=get(("ut", j), g)[:].rearrange("p s n -> p n s"),
                 scalar=-1.0 / C,
-                in1=gc_rep[:],
+                in1=gc_f[:].unsqueeze(1).to_broadcast([P, P, PACK]),
                 op0=ALU.add,
                 op1=ALU.mult,
             )
 
-        def gt(i):
-            r_tok = put("r_tok", i, work.tile([P, C], BF16, name="r_tok"))
-            nc.gpsimd.tensor_tensor(out=r_tok[:], in0=get(("u", 1), i)[:], in1=gc_tok[:], op=ALU.mult)
+        def qr_pair(g, b):
+            if ("rcodes", g) not in st:
+                put("rcodes", g, work.tile([P, GT], U32, name="rcodes", align_bytes=64))
+                put("rscales", g, work.tile([P, GT], U8, name="rscales", align_bytes=64))
+            cols = slice(b * TOK, (b + 1) * TOK)
+            nc.vector.quantize_mx(
+                out=get("rcodes", g)[:, cols].bitcast(FP8X4),
+                scales=get("rscales", g)[:, cols],
+                in_=get("r", g)[:, cols, :].rearrange("p n s -> p (n s)"),
+            )
 
-        def tw(i):
-            words = get("r_tok", i)[:].bitcast(F32)
-            for u in range(2):
-                nc.tensor.transpose(rw[:, u, :], words[:, u * P : (u + 1) * P], ident[:])
+        def qr(g):
+            rcodes = put("rcodes", g, work.tile([P, GT], U32, name="rcodes", align_bytes=64))
+            rscales = put("rscales", g, work.tile([P, GT], U8, name="rscales", align_bytes=64))
+            nc.vector.quantize_mx(out=rcodes[:].bitcast(FP8X4), scales=rscales[:], in_=get("r", g)[:].rearrange("p n s -> p (n s)"))
 
-        def cw(i):
-            words = r_tile(i)[:, P:TOK, :].rearrange("p n s -> p (n s)").bitcast(F32)
-            nc.scalar.copy(out=words.rearrange("p (n u) -> p n u", u=2), in_=rw.rearrange("p u n -> p n u"))
-
-        def qr(i):
-            rcodes = put("rcodes", i, work.tile([P, TOK], U32, name="rcodes", align_bytes=64))
-            rscales = put("rscales", i, work.tile([P, TOK], U8, name="rscales", align_bytes=64))
-            nc.vector.quantize_mx(out=rcodes[:].bitcast(FP8X4), scales=rscales[:], in_=get("r", i)[:].rearrange("p n s -> p (n s)"))
-
-        def ou(i, bank="o_ps"):
-            o_ps = put("o_ps", i, psum.tile([P, J * O], F32, name=bank))
+        def ou(g, b, name="o_ps"):
+            o_ps = put(("o_ps", b), g, bank([P, 2 * O], name))
             w_codes, w_scales = get("w", 0)
-            for j in range(J):
-                cols = slice(j * P, (j + 1) * P)
+            for j in range(2):
+                cols = slice((2 * b + j) * P, (2 * b + j + 1) * P)
                 nc.tensor.matmul_mx(
                     out=o_ps[:, j * O : (j + 1) * O],
-                    lhsT=get("rcodes", i)[:, cols].bitcast(FP8X4),
-                    lhsT_scale=get("rscales", i)[:, cols],
+                    lhsT=get("rcodes", g)[:, cols].bitcast(FP8X4),
+                    lhsT_scale=get("rscales", g)[:, cols],
                     rhs=w_codes[:].bitcast(FP8X4),
                     rhs_scale=w_scales[:],
                     start=True,
                     stop=True,
                 )
 
-        def out_scalar(i):
-            o_sb = work.tile([P, J * O], F32, name="o_sb")
-            nc.scalar.copy(out=o_sb[:], in_=get("o_ps", i)[:])
-            nc.sync.dma_start(out=out_v[i], in_=o_sb[:].rearrange("p (j o) -> p j o", j=J))
+        def store(g, b, copy=nc.scalar.copy):
+            o_sb = work.tile([P, 2 * O], F32, name="o_sb", bufs=8)
+            copy(out=o_sb[:], in_=get(("o_ps", b), g)[:])
+            nc.sync.dma_start(out=out_v[2 * g + b], in_=o_sb[:].rearrange("p (j o) -> p j o", j=2))
 
+        p_w = keep.tile([P, PACK, C], BF16, name="p_w")
         for t in range(PACK):
             nc.vector.tensor_scalar(out=p_w[:, t, :], in0=pb_sb[:, t, :].bitcast(FP8), scalar1=ps_sb[:, t : t + 1], scalar2=None, op0=ALU.mult)
+        tx(0, 0, "q0")
+        tx(0, 1, "q1")
+        nc.vector.tensor_copy(out=interleaved("p", C), in_=by_fours(p_w[:]))
         a_f = keep.tile([P, PACK], F32, name="a_f")
-        gp_copy(a_f[:], a_sb[:], -1.0)
-        a_rep = keep.tile([P, TOK, PACK], BF16, name="a_rep", align_bytes=64)
-        gp_copy(a_rep[:], a_sb[:].unsqueeze(1).to_broadcast([P, TOK, PACK]))
-        tx(0, "q0")
-        side = psum.tile([P, C], F32, name="side")
-        rw = side[:, 0:TOK].rearrange("p (u n) -> p u n", u=2)
-        a_ps = side[:, TOK : TOK + PACK]
-        nc.tensor.matmul(a_ps, lhsT=ident[:], rhs=a_f[:], start=True, stop=True)
-        tx(1, "ut0")
-        tx(2)
-        p_half(0)
-        sq(0)
-        m_half(0)
-        p_half(1)
-        h(0)
-        k(0)
-        m_half(1)
-        quantise("p", 0, HALF)
-        quantise("m", 0, HALF)
-        qz(0)
-        sq(1)
+        nc.scalar.activation(out=a_f[:], in_=a_sb[:], func=ACT.Copy, scale=-1.0)
+        a_ps = psum.tile([P, PACK], F32, name="a_ps")
+        nc.tensor.matmul(a_ps[:], lhsT=ident[:], rhs=a_f[:], start=True, stop=True)
+        tx(1, 0, "o_ps")
+        tx(1, 1)
+        sq(0, 0)
+        sq(0, 1)
+        h(0, 0)
+        k(0, 0)
         gc_f = keep.tile([P, PACK], F32, name="gc_f")
-        gp_copy(gc_f[:], gc_sb[:], float(C))
-        gc_ps = psum.tile([P, PACK, P], F32, name="o_ps")
-        for t in range(PACK):
-            nc.tensor.matmul(gc_ps[:, t, :], lhsT=gc_f[:, t : t + 1].to_broadcast([P, P]), rhs=ident[:], start=True, stop=True)
-        q_half(0, 0)
-        quantise("p", 1, HALF)
-        quantise("m", 1, HALF)
-        sq(2)
-        lp_f = keep.tile([P, PACK], F32, name="lp_f")
-        gp_copy(lp_f[:], lp_sb[:, :, 0])
-        gc_rep = keep.tile([P, P, PACK], F32, name="gc_rep", align_bytes=64)
-        gp_copy(gc_rep[:], gc_sb[:].unsqueeze(1).to_broadcast([P, P, PACK]), float(C))
-        gc_tok = keep.tile([P, C], F32, name="gc_tok")
+        nc.scalar.activation(out=gc_f[:], in_=gc_sb[:], func=ACT.Copy, scale=float(C))
+        nc.scalar.copy(out=interleaved("m", C), in_=by_fours(m_sb[:]))
+        tx(2, 0, "q0")
+        h(0, 1)
+        k(0, 1)
+        quantise("p", C)
+        quantise("m", C)
+        sq(1, 0)
+        qz(0)
         minus_mean = keep.tile([P, 1], F32, name="minus_mean")
         nc.gpsimd.memset(minus_mean[:], -1.0 / C)
+        gp_copy(interleaved("w", O), by_fours(w_sb[:]))
+        gc_ps = bank([P, PACK, P], "pa")
+        for t in range(PACK):
+            nc.tensor.matmul(gc_ps[:, t, :], lhsT=gc_f[:, t : t + 1].to_broadcast([P, P]), rhs=ident[:], start=True, stop=True)
+        sq(1, 1)
+        sq(2, 0)
+        gc_tok = keep.tile([P, C], F32, name="gc_tok")
+        nc.scalar.copy(out=gc_tok[:].rearrange("n (u p e) -> n u p e", u=2, e=2), in_=gc_ps[:].rearrange("n (u e) p -> n u p e", u=2))
+        plane(0, 0)
+        plane(0, 1)
+        plane(0, 2)
+        h(1, 0)
+        k(1, 0)
+        add_lp(0, 0)
+        plane(0, 3, "pc")
+        tx(2, 1, "o_ps")
+        add_lp(0, 1)
+        h(1, 1)
+        h(2, 0)
+        tx(3, 0)
+        add_lp(0, 2)
+        add_lp(0, 3)
+        k(1, 1)
+        tq(0, 0)
+        tq(0, 1)
+        tq(0, 2, "pa")
+        quantise("w", O)
+        qz(1)
+        sq(2, 1)
+        sq(3, 0)
+        plane(1, 0)
+        plane(1, 1)
+        mx(0, 0)
+        ex(0, 0)
+        k(2, 0)
+        add_lp(1, 0)
+        plane(1, 2, "q0")
+        mx(0, 1)
+        add_lp(1, 1)
+        ex(0, 1)
+        h(2, 1)
+        mx(0, 2)
+        add_lp(1, 2)
+        plane(1, 3, "pb")
+        tx(3, 1, "o_ps")
+        k(2, 1)
 
-        def w_operand(i):
-            gp_copy(interleaved("w", 0, O), by_fours(w_sb[:]))
-            quantise("w", 0, O)
-
-        def gc_rows(i):
-            nc.scalar.copy(out=gc_tok[:].rearrange("n (u p e) -> n u p e", u=2, e=2), in_=gc_ps[:].rearrange("n (u e) p -> n u p e", u=2))
-
+        every = (0, GROUPS)
         order = [
-            (5, dg, 0, PAIRS),
-            (4, lambda i: us(i, 1), 0, PAIRS),
-            (4, gt, 0, PAIRS),
-            (4, lambda i: mx(i, 0), 0, PAIRS),
-            (5, cw, 0, PAIRS),
-            (5, dm, 0, PAIRS),
-            (7, out_scalar, 0, PAIRS),
-            (1, h, 0, PAIRS),
-            (2, lambda i: lp_half(i, 0), 0, PAIRS),
-            (3, lambda i: mx(i, 1), 0, PAIRS),
-            (4, lambda i: ex(i, 0), 0, PAIRS),
-            (1, k, 0, PAIRS),
-            (2, lambda i: q_half(i, 1), 0, PAIRS),
-            (3, lambda i: ex(i, 1), 0, PAIRS),
-            (0, tx, 3, PAIRS),
-            (5, rd, 0, PAIRS),
-            (2, w_operand, 0, 1),
-            (2, lambda i: lp_half(i, 1), 0, PAIRS),
-            (3, lambda i: tq(i, 0, plain=2 if i < 3 else 1), 0, PAIRS),
-            (6, ou, 0, PAIRS),
-            (1, qz, 0, PAIRS),
-            (4, tw, 0, PAIRS),
-            (0, sq, 3, PAIRS),
-            (2, lambda i: tq(i, 1), 0, PAIRS),
-            (3, lambda g: rc(g, first=1 if g == 0 else 0), 0, PAIRS),
-            (5, qr, 0, PAIRS),
-            (1, lambda i: q_half(i, 0), 0, PAIRS),
-            (2, gc_rows, 0, 1),
+            (1, qz, (), every),
+            (0, sq, (0,), (4,GROUPS)),
+            (4, tu, (2,), every),
+            (3, tq, (3,), every),
+            (3, rc, (0,), every),
+            (3, us, (0,), every),
+            (3, us, (1,), every),
+            (3, gt, (), every),
+            (3, ex, (2,), every),
+            (0, h, (0,), every),
+            (1, plane, (0,), every),
+            (2, add_lp, (3,), every),
+            (4, rr, (2,), every),
+            (4, tu, (3,), every),
+            (5, store, (1,), every),
+            (0, tx, (1,), (4,GROUPS)),
+            (3, mx, (3,), every),
+            (1, add_lp, (0,), every),
+            (4, tw, (), every),
+            (4, rr, (3,), every),
+            (3, ex, (3,), every),
+            (1, plane, (1,), every),
+            (0, h, (1,), every),
+            (4, cw, (), every),
+            (2, tq, (0,), every),
+            (0, k, (0,), every),
+            (2, tq, (1,), every),
+            (0, sq, (1,), every),
+            (2, mx, (0,), every),
+            (1, plane, (2,), every),
+            (1, add_lp, (1,), every),
+            (4, qr, (), every),
+            (2, ex, (0,), every),
+            (3, rc, (1,), every),
+            (3, us, (2,), every),
+            (3, us, (3,), every),
+            (4, ou, (0,), every),
+            (2, mx, (1,), every),
+            (1, add_lp, (2,), every),
+            (2, tq, (2,), every),
+            (0, k, (1,), every),
+            (-1, tx, (0,), (1,GROUPS)),
+            (2, ex, (1,), every),
+            (4, store, (0,), every),
+            (2, mx, (2,), every),
+            (1, plane, (3,), every),
+            (4, ou, (1,), every),
         ]
-        for step in range(2, PAIRS):
-            for lag, stage, first, last in order:
+        for step in range(3, GROUPS):
+            for lag, stage, args, (first, last) in order:
                 if first <= step - lag < last:
-                    stage(step - lag)
+                    stage(step - lag, *args)
 
-        z = PAIRS - 1
-        dg(z - 4)
-        us(z - 3, 1)
-        gt(z - 3)
-        cw(z - 4)
-        mx(z - 3, 0)
-        h(z)
-        dm(z - 4)
-        lp_half(z - 1, 0)
-        k(z)
-        ex(z - 3, 0)
-        q_half(z - 1, 1)
-        out_scalar(z - 6)
-        mx(z - 2, 1)
-        tq(z - 2, 0)
-        lp_half(z - 1, 1)
-        ou(z - 5)
+        z = GROUPS - 1
         qz(z)
-        tw(z - 3)
-        ex(z - 2, 1)
-        tq(z - 1, 1, "xt")
-        rd(z - 4)
-        q_half(z, 0)
-        q_half(z, 1)
-        out_scalar(z - 5)
-        mx(z - 2, 0)
-        rc(z - 2)
-        qr(z - 4)
-        dg(z - 3)
+        tu(z - 3, 2)
+        tq(z - 2, 3)
+        tu(z - 3, 3, "xt")
+        tw(z - 3, "pc")
+        rc(z - 2, 0)
+        us(z - 2, 0)
         us(z - 2, 1)
-        tq(z - 1, 0, "q1")
-        ou(z - 4)
-        ex(z - 2, 0)
-        lp_half(z, 0)
-        mx(z - 1, 1)
-        rc(z - 1, 0, 1)
-        dg(z - 2)
         gt(z - 2)
-        dm(z - 3)
-        lp_half(z, 1)
-        mx(z - 1, 0)
-        ex(z - 1, 1)
+        ex(z - 2, 2)
+        add_lp(z - 1, 3)
+        rr(z - 3, 2)
+        plane(z, 0, "q0")
+        mx(z - 2, 3)
+        tq(z - 1, 0, "pa")
+        store(z - 4, 1)
+        plane(z, 1, "pb")
+        rr(z - 3, 3)
         cw(z - 3)
-        tq(z, 1, "q0")
-        tq(z, 0, "xt")
-        rd(z - 3)
-        dm(z - 2, "mx0")
+        tq(z - 1, 1, "o_ps")
+        ex(z - 2, 3)
+        plane(z, 2, "xt")
+        plane(z, 3, "pc")
+        mx(z - 1, 0)
+        add_lp(z, 0)
+        add_lp_vector(z, 1)
+        tq(z - 1, 2, "q1")
         ex(z - 1, 0)
-        mx(z, 1)
+        mx(z - 1, 1)
+        tq(z - 1, 3, "q0")
+        add_lp(z, 2)
+        add_lp_vector(z, 3)
+        tw(z - 2, "pb")
+        ex(z - 1, 1)
         qr(z - 3)
-        rc(z - 1, 1, 2)
-        us(z - 1, 1)
-        mx(z, 0)
-        ex(z, 1)
-        ex(z, 0)
-        tw(z - 2)
-        ou(z - 3, "ut0")
-        rd(z - 2)
-        rc(z)
-        uv(z - 1, 0)
-        ua(z, 1)
-        tu(z - 1, 1, "mx1")
-        tu(z - 1, 0, "q1")
-        rc(z + 1, 0, 1)
-        uv(z, 0)
+        rc(z - 2, 1)
+        us(z - 2, 2)
+        us(z - 2, 3)
+        tq(z, 0, "pa")
+        tq(z, 1, "xt")
+        mx(z - 1, 2)
         cw(z - 2)
-        tu(z, 1, "q0")
-        tu(z, 0, "xt")
-        rr(z - 1, 1)
-        out_scalar(z - 4)
+        ou(z - 3, 0, "pc")
+        mx(z - 1, 3)
+        ex(z - 1, 2)
+        rc(z - 1, 0)
+        us(z - 1, 0)
+        us(z - 1, 1)
+        gt(z - 1)
+        tq(z, 2, "o_ps")
+        mx(z, 0)
+        tu(z - 2, 2, "pb", 1)
+        ex(z - 1, 3)
+        mx(z, 1)
+        tu(z - 2, 3, "q1", 1)
+        store(z - 3, 0)
+        rc(z - 1, 1)
+        tq(z, 3, "q0")
+        rr(z - 2, 2)
+        ex(z, 0)
+        ou(z - 3, 1, "pc")
+        mx(z, 2)
+        dm(z - 1, 2, "pb")
+        ex(z, 1)
+        rr(z - 2, 3)
+        dm(z - 1, 3, "pa")
+        mx(z, 3)
+        ex(z, 2)
+        rc(z, 0)
+        ex(z, 3)
+        rd(z - 1, 2)
+        dm(z, 0, "q1")
+        rc(z, 1)
+        tw(z - 1, "xt")
+        rd(z - 1, 3)
+        ua(z, 1)
         qr(z - 2)
-        rr(z - 1, 0)
-        ou(z - 2)
-        out_scalar(z - 3)
+        ua(z, 2)
+        tu(z, 1, "o_ps")
+        cw(z - 1)
+        ou(z - 2, 0, "q0")
+        ou(z - 2, 1, "pb")
+        tu(z, 2, "pa")
+        rd(z, 0)
+        ua(z, 3)
         rr(z, 1)
+        tu(z, 3, "xt")
+        store(z - 3, 1)
         qr(z - 1)
-        rr(z, 0)
-        ou(z - 1, "mx0")
-        out_scalar(z - 2)
-        qr_tile(z, 1)
-        out_scalar(z - 1)
-        out_tile(z, 1, "q1", nc.scalar.copy, nc.scalar)
-        qr_tile(z, 0)
-        out_tile(z, 0, "mx1", nc.vector.tensor_copy, nc.sync)
+        store(z - 2, 0)
+        rr(z, 2)
+        ou(z - 1, 0, "q1")
+        ou(z - 1, 1, "o_ps")
+        qr_pair(z, 0)
+        store(z - 2, 1)
+        rr(z, 3)
+        ou(z, 0, "pc")
+        store(z - 1, 0)
+        qr_pair(z, 1)
+        store(z - 1, 1)
+        ou(z, 1, "q0")
+        store(z, 0)
+        store(z, 1, nc.vector.tensor_copy)

@@ -23,7 +23,7 @@ GT = 4 * P
 GROUPS = N // GT
 DIRECT = GROUPS - 1
 AHEAD = 4
-PLAIN_Q = ((3, 3), (1, 3))
+PLAIN_Q = ((2, 3), (), (), (3,))
 
 
 def tile_ellipticalnormalizedrbfnet_t_kernel(tc, x, a, m, p_bytes, p_scale, lp, gc, w, out):
@@ -145,7 +145,7 @@ def tile_ellipticalnormalizedrbfnet_t_kernel(tc, x, a, m, p_bytes, p_scale, lp, 
             )
 
         def plane(g, s, name=None):
-            qt = put(("qt", s), g, bank([P, GT], name or ("pc", "pb", "pa", "pa")[s]))
+            qt = put(("qt", s), g, bank([P, GT], name or ("b5", "b1", "b3", "b5")[s]))
             codes, scales = get("codes", g), get("scales", g)
             cols = slice(s * P, (s + 1) * P)
             for b, name in enumerate(("m", "p")):
@@ -161,11 +161,11 @@ def tile_ellipticalnormalizedrbfnet_t_kernel(tc, x, a, m, p_bytes, p_scale, lp, 
                 )
 
         def add_lp(g, s):
-            ql = put(("ql", s), g, work.tile([P, GT], F32, name="ql" + str(s)))
+            ql = put(("ql", s), g, work.tile([P, GT], F32, name="ql" + str(s), bufs=2))
             nc.scalar.activation(out=ql[:], in_=get(("qt", s), g)[:], func=ACT.Identity, bias=lp_sb[:, s, 0:1], scale=1.0)
 
         def add_lp_vector(g, s):
-            ql = put(("ql", s), g, work.tile([P, GT], F32, name="ql" + str(s)))
+            ql = put(("ql", s), g, work.tile([P, GT], F32, name="ql" + str(s), bufs=2))
             nc.vector.tensor_scalar(out=ql[:], in0=get(("qt", s), g)[:], scalar1=lp_sb[:, s, 0:1], scalar2=None, op0=ALU.add)
 
         def turn(dst, src, plain):
@@ -174,10 +174,10 @@ def tile_ellipticalnormalizedrbfnet_t_kernel(tc, x, a, m, p_bytes, p_scale, lp, 
             else:
                 nc.tensor.transpose(dst, src, ident[:])
 
-        def tq(g, j, name=None):
-            q = put(("q", j), g, bank([P, C], name or "q" + str(j % 2)))
+        def tq(g, j, name=None, plain=None):
+            q = put(("q", j), g, bank([P, C], name or ("b1", "b6", "b2", "b4")[j]))
             for s in range(PACK):
-                turn(q[:, s * P : (s + 1) * P], get(("ql", s), g)[:, j * P : (j + 1) * P], (j, s) in PLAIN_Q)
+                turn(q[:, s * P : (s + 1) * P], get(("ql", s), g)[:, j * P : (j + 1) * P], s in (PLAIN_Q[j] if plain is None else plain))
 
         def mx(g, j):
             nm = put(("nm", j), g, work.tile([P, 1], F32, name="nm" + str(j)))
@@ -185,20 +185,21 @@ def tile_ellipticalnormalizedrbfnet_t_kernel(tc, x, a, m, p_bytes, p_scale, lp, 
 
         def ex(g, j):
             e = put(("e", j), g, work.tile([P, C], F32, name="e" + str(j), bufs=2))
-            if j % 2 == 0:
-                put(("ssum", j // 2), g, work.tile([P, 2], F32, name="ssum" + str(j // 2)))
-            if j >= 2 or g >= DIRECT:
+            if j == 0:
+                put("ssum", g, work.tile([P, 4], F32, name="ssum"))
+            if j >= 2 or g == 0 or g >= DIRECT:
                 e_v = e[:].rearrange("n (t p) -> n t p", t=PACK)
                 q_v = get(("q", j), g)[:].rearrange("n (p t) -> n t p", t=PACK)
             else:
                 e_v = e[:].rearrange("n (u p e) -> n u p e", u=2, e=2)
                 q_v = get(("q", j), g)[:].rearrange("n (p u e) -> n u p e", u=2, e=2)
-            total = get(("ssum", j // 2), g)[:, j % 2 : j % 2 + 1]
+            total = get("ssum", g)[:, j : j + 1]
             nc.scalar.activation(out=e_v, in_=q_v, func=ACT.Exp, bias=get(("nm", j), g)[:], scale=1.0, accum_out=total)
 
-        def rc(g, b):
-            rs = put(("rs", b), g, work.tile([P, 2], F32, name="rs" + str(b)))
-            nc.vector.reciprocal(out=rs[:], in_=get(("ssum", b), g)[:])
+        def rc(g, first=0, last=4):
+            if ("rs", g) not in st:
+                put("rs", g, work.tile([P, 4], F32, name="rs"))
+            nc.vector.reciprocal(out=get("rs", g)[:, first:last], in_=get("ssum", g)[:, first:last])
 
         def u_part(g, j):
             if (("u", j // 2), g) not in st:
@@ -209,7 +210,7 @@ def tile_ellipticalnormalizedrbfnet_t_kernel(tc, x, a, m, p_bytes, p_scale, lp, 
             engine.tensor_scalar(
                 out=u_part(g, j),
                 in0=get(("e", j), g)[:],
-                scalar1=get(("rs", j // 2), g)[:, j % 2 : j % 2 + 1],
+                scalar1=get("rs", g)[:, j : j + 1],
                 scalar2=-1.0 / C,
                 op0=ALU.mult,
                 op1=ALU.add,
@@ -217,42 +218,43 @@ def tile_ellipticalnormalizedrbfnet_t_kernel(tc, x, a, m, p_bytes, p_scale, lp, 
 
         def ua(g, j):
             nc.scalar.activation(
-                out=u_part(g, j), in_=get(("e", j), g)[:], func=ACT.Identity, scale=get(("rs", j // 2), g)[:, j % 2 : j % 2 + 1], bias=minus_mean[:]
+                out=u_part(g, j), in_=get(("e", j), g)[:], func=ACT.Identity, scale=get("rs", g)[:, j : j + 1], bias=minus_mean[:]
             )
 
         def gt(g):
             r_tok = put("r_tok", g, work.tile([P, 2, C], BF16, name="r_tok", bufs=2))
             nc.gpsimd.tensor_tensor(out=r_tok[:], in0=get(("u", 0), g)[:], in1=gc_tok[:].unsqueeze(1).to_broadcast([P, 2, C]), op=ALU.mult)
 
-        def tw(g, name="pa"):
+        def tw(g, name="b1"):
             words = get("r_tok", g)[:].rearrange("n j c -> n (j c)").bitcast(F32)
             rw = put("rw", g, bank([P, PACK, P], name))
             for ju in range(4):
                 nc.tensor.transpose(rw[:, ju, :], words[:, ju * P : (ju + 1) * P], ident[:])
 
-        def r_tile(g):
-            if ("r", g) not in st:
-                put("r", g, work.tile([P, GT, PACK], BF16, name="r", align_bytes=64))
-            return get("r", g)
+        def r_cols(g, j, tiles=1):
+            r_set, first = g + j // 2, (j + 2) % 4
+            if ("r", r_set) not in st:
+                put("r", r_set, work.tile([P, GT, PACK], BF16, name="r", align_bytes=64))
+            return get("r", r_set)[:, first * P : (first + tiles) * P, :]
 
         def cw(g):
-            words = r_tile(g)[:, 0:TOK, :].rearrange("p n s -> p (n s)").bitcast(F32)
+            words = r_cols(g, 0, 2).rearrange("p n s -> p (n s)").bitcast(F32)
             nc.scalar.copy(out=words.rearrange("p (j n u) -> p j n u", j=2, u=2), in_=get("rw", g)[:].rearrange("p (j u) n -> p j n u", u=2))
 
         def tu(g, j, name=None, plain=0):
-            ut = put(("ut", j), g, bank([P, PACK, P], name or ("pb" if j == 2 else "q0")))
+            ut = put(("ut", j), g, bank([P, PACK, P], name or "b4"))
             u = get(("u", j // 2), g)
             for s in range(PACK):
                 turn(ut[:, s, :], u[:, j % 2, s * P : (s + 1) * P], s >= PACK - plain)
 
         def rr(g, j):
             nc.vector.tensor_tensor(
-                out=r_tile(g)[:, j * P : (j + 1) * P, :], in0=get(("ut", j), g)[:].rearrange("p s n -> p n s"), in1=gc_f[:].unsqueeze(1).to_broadcast([P, P, PACK]), op=ALU.mult
+                out=r_cols(g, j), in0=get(("ut", j), g)[:].rearrange("p s n -> p n s"), in1=gc_f[:].unsqueeze(1).to_broadcast([P, P, PACK]), op=ALU.mult
             )
 
         def dm(g, j, name):
             diag = work.tile([P, P], F32, name="diag")
-            nc.scalar.activation(out=diag[:], in_=ident[:], func=ACT.Copy, scale=get(("rs", j // 2), g)[:, j % 2 : j % 2 + 1])
+            nc.scalar.activation(out=diag[:], in_=ident[:], func=ACT.Copy, scale=get("rs", g)[:, j : j + 1])
             ut = put(("ut", j), g, bank([P, PACK, P], name))
             e = get(("e", j), g)
             for s in range(PACK):
@@ -260,7 +262,7 @@ def tile_ellipticalnormalizedrbfnet_t_kernel(tc, x, a, m, p_bytes, p_scale, lp, 
 
         def rd(g, j):
             nc.vector.scalar_tensor_tensor(
-                out=r_tile(g)[:, j * P : (j + 1) * P, :],
+                out=r_cols(g, j),
                 in0=get(("ut", j), g)[:].rearrange("p s n -> p n s"),
                 scalar=-1.0 / C,
                 in1=gc_f[:].unsqueeze(1).to_broadcast([P, P, PACK]),
@@ -268,53 +270,62 @@ def tile_ellipticalnormalizedrbfnet_t_kernel(tc, x, a, m, p_bytes, p_scale, lp, 
                 op1=ALU.mult,
             )
 
-        def qr_pair(g, b):
-            if ("rcodes", g) not in st:
-                put("rcodes", g, work.tile([P, GT], U32, name="rcodes", align_bytes=64))
-                put("rscales", g, work.tile([P, GT], U8, name="rscales", align_bytes=64))
-            cols = slice(b * TOK, (b + 1) * TOK)
+        def qr(r_set, first=0, tiles=4):
+            if ("rcodes", r_set) not in st:
+                put("rcodes", r_set, work.tile([P, GT], U32, name="rcodes", align_bytes=64))
+                put("rscales", r_set, work.tile([P, GT], U8, name="rscales", align_bytes=64))
+            cols = slice(first * P, (first + tiles) * P)
             nc.vector.quantize_mx(
-                out=get("rcodes", g)[:, cols].bitcast(FP8X4),
-                scales=get("rscales", g)[:, cols],
-                in_=get("r", g)[:, cols, :].rearrange("p n s -> p (n s)"),
+                out=get("rcodes", r_set)[:, cols].bitcast(FP8X4),
+                scales=get("rscales", r_set)[:, cols],
+                in_=get("r", r_set)[:, cols, :].rearrange("p n s -> p (n s)"),
             )
 
-        def qr(g):
-            rcodes = put("rcodes", g, work.tile([P, GT], U32, name="rcodes", align_bytes=64))
-            rscales = put("rscales", g, work.tile([P, GT], U8, name="rscales", align_bytes=64))
-            nc.vector.quantize_mx(out=rcodes[:].bitcast(FP8X4), scales=rscales[:], in_=get("r", g)[:].rearrange("p n s -> p (n s)"))
-
-        def ou(g, b, name="o_ps"):
-            o_ps = put(("o_ps", b), g, bank([P, 2 * O], name))
+        def last_product(dst, r_set, tile):
             w_codes, w_scales = get("w", 0)
-            for j in range(2):
-                cols = slice((2 * b + j) * P, (2 * b + j + 1) * P)
-                nc.tensor.matmul_mx(
-                    out=o_ps[:, j * O : (j + 1) * O],
-                    lhsT=get("rcodes", g)[:, cols].bitcast(FP8X4),
-                    lhsT_scale=get("rscales", g)[:, cols],
-                    rhs=w_codes[:].bitcast(FP8X4),
-                    rhs_scale=w_scales[:],
-                    start=True,
-                    stop=True,
-                )
+            cols = slice(tile * P, (tile + 1) * P)
+            nc.tensor.matmul_mx(
+                out=dst,
+                lhsT=get("rcodes", r_set)[:, cols].bitcast(FP8X4),
+                lhsT_scale=get("rscales", r_set)[:, cols],
+                rhs=w_codes[:].bitcast(FP8X4),
+                rhs_scale=w_scales[:],
+                start=True,
+                stop=True,
+            )
 
-        def store(g, b, copy=nc.scalar.copy):
-            o_sb = work.tile([P, 2 * O], F32, name="o_sb", bufs=8)
-            copy(out=o_sb[:], in_=get(("o_ps", b), g)[:])
-            nc.sync.dma_start(out=out_v[2 * g + b], in_=o_sb[:].rearrange("p (j o) -> p j o", j=2))
+        def ou(r_set, b, name=None):
+            if 2 * r_set + b < 1:
+                return
+            o_ps = put(("o_ps", b), r_set, bank([P, 2 * O], name or ("b2", "b3")[b]))
+            for j in range(2):
+                last_product(o_ps[:, j * O : (j + 1) * O], r_set, 2 * b + j)
+
+        def out_tile(r_set, j, name, copy, queue):
+            o_ps = bank([P, O], name)
+            last_product(o_ps[:], r_set, j)
+            o_sb = work.tile([P, O], F32, name="o_last", bufs=2)
+            copy(out=o_sb[:], in_=o_ps[:])
+            queue.dma_start(out=out_v[2 * r_set - 1 + j // 2][:, j % 2, :], in_=o_sb[:])
+
+        def store(r_set, b, copy=nc.scalar.copy):
+            if 2 * r_set + b < 1:
+                return
+            o_sb = work.tile([P, 2 * O], F32, name="o_sb", bufs=2 * GROUPS - 1)
+            copy(out=o_sb[:], in_=get(("o_ps", b), r_set)[:])
+            nc.sync.dma_start(out=out_v[2 * r_set - 1 + b], in_=o_sb[:].rearrange("p (j o) -> p j o", j=2))
 
         p_w = keep.tile([P, PACK, C], BF16, name="p_w")
         for t in range(PACK):
             nc.vector.tensor_scalar(out=p_w[:, t, :], in0=pb_sb[:, t, :].bitcast(FP8), scalar1=ps_sb[:, t : t + 1], scalar2=None, op0=ALU.mult)
-        tx(0, 0, "q0")
-        tx(0, 1, "q1")
+        tx(0, 0, "b1")
+        tx(0, 1, "b6")
         nc.vector.tensor_copy(out=interleaved("p", C), in_=by_fours(p_w[:]))
         a_f = keep.tile([P, PACK], F32, name="a_f")
         nc.scalar.activation(out=a_f[:], in_=a_sb[:], func=ACT.Copy, scale=-1.0)
         a_ps = psum.tile([P, PACK], F32, name="a_ps")
         nc.tensor.matmul(a_ps[:], lhsT=ident[:], rhs=a_f[:], start=True, stop=True)
-        tx(1, 0, "o_ps")
+        tx(1, 0, "b2")
         tx(1, 1)
         sq(0, 0)
         sq(0, 1)
@@ -323,7 +334,7 @@ def tile_ellipticalnormalizedrbfnet_t_kernel(tc, x, a, m, p_bytes, p_scale, lp, 
         gc_f = keep.tile([P, PACK], F32, name="gc_f")
         nc.scalar.activation(out=gc_f[:], in_=gc_sb[:], func=ACT.Copy, scale=float(C))
         nc.scalar.copy(out=interleaved("m", C), in_=by_fours(m_sb[:]))
-        tx(2, 0, "q0")
+        tx(2, 0, "b1")
         h(0, 1)
         k(0, 1)
         quantise("p", C)
@@ -333,7 +344,7 @@ def tile_ellipticalnormalizedrbfnet_t_kernel(tc, x, a, m, p_bytes, p_scale, lp, 
         minus_mean = keep.tile([P, 1], F32, name="minus_mean")
         nc.gpsimd.memset(minus_mean[:], -1.0 / C)
         gp_copy(interleaved("w", O), by_fours(w_sb[:]))
-        gc_ps = bank([P, PACK, P], "pa")
+        gc_ps = bank([P, PACK, P], "b3")
         for t in range(PACK):
             nc.tensor.matmul(gc_ps[:, t, :], lhsT=gc_f[:, t : t + 1].to_broadcast([P, P]), rhs=ident[:], start=True, stop=True)
         sq(1, 1)
@@ -341,13 +352,13 @@ def tile_ellipticalnormalizedrbfnet_t_kernel(tc, x, a, m, p_bytes, p_scale, lp, 
         gc_tok = keep.tile([P, C], F32, name="gc_tok")
         nc.scalar.copy(out=gc_tok[:].rearrange("n (u p e) -> n u p e", u=2, e=2), in_=gc_ps[:].rearrange("n (u e) p -> n u p e", u=2))
         plane(0, 0)
-        plane(0, 1)
+        plane(0, 1, "b4")
         plane(0, 2)
         h(1, 0)
         k(1, 0)
         add_lp(0, 0)
-        plane(0, 3, "pc")
-        tx(2, 1, "o_ps")
+        plane(0, 3, "b5")
+        tx(2, 1, "b2")
         add_lp(0, 1)
         h(1, 1)
         h(2, 0)
@@ -355,79 +366,91 @@ def tile_ellipticalnormalizedrbfnet_t_kernel(tc, x, a, m, p_bytes, p_scale, lp, 
         add_lp(0, 2)
         add_lp(0, 3)
         k(1, 1)
-        tq(0, 0)
-        tq(0, 1)
-        tq(0, 2, "pa")
+        tq(0, 0, "b1", (2, 3))
+        tq(0, 1, "b6", (2, 3))
+        tq(0, 2, "b3", (2, 3))
         quantise("w", O)
         qz(1)
         sq(2, 1)
         sq(3, 0)
         plane(1, 0)
-        plane(1, 1)
+        plane(1, 1, "b4")
         mx(0, 0)
         ex(0, 0)
         k(2, 0)
         add_lp(1, 0)
-        plane(1, 2, "q0")
+        plane(1, 2, "b1")
+        plane(1, 3, "b5")
         mx(0, 1)
-        add_lp(1, 1)
         ex(0, 1)
+        add_lp(1, 1)
+        tq(0, 3, "b6")
         h(2, 1)
         mx(0, 2)
+        tx(3, 1, "b4")
         add_lp(1, 2)
-        plane(1, 3, "pb")
-        tx(3, 1, "o_ps")
+        add_lp(1, 3)
+        ex(0, 2)
         k(2, 1)
+        mx(0, 3)
 
         every = (0, GROUPS)
         order = [
+            (4, qr, (), (1,GROUPS)),
+            (4, qr, (2,2,), (0,1)),
+            (3, ex, (3,), every),
+            (2, tq, (0,), every),
+            (2, tq, (1,"b3",(2,3),), (1,2)),
+            (0, sq, (1,), (3,4)),
             (1, qz, (), every),
-            (0, sq, (0,), (4,GROUPS)),
-            (4, tu, (2,), every),
-            (3, tq, (3,), every),
-            (3, rc, (0,), every),
+            (0, sq, (0,), (5,GROUPS)),
+            (4, ou, (0,), every),
+            (4, ou, (1,), every),
+            (3, rc, (), every),
             (3, us, (0,), every),
             (3, us, (1,), every),
-            (3, gt, (), every),
-            (3, ex, (2,), every),
-            (0, h, (0,), every),
-            (1, plane, (0,), every),
-            (2, add_lp, (3,), every),
-            (4, rr, (2,), every),
-            (4, tu, (3,), every),
-            (5, store, (1,), every),
-            (0, tx, (1,), (4,GROUPS)),
-            (3, mx, (3,), every),
-            (1, add_lp, (0,), every),
-            (4, tw, (), every),
-            (4, rr, (3,), every),
-            (3, ex, (3,), every),
-            (1, plane, (1,), every),
-            (0, h, (1,), every),
-            (4, cw, (), every),
-            (2, tq, (0,), every),
-            (0, k, (0,), every),
-            (2, tq, (1,), every),
-            (0, sq, (1,), every),
-            (2, mx, (0,), every),
-            (1, plane, (2,), every),
-            (1, add_lp, (1,), every),
-            (4, qr, (), every),
-            (2, ex, (0,), every),
-            (3, rc, (1,), every),
+            (3, gt, (), (1,GROUPS)),
             (3, us, (2,), every),
             (3, us, (3,), every),
-            (4, ou, (0,), every),
+            (4, tu, (2,), every),
+            (2, mx, (0,), every),
+            (4, store, (1,), every),
+            (1, plane, (0,), every),
+            (0, h, (0,), every),
+            (2, ex, (0,), every),
+            (2, tq, (1,), (2,GROUPS)),
+            (-1, tx, (0,), (4,5)),
+            (0, tx, (1,), (4,GROUPS)),
+            (4, rr, (2,), every),
+            (1, add_lp, (0,), every),
+            (-1, sq, (0,), (4,5)),
             (2, mx, (1,), every),
-            (1, add_lp, (2,), every),
-            (2, tq, (2,), every),
-            (0, k, (1,), every),
-            (-1, tx, (0,), (1,GROUPS)),
-            (2, ex, (1,), every),
+            (1, plane, (1,), every),
             (4, store, (0,), every),
+            (0, h, (1,), every),
+            (4, tu, (3,), every),
+            (3, tu, (0,"b6",1,), (0,1)),
+            (2, tq, (2,), every),
+            (2, ex, (1,), every),
+            (0, k, (0,), every),
+            (1, plane, (2,), every),
+            (1, add_lp, (1,), every),
+            (0, sq, (1,), (4,GROUPS)),
+            (4, rr, (3,), every),
+            (3, rr, (0,), (0,1)),
+            (3, tu, (1,"b1",1,), (0,1)),
+            (3, tw, (), (1,GROUPS)),
+            (2, tq, (3,), every),
             (2, mx, (2,), every),
+            (1, add_lp, (2,), every),
             (1, plane, (3,), every),
-            (4, ou, (1,), every),
+            (3, cw, (), (1,GROUPS)),
+            (0, k, (1,), every),
+            (3, rr, (1,), (0,1)),
+            (-1, tx, (0,), (5,GROUPS)),
+            (2, ex, (2,), every),
+            (2, mx, (3,), every),
+            (1, add_lp, (3,), every),
         ]
         for step in range(3, GROUPS):
             for lag, stage, args, (first, last) in order:
@@ -435,106 +458,102 @@ def tile_ellipticalnormalizedrbfnet_t_kernel(tc, x, a, m, p_bytes, p_scale, lp, 
                     stage(step - lag, *args)
 
         z = GROUPS - 1
+        tu(z - 3, 2, "xt")
+        tu(z - 3, 3, "b6")
+        qr(z - 3)
+        ex(z - 2, 3)
+        tq(z - 1, 0, "b1", (0, 1))
         qz(z)
-        tu(z - 3, 2)
-        tq(z - 2, 3)
-        tu(z - 3, 3, "xt")
-        tw(z - 3, "pc")
-        rc(z - 2, 0)
+        ou(z - 3, 0)
+        ou(z - 3, 1)
+        tq(z - 1, 1, "b5")
+        rc(z - 2)
         us(z - 2, 0)
         us(z - 2, 1)
         gt(z - 2)
-        ex(z - 2, 2)
-        add_lp(z - 1, 3)
-        rr(z - 3, 2)
-        plane(z, 0, "q0")
-        mx(z - 2, 3)
-        tq(z - 1, 0, "pa")
-        store(z - 4, 1)
-        plane(z, 1, "pb")
-        rr(z - 3, 3)
-        cw(z - 3)
-        tq(z - 1, 1, "o_ps")
-        ex(z - 2, 3)
-        plane(z, 2, "xt")
-        plane(z, 3, "pc")
-        mx(z - 1, 0)
-        add_lp(z, 0)
-        add_lp_vector(z, 1)
-        tq(z - 1, 2, "q1")
-        ex(z - 1, 0)
-        mx(z - 1, 1)
-        tq(z - 1, 3, "q0")
-        add_lp(z, 2)
-        add_lp_vector(z, 3)
-        tw(z - 2, "pb")
-        ex(z - 1, 1)
-        qr(z - 3)
-        rc(z - 2, 1)
         us(z - 2, 2)
         us(z - 2, 3)
-        tq(z, 0, "pa")
-        tq(z, 1, "xt")
+        rr(z - 3, 2)
+        store(z - 3, 0)
+        plane(z, 0, "b4")
+        mx(z - 1, 0)
+        plane(z, 1, "xt")
+        store(z - 3, 1)
+        rr(z - 3, 3)
+        plane(z, 2, "b2")
+        plane(z, 3, "b3")
+        add_lp(z, 0)
+        mx(z - 1, 1)
+        tq(z - 1, 2, "b6")
+        tq(z - 1, 3, "b4", ())
+        add_lp(z, 1)
+        add_lp_vector(z, 3)
+        add_lp(z, 2)
+        ex(z - 1, 0)
         mx(z - 1, 2)
-        cw(z - 2)
-        ou(z - 3, 0, "pc")
+        tq(z, 0, "xt", (0,))
+        tq(z, 1, "b2", (0,))
+        ex(z - 1, 1)
         mx(z - 1, 3)
+        tw(z - 2, "b3")
+        tq(z, 2, "b1", (3,))
         ex(z - 1, 2)
-        rc(z - 1, 0)
+        mx(z, 0)
+        rc(z - 1, 0, 2)
         us(z - 1, 0)
         us(z - 1, 1)
         gt(z - 1)
-        tq(z, 2, "o_ps")
-        mx(z, 0)
-        tu(z - 2, 2, "pb", 1)
+        tq(z, 3, "b5", (3,))
         ex(z - 1, 3)
         mx(z, 1)
-        tu(z - 2, 3, "q1", 1)
-        store(z - 3, 0)
-        rc(z - 1, 1)
-        tq(z, 3, "q0")
-        rr(z - 2, 2)
-        ex(z, 0)
-        ou(z - 3, 1, "pc")
+        cw(z - 2)
+        tu(z - 2, 2, "b6", 1)
         mx(z, 2)
-        dm(z - 1, 2, "pb")
-        ex(z, 1)
-        rr(z - 2, 3)
-        dm(z - 1, 3, "pa")
+        rc(z - 1, 2, 4)
+        tu(z - 2, 3, "b4", 1)
+        qr(z - 2)
+        ex(z, 0)
+        dm(z - 1, 2, "b3")
         mx(z, 3)
+        ex(z, 1)
+        dm(z - 1, 3, "xt")
+        rc(z, 0, 2)
+        rr(z - 2, 2)
         ex(z, 2)
-        rc(z, 0)
+        ua(z, 0)
+        rr(z - 2, 3)
+        ua(z, 1)
+        tu(z, 0, "b4")
+        ou(z - 2, 0, "b6")
+        ou(z - 2, 1, "b2")
         ex(z, 3)
         rd(z - 1, 2)
-        dm(z, 0, "q1")
-        rc(z, 1)
-        tw(z - 1, "xt")
+        tu(z, 1, "b3", 1)
         rd(z - 1, 3)
-        ua(z, 1)
-        qr(z - 2)
-        ua(z, 2)
-        tu(z, 1, "o_ps")
-        cw(z - 1)
-        ou(z - 2, 0, "q0")
-        ou(z - 2, 1, "pb")
-        tu(z, 2, "pa")
-        rd(z, 0)
-        ua(z, 3)
-        rr(z, 1)
-        tu(z, 3, "xt")
-        store(z - 3, 1)
-        qr(z - 1)
+        rc(z, 2, 4)
+        us(z, 2)
+        us(z, 3)
         store(z - 2, 0)
-        rr(z, 2)
-        ou(z - 1, 0, "q1")
-        ou(z - 1, 1, "o_ps")
-        qr_pair(z, 0)
+        tw(z - 1, "b1")
+        rr(z, 0)
         store(z - 2, 1)
-        rr(z, 3)
-        ou(z, 0, "pc")
-        store(z - 1, 0)
-        qr_pair(z, 1)
-        store(z - 1, 1)
-        ou(z, 1, "q0")
+        rr(z, 1)
+        cw(z - 1)
+        tu(z, 2, "b5", 1)
+        qr(z)
+        tu(z, 3, "b6")
+        ou(z, 0, "b4")
+        ou(z, 1, "xt")
+        rr(z, 2)
+        qr(z - 1)
         store(z, 0)
-        store(z, 1, nc.vector.tensor_copy)
+        ou(z - 1, 0, "b2")
+        ou(z - 1, 1, "b3")
+        rr(z, 3)
+        store(z, 1)
+        qr(z + 1, 0, 1)
+        qr(z + 1, 1, 1)
+        store(z - 1, 0)
+        store(z - 1, 1, nc.vector.tensor_copy)
+        out_tile(z + 1, 0, "b1", nc.scalar.copy, nc.scalar)
+        out_tile(z + 1, 1, "b5", nc.vector.tensor_copy, nc.sync)

@@ -21,9 +21,9 @@ PACK = 4
 TOK = 2 * P
 GT = 4 * P
 GROUPS = N // GT
-DIRECT = GROUPS - 1
+DIRECT = GROUPS - 2
 AHEAD = 4
-PLAIN_Q = ((2, 3), (), (), (3,))
+PLAIN_Q = ((0, 1, 2), (), (), (3,))
 
 
 def tile_ellipticalnormalizedrbfnet_t_kernel(tc, x, a, m, p_bytes, p_scale, lp, gc, w, out):
@@ -93,12 +93,12 @@ def tile_ellipticalnormalizedrbfnet_t_kernel(tc, x, a, m, p_bytes, p_scale, lp, 
         def by_fours(rows):
             return rows.rearrange("p t (c i) -> p c t i", i=4)
 
-        def tx(g, b, name="xt"):
+        def tx(g, b, name=None):
             i = 2 * g + b
             if i + AHEAD < 2 * GROUPS:
                 load(i + AHEAD)
             words = get("x", i)[:].rearrange("p j d -> p (j d)").bitcast(F32)
-            xt = put(("xt", b), g, bank([P, 2, TOK], name))
+            xt = put(("xt", b), g, bank([P, 2, TOK], name or ("xt", "b3")[b]))
             half = D // 2
             for j in range(2):
                 for u in range(2):
@@ -145,7 +145,7 @@ def tile_ellipticalnormalizedrbfnet_t_kernel(tc, x, a, m, p_bytes, p_scale, lp, 
             )
 
         def plane(g, s, name=None):
-            qt = put(("qt", s), g, bank([P, GT], name or ("b5", "b1", "b3", "b5")[s]))
+            qt = put(("qt", s), g, bank([P, GT], name or ("b5", "b5", "b1", "b2")[s]))
             codes, scales = get("codes", g), get("scales", g)
             cols = slice(s * P, (s + 1) * P)
             for b, name in enumerate(("m", "p")):
@@ -174,10 +174,11 @@ def tile_ellipticalnormalizedrbfnet_t_kernel(tc, x, a, m, p_bytes, p_scale, lp, 
             else:
                 nc.tensor.transpose(dst, src, ident[:])
 
-        def tq(g, j, name=None, plain=None):
-            q = put(("q", j), g, bank([P, C], name or ("b1", "b6", "b2", "b4")[j]))
-            for s in range(PACK):
-                turn(q[:, s * P : (s + 1) * P], get(("ql", s), g)[:, j * P : (j + 1) * P], s in (PLAIN_Q[j] if plain is None else plain))
+        def tq(g, j, name=None, plain=None, first=0, last=PACK):
+            if first == 0:
+                put(("q", j), g, bank([P, C], name or ("b1", "b6", "xt", "b6")[j]))
+            for s in range(first, last):
+                turn(get(("q", j), g)[:, s * P : (s + 1) * P], get(("ql", s), g)[:, j * P : (j + 1) * P], s in (PLAIN_Q[j] if plain is None else plain))
 
         def mx(g, j):
             nm = put(("nm", j), g, work.tile([P, 1], F32, name="nm" + str(j)))
@@ -187,7 +188,7 @@ def tile_ellipticalnormalizedrbfnet_t_kernel(tc, x, a, m, p_bytes, p_scale, lp, 
             e = put(("e", j), g, work.tile([P, C], F32, name="e" + str(j), bufs=2))
             if j == 0:
                 put("ssum", g, work.tile([P, 4], F32, name="ssum"))
-            if j >= 2 or g == 0 or g >= DIRECT:
+            if j >= 2 or g >= DIRECT:
                 e_v = e[:].rearrange("n (t p) -> n t p", t=PACK)
                 q_v = get(("q", j), g)[:].rearrange("n (p t) -> n t p", t=PACK)
             else:
@@ -225,7 +226,7 @@ def tile_ellipticalnormalizedrbfnet_t_kernel(tc, x, a, m, p_bytes, p_scale, lp, 
             r_tok = put("r_tok", g, work.tile([P, 2, C], BF16, name="r_tok", bufs=2))
             nc.gpsimd.tensor_tensor(out=r_tok[:], in0=get(("u", 0), g)[:], in1=gc_tok[:].unsqueeze(1).to_broadcast([P, 2, C]), op=ALU.mult)
 
-        def tw(g, name="b1"):
+        def tw(g, name="b4"):
             words = get("r_tok", g)[:].rearrange("n j c -> n (j c)").bitcast(F32)
             rw = put("rw", g, bank([P, PACK, P], name))
             for ju in range(4):
@@ -326,7 +327,7 @@ def tile_ellipticalnormalizedrbfnet_t_kernel(tc, x, a, m, p_bytes, p_scale, lp, 
         a_ps = psum.tile([P, PACK], F32, name="a_ps")
         nc.tensor.matmul(a_ps[:], lhsT=ident[:], rhs=a_f[:], start=True, stop=True)
         tx(1, 0, "b2")
-        tx(1, 1)
+        tx(1, 1, "xt")
         sq(0, 0)
         sq(0, 1)
         h(0, 0)
@@ -384,176 +385,211 @@ def tile_ellipticalnormalizedrbfnet_t_kernel(tc, x, a, m, p_bytes, p_scale, lp, 
         mx(0, 1)
         ex(0, 1)
         add_lp(1, 1)
-        tq(0, 3, "b6")
+        tq(0, 3, "b6", (2, 3))
         h(2, 1)
         mx(0, 2)
-        tx(3, 1, "b4")
+        tx(3, 1, "b2")
         add_lp(1, 2)
         add_lp(1, 3)
         ex(0, 2)
         k(2, 1)
         mx(0, 3)
+        tq(1, 0)
+        tq(1, 1, "b4", (2, 3))
+        qz(2)
+        ex(0, 3)
+        tq(1, 2, "b6", (2, 3))
+        sq(3, 1)
+        plane(2, 0)
+        plane(2, 1, "b3")
+        rc(0)
+        us(0, 0)
+        us(0, 1)
+        gt(0)
+        us(0, 2)
+        mx(1, 0)
+        h(3, 0)
+        tx(4, 0)
+        ex(1, 0)
+        mx(1, 1)
+        add_lp(2, 0)
+        plane(2, 2)
+        h(3, 1)
+        plane(2, 3)
+        ex(1, 1)
+        tq(1, 3, "b4")
+        k(3, 0)
+        add_lp(2, 1)
+        sq(4, 0)
+        mx(1, 2)
+        tw(0, "b3")
+        k(3, 1)
+        add_lp(2, 2)
+        ex(1, 2)
+        mx(1, 3)
+        cw(0)
+        add_lp(2, 3)
+        tq(2, 0)
 
         every = (0, GROUPS)
         order = [
+            (1, qz, (), every),
+            (4, tu, (2,"b2",), (0,1)),
+            (4, tu, (2,), (1,GROUPS)),
+            (3, ex, (3,), every),
             (4, qr, (), (1,GROUPS)),
             (4, qr, (2,2,), (0,1)),
-            (3, ex, (3,), every),
-            (2, tq, (0,), every),
-            (2, tq, (1,"b3",(2,3),), (1,2)),
-            (0, sq, (1,), (3,4)),
-            (1, qz, (), every),
+            (0, h, (0,), (4,5)),
             (0, sq, (0,), (5,GROUPS)),
-            (4, ou, (0,), every),
-            (4, ou, (1,), every),
+            (1, plane, (0,), every),
             (3, rc, (), every),
             (3, us, (0,), every),
             (3, us, (1,), every),
-            (3, gt, (), (1,GROUPS)),
+            (3, gt, (), every),
             (3, us, (2,), every),
             (3, us, (3,), every),
-            (4, tu, (2,), every),
+            (4, ou, (0,), every),
             (2, mx, (0,), every),
-            (4, store, (1,), every),
-            (1, plane, (0,), every),
-            (0, h, (0,), every),
-            (2, ex, (0,), every),
-            (2, tq, (1,), (2,GROUPS)),
-            (-1, tx, (0,), (4,5)),
-            (0, tx, (1,), (4,GROUPS)),
+            (2, tq, (1,), every),
+            (5, store, (1,), every),
+            (4, ua, (3,), (0,1)),
+            (0, tx, (1,), every),
             (4, rr, (2,), every),
             (1, add_lp, (0,), every),
-            (-1, sq, (0,), (4,5)),
-            (2, mx, (1,), every),
+            (4, tu, (3,None,1,), every),
             (1, plane, (1,), every),
+            (0, h, (0,), (5,GROUPS)),
             (4, store, (0,), every),
-            (0, h, (1,), every),
-            (4, tu, (3,), every),
-            (3, tu, (0,"b6",1,), (0,1)),
             (2, tq, (2,), every),
-            (2, ex, (1,), every),
-            (0, k, (0,), every),
+            (2, mx, (1,), every),
+            (2, ex, (0,), every),
             (1, plane, (2,), every),
-            (1, add_lp, (1,), every),
-            (0, sq, (1,), (4,GROUPS)),
+            (0, k, (0,), every),
+            (0, sq, (1,), every),
+            (1, plane, (3,), every),
             (4, rr, (3,), every),
-            (3, rr, (0,), (0,1)),
-            (3, tu, (1,"b1",1,), (0,1)),
-            (3, tw, (), (1,GROUPS)),
+            (2, ex, (1,), every),
             (2, tq, (3,), every),
             (2, mx, (2,), every),
+            (1, add_lp, (1,), every),
+            (3, tw, (), every),
+            (0, h, (1,), every),
+            (4, ou, (1,), every),
             (1, add_lp, (2,), every),
-            (1, plane, (3,), every),
-            (3, cw, (), (1,GROUPS)),
             (0, k, (1,), every),
-            (3, rr, (1,), (0,1)),
-            (-1, tx, (0,), (5,GROUPS)),
             (2, ex, (2,), every),
-            (2, mx, (3,), every),
+            (-1, tx, (0,), (1,GROUPS)),
             (1, add_lp, (3,), every),
+            (1, tq, (0,), every),
+            (2, mx, (3,), every),
+            (3, cw, (), every),
         ]
-        for step in range(3, GROUPS):
+        for step in range(4, GROUPS):
             for lag, stage, args, (first, last) in order:
                 if first <= step - lag < last:
                     stage(step - lag, *args)
 
         z = GROUPS - 1
-        tu(z - 3, 2, "xt")
-        tu(z - 3, 3, "b6")
-        qr(z - 3)
-        ex(z - 2, 3)
-        tq(z - 1, 0, "b1", (0, 1))
         qz(z)
-        ou(z - 3, 0)
-        ou(z - 3, 1)
-        tq(z - 1, 1, "b5")
+        tu(z - 3, 2, "xt")
+        tu(z - 3, 3, "b5", 1)
+        tq(z - 1, 1, "b2")
+        ex(z - 2, 3)
+        qr(z - 3)
+        store(z - 4, 1)
+        plane(z, 0, "b4")
+        plane(z, 1, "b6")
+        plane(z, 2, "b3")
         rc(z - 2)
         us(z - 2, 0)
         us(z - 2, 1)
         gt(z - 2)
         us(z - 2, 2)
         us(z - 2, 3)
-        rr(z - 3, 2)
-        store(z - 3, 0)
-        plane(z, 0, "b4")
         mx(z - 1, 0)
-        plane(z, 1, "xt")
-        store(z - 3, 1)
-        rr(z - 3, 3)
-        plane(z, 2, "b2")
-        plane(z, 3, "b3")
+        rr(z - 3, 2)
+        plane(z, 3, "xt")
         add_lp(z, 0)
         mx(z - 1, 1)
-        tq(z - 1, 2, "b6")
-        tq(z - 1, 3, "b4", ())
         add_lp(z, 1)
-        add_lp_vector(z, 3)
+        tq(z - 1, 2, "b4")
+        tq(z - 1, 3, "b6", ())
+        rr(z - 3, 3)
         add_lp(z, 2)
+        add_lp_vector(z, 3)
+        ou(z - 3, 0, "b5")
         ex(z - 1, 0)
         mx(z - 1, 2)
-        tq(z, 0, "xt", (0,))
-        tq(z, 1, "b2", (0,))
+        tq(z, 0, "b3", ())
+        tq(z, 1, "xt", (3,))
         ex(z - 1, 1)
         mx(z - 1, 3)
-        tw(z - 2, "b3")
         tq(z, 2, "b1", (3,))
-        ex(z - 1, 2)
+        store(z - 3, 0)
+        tq(z, 3, "b2", (3,))
         mx(z, 0)
+        ex(z - 1, 2)
+        tw(z - 2, "b5")
         rc(z - 1, 0, 2)
+        mx(z, 1)
+        ex(z - 1, 3)
+        tu(z - 2, 2, "b4", 1)
+        mx(z, 2)
+        ex(z, 0)
+        rc(z - 1, 2, 4)
         us(z - 1, 0)
         us(z - 1, 1)
-        gt(z - 1)
-        tq(z, 3, "b5", (3,))
-        ex(z - 1, 3)
-        mx(z, 1)
+        us(z - 1, 2)
+        ou(z - 3, 1, "b6")
         cw(z - 2)
-        tu(z - 2, 2, "b6", 1)
-        mx(z, 2)
-        rc(z - 1, 2, 4)
-        tu(z - 2, 3, "b4", 1)
-        qr(z - 2)
-        ex(z, 0)
-        dm(z - 1, 2, "b3")
+        tu(z - 2, 3, "b3", 1)
         mx(z, 3)
         ex(z, 1)
-        dm(z - 1, 3, "xt")
-        rc(z, 0, 2)
         rr(z - 2, 2)
+        tu(z - 1, 0, "b5", 1)
         ex(z, 2)
-        ua(z, 0)
         rr(z - 2, 3)
-        ua(z, 1)
-        tu(z, 0, "b4")
-        ou(z - 2, 0, "b6")
-        ou(z - 2, 1, "b2")
+        rc(z, 0, 2)
         ex(z, 3)
-        rd(z - 1, 2)
-        tu(z, 1, "b3", 1)
-        rd(z - 1, 3)
+        tu(z - 1, 1, "b4", 1)
+        ua(z - 1, 3)
+        rr(z - 1, 0)
+        tu(z - 1, 2, "b3", 1)
+        qr(z - 2)
         rc(z, 2, 4)
-        us(z, 2)
         us(z, 3)
-        store(z - 2, 0)
-        tw(z - 1, "b1")
-        rr(z, 0)
-        store(z - 2, 1)
-        rr(z, 1)
-        cw(z - 1)
-        tu(z, 2, "b5", 1)
-        qr(z)
-        tu(z, 3, "b6")
-        ou(z, 0, "b4")
-        ou(z, 1, "xt")
-        rr(z, 2)
+        ua(z, 0)
+        tu(z - 1, 3, "b2")
+        ou(z - 2, 0, "xt")
+        ou(z - 2, 1, "b1")
+        rr(z - 1, 1)
+        ua(z, 1)
+        tu(z, 0, "b5")
+        ua(z, 2)
+        rr(z - 1, 2)
+        tu(z, 1, "b4", 1)
+        store(z - 3, 1)
         qr(z - 1)
-        store(z, 0)
-        ou(z - 1, 0, "b2")
-        ou(z - 1, 1, "b3")
-        rr(z, 3)
-        store(z, 1)
-        qr(z + 1, 0, 1)
-        qr(z + 1, 1, 1)
+        tu(z, 2, "b3", 1)
+        store(z - 2, 0)
+        ou(z - 1, 0, "b6")
+        rr(z - 1, 3)
+        store(z - 2, 1)
+        ou(z - 1, 1, "xt")
+        tu(z, 3, "b2", 1)
+        rr(z, 0)
+        qr(z, 0, 2)
         store(z - 1, 0)
-        store(z - 1, 1, nc.vector.tensor_copy)
-        out_tile(z + 1, 0, "b1", nc.scalar.copy, nc.scalar)
-        out_tile(z + 1, 1, "b5", nc.vector.tensor_copy, nc.sync)
+        ou(z, 0, "b1")
+        rr(z, 1)
+        store(z - 1, 1)
+        rr(z, 2)
+        store(z, 0)
+        qr(z, 2, 2)
+        ou(z, 1, "b5")
+        rr(z, 3)
+        qr(z + 1, 0, 1)
+        store(z, 1)
+        qr(z + 1, 1, 1)
+        out_tile(z + 1, 0, "b4", nc.vector.tensor_copy, nc.sync)
+        out_tile(z + 1, 1, "b3", nc.scalar.copy, nc.scalar)

@@ -354,7 +354,7 @@ def tile_ellipticalnormalizedrbfnet_t_kernel(tc, x, a, m, p_bytes, p_scale, lp, 
         nc.scalar.copy(out=gc_tok[:].rearrange("n (u p e) -> n u p e", u=2, e=2), in_=gc_ps[:].rearrange("n (u e) p -> n u p e", u=2))
         plane(0, 0)
         plane(0, 1, "b4")
-        plane(0, 2)
+        plane(0, 2, "b3")
         h(1, 0)
         k(1, 0)
         add_lp(0, 0)

@@ -21,9 +21,8 @@ PACK = 4
 TOK = 2 * P
 GT = 4 * P
 GROUPS = N // GT
-DIRECT = GROUPS - 2
+WORD_TILES = {0: 2, GROUPS - 3: 2, GROUPS - 2: 0, GROUPS - 1: 0}
 AHEAD = 4
-PLAIN_Q = ((0, 1, 2), (), (), (3,))
 
 
 def tile_ellipticalnormalizedrbfnet_t_kernel(tc, x, a, m, p_bytes, p_scale, lp, gc, w, out):
@@ -130,7 +129,7 @@ def tile_ellipticalnormalizedrbfnet_t_kernel(tc, x, a, m, p_bytes, p_scale, lp, 
                 out=hk_part(g, 1, b).rearrange("p (r t) -> p r t", t=PACK),
                 in0=get(("x2", b), g)[:].rearrange("p (r t) -> p r t", t=PACK),
                 scalar=-1.0,
-                in1=a_ps[:].unsqueeze(1).to_broadcast([P, TOK, PACK]),
+                in1=a_ps.unsqueeze(1).to_broadcast([P, TOK, PACK]),
                 op0=ALU.add,
                 op1=ALU.mult,
             )
@@ -174,21 +173,24 @@ def tile_ellipticalnormalizedrbfnet_t_kernel(tc, x, a, m, p_bytes, p_scale, lp, 
             else:
                 nc.tensor.transpose(dst, src, ident[:])
 
-        def tq(g, j, name=None, plain=None, first=0, last=PACK):
+        def tq(g, j, name=None, plain=(), first=0, last=PACK):
             if first == 0:
                 put(("q", j), g, bank([P, C], name or ("b1", "b6", "xt", "b6")[j]))
             for s in range(first, last):
-                turn(get(("q", j), g)[:, s * P : (s + 1) * P], get(("ql", s), g)[:, j * P : (j + 1) * P], s in (PLAIN_Q[j] if plain is None else plain))
+                turn(get(("q", j), g)[:, s * P : (s + 1) * P], get(("ql", s), g)[:, j * P : (j + 1) * P], s in plain)
 
         def mx(g, j):
             nm = put(("nm", j), g, work.tile([P, 1], F32, name="nm" + str(j)))
             nc.vector.tensor_reduce(out=nm[:], in_=get(("q", j), g)[:], axis=AX.X, op=ALU.max, negate=True)
 
+        def by_words(g):
+            return WORD_TILES.get(g, 3)
+
         def ex(g, j):
             e = put(("e", j), g, work.tile([P, C], F32, name="e" + str(j), bufs=2))
             if j == 0:
                 put("ssum", g, work.tile([P, 4], F32, name="ssum"))
-            if j >= 2 or g >= DIRECT:
+            if j >= by_words(g):
                 e_v = e[:].rearrange("n (t p) -> n t p", t=PACK)
                 q_v = get(("q", j), g)[:].rearrange("n (p t) -> n t p", t=PACK)
             else:
@@ -203,9 +205,9 @@ def tile_ellipticalnormalizedrbfnet_t_kernel(tc, x, a, m, p_bytes, p_scale, lp, 
             nc.vector.reciprocal(out=get("rs", g)[:, first:last], in_=get("ssum", g)[:, first:last])
 
         def u_part(g, j):
-            if (("u", j // 2), g) not in st:
-                put(("u", j // 2), g, work.tile([P, 2, C], F32, name="u" + str(j // 2)))
-            return get(("u", j // 2), g)[:, j % 2, :]
+            if ("u", g) not in st:
+                put("u", g, work.tile([P, 4, C], F32, name="u", bufs=2))
+            return get("u", g)[:, j, :]
 
         def us(g, j, engine=nc.gpsimd):
             engine.tensor_scalar(
@@ -222,44 +224,49 @@ def tile_ellipticalnormalizedrbfnet_t_kernel(tc, x, a, m, p_bytes, p_scale, lp, 
                 out=u_part(g, j), in_=get(("e", j), g)[:], func=ACT.Identity, scale=get("rs", g)[:, j : j + 1], bias=minus_mean[:]
             )
 
-        def gt(g):
-            r_tok = put("r_tok", g, work.tile([P, 2, C], BF16, name="r_tok", bufs=2))
-            nc.gpsimd.tensor_tensor(out=r_tok[:], in0=get(("u", 0), g)[:], in1=gc_tok[:].unsqueeze(1).to_broadcast([P, 2, C]), op=ALU.mult)
+        def gt(g, tiles=3):
+            r_tok = put("r_tok", g, work.tile([P, 3, C], BF16, name="r_tok", bufs=2))
+            nc.gpsimd.tensor_tensor(
+                out=r_tok[:, 0:tiles, :], in0=get("u", g)[:, 0:tiles, :], in1=gc_tok[:].unsqueeze(1).to_broadcast([P, tiles, C]), op=ALU.mult
+            )
 
-        def tw(g, name="b4"):
+        def tw(g, first, tiles, name):
             words = get("r_tok", g)[:].rearrange("n j c -> n (j c)").bitcast(F32)
-            rw = put("rw", g, bank([P, PACK, P], name))
-            for ju in range(4):
-                nc.tensor.transpose(rw[:, ju, :], words[:, ju * P : (ju + 1) * P], ident[:])
+            rw = put(("rw", first), g, bank([P, 2 * tiles, P], name))
+            for ju in range(2 * tiles):
+                nc.tensor.transpose(rw[:, ju, :], words[:, (2 * first + ju) * P : (2 * first + ju + 1) * P], ident[:])
 
         def r_cols(g, j, tiles=1):
-            r_set, first = g + j // 2, (j + 2) % 4
-            if ("r", r_set) not in st:
-                put("r", r_set, work.tile([P, GT, PACK], BF16, name="r", align_bytes=64))
-            return get("r", r_set)[:, first * P : (first + tiles) * P, :]
+            if ("r", g) not in st:
+                put("r", g, work.tile([P, GT, PACK], BF16, name="r", align_bytes=64))
+            return get("r", g)[:, j * P : (j + tiles) * P, :]
 
-        def cw(g):
-            words = r_cols(g, 0, 2).rearrange("p n s -> p (n s)").bitcast(F32)
-            nc.scalar.copy(out=words.rearrange("p (j n u) -> p j n u", j=2, u=2), in_=get("rw", g)[:].rearrange("p (j u) n -> p j n u", u=2))
+        def cw(g, first, tiles, copy):
+            words = r_cols(g, first, tiles).rearrange("p n s -> p (n s)").bitcast(F32)
+            copy(out=words.rearrange("p (j n u) -> p j n u", j=tiles, u=2), in_=get(("rw", first), g)[:].rearrange("p (j u) n -> p j n u", u=2))
 
         def tu(g, j, name=None, plain=0):
             ut = put(("ut", j), g, bank([P, PACK, P], name or "b4"))
-            u = get(("u", j // 2), g)
+            u = get("u", g)
             for s in range(PACK):
-                turn(ut[:, s, :], u[:, j % 2, s * P : (s + 1) * P], s >= PACK - plain)
+                turn(ut[:, s, :], u[:, j, s * P : (s + 1) * P], s >= PACK - plain)
 
         def rr(g, j):
             nc.vector.tensor_tensor(
                 out=r_cols(g, j), in0=get(("ut", j), g)[:].rearrange("p s n -> p n s"), in1=gc_f[:].unsqueeze(1).to_broadcast([P, P, PACK]), op=ALU.mult
             )
 
-        def dm(g, j, name):
-            diag = work.tile([P, P], F32, name="diag")
-            nc.scalar.activation(out=diag[:], in_=ident[:], func=ACT.Copy, scale=get("rs", g)[:, j : j + 1])
-            ut = put(("ut", j), g, bank([P, PACK, P], name))
-            e = get(("e", j), g)
-            for s in range(PACK):
-                nc.tensor.matmul(ut[:, s, :], lhsT=e[:, s * P : (s + 1) * P], rhs=diag[:], start=True, stop=True)
+        def dg(g, j):
+            diag = put(("diag", j), g, work.tile([P, P], F32, name="diag"))
+            nc.vector.tensor_scalar(out=diag[:], in0=ident_ps, scalar1=get("rs", g)[:, j : j + 1], scalar2=None, op0=ALU.mult)
+
+        def dm(g, j, name, first=0, last=PACK):
+            if first == 0:
+                put(("ut", j), g, bank([P, PACK, P], name))
+            for s in range(first, last):
+                nc.tensor.matmul(
+                    get(("ut", j), g)[:, s, :], lhsT=get(("e", j), g)[:, s * P : (s + 1) * P], rhs=get(("diag", j), g)[:], start=True, stop=True
+                )
 
         def rd(g, j):
             nc.vector.scalar_tensor_tensor(
@@ -296,8 +303,6 @@ def tile_ellipticalnormalizedrbfnet_t_kernel(tc, x, a, m, p_bytes, p_scale, lp, 
             )
 
         def ou(r_set, b, name=None):
-            if 2 * r_set + b < 1:
-                return
             o_ps = put(("o_ps", b), r_set, bank([P, 2 * O], name or ("b2", "b3")[b]))
             for j in range(2):
                 last_product(o_ps[:, j * O : (j + 1) * O], r_set, 2 * b + j)
@@ -307,14 +312,12 @@ def tile_ellipticalnormalizedrbfnet_t_kernel(tc, x, a, m, p_bytes, p_scale, lp, 
             last_product(o_ps[:], r_set, j)
             o_sb = work.tile([P, O], F32, name="o_last", bufs=2)
             copy(out=o_sb[:], in_=o_ps[:])
-            queue.dma_start(out=out_v[2 * r_set - 1 + j // 2][:, j % 2, :], in_=o_sb[:])
+            queue.dma_start(out=out_v[2 * r_set + j // 2][:, j % 2, :], in_=o_sb[:])
 
         def store(r_set, b, copy=nc.scalar.copy):
-            if 2 * r_set + b < 1:
-                return
             o_sb = work.tile([P, 2 * O], F32, name="o_sb", bufs=2 * GROUPS - 1)
             copy(out=o_sb[:], in_=get(("o_ps", b), r_set)[:])
-            nc.sync.dma_start(out=out_v[2 * r_set - 1 + b], in_=o_sb[:].rearrange("p (j o) -> p j o", j=2))
+            nc.sync.dma_start(out=out_v[2 * r_set + b], in_=o_sb[:].rearrange("p (j o) -> p j o", j=2))
 
         p_w = keep.tile([P, PACK, C], BF16, name="p_w")
         for t in range(PACK):
@@ -324,8 +327,10 @@ def tile_ellipticalnormalizedrbfnet_t_kernel(tc, x, a, m, p_bytes, p_scale, lp, 
         nc.vector.tensor_copy(out=interleaved("p", C), in_=by_fours(p_w[:]))
         a_f = keep.tile([P, PACK], F32, name="a_f")
         nc.scalar.activation(out=a_f[:], in_=a_sb[:], func=ACT.Copy, scale=-1.0)
-        a_ps = psum.tile([P, PACK], F32, name="a_ps")
-        nc.tensor.matmul(a_ps[:], lhsT=ident[:], rhs=a_f[:], start=True, stop=True)
+        side = psum.tile([P, P + PACK], F32, name="side")
+        ident_ps, a_ps = side[:, 0:P], side[:, P : P + PACK]
+        nc.tensor.transpose(ident_ps, ident[:], ident[:])
+        nc.tensor.matmul(a_ps, lhsT=ident[:], rhs=a_f[:], start=True, stop=True)
         tx(1, 0, "b2")
         tx(1, 1, "xt")
         sq(0, 0)
@@ -394,7 +399,7 @@ def tile_ellipticalnormalizedrbfnet_t_kernel(tc, x, a, m, p_bytes, p_scale, lp, 
         ex(0, 2)
         k(2, 1)
         mx(0, 3)
-        tq(1, 0)
+        tq(1, 0, None, (0, 1, 2))
         tq(1, 1, "b4", (2, 3))
         qz(2)
         ex(0, 3)
@@ -405,7 +410,7 @@ def tile_ellipticalnormalizedrbfnet_t_kernel(tc, x, a, m, p_bytes, p_scale, lp, 
         rc(0)
         us(0, 0)
         us(0, 1)
-        gt(0)
+        gt(0, 2)
         us(0, 2)
         mx(1, 0)
         h(3, 0)
@@ -417,49 +422,50 @@ def tile_ellipticalnormalizedrbfnet_t_kernel(tc, x, a, m, p_bytes, p_scale, lp, 
         h(3, 1)
         plane(2, 3)
         ex(1, 1)
-        tq(1, 3, "b4")
+        tq(1, 3, "b4", (3,))
         k(3, 0)
         add_lp(2, 1)
         sq(4, 0)
         mx(1, 2)
-        tw(0, "b3")
+        tw(0, 0, 2, "b3")
         k(3, 1)
         add_lp(2, 2)
         ex(1, 2)
         mx(1, 3)
-        cw(0)
+        tq(2, 0, None, (0, 1, 2), 0, 3)
         add_lp(2, 3)
-        tq(2, 0)
 
         every = (0, GROUPS)
         order = [
             (1, qz, (), every),
-            (4, tu, (2,"b2",), (0,1)),
-            (4, tu, (2,), (1,GROUPS)),
+            (2, tq, (0,None,(),3,4,), every),
+            (2, tq, (1,), (2,3)),
+            (4, tu, (2,"b2",1,), (0,1)),
+            (4, tw, (0,2,"b3",), (1,GROUPS)),
             (3, ex, (3,), every),
-            (4, qr, (), (1,GROUPS)),
-            (4, qr, (2,2,), (0,1)),
+            (5, qr, (), every),
             (0, h, (0,), (4,5)),
             (0, sq, (0,), (5,GROUPS)),
             (1, plane, (0,), every),
             (3, rc, (), every),
             (3, us, (0,), every),
             (3, us, (1,), every),
-            (3, gt, (), every),
             (3, us, (2,), every),
-            (3, us, (3,), every),
-            (4, ou, (0,), every),
+            (3, gt, (), every),
+            (5, ou, (0,), every),
             (2, mx, (0,), every),
-            (2, tq, (1,), every),
-            (5, store, (1,), every),
-            (4, ua, (3,), (0,1)),
+            (2, tq, (1,None,(3,),), (3,GROUPS)),
+            (4, cw, (0,2,nc.scalar.copy,), every),
             (0, tx, (1,), every),
-            (4, rr, (2,), every),
+            (4, ua, (3,), (0,1)),
+            (4, rr, (2,), (0,1)),
+            (4, rd, (3,), (1,GROUPS)),
             (1, add_lp, (0,), every),
-            (4, tu, (3,None,1,), every),
+            (4, tw, (2,1,"b4",), (1,GROUPS)),
+            (4, tu, (3,"b4",1,), (0,1)),
             (1, plane, (1,), every),
             (0, h, (0,), (5,GROUPS)),
-            (4, store, (0,), every),
+            (5, store, (0,), every),
             (2, tq, (2,), every),
             (2, mx, (1,), every),
             (2, ex, (0,), every),
@@ -467,22 +473,27 @@ def tile_ellipticalnormalizedrbfnet_t_kernel(tc, x, a, m, p_bytes, p_scale, lp, 
             (0, k, (0,), every),
             (0, sq, (1,), every),
             (1, plane, (3,), every),
-            (4, rr, (3,), every),
+            (4, cw, (2,1,nc.vector.tensor_copy,), (1,GROUPS)),
+            (4, rr, (3,), (0,1)),
+            (3, dg, (3,), every),
             (2, ex, (1,), every),
             (2, tq, (3,), every),
+            (3, dm, (3,"b4",0,1,), every),
             (2, mx, (2,), every),
             (1, add_lp, (1,), every),
-            (3, tw, (), every),
+            (3, dm, (3,"b4",1,2,), every),
             (0, h, (1,), every),
-            (4, ou, (1,), every),
+            (5, ou, (1,), every),
             (1, add_lp, (2,), every),
             (0, k, (1,), every),
             (2, ex, (2,), every),
             (-1, tx, (0,), (1,GROUPS)),
+            (3, dm, (3,"b4",2,3,), every),
+            (1, tq, (0,None,(),0,3,), every),
+            (3, dm, (3,"b4",3,4,), every),
             (1, add_lp, (3,), every),
-            (1, tq, (0,), every),
             (2, mx, (3,), every),
-            (3, cw, (), every),
+            (5, store, (1,), every),
         ]
         for step in range(4, GROUPS):
             for lag, stage, args, (first, last) in order:
@@ -491,105 +502,108 @@ def tile_ellipticalnormalizedrbfnet_t_kernel(tc, x, a, m, p_bytes, p_scale, lp, 
 
         z = GROUPS - 1
         qz(z)
-        tu(z - 3, 2, "xt")
-        tu(z - 3, 3, "b5", 1)
-        tq(z - 1, 1, "b2")
+        tq(z - 1, 0, None, (), 3, 4)
+        tw(z - 3, 0, 2, "b3")
+        tw(z - 3, 2, 1, "xt")
+        tq(z - 1, 1, "b2", (3,))
         ex(z - 2, 3)
-        qr(z - 3)
-        store(z - 4, 1)
-        plane(z, 0, "b4")
+        qr(z - 4)
+        cw(z - 3, 0, 2, nc.scalar.copy)
+        plane(z, 0, "b5")
         plane(z, 1, "b6")
+        cw(z - 3, 2, 1, nc.scalar.copy)
         plane(z, 2, "b3")
         rc(z - 2)
         us(z - 2, 0)
         us(z - 2, 1)
-        gt(z - 2)
+        gt(z - 2, 2)
         us(z - 2, 2)
         us(z - 2, 3)
-        mx(z - 1, 0)
-        rr(z - 3, 2)
+        rd(z - 3, 3)
         plane(z, 3, "xt")
+        mx(z - 1, 0)
         add_lp(z, 0)
         mx(z - 1, 1)
+        qr(z - 3)
+        ou(z - 4, 0, "b4")
         add_lp(z, 1)
-        tq(z - 1, 2, "b4")
-        tq(z - 1, 3, "b6", ())
-        rr(z - 3, 3)
+        tq(z - 1, 2, "b5")
+        tq(z - 1, 3, "b6")
         add_lp(z, 2)
         add_lp_vector(z, 3)
-        ou(z - 3, 0, "b5")
         ex(z - 1, 0)
         mx(z - 1, 2)
-        tq(z, 0, "b3", ())
+        tq(z, 0, "b3")
         tq(z, 1, "xt", (3,))
         ex(z - 1, 1)
         mx(z - 1, 3)
         tq(z, 2, "b1", (3,))
-        store(z - 3, 0)
+        store(z - 4, 0)
         tq(z, 3, "b2", (3,))
         mx(z, 0)
         ex(z - 1, 2)
-        tw(z - 2, "b5")
+        ou(z - 4, 1, "b4")
         rc(z - 1, 0, 2)
         mx(z, 1)
         ex(z - 1, 3)
-        tu(z - 2, 2, "b4", 1)
+        tw(z - 2, 0, 2, "b5")
         mx(z, 2)
         ex(z, 0)
+        tu(z - 2, 2, "b6", 1)
         rc(z - 1, 2, 4)
         us(z - 1, 0)
         us(z - 1, 1)
         us(z - 1, 2)
-        ou(z - 3, 1, "b6")
-        cw(z - 2)
+        store(z - 4, 1, nc.vector.tensor_copy)
         tu(z - 2, 3, "b3", 1)
         mx(z, 3)
         ex(z, 1)
+        ou(z - 3, 0, "b4")
+        cw(z - 2, 0, 2, nc.scalar.copy)
         rr(z - 2, 2)
         tu(z - 1, 0, "b5", 1)
         ex(z, 2)
         rr(z - 2, 3)
         rc(z, 0, 2)
         ex(z, 3)
-        tu(z - 1, 1, "b4", 1)
+        tu(z - 1, 1, "b6", 1)
         ua(z - 1, 3)
         rr(z - 1, 0)
         tu(z - 1, 2, "b3", 1)
         qr(z - 2)
         rc(z, 2, 4)
+        us(z, 2)
         us(z, 3)
         ua(z, 0)
-        tu(z - 1, 3, "b2")
-        ou(z - 2, 0, "xt")
-        ou(z - 2, 1, "b1")
+        tu(z - 1, 3, "xt")
+        ou(z - 3, 1, "b1")
+        ou(z - 2, 0, "b2")
         rr(z - 1, 1)
         ua(z, 1)
         tu(z, 0, "b5")
-        ua(z, 2)
+        store(z - 3, 0)
         rr(z - 1, 2)
-        tu(z, 1, "b4", 1)
+        ou(z - 2, 1, "b4")
+        tu(z, 1, "b6", 1)
         store(z - 3, 1)
-        qr(z - 1)
+        rr(z - 1, 3)
         tu(z, 2, "b3", 1)
         store(z - 2, 0)
-        ou(z - 1, 0, "b6")
-        rr(z - 1, 3)
-        store(z - 2, 1)
-        ou(z - 1, 1, "xt")
-        tu(z, 3, "b2", 1)
         rr(z, 0)
-        qr(z, 0, 2)
-        store(z - 1, 0)
-        ou(z, 0, "b1")
+        tu(z, 3, "xt", 1)
+        qr(z - 1)
+        store(z - 2, 1)
+        ou(z - 1, 0, "b1")
+        ou(z - 1, 1, "b2")
         rr(z, 1)
-        store(z - 1, 1)
         rr(z, 2)
-        store(z, 0)
-        qr(z, 2, 2)
-        ou(z, 1, "b5")
+        store(z - 1, 0)
+        qr(z, 0, 2)
+        ou(z, 0, "b5")
         rr(z, 3)
-        qr(z + 1, 0, 1)
-        store(z, 1)
-        qr(z + 1, 1, 1)
-        out_tile(z + 1, 0, "b4", nc.vector.tensor_copy, nc.sync)
-        out_tile(z + 1, 1, "b3", nc.scalar.copy, nc.scalar)
+        store(z - 1, 1)
+        qr(z, 2, 1)
+        store(z, 0)
+        qr(z, 3, 1)
+        out_tile(z, 2, "b4", nc.vector.tensor_copy, nc.sync)
+        out_tile(z, 3, "b6", nc.scalar.copy, nc.scalar)

@@ -144,7 +144,7 @@ def tile_ellipticalnormalizedrbfnet_t_kernel(tc, x, a, m, p_bytes, p_scale, lp, 
             )
 
         def plane(g, s, name=None):
-            qt = put(("qt", s), g, bank([P, GT], name or ("b5", "b5", "b1", "b2")[s]))
+            qt = put(("qt", s), g, bank([P, GT], name or ("b4", "b5", "b1", "b4")[s]))
             codes, scales = get("codes", g), get("scales", g)
             cols = slice(s * P, (s + 1) * P)
             for b, name in enumerate(("m", "p")):
@@ -175,7 +175,7 @@ def tile_ellipticalnormalizedrbfnet_t_kernel(tc, x, a, m, p_bytes, p_scale, lp, 
 
         def tq(g, j, name=None, plain=(), first=0, last=PACK):
             if first == 0:
-                put(("q", j), g, bank([P, C], name or ("b1", "b6", "xt", "b6")[j]))
+                put(("q", j), g, bank([P, C], name or ("b1", "b6", "xt", "b2")[j]))
             for s in range(first, last):
                 turn(get(("q", j), g)[:, s * P : (s + 1) * P], get(("ql", s), g)[:, j * P : (j + 1) * P], s in plain)
 
@@ -357,7 +357,7 @@ def tile_ellipticalnormalizedrbfnet_t_kernel(tc, x, a, m, p_bytes, p_scale, lp, 
         sq(2, 0)
         gc_tok = keep.tile([P, C], F32, name="gc_tok")
         nc.scalar.copy(out=gc_tok[:].rearrange("n (u p e) -> n u p e", u=2, e=2), in_=gc_ps[:].rearrange("n (u e) p -> n u p e", u=2))
-        plane(0, 0)
+        plane(0, 0, "b5")
         plane(0, 1, "b4")
         plane(0, 2, "b3")
         h(1, 0)
@@ -379,7 +379,7 @@ def tile_ellipticalnormalizedrbfnet_t_kernel(tc, x, a, m, p_bytes, p_scale, lp, 
         qz(1)
         sq(2, 1)
         sq(3, 0)
-        plane(1, 0)
+        plane(1, 0, "b5")
         plane(1, 1, "b4")
         mx(0, 0)
         ex(0, 0)
@@ -405,7 +405,7 @@ def tile_ellipticalnormalizedrbfnet_t_kernel(tc, x, a, m, p_bytes, p_scale, lp, 
         ex(0, 3)
         tq(1, 2, "b6", (2, 3))
         sq(3, 1)
-        plane(2, 0)
+        plane(2, 0, "b5")
         plane(2, 1, "b3")
         rc(0)
         us(0, 0)
@@ -420,7 +420,7 @@ def tile_ellipticalnormalizedrbfnet_t_kernel(tc, x, a, m, p_bytes, p_scale, lp, 
         add_lp(2, 0)
         plane(2, 2)
         h(3, 1)
-        plane(2, 3)
+        plane(2, 3, "b2")
         ex(1, 1)
         tq(1, 3, "b4", (3,))
         k(3, 0)
@@ -434,66 +434,67 @@ def tile_ellipticalnormalizedrbfnet_t_kernel(tc, x, a, m, p_bytes, p_scale, lp, 
         mx(1, 3)
         tq(2, 0, None, (0, 1, 2), 0, 3)
         add_lp(2, 3)
+        ex(1, 3)
 
         every = (0, GROUPS)
         order = [
             (1, qz, (), every),
+            (4, tw, (0,2,"b3",), (1,GROUPS)),
             (2, tq, (0,None,(),3,4,), every),
             (2, tq, (1,), (2,3)),
-            (4, tu, (2,"b2",1,), (0,1)),
-            (4, tw, (0,2,"b3",), (1,GROUPS)),
-            (3, ex, (3,), every),
-            (5, qr, (), every),
+            (4, tu, (2,"b5",1,), (0,1)),
             (0, h, (0,), (4,5)),
+            (3, rc, (), every),
+            (5, qr, (), every),
             (0, sq, (0,), (5,GROUPS)),
             (1, plane, (0,), every),
-            (3, rc, (), every),
             (3, us, (0,), every),
             (3, us, (1,), every),
             (3, us, (2,), every),
             (3, gt, (), every),
             (5, ou, (0,), every),
-            (2, mx, (0,), every),
+            (4, rd, (3,), (1,GROUPS)),
             (2, tq, (1,None,(3,),), (3,GROUPS)),
             (4, cw, (0,2,nc.scalar.copy,), every),
             (0, tx, (1,), every),
+            (2, mx, (0,), every),
             (4, ua, (3,), (0,1)),
             (4, rr, (2,), (0,1)),
-            (4, rd, (3,), (1,GROUPS)),
             (1, add_lp, (0,), every),
-            (4, tw, (2,1,"b4",), (1,GROUPS)),
-            (4, tu, (3,"b4",1,), (0,1)),
             (1, plane, (1,), every),
             (0, h, (0,), (5,GROUPS)),
             (5, store, (0,), every),
             (2, tq, (2,), every),
-            (2, mx, (1,), every),
+            (2, tq, (3,), every),
+            (0, k, (0,), every),
             (2, ex, (0,), every),
             (1, plane, (2,), every),
-            (0, k, (0,), every),
+            (2, mx, (1,), every),
             (0, sq, (1,), every),
             (1, plane, (3,), every),
-            (4, cw, (2,1,nc.vector.tensor_copy,), (1,GROUPS)),
-            (4, rr, (3,), (0,1)),
             (3, dg, (3,), every),
-            (2, ex, (1,), every),
-            (2, tq, (3,), every),
-            (3, dm, (3,"b4",0,1,), every),
-            (2, mx, (2,), every),
             (1, add_lp, (1,), every),
-            (3, dm, (3,"b4",1,2,), every),
+            (3, dm, (3,"b5",0,1,), every),
+            (2, mx, (2,), every),
+            (2, ex, (1,), every),
+            (4, tw, (2,1,"b6",), (1,GROUPS)),
+            (4, tu, (3,"b6",), (0,1)),
+            (2, mx, (3,), every),
+            (1, add_lp, (2,), every),
             (0, h, (1,), every),
             (5, ou, (1,), every),
-            (1, add_lp, (2,), every),
-            (0, k, (1,), every),
+            (3, dm, (3,"b5",1,2,), every),
             (2, ex, (2,), every),
-            (-1, tx, (0,), (1,GROUPS)),
-            (3, dm, (3,"b4",2,3,), every),
+            (-1, tx, (0,), (5,GROUPS)),
+            (0, k, (1,), every),
+            (2, ex, (3,), every),
+            (3, dm, (3,"b5",2,3,), every),
+            (4, cw, (2,1,nc.vector.tensor_copy,), (1,GROUPS)),
+            (4, rr, (3,), (0,1)),
             (1, tq, (0,None,(),0,3,), every),
-            (3, dm, (3,"b4",3,4,), every),
-            (1, add_lp, (3,), every),
-            (2, mx, (3,), every),
+            (3, dm, (3,"b5",3,4,), every),
             (5, store, (1,), every),
+            (1, add_lp, (3,), every),
         ]
         for step in range(4, GROUPS):
             for lag, stage, args, (first, last) in order:
@@ -502,51 +503,50 @@ def tile_ellipticalnormalizedrbfnet_t_kernel(tc, x, a, m, p_bytes, p_scale, lp, 
 
         z = GROUPS - 1
         qz(z)
+        tw(z - 3, 0, 2, "xt")
+        tw(z - 3, 2, 1, "b2")
         tq(z - 1, 0, None, (), 3, 4)
-        tw(z - 3, 0, 2, "b3")
-        tw(z - 3, 2, 1, "xt")
-        tq(z - 1, 1, "b2", (3,))
-        ex(z - 2, 3)
+        tq(z - 1, 1, "b3")
+        rc(z - 2)
         qr(z - 4)
         cw(z - 3, 0, 2, nc.scalar.copy)
-        plane(z, 0, "b5")
-        plane(z, 1, "b6")
         cw(z - 3, 2, 1, nc.scalar.copy)
-        plane(z, 2, "b3")
-        rc(z - 2)
+        plane(z, 0, "b4")
+        plane(z, 1, "b6")
+        plane(z, 2, "xt")
         us(z - 2, 0)
         us(z - 2, 1)
         gt(z - 2, 2)
         us(z - 2, 2)
         us(z - 2, 3)
         rd(z - 3, 3)
-        plane(z, 3, "xt")
+        plane(z, 3, "b2")
         mx(z - 1, 0)
         add_lp(z, 0)
         mx(z - 1, 1)
         qr(z - 3)
-        ou(z - 4, 0, "b4")
+        ou(z - 4, 0, "b5")
         add_lp(z, 1)
-        tq(z - 1, 2, "b5")
+        tq(z - 1, 2, "b4")
         tq(z - 1, 3, "b6")
         add_lp(z, 2)
         add_lp_vector(z, 3)
         ex(z - 1, 0)
         mx(z - 1, 2)
-        tq(z, 0, "b3")
-        tq(z, 1, "xt", (3,))
+        tq(z, 0, "xt")
+        tq(z, 1, "b2", (3,))
         ex(z - 1, 1)
         mx(z - 1, 3)
         tq(z, 2, "b1", (3,))
         store(z - 4, 0)
-        tq(z, 3, "b2", (3,))
+        tq(z, 3, "b3", (3,))
         mx(z, 0)
         ex(z - 1, 2)
-        ou(z - 4, 1, "b4")
+        ou(z - 4, 1, "b5")
         rc(z - 1, 0, 2)
         mx(z, 1)
         ex(z - 1, 3)
-        tw(z - 2, 0, 2, "b5")
+        tw(z - 2, 0, 2, "b4")
         mx(z, 2)
         ex(z, 0)
         tu(z - 2, 2, "b6", 1)
@@ -555,13 +555,13 @@ def tile_ellipticalnormalizedrbfnet_t_kernel(tc, x, a, m, p_bytes, p_scale, lp, 
         us(z - 1, 1)
         us(z - 1, 2)
         store(z - 4, 1, nc.vector.tensor_copy)
-        tu(z - 2, 3, "b3", 1)
+        tu(z - 2, 3, "xt", 1)
         mx(z, 3)
         ex(z, 1)
-        ou(z - 3, 0, "b4")
+        ou(z - 3, 0, "b5")
         cw(z - 2, 0, 2, nc.scalar.copy)
         rr(z - 2, 2)
-        tu(z - 1, 0, "b5", 1)
+        tu(z - 1, 0, "b4", 1)
         ex(z, 2)
         rr(z - 2, 3)
         rc(z, 0, 2)
@@ -569,41 +569,41 @@ def tile_ellipticalnormalizedrbfnet_t_kernel(tc, x, a, m, p_bytes, p_scale, lp, 
         tu(z - 1, 1, "b6", 1)
         ua(z - 1, 3)
         rr(z - 1, 0)
-        tu(z - 1, 2, "b3", 1)
+        tu(z - 1, 2, "xt", 1)
         qr(z - 2)
         rc(z, 2, 4)
         us(z, 2)
         us(z, 3)
         ua(z, 0)
-        tu(z - 1, 3, "xt")
+        tu(z - 1, 3, "b2")
+        tu(z, 0, "b4")
         ou(z - 3, 1, "b1")
-        ou(z - 2, 0, "b2")
+        ou(z - 2, 0, "b3")
         rr(z - 1, 1)
         ua(z, 1)
-        tu(z, 0, "b5")
         store(z - 3, 0)
         rr(z - 1, 2)
-        ou(z - 2, 1, "b4")
+        ou(z - 2, 1, "b5")
         tu(z, 1, "b6", 1)
         store(z - 3, 1)
         rr(z - 1, 3)
-        tu(z, 2, "b3", 1)
+        tu(z, 2, "xt", 1)
         store(z - 2, 0)
         rr(z, 0)
-        tu(z, 3, "xt", 1)
+        tu(z, 3, "b2", 1)
         qr(z - 1)
         store(z - 2, 1)
         ou(z - 1, 0, "b1")
-        ou(z - 1, 1, "b2")
+        ou(z - 1, 1, "b3")
         rr(z, 1)
         rr(z, 2)
         store(z - 1, 0)
         qr(z, 0, 2)
-        ou(z, 0, "b5")
+        ou(z, 0, "b4")
         rr(z, 3)
         store(z - 1, 1)
         qr(z, 2, 1)
         store(z, 0)
         qr(z, 3, 1)
-        out_tile(z, 2, "b4", nc.vector.tensor_copy, nc.sync)
+        out_tile(z, 2, "b5", nc.vector.tensor_copy, nc.sync)
         out_tile(z, 3, "b6", nc.scalar.copy, nc.scalar)

@@ -129,7 +129,7 @@ def tile_ellipticalnormalizedrbfnet_t_kernel(tc, x, a, m, p_bytes, p_scale, lp, 
                 out=hk_part(g, 1, b).rearrange("p (r t) -> p r t", t=PACK),
                 in0=get(("x2", b), g)[:].rearrange("p (r t) -> p r t", t=PACK),
                 scalar=-1.0,
-                in1=a_ps.unsqueeze(1).to_broadcast([P, TOK, PACK]),
+                in1=a_ps[:].unsqueeze(1).to_broadcast([P, TOK, PACK]),
                 op0=ALU.add,
                 op1=ALU.mult,
             )
@@ -159,13 +159,18 @@ def tile_ellipticalnormalizedrbfnet_t_kernel(tc, x, a, m, p_bytes, p_scale, lp, 
                     stop=(b == 1),
                 )
 
-        def add_lp(g, s):
-            ql = put(("ql", s), g, work.tile([P, GT], F32, name="ql" + str(s), bufs=2))
-            nc.scalar.activation(out=ql[:], in_=get(("qt", s), g)[:], func=ACT.Identity, bias=lp_sb[:, s, 0:1], scale=1.0)
+        def ql_tile(g, s):
+            if (("ql", s), g) not in st:
+                put(("ql", s), g, work.tile([P, GT], F32, name="ql" + str(s), bufs=2))
+            return get(("ql", s), g)
 
-        def add_lp_vector(g, s):
-            ql = put(("ql", s), g, work.tile([P, GT], F32, name="ql" + str(s), bufs=2))
-            nc.vector.tensor_scalar(out=ql[:], in0=get(("qt", s), g)[:], scalar1=lp_sb[:, s, 0:1], scalar2=None, op0=ALU.add)
+        def add_lp(g, s, last=GT):
+            nc.scalar.activation(out=ql_tile(g, s)[:, 0:last], in_=get(("qt", s), g)[:, 0:last], func=ACT.Identity, bias=lp_sb[:, s, 0:1], scale=1.0)
+
+        def add_lp_vector(g, s, first=0):
+            nc.vector.tensor_scalar(
+                out=ql_tile(g, s)[:, first:GT], in0=get(("qt", s), g)[:, first:GT], scalar1=lp_sb[:, s, 0:1], scalar2=None, op0=ALU.add
+            )
 
         def turn(dst, src, plain):
             if plain:
@@ -258,7 +263,11 @@ def tile_ellipticalnormalizedrbfnet_t_kernel(tc, x, a, m, p_bytes, p_scale, lp, 
 
         def dg(g, j):
             diag = put(("diag", j), g, work.tile([P, P], F32, name="diag"))
-            nc.vector.tensor_scalar(out=diag[:], in0=ident_ps, scalar1=get("rs", g)[:, j : j + 1], scalar2=None, op0=ALU.mult)
+            gp_copy(diag[:], ident[:], get("rs", g)[:, j : j + 1])
+
+        def dg_scalar(g, j):
+            diag = put(("diag", j), g, work.tile([P, P], F32, name="diag"))
+            nc.scalar.activation(out=diag[:], in_=ident[:], func=ACT.Copy, scale=get("rs", g)[:, j : j + 1])
 
         def dm(g, j, name, first=0, last=PACK):
             if first == 0:
@@ -327,10 +336,8 @@ def tile_ellipticalnormalizedrbfnet_t_kernel(tc, x, a, m, p_bytes, p_scale, lp, 
         nc.vector.tensor_copy(out=interleaved("p", C), in_=by_fours(p_w[:]))
         a_f = keep.tile([P, PACK], F32, name="a_f")
         nc.scalar.activation(out=a_f[:], in_=a_sb[:], func=ACT.Copy, scale=-1.0)
-        side = psum.tile([P, P + PACK], F32, name="side")
-        ident_ps, a_ps = side[:, 0:P], side[:, P : P + PACK]
-        nc.tensor.transpose(ident_ps, ident[:], ident[:])
-        nc.tensor.matmul(a_ps, lhsT=ident[:], rhs=a_f[:], start=True, stop=True)
+        a_ps = psum.tile([P, PACK], F32, name="a_ps")
+        nc.tensor.matmul(a_ps[:], lhsT=ident[:], rhs=a_f[:], start=True, stop=True)
         tx(1, 0, "b2")
         tx(1, 1, "xt")
         sq(0, 0)
@@ -448,32 +455,34 @@ def tile_ellipticalnormalizedrbfnet_t_kernel(tc, x, a, m, p_bytes, p_scale, lp, 
             (5, qr, (), every),
             (0, sq, (0,), (5,GROUPS)),
             (1, plane, (0,), every),
+            (3, dg, (3,), (2,GROUPS)),
             (3, us, (0,), every),
             (3, us, (1,), every),
             (3, us, (2,), every),
             (3, gt, (), every),
             (5, ou, (0,), every),
             (4, rd, (3,), (1,GROUPS)),
-            (2, tq, (1,None,(3,),), (3,GROUPS)),
+            (2, tq, (1,), (3,GROUPS)),
             (4, cw, (0,2,nc.scalar.copy,), every),
             (0, tx, (1,), every),
             (2, mx, (0,), every),
             (4, ua, (3,), (0,1)),
+            (3, dg_scalar, (3,), (1,2)),
             (4, rr, (2,), (0,1)),
             (1, add_lp, (0,), every),
             (1, plane, (1,), every),
             (0, h, (0,), (5,GROUPS)),
             (5, store, (0,), every),
-            (2, tq, (2,), every),
+            (2, tq, (2,None,(0,),), every),
             (2, tq, (3,), every),
             (0, k, (0,), every),
+            (1, add_lp_vector, (1,3*P,), every),
             (2, ex, (0,), every),
             (1, plane, (2,), every),
             (2, mx, (1,), every),
             (0, sq, (1,), every),
             (1, plane, (3,), every),
-            (3, dg, (3,), every),
-            (1, add_lp, (1,), every),
+            (1, add_lp, (1,3*P,), every),
             (3, dm, (3,"b5",0,1,), every),
             (2, mx, (2,), every),
             (2, ex, (1,), every),

@@ -22,6 +22,7 @@ TOK = 2 * P
 GT = 4 * P
 GROUPS = N // GT
 WORD_TILES = {0: 2, GROUPS - 3: 2, GROUPS - 2: 0, GROUPS - 1: 0}
+SPLIT = 3 * P
 AHEAD = 4
 
 
@@ -476,13 +477,14 @@ def tile_ellipticalnormalizedrbfnet_t_kernel(tc, x, a, m, p_bytes, p_scale, lp, 
             (2, tq, (2,None,(0,),), every),
             (2, tq, (3,), every),
             (0, k, (0,), every),
-            (1, add_lp_vector, (1,3*P,), every),
+            (1, add_lp_vector, (1,SPLIT,), (5,GROUPS)),
             (2, ex, (0,), every),
             (1, plane, (2,), every),
             (2, mx, (1,), every),
             (0, sq, (1,), every),
             (1, plane, (3,), every),
-            (1, add_lp, (1,3*P,), every),
+            (1, add_lp, (1,), (0,5)),
+            (1, add_lp, (1,SPLIT,), (5,GROUPS)),
             (3, dm, (3,"b5",0,1,), every),
             (2, mx, (2,), every),
             (2, ex, (1,), every),
@@ -520,6 +522,7 @@ def tile_ellipticalnormalizedrbfnet_t_kernel(tc, x, a, m, p_bytes, p_scale, lp, 
         qr(z - 4)
         cw(z - 3, 0, 2, nc.scalar.copy)
         cw(z - 3, 2, 1, nc.scalar.copy)
+        ua(z - 2, 3)
         plane(z, 0, "b4")
         plane(z, 1, "b6")
         plane(z, 2, "xt")
@@ -527,7 +530,6 @@ def tile_ellipticalnormalizedrbfnet_t_kernel(tc, x, a, m, p_bytes, p_scale, lp, 
         us(z - 2, 1)
         gt(z - 2, 2)
         us(z - 2, 2)
-        us(z - 2, 3)
         rd(z - 3, 3)
         plane(z, 3, "b2")
         mx(z - 1, 0)
@@ -551,7 +553,7 @@ def tile_ellipticalnormalizedrbfnet_t_kernel(tc, x, a, m, p_bytes, p_scale, lp, 
         tq(z, 3, "b3", (3,))
         mx(z, 0)
         ex(z - 1, 2)
-        ou(z - 4, 1, "b5")
+        tu(z - 2, 3, "b5", 1)
         rc(z - 1, 0, 2)
         mx(z, 1)
         ex(z - 1, 3)
@@ -563,48 +565,48 @@ def tile_ellipticalnormalizedrbfnet_t_kernel(tc, x, a, m, p_bytes, p_scale, lp, 
         us(z - 1, 0)
         us(z - 1, 1)
         us(z - 1, 2)
-        store(z - 4, 1, nc.vector.tensor_copy)
-        tu(z - 2, 3, "xt", 1)
+        tu(z - 1, 0, "xt", 1)
         mx(z, 3)
         ex(z, 1)
-        ou(z - 3, 0, "b5")
-        cw(z - 2, 0, 2, nc.scalar.copy)
-        rr(z - 2, 2)
-        tu(z - 1, 0, "b4", 1)
-        ex(z, 2)
         rr(z - 2, 3)
+        cw(z - 2, 0, 2, nc.scalar.copy)
+        ou(z - 4, 1, "b5")
+        rr(z - 2, 2)
+        ex(z, 2)
+        tu(z - 1, 1, "b4", 1)
+        rr(z - 1, 0)
         rc(z, 0, 2)
         ex(z, 3)
-        tu(z - 1, 1, "b6", 1)
+        tu(z - 1, 2, "b6", 1)
         ua(z - 1, 3)
-        rr(z - 1, 0)
-        tu(z - 1, 2, "xt", 1)
         qr(z - 2)
+        ou(z - 3, 0, "b2")
         rc(z, 2, 4)
         us(z, 2)
         us(z, 3)
         ua(z, 0)
-        tu(z - 1, 3, "b2")
-        tu(z, 0, "b4")
-        ou(z - 3, 1, "b1")
-        ou(z - 2, 0, "b3")
+        tu(z - 1, 3, "xt")
         rr(z - 1, 1)
+        tu(z, 0, "b1")
+        ou(z - 3, 1, "b3")
         ua(z, 1)
-        store(z - 3, 0)
         rr(z - 1, 2)
-        ou(z - 2, 1, "b5")
-        tu(z, 1, "b6", 1)
-        store(z - 3, 1)
+        tu(z, 1, "b4", 1)
+        store(z - 4, 1)
         rr(z - 1, 3)
-        tu(z, 2, "xt", 1)
-        store(z - 2, 0)
+        ou(z - 2, 0, "b6")
+        tu(z, 2, "b5", 1)
+        store(z - 3, 0)
         rr(z, 0)
+        ou(z - 2, 1, "xt")
         tu(z, 3, "b2", 1)
+        store(z - 3, 1)
         qr(z - 1)
-        store(z - 2, 1)
+        store(z - 2, 0)
         ou(z - 1, 0, "b1")
         ou(z - 1, 1, "b3")
         rr(z, 1)
+        store(z - 2, 1)
         rr(z, 2)
         store(z - 1, 0)
         qr(z, 0, 2)

@@ -54,11 +54,11 @@ def tile_ellipticalnormalizedrbfnet_t_kernel(tc, x, a, m, p_bytes, p_scale, lp, 
             x_sb = put("x", i, xin.tile([P, 2, D], BF16, name="x_sb"))
             nc.sync.dma_start(out=x_sb[:], in_=x_v[i])
 
-        load(0)
         ps_sb = keep.tile([P, PACK], F32, name="ps_sb")
         nc.sync.dma_start(out=ps_sb[:], in_=p_scale.rearrange("(p t) o -> p (t o)", t=PACK))
         pb_sb = keep.tile([P, PACK, C], U8, name="pb_sb")
         nc.sync.dma_start(out=pb_sb[:], in_=p_bytes.rearrange("(p t) c -> p t c", t=PACK))
+        load(0)
         a_sb = keep.tile([P, PACK], BF16, name="a_sb")
         nc.sync.dma_start(out=a_sb[:], in_=a.rearrange("(p t) -> p t", t=PACK))
         load(1)
@@ -76,15 +76,22 @@ def tile_ellipticalnormalizedrbfnet_t_kernel(tc, x, a, m, p_bytes, p_scale, lp, 
 
         ident = keep.tile([P, P], F32, name="ident")
         make_identity(nc, ident[:])
+        warm = bank([P, PACK, P], "b5")
+        nc.tensor.matmul(warm[:], lhsT=ident[:], rhs=ident[:].unsqueeze(1).to_broadcast([P, PACK, P]), start=True, stop=True)
 
         def gp_copy(dst, src, factor=1.0):
             nc.gpsimd.tensor_scalar(out=dst, in0=src, scalar1=factor, scalar2=0.0, op0=ALU.mult, op1=ALU.add)
 
-        def quantise(name, width):
-            codes = keep.tile([P, width], U32, name=name + "_codes", align_bytes=64)
-            scales = keep.tile([P, width], U8, name=name + "_scales", align_bytes=64)
-            put(name, 0, (codes, scales))
-            nc.vector.quantize_mx(out=codes[:].bitcast(FP8X4), scales=scales[:], in_=get(name + "_g", 0)[:])
+        def quantise(name, width, first=0, last=None):
+            if first == 0:
+                codes = keep.tile([P, width], U32, name=name + "_codes", align_bytes=64)
+                scales = keep.tile([P, width], U8, name=name + "_scales", align_bytes=64)
+                put(name, 0, (codes, scales))
+            codes, scales = get(name, 0)
+            last = last or width
+            nc.vector.quantize_mx(
+                out=codes[:, first:last].bitcast(FP8X4), scales=scales[:, first:last], in_=get(name + "_g", 0)[:, PACK * first : PACK * last]
+            )
 
         def interleaved(name, width):
             g = put(name + "_g", 0, keep.tile([P, PACK * width], BF16, name=name + "_g", align_bytes=64))
@@ -330,11 +337,15 @@ def tile_ellipticalnormalizedrbfnet_t_kernel(tc, x, a, m, p_bytes, p_scale, lp, 
             nc.sync.dma_start(out=out_v[2 * r_set + b], in_=o_sb[:].rearrange("p (j o) -> p j o", j=2))
 
         p_w = keep.tile([P, PACK, C], BF16, name="p_w")
-        for t in range(PACK):
-            nc.vector.tensor_scalar(out=p_w[:, t, :], in0=pb_sb[:, t, :].bitcast(FP8), scalar1=ps_sb[:, t : t + 1], scalar2=None, op0=ALU.mult)
+        halves = (slice(0, C // 2), slice(C // 2, C))
+        for cols in halves:
+            for t in range(PACK):
+                nc.vector.tensor_scalar(out=p_w[:, t, cols], in0=pb_sb[:, t, cols].bitcast(FP8), scalar1=ps_sb[:, t : t + 1], scalar2=None, op0=ALU.mult)
         tx(0, 0, "b1")
         tx(0, 1, "b6")
-        nc.vector.tensor_copy(out=interleaved("p", C), in_=by_fours(p_w[:]))
+        p_g = interleaved("p", C)
+        for b, cols in enumerate(halves):
+            nc.vector.tensor_copy(out=p_g[:, b * C // 8 : (b + 1) * C // 8], in_=by_fours(p_w[:, :, cols]))
         a_f = keep.tile([P, PACK], F32, name="a_f")
         nc.scalar.activation(out=a_f[:], in_=a_sb[:], func=ACT.Copy, scale=-1.0)
         a_ps = psum.tile([P, PACK], F32, name="a_ps")
@@ -343,6 +354,8 @@ def tile_ellipticalnormalizedrbfnet_t_kernel(tc, x, a, m, p_bytes, p_scale, lp, 
         tx(1, 1, "xt")
         sq(0, 0)
         sq(0, 1)
+        quantise("p", C, 0, C // 2)
+        quantise("p", C, C // 2, C)
         h(0, 0)
         k(0, 0)
         gc_f = keep.tile([P, PACK], F32, name="gc_f")
@@ -351,7 +364,6 @@ def tile_ellipticalnormalizedrbfnet_t_kernel(tc, x, a, m, p_bytes, p_scale, lp, 
         tx(2, 0, "b1")
         h(0, 1)
         k(0, 1)
-        quantise("p", C)
         quantise("m", C)
         sq(1, 0)
         qz(0)

@@ -76,8 +76,6 @@ def tile_ellipticalnormalizedrbfnet_t_kernel(tc, x, a, m, p_bytes, p_scale, lp, 
 
         ident = keep.tile([P, P], F32, name="ident")
         make_identity(nc, ident[:])
-        warm = bank([P, PACK, P], "b5")
-        nc.tensor.matmul(warm[:], lhsT=ident[:], rhs=ident[:].unsqueeze(1).to_broadcast([P, PACK, P]), start=True, stop=True)
 
         def gp_copy(dst, src, factor=1.0):
             nc.gpsimd.tensor_scalar(out=dst, in0=src, scalar1=factor, scalar2=0.0, op0=ALU.mult, op1=ALU.add)

@@ -21,8 +21,7 @@ PACK = 4
 TOK = 2 * P
 GT = 4 * P
 GROUPS = N // GT
-WORD_TILES = {0: 2, GROUPS - 3: 2, GROUPS - 2: 0, GROUPS - 1: 0}
-SPLIT = 3 * P
+K_SPLIT = 384
 AHEAD = 4
 
 
@@ -34,18 +33,23 @@ def tile_ellipticalnormalizedrbfnet_t_kernel(tc, x, a, m, p_bytes, p_scale, lp, 
     with ExitStack() as ctx:
         keep = ctx.enter_context(tc.tile_pool(name="keep", bufs=1))
         xin = ctx.enter_context(tc.tile_pool(name="xin", bufs=AHEAD + 2))
-        work = ctx.enter_context(tc.tile_pool(name="work", bufs=3))
+        work = ctx.enter_context(tc.tile_pool(name="work", bufs=2))
         psum = ctx.enter_context(tc.psum_pool(name="psum", bufs=1))
         ctx.enter_context(tc.manual_schedule())
 
-        st = {}
+        tiles = {}
 
-        def put(kind, i, t):
-            st[(kind, i)] = t
+        def put(kind, g, t):
+            tiles[(kind, g)] = t
             return t
 
-        def get(kind, i):
-            return st[(kind, i)]
+        def get(kind, g):
+            return tiles[(kind, g)]
+
+        def once(kind, g, shape, dtype, bufs=2):
+            if (kind, g) not in tiles:
+                put(kind, g, work.tile(shape, dtype, name=kind, align_bytes=64, bufs=bufs))
+            return get(kind, g)
 
         def bank(shape, name):
             return psum.tile(shape, F32, name=name)
@@ -53,29 +57,6 @@ def tile_ellipticalnormalizedrbfnet_t_kernel(tc, x, a, m, p_bytes, p_scale, lp, 
         def load(i):
             x_sb = put("x", i, xin.tile([P, 2, D], BF16, name="x_sb"))
             nc.sync.dma_start(out=x_sb[:], in_=x_v[i])
-
-        ps_sb = keep.tile([P, PACK], F32, name="ps_sb")
-        nc.sync.dma_start(out=ps_sb[:], in_=p_scale.rearrange("(p t) o -> p (t o)", t=PACK))
-        pb_sb = keep.tile([P, PACK, C], U8, name="pb_sb")
-        nc.sync.dma_start(out=pb_sb[:], in_=p_bytes.rearrange("(p t) c -> p t c", t=PACK))
-        load(0)
-        a_sb = keep.tile([P, PACK], BF16, name="a_sb")
-        nc.sync.dma_start(out=a_sb[:], in_=a.rearrange("(p t) -> p t", t=PACK))
-        load(1)
-        m_sb = keep.tile([P, PACK, C], BF16, name="m_sb")
-        nc.sync.dma_start(out=m_sb[:], in_=m.rearrange("(p t) c -> p t c", t=PACK))
-        load(2)
-        load(3)
-        gc_sb = keep.tile([P, PACK], BF16, name="gc_sb")
-        nc.sync.dma_start(out=gc_sb[:], in_=gc.rearrange("(p t) -> p t", t=PACK))
-        lp_sb = keep.tile([P, PACK, 2], BF16, name="lp_sb")
-        with nc.allow_non_contiguous_dma("512 values, one to a partition and slice"):
-            nc.sync.dma_start(out=lp_sb[:, :, 0:1], in_=lp.rearrange("(s p o) -> p s o", p=P, o=1))
-        w_sb = keep.tile([P, PACK, O], BF16, name="w_sb")
-        nc.sync.dma_start(out=w_sb[:], in_=w.rearrange("(p t) o -> p t o", t=PACK))
-
-        ident = keep.tile([P, P], F32, name="ident")
-        make_identity(nc, ident[:])
 
         def gp_copy(dst, src, factor=1.0):
             nc.gpsimd.tensor_scalar(out=dst, in0=src, scalar1=factor, scalar2=0.0, op0=ALU.mult, op1=ALU.add)
@@ -91,19 +72,19 @@ def tile_ellipticalnormalizedrbfnet_t_kernel(tc, x, a, m, p_bytes, p_scale, lp, 
                 out=codes[:, first:last].bitcast(FP8X4), scales=scales[:, first:last], in_=get(name + "_g", 0)[:, PACK * first : PACK * last]
             )
 
-        def interleaved(name, width):
-            g = put(name + "_g", 0, keep.tile([P, PACK * width], BF16, name=name + "_g", align_bytes=64))
+        def interleaved(name, width, tag):
+            g = put(name + "_g", 0, keep.tile([P, PACK * width], BF16, name=tag, align_bytes=64))
             return g[:].rearrange("p (c i t) -> p c t i", i=4, t=PACK)
 
         def by_fours(rows):
             return rows.rearrange("p t (c i) -> p c t i", i=4)
 
-        def tx(g, b, name=None):
+        def tx(g, b, name):
             i = 2 * g + b
             if i + AHEAD < 2 * GROUPS:
                 load(i + AHEAD)
             words = get("x", i)[:].rearrange("p j d -> p (j d)").bitcast(F32)
-            xt = put(("xt", b), g, bank([P, 2, TOK], name or ("xt", "b3")[b]))
+            xt = put(("xt", b), g, bank([P, 2, TOK], name))
             half = D // 2
             for j in range(2):
                 for u in range(2):
@@ -111,50 +92,76 @@ def tile_ellipticalnormalizedrbfnet_t_kernel(tc, x, a, m, p_bytes, p_scale, lp, 
 
         def x_turned(g, b):
             halves = get(("xt", b), g)[:].rearrange("p u r -> p (u r)").bitcast(BF16)
-            return halves.rearrange("p (u r e) -> p r u e", u=2, e=2)
+            return halves.rearrange("p (u r e) -> p u e r", u=2, e=2)
 
         def sq(g, b):
+            y = once("y", g, [P, GT // 4, PACK, 4], F32)
+            for t in range(PACK):
+                nc.scalar.activation(
+                    out=y[:, b * TOK // 4 : (b + 1) * TOK // 4, t, :],
+                    in_=x_turned(g, b)[:, t // 2, t % 2, :].rearrange("p (c i) -> p c i", i=4),
+                    func=ACT.Square,
+                    scale=root[:, t : t + 1],
+                )
+
+        def sq_plain(g, b):
             x2 = put(("x2", b), g, work.tile([P, TOK * PACK], F32, name="x2", bufs=4))
-            nc.scalar.activation(out=x2[:].rearrange("p (r u e) -> p r u e", u=2, e=2), in_=x_turned(g, b), func=ACT.Square)
-
-        def hk_part(g, which, b):
-            if ("hk", g) not in st:
-                put("hk", g, work.tile([P, 2, GT * PACK], BF16, name="hk", align_bytes=64, bufs=2))
-            return get("hk", g)[:, which, b * TOK * PACK : (b + 1) * TOK * PACK]
-
-        def h(g, b):
-            nc.vector.tensor_tensor(
-                out=hk_part(g, 0, b).rearrange("p (r u e) -> p r u e", u=2, e=2),
-                in0=x_turned(g, b),
-                in1=a_sb[:].rearrange("p (u e) -> p u e", e=2).unsqueeze(1).to_broadcast([P, TOK, 2, 2]),
-                op=ALU.mult,
+            nc.scalar.activation(
+                out=x2[:].rearrange("p (r u e) -> p r u e", u=2, e=2), in_=x_turned(g, b).rearrange("p u e r -> p r u e"), func=ACT.Square
             )
 
-        def k(g, b):
+        def k_plain(g, b):
             nc.vector.scalar_tensor_tensor(
-                out=hk_part(g, 1, b).rearrange("p (r t) -> p r t", t=PACK),
+                out=hk_part(g, 1, b * TOK, (b + 1) * TOK).rearrange("p (r t) -> p r t", t=PACK),
                 in0=get(("x2", b), g)[:].rearrange("p (r t) -> p r t", t=PACK),
                 scalar=-1.0,
-                in1=a_ps[:].unsqueeze(1).to_broadcast([P, TOK, PACK]),
+                in1=abs_ps.unsqueeze(1).to_broadcast([P, TOK, PACK]),
                 op0=ALU.add,
                 op1=ALU.mult,
             )
 
+        def hk_part(g, which, first, last):
+            return once("hk", g, [P, 2, GT * PACK], BF16)[:, which, first * PACK : last * PACK]
+
+        def h(g, b):
+            nc.vector.tensor_tensor(
+                out=hk_part(g, 0, b * TOK, (b + 1) * TOK).rearrange("p (r u e) -> p r u e", u=2, e=2),
+                in0=x_turned(g, b).rearrange("p u e r -> p r u e"),
+                in1=a_sb[:].rearrange("p (u e) -> p u e", e=2).unsqueeze(1).to_broadcast([P, TOK, 2, 2]),
+                op=ALU.mult,
+            )
+
+        def k_gp(g, first=0, last=K_SPLIT):
+            nc.gpsimd.tensor_tensor(
+                out=hk_part(g, 1, first, last).rearrange("p (c i t) -> p c i t", i=4, t=PACK),
+                in0=get("y", g)[:, first // 4 : last // 4].rearrange("p c t i -> p c i t"),
+                in1=mag[:].unsqueeze(1).unsqueeze(2).to_broadcast([P, (last - first) // 4, 4, PACK]),
+                op=ALU.subtract,
+            )
+
+        def k_ve(g, first=K_SPLIT, last=GT):
+            nc.vector.tensor_tensor(
+                out=hk_part(g, 1, first, last).rearrange("p (c i t) -> p c t i", i=4, t=PACK),
+                in0=get("y", g)[:, first // 4 : last // 4],
+                in1=mag_ps.unsqueeze(1).unsqueeze(3).to_broadcast([P, (last - first) // 4, PACK, 4]),
+                op=ALU.subtract,
+            )
+
         def qz(g):
-            codes = put("codes", g, work.tile([P, 2, GT], U32, name="codes", align_bytes=64))
-            scales = put("scales", g, work.tile([P, 2, GT], U8, name="scales", align_bytes=64))
+            codes = once("codes", g, [P, 2, GT], U32)
+            scales = once("scales", g, [P, 2, GT], U8)
             nc.vector.quantize_mx(
                 out=codes[:].rearrange("p b r -> p (b r)").bitcast(FP8X4),
                 scales=scales[:].rearrange("p b r -> p (b r)"),
                 in_=get("hk", g)[:].rearrange("p b r -> p (b r)"),
             )
 
-        def plane(g, s, name=None):
-            qt = put(("qt", s), g, bank([P, GT], name or ("b4", "b5", "b1", "b4")[s]))
+        def plane(g, s, name):
+            qt = put(("qt", s), g, bank([P, GT], name))
             codes, scales = get("codes", g), get("scales", g)
             cols = slice(s * P, (s + 1) * P)
-            for b, name in enumerate(("m", "p")):
-                wc, ws = get(name, 0)
+            for b, weight in enumerate(("m", "p")):
+                wc, ws = get(weight, 0)
                 nc.tensor.matmul_mx(
                     out=qt[:],
                     lhsT=wc[:, cols].bitcast(FP8X4),
@@ -165,17 +172,16 @@ def tile_ellipticalnormalizedrbfnet_t_kernel(tc, x, a, m, p_bytes, p_scale, lp, 
                     stop=(b == 1),
                 )
 
-        def ql_tile(g, s):
-            if (("ql", s), g) not in st:
-                put(("ql", s), g, work.tile([P, GT], F32, name="ql" + str(s), bufs=2))
-            return get(("ql", s), g)
+        def add_lp(g, s, first=0, last=GT):
+            ql = once("ql" + str(s), g, [P, GT], F32)
+            nc.scalar.activation(
+                out=ql[:, first:last], in_=get(("qt", s), g)[:, first:last], func=ACT.Identity, bias=lp_sb[:, s, 0:1], scale=1.0
+            )
 
-        def add_lp(g, s, last=GT):
-            nc.scalar.activation(out=ql_tile(g, s)[:, 0:last], in_=get(("qt", s), g)[:, 0:last], func=ACT.Identity, bias=lp_sb[:, s, 0:1], scale=1.0)
-
-        def add_lp_vector(g, s, first=0):
+        def add_lp_ve(g, s, first=0, last=GT):
+            ql = once("ql" + str(s), g, [P, GT], F32)
             nc.vector.tensor_scalar(
-                out=ql_tile(g, s)[:, first:GT], in0=get(("qt", s), g)[:, first:GT], scalar1=lp_sb[:, s, 0:1], scalar2=None, op0=ALU.add
+                out=ql[:, first:last], in0=get(("qt", s), g)[:, first:last], scalar1=lp_sb[:, s, 0:1], scalar2=None, op0=ALU.add
             )
 
         def turn(dst, src, plain):
@@ -184,103 +190,67 @@ def tile_ellipticalnormalizedrbfnet_t_kernel(tc, x, a, m, p_bytes, p_scale, lp, 
             else:
                 nc.tensor.transpose(dst, src, ident[:])
 
-        def tq(g, j, name=None, plain=(), first=0, last=PACK):
-            if first == 0:
-                put(("q", j), g, bank([P, C], name or ("b1", "b6", "xt", "b2")[j]))
-            for s in range(first, last):
-                turn(get(("q", j), g)[:, s * P : (s + 1) * P], get(("ql", s), g)[:, j * P : (j + 1) * P], s in plain)
+        def tq(g, j, name, plain=0):
+            q = put(("q", j), g, bank([P, C], name))
+            for s in range(PACK):
+                turn(q[:, s * P : (s + 1) * P], get("ql" + str(s), g)[:, j * P : (j + 1) * P], s >= PACK - plain)
 
         def mx(g, j):
-            nm = put(("nm", j), g, work.tile([P, 1], F32, name="nm" + str(j)))
+            nm = once("nm" + str(j), g, [P, 1], F32)
             nc.vector.tensor_reduce(out=nm[:], in_=get(("q", j), g)[:], axis=AX.X, op=ALU.max, negate=True)
 
-        def by_words(g):
-            return WORD_TILES.get(g, 3)
-
         def ex(g, j):
-            e = put(("e", j), g, work.tile([P, C], F32, name="e" + str(j), bufs=2))
-            if j == 0:
-                put("ssum", g, work.tile([P, 4], F32, name="ssum"))
-            if j >= by_words(g):
-                e_v = e[:].rearrange("n (t p) -> n t p", t=PACK)
-                q_v = get(("q", j), g)[:].rearrange("n (p t) -> n t p", t=PACK)
-            else:
-                e_v = e[:].rearrange("n (u p e) -> n u p e", u=2, e=2)
-                q_v = get(("q", j), g)[:].rearrange("n (p u e) -> n u p e", u=2, e=2)
-            total = get("ssum", g)[:, j : j + 1]
-            nc.scalar.activation(out=e_v, in_=q_v, func=ACT.Exp, bias=get(("nm", j), g)[:], scale=1.0, accum_out=total)
+            e = once("e" + str(j), g, [P, C], F32)
+            total = once("total", g, [P, 4], F32)
+            nc.scalar.activation(
+                out=e[:].rearrange("n (t p) -> n t p", t=PACK),
+                in_=get(("q", j), g)[:].rearrange("n (p t) -> n t p", t=PACK),
+                func=ACT.Exp,
+                bias=get("nm" + str(j), g)[:],
+                scale=1.0,
+                accum_out=total[:, j : j + 1],
+            )
 
         def rc(g, first=0, last=4):
-            if ("rs", g) not in st:
-                put("rs", g, work.tile([P, 4], F32, name="rs"))
-            nc.vector.reciprocal(out=get("rs", g)[:, first:last], in_=get("ssum", g)[:, first:last])
+            rs = once("rs", g, [P, 4], F32)
+            nc.vector.reciprocal(out=rs[:, first:last], in_=get("total", g)[:, first:last])
 
-        def u_part(g, j):
-            if ("u", g) not in st:
-                put("u", g, work.tile([P, 4, C], F32, name="u", bufs=2))
-            return get("u", g)[:, j, :]
-
-        def us(g, j, engine=nc.gpsimd):
-            engine.tensor_scalar(
-                out=u_part(g, j),
-                in0=get(("e", j), g)[:],
-                scalar1=get("rs", g)[:, j : j + 1],
-                scalar2=-1.0 / C,
-                op0=ALU.mult,
-                op1=ALU.add,
+        def us(g, j):
+            u = once("u" + str(j), g, [P, C], F32)
+            nc.gpsimd.tensor_scalar(
+                out=u[:], in0=get("e" + str(j), g)[:], scalar1=get("rs", g)[:, j : j + 1], scalar2=-1.0 / C, op0=ALU.mult, op1=ALU.add
             )
 
-        def ua(g, j):
-            nc.scalar.activation(
-                out=u_part(g, j), in_=get(("e", j), g)[:], func=ACT.Identity, scale=get("rs", g)[:, j : j + 1], bias=minus_mean[:]
-            )
+        def r_cols(g, j, count=1):
+            return once("r", g, [P, GT, PACK], BF16, bufs=3)[:, j * P : (j + count) * P, :]
 
-        def gt(g, tiles=3):
-            r_tok = put("r_tok", g, work.tile([P, 3, C], BF16, name="r_tok", bufs=2))
-            nc.gpsimd.tensor_tensor(
-                out=r_tok[:, 0:tiles, :], in0=get("u", g)[:, 0:tiles, :], in1=gc_tok[:].unsqueeze(1).to_broadcast([P, tiles, C]), op=ALU.mult
-            )
-
-        def tw(g, first, tiles, name):
-            words = get("r_tok", g)[:].rearrange("n j c -> n (j c)").bitcast(F32)
-            rw = put(("rw", first), g, bank([P, 2 * tiles, P], name))
-            for ju in range(2 * tiles):
-                nc.tensor.transpose(rw[:, ju, :], words[:, (2 * first + ju) * P : (2 * first + ju + 1) * P], ident[:])
-
-        def r_cols(g, j, tiles=1):
-            if ("r", g) not in st:
-                put("r", g, work.tile([P, GT, PACK], BF16, name="r", align_bytes=64))
-            return get("r", g)[:, j * P : (j + tiles) * P, :]
-
-        def cw(g, first, tiles, copy):
-            words = r_cols(g, first, tiles).rearrange("p n s -> p (n s)").bitcast(F32)
-            copy(out=words.rearrange("p (j n u) -> p j n u", j=tiles, u=2), in_=get(("rw", first), g)[:].rearrange("p (j u) n -> p j n u", u=2))
-
-        def tu(g, j, name=None, plain=0):
-            ut = put(("ut", j), g, bank([P, PACK, P], name or "b4"))
-            u = get("u", g)
+        def tu(g, j, name, plain=0):
+            ut = put(("ut", j), g, bank([P, PACK, P], name))
+            u = get("u" + str(j), g)
             for s in range(PACK):
-                turn(ut[:, s, :], u[:, j, s * P : (s + 1) * P], s >= PACK - plain)
+                turn(ut[:, s, :], u[:, s * P : (s + 1) * P], s >= PACK - plain)
 
         def rr(g, j):
             nc.vector.tensor_tensor(
-                out=r_cols(g, j), in0=get(("ut", j), g)[:].rearrange("p s n -> p n s"), in1=gc_f[:].unsqueeze(1).to_broadcast([P, P, PACK]), op=ALU.mult
+                out=r_cols(g, j),
+                in0=get(("ut", j), g)[:].rearrange("p s n -> p n s"),
+                in1=gc_f[:].unsqueeze(1).to_broadcast([P, P, PACK]),
+                op=ALU.mult,
             )
 
         def dg(g, j):
-            diag = put(("diag", j), g, work.tile([P, P], F32, name="diag"))
-            gp_copy(diag[:], ident[:], get("rs", g)[:, j : j + 1])
-
-        def dg_scalar(g, j):
-            diag = put(("diag", j), g, work.tile([P, P], F32, name="diag"))
-            nc.scalar.activation(out=diag[:], in_=ident[:], func=ACT.Copy, scale=get("rs", g)[:, j : j + 1])
+            gp_copy(once("diag" + str(j), g, [P, P], F32)[:], ident[:], get("rs", g)[:, j : j + 1])
 
         def dm(g, j, name, first=0, last=PACK):
             if first == 0:
                 put(("ut", j), g, bank([P, PACK, P], name))
             for s in range(first, last):
                 nc.tensor.matmul(
-                    get(("ut", j), g)[:, s, :], lhsT=get(("e", j), g)[:, s * P : (s + 1) * P], rhs=get(("diag", j), g)[:], start=True, stop=True
+                    get(("ut", j), g)[:, s, :],
+                    lhsT=get("e" + str(j), g)[:, s * P : (s + 1) * P],
+                    rhs=get("diag" + str(j), g)[:],
+                    start=True,
+                    stop=True,
                 )
 
         def rd(g, j):
@@ -293,338 +263,277 @@ def tile_ellipticalnormalizedrbfnet_t_kernel(tc, x, a, m, p_bytes, p_scale, lp, 
                 op1=ALU.mult,
             )
 
-        def qr(r_set, first=0, tiles=4):
-            if ("rcodes", r_set) not in st:
-                put("rcodes", r_set, work.tile([P, GT], U32, name="rcodes", align_bytes=64))
-                put("rscales", r_set, work.tile([P, GT], U8, name="rscales", align_bytes=64))
-            cols = slice(first * P, (first + tiles) * P)
+        def qr(g, first=0, count=4):
+            cols = slice(first * P, (first + count) * P)
             nc.vector.quantize_mx(
-                out=get("rcodes", r_set)[:, cols].bitcast(FP8X4),
-                scales=get("rscales", r_set)[:, cols],
-                in_=get("r", r_set)[:, cols, :].rearrange("p n s -> p (n s)"),
+                out=once("rcodes", g, [P, GT], U32)[:, cols].bitcast(FP8X4),
+                scales=once("rscales", g, [P, GT], U8)[:, cols],
+                in_=get("r", g)[:, cols, :].rearrange("p n s -> p (n s)"),
             )
 
-        def last_product(dst, r_set, tile):
+        def last_product(dst, g, j):
             w_codes, w_scales = get("w", 0)
-            cols = slice(tile * P, (tile + 1) * P)
+            cols = slice(j * P, (j + 1) * P)
             nc.tensor.matmul_mx(
                 out=dst,
-                lhsT=get("rcodes", r_set)[:, cols].bitcast(FP8X4),
-                lhsT_scale=get("rscales", r_set)[:, cols],
+                lhsT=get("rcodes", g)[:, cols].bitcast(FP8X4),
+                lhsT_scale=get("rscales", g)[:, cols],
                 rhs=w_codes[:].bitcast(FP8X4),
                 rhs_scale=w_scales[:],
                 start=True,
                 stop=True,
             )
 
-        def ou(r_set, b, name=None):
-            o_ps = put(("o_ps", b), r_set, bank([P, 2 * O], name or ("b2", "b3")[b]))
+        def ou(g, b, name):
+            o_ps = put(("o_ps", b), g, bank([P, 2 * O], name))
             for j in range(2):
-                last_product(o_ps[:, j * O : (j + 1) * O], r_set, 2 * b + j)
+                last_product(o_ps[:, j * O : (j + 1) * O], g, 2 * b + j)
 
-        def out_tile(r_set, j, name, copy, queue):
-            o_ps = bank([P, O], name)
-            last_product(o_ps[:], r_set, j)
-            o_sb = work.tile([P, O], F32, name="o_last", bufs=2)
-            copy(out=o_sb[:], in_=o_ps[:])
-            queue.dma_start(out=out_v[2 * r_set + j // 2][:, j % 2, :], in_=o_sb[:])
-
-        def store(r_set, b, copy=nc.scalar.copy):
+        def store(g, b, copy=nc.scalar.copy):
             o_sb = work.tile([P, 2 * O], F32, name="o_sb", bufs=2 * GROUPS - 1)
-            copy(out=o_sb[:], in_=get(("o_ps", b), r_set)[:])
-            nc.sync.dma_start(out=out_v[2 * r_set + b], in_=o_sb[:].rearrange("p (j o) -> p j o", j=2))
+            copy(out=o_sb[:], in_=get(("o_ps", b), g)[:])
+            nc.sync.dma_start(out=out_v[2 * g + b], in_=o_sb[:].rearrange("p (j o) -> p j o", j=2))
 
+        def out_tile(g, j, name, copy, queue):
+            o_ps = bank([P, O], name)
+            last_product(o_ps[:], g, j)
+            o_sb = work.tile([P, O], F32, name="o_last")
+            copy(out=o_sb[:], in_=o_ps[:])
+            queue.dma_start(out=out_v[2 * g + j // 2][:, j % 2, :], in_=o_sb[:])
+
+        a_sb = keep.tile([P, PACK], BF16, name="a_sb")
+        nc.sync.dma_start(out=a_sb[:], in_=a.rearrange("(p t) -> p t", t=PACK))
+        ps_sb = keep.tile([P, PACK], F32, name="ps_sb")
+        nc.sync.dma_start(out=ps_sb[:], in_=p_scale.rearrange("(p t) o -> p (t o)", t=PACK))
+        pb_sb = keep.tile([P, PACK, C], U8, name="pb_sb")
+        nc.sync.dma_start(out=pb_sb[:], in_=p_bytes.rearrange("(p t) c -> p t c", t=PACK))
+        load(0)
+        load(1)
+        m_sb = keep.tile([P, PACK, C], BF16, name="m_sb")
+        nc.sync.dma_start(out=m_sb[:], in_=m.rearrange("(p t) c -> p t c", t=PACK))
+        load(2)
+        load(3)
+        lp_sb = keep.tile([P, PACK, 2], BF16, name="lp_sb")
+        with nc.allow_non_contiguous_dma("512 values, one to a partition and slice"):
+            nc.sync.dma_start(out=lp_sb[:, :, 0:1], in_=lp.rearrange("(s p o) -> p s o", p=P, o=1))
+        gc_sb = keep.tile([P, PACK], BF16, name="gc_sb")
+        nc.sync.dma_start(out=gc_sb[:], in_=gc.rearrange("(p t) -> p t", t=PACK))
+        w_sb = keep.tile([P, PACK, O], BF16, name="w_sb")
+        nc.sync.dma_start(out=w_sb[:], in_=w.rearrange("(p t) o -> p t o", t=PACK))
+
+        ident = keep.tile([P, P], F32, name="ident")
+        make_identity(nc, ident[:])
+        a_abs = keep.tile([P, PACK], F32, name="a_abs")
+        nc.scalar.activation(out=a_abs[:], in_=a_sb[:], func=ACT.Abs)
+        twice_neg = keep.tile([P, PACK], F32, name="twice_neg")
+        nc.vector.tensor_scalar(out=twice_neg[:], in0=a_sb[:], scalar1=0.0, scalar2=2.0, op0=ALU.is_lt, op1=ALU.mult)
+        signed = keep.tile([P, PACK], F32, name="signed")
+        nc.vector.scalar_tensor_tensor(out=signed[:], in0=twice_neg[:], scalar=-1.0, in1=ps_sb[:], op0=ALU.add, op1=ALU.mult)
         p_w = keep.tile([P, PACK, C], BF16, name="p_w")
         halves = (slice(0, C // 2), slice(C // 2, C))
         for cols in halves:
             for t in range(PACK):
-                nc.vector.tensor_scalar(out=p_w[:, t, cols], in0=pb_sb[:, t, cols].bitcast(FP8), scalar1=ps_sb[:, t : t + 1], scalar2=None, op0=ALU.mult)
-        tx(0, 0, "b1")
-        tx(0, 1, "b6")
-        p_g = interleaved("p", C)
+                nc.vector.tensor_scalar(
+                    out=p_w[:, t, cols], in0=pb_sb[:, t, cols].bitcast(FP8), scalar1=signed[:, t : t + 1], scalar2=None, op0=ALU.mult
+                )
+        tx(0, 0, "b0")
+        const_ps = psum.tile([P, 2, PACK], F32, name="const_ps")
+        abs_ps, mag_ps = const_ps[:, 0, :], const_ps[:, 1, :]
+        nc.tensor.matmul(abs_ps, lhsT=ident[:], rhs=a_abs[:], start=True, stop=True)
+        tx(0, 1, "b1")
+        p_g = interleaved("p", C, "p_g")
         for b, cols in enumerate(halves):
             nc.vector.tensor_copy(out=p_g[:, b * C // 8 : (b + 1) * C // 8], in_=by_fours(p_w[:, :, cols]))
-        a_f = keep.tile([P, PACK], F32, name="a_f")
-        nc.scalar.activation(out=a_f[:], in_=a_sb[:], func=ACT.Copy, scale=-1.0)
-        a_ps = psum.tile([P, PACK], F32, name="a_ps")
-        nc.tensor.matmul(a_ps[:], lhsT=ident[:], rhs=a_f[:], start=True, stop=True)
         tx(1, 0, "b2")
-        tx(1, 1, "xt")
-        sq(0, 0)
-        sq(0, 1)
+        tx(1, 1, "b3")
+        tx(2, 0, "b4")
+        tx(2, 1, "b5")
+        sq_plain(0, 0)
+        sq_plain(0, 1)
         quantise("p", C, 0, C // 2)
+        half = keep.tile([P, PACK], F32, name="half")
+        nc.vector.memset(half[:], 0.5)
         quantise("p", C, C // 2, C)
+        root = keep.tile([P, PACK], F32, name="root")
+        nc.gpsimd.tensor_tensor(out=root[:], in0=a_abs[:], in1=half[:], op=ALU.pow)
+        gp_copy(interleaved("w", O, "w_g"), by_fours(w_sb[:]))
+        nc.scalar.copy(out=interleaved("m", C, "m_g"), in_=by_fours(m_sb[:]))
+        mag = keep.tile([P, PACK], F32, name="mag")
+        nc.scalar.activation(out=mag[:], in_=root[:], func=ACT.Square)
         h(0, 0)
-        k(0, 0)
+        k_plain(0, 0)
+        h(0, 1)
+        k_plain(0, 1)
+        tx(3, 0, "b6")
+        nc.tensor.matmul(mag_ps, lhsT=ident[:], rhs=mag[:], start=True, stop=True)
+        sq(1, 0)
+        quantise("m", C)
+        quantise("w", O)
+        qz(0)
+        k_gp(1, 0, TOK)
+        sq(1, 1)
+        sq_plain(2, 0)
         gc_f = keep.tile([P, PACK], F32, name="gc_f")
         nc.scalar.activation(out=gc_f[:], in_=gc_sb[:], func=ACT.Copy, scale=float(C))
-        nc.scalar.copy(out=interleaved("m", C), in_=by_fours(m_sb[:]))
-        tx(2, 0, "b1")
-        h(0, 1)
-        k(0, 1)
-        quantise("m", C)
-        sq(1, 0)
-        qz(0)
-        minus_mean = keep.tile([P, 1], F32, name="minus_mean")
-        nc.gpsimd.memset(minus_mean[:], -1.0 / C)
-        gp_copy(interleaved("w", O), by_fours(w_sb[:]))
-        gc_ps = bank([P, PACK, P], "b3")
-        for t in range(PACK):
-            nc.tensor.matmul(gc_ps[:, t, :], lhsT=gc_f[:, t : t + 1].to_broadcast([P, P]), rhs=ident[:], start=True, stop=True)
-        sq(1, 1)
-        sq(2, 0)
-        gc_tok = keep.tile([P, C], F32, name="gc_tok")
-        nc.scalar.copy(out=gc_tok[:].rearrange("n (u p e) -> n u p e", u=2, e=2), in_=gc_ps[:].rearrange("n (u e) p -> n u p e", u=2))
-        plane(0, 0, "b5")
-        plane(0, 1, "b4")
-        plane(0, 2, "b3")
+        plane(0, 0, "b0")
+        plane(0, 1, "b1")
         h(1, 0)
-        k(1, 0)
-        add_lp(0, 0)
-        plane(0, 3, "b5")
-        tx(2, 1, "b2")
-        add_lp(0, 1)
         h(1, 1)
-        h(2, 0)
-        tx(3, 0)
+        plane(0, 2, "b2")
+        plane(0, 3, "b3")
+        k_ve(1, TOK, GT)
+        add_lp(0, 0)
+        h(2, 1)
+        qz(1)
+        add_lp(0, 1)
         add_lp(0, 2)
         add_lp(0, 3)
-        k(1, 1)
-        tq(0, 0, "b1", (2, 3))
-        tq(0, 1, "b6", (2, 3))
-        tq(0, 2, "b3", (2, 3))
-        quantise("w", O)
-        qz(1)
+        tq(0, 0, "b0", 2)
+        tq(0, 1, "b1", 2)
         sq(2, 1)
-        sq(3, 0)
-        plane(1, 0, "b5")
-        plane(1, 1, "b4")
+        k_gp(2, TOK, GT)
+        h(2, 0)
+        k_plain(2, 0)
+        plane(1, 0, "b2")
+        plane(1, 1, "b3")
+        tq(0, 2, "b4", 2)
+        tq(0, 3, "b5", 2)
         mx(0, 0)
-        ex(0, 0)
-        k(2, 0)
-        add_lp(1, 0)
-        plane(1, 2, "b1")
-        plane(1, 3, "b5")
         mx(0, 1)
+        ex(0, 0)
+        add_lp(1, 0)
+        add_lp_ve(1, 1)
+        plane(1, 2, "b0")
+        plane(1, 3, "b2")
         ex(0, 1)
-        add_lp(1, 1)
-        tq(0, 3, "b6", (2, 3))
-        h(2, 1)
         mx(0, 2)
-        tx(3, 1, "b2")
-        add_lp(1, 2)
-        add_lp(1, 3)
-        ex(0, 2)
-        k(2, 1)
+        tx(3, 1, "b1")
         mx(0, 3)
-        tq(1, 0, None, (0, 1, 2))
-        tq(1, 1, "b4", (2, 3))
-        qz(2)
-        ex(0, 3)
-        tq(1, 2, "b6", (2, 3))
-        sq(3, 1)
-        plane(2, 0, "b5")
-        plane(2, 1, "b3")
-        rc(0)
-        us(0, 0)
-        us(0, 1)
-        gt(0, 2)
-        us(0, 2)
-        mx(1, 0)
+        ex(0, 2)
         h(3, 0)
-        tx(4, 0)
-        ex(1, 0)
-        mx(1, 1)
-        add_lp(2, 0)
-        plane(2, 2)
-        h(3, 1)
-        plane(2, 3, "b2")
-        ex(1, 1)
-        tq(1, 3, "b4", (3,))
-        k(3, 0)
-        add_lp(2, 1)
-        sq(4, 0)
-        mx(1, 2)
-        tw(0, 0, 2, "b3")
-        k(3, 1)
-        add_lp(2, 2)
-        ex(1, 2)
-        mx(1, 3)
-        tq(2, 0, None, (0, 1, 2), 0, 3)
-        add_lp(2, 3)
-        ex(1, 3)
+        ex(0, 3)
+        add_lp_ve(1, 2)
+        add_lp(1, 3)
+        sq(3, 0)
+        tq(1, 0, "b2", 1)
 
-        every = (0, GROUPS)
         order = [
-            (1, qz, (), every),
-            (4, tw, (0,2,"b3",), (1,GROUPS)),
-            (2, tq, (0,None,(),3,4,), every),
-            (2, tq, (1,), (2,3)),
-            (4, tu, (2,"b5",1,), (0,1)),
-            (0, h, (0,), (4,5)),
-            (3, rc, (), every),
-            (5, qr, (), every),
-            (0, sq, (0,), (5,GROUPS)),
-            (1, plane, (0,), every),
-            (3, dg, (3,), (2,GROUPS)),
-            (3, us, (0,), every),
-            (3, us, (1,), every),
-            (3, us, (2,), every),
-            (3, gt, (), every),
-            (5, ou, (0,), every),
-            (4, rd, (3,), (1,GROUPS)),
-            (2, tq, (1,), (3,GROUPS)),
-            (4, cw, (0,2,nc.scalar.copy,), every),
-            (0, tx, (1,), every),
-            (2, mx, (0,), every),
-            (4, ua, (3,), (0,1)),
-            (3, dg_scalar, (3,), (1,2)),
-            (4, rr, (2,), (0,1)),
-            (1, add_lp, (0,), every),
-            (1, plane, (1,), every),
-            (0, h, (0,), (5,GROUPS)),
-            (5, store, (0,), every),
-            (2, tq, (2,None,(0,),), every),
-            (2, tq, (3,), every),
-            (0, k, (0,), every),
-            (1, add_lp_vector, (1,SPLIT,), (5,GROUPS)),
-            (2, ex, (0,), every),
-            (1, plane, (2,), every),
-            (2, mx, (1,), every),
-            (0, sq, (1,), every),
-            (1, plane, (3,), every),
-            (1, add_lp, (1,), (0,5)),
-            (1, add_lp, (1,SPLIT,), (5,GROUPS)),
-            (3, dm, (3,"b5",0,1,), every),
-            (2, mx, (2,), every),
-            (2, ex, (1,), every),
-            (4, tw, (2,1,"b6",), (1,GROUPS)),
-            (4, tu, (3,"b6",), (0,1)),
-            (2, mx, (3,), every),
-            (1, add_lp, (2,), every),
-            (0, h, (1,), every),
-            (5, ou, (1,), every),
-            (3, dm, (3,"b5",1,2,), every),
-            (2, ex, (2,), every),
-            (-1, tx, (0,), (5,GROUPS)),
-            (0, k, (1,), every),
-            (2, ex, (3,), every),
-            (3, dm, (3,"b5",2,3,), every),
-            (4, cw, (2,1,nc.vector.tensor_copy,), (1,GROUPS)),
-            (4, rr, (3,), (0,1)),
-            (1, tq, (0,None,(),0,3,), every),
-            (3, dm, (3,"b5",3,4,), every),
-            (5, store, (1,), every),
-            (1, add_lp, (3,), every),
+            (1, qz, ()), (6, store, (0,)), (3, rc, ()), (6, store, (1,)), (5, qr, ()), (0, sq, (1,)),
+            (1, plane, (0, "b3")), (2, mx, (0,)), (3, dg, (3,)), (1, plane, (1, "b4")), (3, us, (0,)), (4, rd, (3,)),
+            (1, add_lp, (0,)), (2, tq, (1, "b5")), (0, h, (1,)), (3, us, (1,)), (4, tu, (2, "b6")), (2, ex, (0,)),
+            (2, tq, (2, "b3")), (2, mx, (1,)), (0, k_gp, ()), (1, add_lp, (1,)), (1, plane, (2, "b0")), (4, rr, (2,)),
+            (2, ex, (1,)), (1, plane, (3, "b1")), (2, mx, (2,)), (1, add_lp, (2,)), (2, tq, (3, "b4")), (0, k_ve, ()),
+            (-1, tx, (0, "b2")), (2, ex, (2,)), (2, mx, (3,)), (3, dm, (3, "b0", 0, 1)), (1, add_lp, (3,)), (3, tu, (0, "b5")),
+            (-1, h, (0,)), (3, dm, (3, "b0", 1, 2)), (2, ex, (3,)), (3, tu, (1, "b6")), (3, rr, (0,)), (3, us, (2,)),
+            (-1, sq, (0,)), (5, ou, (0, "b3")), (3, rr, (1,)), (5, ou, (1, "b4")), (3, dm, (3, "b0", 2, 3)),
+            (-1, tx, (1, "b1")), (3, dm, (3, "b0", 3, 4)), (1, tq, (0, "b2")),
         ]
-        for step in range(4, GROUPS):
-            for lag, stage, args, (first, last) in order:
-                if first <= step - lag < last:
+        for step in range(3, GROUPS):
+            for lag, stage, args in order:
+                if 0 <= step - lag < GROUPS:
                     stage(step - lag, *args)
 
         z = GROUPS - 1
         qz(z)
-        tw(z - 3, 0, 2, "xt")
-        tw(z - 3, 2, 1, "b2")
-        tq(z - 1, 0, None, (), 3, 4)
-        tq(z - 1, 1, "b3")
+        store(z - 5, 0)
         rc(z - 2)
+        store(z - 5, 1)
         qr(z - 4)
-        cw(z - 3, 0, 2, nc.scalar.copy)
-        cw(z - 3, 2, 1, nc.scalar.copy)
-        ua(z - 2, 3)
-        plane(z, 0, "b4")
-        plane(z, 1, "b6")
-        plane(z, 2, "xt")
+        plane(z, 0, "b3")
+        mx(z - 1, 0)
+        dg(z - 2, 3)
+        plane(z, 1, "b4")
         us(z - 2, 0)
         us(z - 2, 1)
-        gt(z - 2, 2)
         us(z - 2, 2)
+        plane(z, 2, "b1")
         rd(z - 3, 3)
-        plane(z, 3, "b2")
-        mx(z - 1, 0)
         add_lp(z, 0)
-        mx(z - 1, 1)
-        qr(z - 3)
-        ou(z - 4, 0, "b5")
+        tq(z - 1, 1, "b5")
+        tu(z - 3, 2, "b6")
+        plane(z, 3, "b0")
         add_lp(z, 1)
-        tq(z - 1, 2, "b4")
-        tq(z - 1, 3, "b6")
-        add_lp(z, 2)
-        add_lp_vector(z, 3)
+        tq(z - 1, 2, "b3")
+        mx(z - 1, 1)
         ex(z - 1, 0)
+        add_lp(z, 2)
+        tq(z - 1, 3, "b4")
+        rr(z - 3, 2)
+        tu(z - 2, 0, "b2")
+        add_lp(z, 3)
         mx(z - 1, 2)
-        tq(z, 0, "xt")
-        tq(z, 1, "b2", (3,))
         ex(z - 1, 1)
+        ou(z - 4, 0, "b1")
+        tu(z - 2, 1, "b6")
         mx(z - 1, 3)
-        tq(z, 2, "b1", (3,))
-        store(z - 4, 0)
-        tq(z, 3, "b3", (3,))
-        mx(z, 0)
         ex(z - 1, 2)
-        tu(z - 2, 3, "b5", 1)
-        rc(z - 1, 0, 2)
-        mx(z, 1)
+        tq(z, 0, "b0", 1)
+        rr(z - 2, 0)
+        tq(z, 1, "b5", 1)
         ex(z - 1, 3)
-        tw(z - 2, 0, 2, "b4")
-        mx(z, 2)
-        ex(z, 0)
-        tu(z - 2, 2, "b6", 1)
-        rc(z - 1, 2, 4)
+        qr(z - 3)
+        tq(z, 2, "b3", 1)
+        rr(z - 2, 1)
+        store(z - 4, 0)
+        tq(z, 3, "b2", 1)
+        mx(z, 0)
+        rc(z - 1)
         us(z - 1, 0)
+        dg(z - 1, 3)
         us(z - 1, 1)
         us(z - 1, 2)
-        tu(z - 1, 0, "xt", 1)
-        mx(z, 3)
+        dm(z - 2, 3, "b4")
+        mx(z, 1)
+        ex(z, 0)
+        tu(z - 2, 2, "b6")
+        mx(z, 2)
         ex(z, 1)
-        rr(z - 2, 3)
-        cw(z - 2, 0, 2, nc.scalar.copy)
-        ou(z - 4, 1, "b5")
-        rr(z - 2, 2)
+        ou(z - 4, 1, "b1")
+        tu(z - 1, 0, "b0", 1)
+        mx(z, 3)
         ex(z, 2)
-        tu(z - 1, 1, "b4", 1)
-        rr(z - 1, 0)
-        rc(z, 0, 2)
+        rd(z - 2, 3)
+        tu(z - 1, 1, "b5", 1)
         ex(z, 3)
-        tu(z - 1, 2, "b6", 1)
-        ua(z - 1, 3)
+        rr(z - 2, 2)
+        store(z - 4, 1)
+        dm(z - 1, 3, "b4")
+        rr(z - 1, 0)
+        rc(z)
         qr(z - 2)
-        ou(z - 3, 0, "b2")
-        rc(z, 2, 4)
+        dg(z, 0)
+        us(z, 1)
         us(z, 2)
         us(z, 3)
-        ua(z, 0)
-        tu(z - 1, 3, "xt")
+        ou(z - 3, 0, "b3")
+        ou(z - 3, 1, "b2")
+        tu(z - 1, 2, "b6")
         rr(z - 1, 1)
-        tu(z, 0, "b1")
-        ou(z - 3, 1, "b3")
-        ua(z, 1)
+        store(z - 3, 0)
+        dm(z, 0, "b1")
+        rd(z - 1, 3)
+        store(z - 3, 1)
+        ou(z - 2, 0, "b0")
+        ou(z - 2, 1, "b5")
         rr(z - 1, 2)
         tu(z, 1, "b4", 1)
-        store(z - 4, 1)
-        rr(z - 1, 3)
-        ou(z - 2, 0, "b6")
-        tu(z, 2, "b5", 1)
-        store(z - 3, 0)
-        rr(z, 0)
-        ou(z - 2, 1, "xt")
-        tu(z, 3, "b2", 1)
-        store(z - 3, 1)
-        qr(z - 1)
         store(z - 2, 0)
-        ou(z - 1, 0, "b1")
-        ou(z - 1, 1, "b3")
-        rr(z, 1)
+        tu(z, 2, "b3", 1)
+        rd(z, 0)
         store(z - 2, 1)
+        tu(z, 3, "b2", 1)
+        qr(z - 1)
+        rr(z, 1)
+        ou(z - 1, 0, "b6")
+        ou(z - 1, 1, "b0")
         rr(z, 2)
         store(z - 1, 0)
         qr(z, 0, 2)
-        ou(z, 0, "b4")
+        ou(z, 0, "b5")
         rr(z, 3)
         store(z - 1, 1)
         qr(z, 2, 1)
         store(z, 0)
         qr(z, 3, 1)
-        out_tile(z, 2, "b5", nc.vector.tensor_copy, nc.sync)
-        out_tile(z, 3, "b6", nc.scalar.copy, nc.scalar)
+        out_tile(z, 2, "b1", nc.vector.tensor_copy, nc.sync)
+        out_tile(z, 3, "b4", nc.scalar.copy, nc.scalar)

@@ -22,6 +22,8 @@ TOK = 2 * P
 GT = 4 * P
 GROUPS = N // GT
 K_SPLIT = 384
+EARLY_SPLIT = {3: 256, GROUPS - 1: 448}
+WORD_GROUP = GROUPS - 3
 AHEAD = 4
 
 
@@ -95,7 +97,7 @@ def tile_ellipticalnormalizedrbfnet_t_kernel(tc, x, a, m, p_bytes, p_scale, lp, 
             return halves.rearrange("p (u r e) -> p u e r", u=2, e=2)
 
         def sq(g, b):
-            y = once("y", g, [P, GT // 4, PACK, 4], F32)
+            y = once("y", g, [P, GT // 4, PACK, 4], F32, bufs=3)
             for t in range(PACK):
                 nc.scalar.activation(
                     out=y[:, b * TOK // 4 : (b + 1) * TOK // 4, t, :],
@@ -105,7 +107,7 @@ def tile_ellipticalnormalizedrbfnet_t_kernel(tc, x, a, m, p_bytes, p_scale, lp, 
                 )
 
         def sq_plain(g, b):
-            x2 = put(("x2", b), g, work.tile([P, TOK * PACK], F32, name="x2", bufs=4))
+            x2 = put(("x2", b), g, work.tile([P, TOK * PACK], F32, name="x2", bufs=2))
             nc.scalar.activation(
                 out=x2[:].rearrange("p (r u e) -> p r u e", u=2, e=2), in_=x_turned(g, b).rearrange("p u e r -> p r u e"), func=ACT.Square
             )
@@ -131,7 +133,11 @@ def tile_ellipticalnormalizedrbfnet_t_kernel(tc, x, a, m, p_bytes, p_scale, lp, 
                 op=ALU.mult,
             )
 
-        def k_gp(g, first=0, last=K_SPLIT):
+        def k_split(g):
+            return EARLY_SPLIT.get(g, K_SPLIT)
+
+        def k_gp(g, first=0, last=None):
+            last = last or k_split(g)
             nc.gpsimd.tensor_tensor(
                 out=hk_part(g, 1, first, last).rearrange("p (c i t) -> p c i t", i=4, t=PACK),
                 in0=get("y", g)[:, first // 4 : last // 4].rearrange("p c t i -> p c i t"),
@@ -139,7 +145,8 @@ def tile_ellipticalnormalizedrbfnet_t_kernel(tc, x, a, m, p_bytes, p_scale, lp, 
                 op=ALU.subtract,
             )
 
-        def k_ve(g, first=K_SPLIT, last=GT):
+        def k_ve(g, first=None, last=GT):
+            first = first or k_split(g)
             nc.vector.tensor_tensor(
                 out=hk_part(g, 1, first, last).rearrange("p (c i t) -> p c t i", i=4, t=PACK),
                 in0=get("y", g)[:, first // 4 : last // 4],
@@ -202,9 +209,14 @@ def tile_ellipticalnormalizedrbfnet_t_kernel(tc, x, a, m, p_bytes, p_scale, lp, 
         def ex(g, j):
             e = once("e" + str(j), g, [P, C], F32)
             total = once("total", g, [P, 4], F32)
+            if g == WORD_GROUP and j < 2:
+                e_v, q_v = e[:], get(("q", j), g)[:]
+            else:
+                e_v = e[:].rearrange("n (t p) -> n t p", t=PACK)
+                q_v = get(("q", j), g)[:].rearrange("n (p t) -> n t p", t=PACK)
             nc.scalar.activation(
-                out=e[:].rearrange("n (t p) -> n t p", t=PACK),
-                in_=get(("q", j), g)[:].rearrange("n (p t) -> n t p", t=PACK),
+                out=e_v,
+                in_=q_v,
                 func=ACT.Exp,
                 bias=get("nm" + str(j), g)[:],
                 scale=1.0,
@@ -215,18 +227,53 @@ def tile_ellipticalnormalizedrbfnet_t_kernel(tc, x, a, m, p_bytes, p_scale, lp, 
             rs = once("rs", g, [P, 4], F32)
             nc.vector.reciprocal(out=rs[:, first:last], in_=get("total", g)[:, first:last])
 
+        def u_tile(g, j):
+            if g == WORD_GROUP and j < 2:
+                return once("u_words", g, [P, 2, C], F32, bufs=1)[:, j, :]
+            return once("u" + str(j), g, [P, C], F32)[:]
+
         def us(g, j):
-            u = once("u" + str(j), g, [P, C], F32)
             nc.gpsimd.tensor_scalar(
-                out=u[:], in0=get("e" + str(j), g)[:], scalar1=get("rs", g)[:, j : j + 1], scalar2=-1.0 / C, op0=ALU.mult, op1=ALU.add
+                out=u_tile(g, j), in0=get("e" + str(j), g)[:], scalar1=get("rs", g)[:, j : j + 1], scalar2=-1.0 / C, op0=ALU.mult, op1=ALU.add
             )
+
+        def uw(g):
+            big = once("big", g, [P, 2], F32, bufs=1)
+            gp_copy(big[:], get("rs", g)[:, 0:2], float(C))
+            dg(g, 3)
+            for j in range(2):
+                nc.gpsimd.tensor_scalar(
+                    out=u_tile(g, j), in0=get("e" + str(j), g)[:], scalar1=big[:, j : j + 1], scalar2=-1.0, op0=ALU.mult, op1=ALU.add
+                )
+
+        def ua(g, j):
+            nc.scalar.activation(
+                out=u_tile(g, j), in_=get("e" + str(j), g)[:], func=ACT.Identity, scale=get("rs", g)[:, j : j + 1], bias=minus_mean[:]
+            )
+
+        def gt(g):
+            r_tok = once("r_tok", g, [P, 2, C], BF16, bufs=1)
+            nc.gpsimd.tensor_tensor(
+                out=r_tok[:], in0=get("u_words", g)[:], in1=gc_row[:].unsqueeze(1).to_broadcast([P, 2, C]), op=ALU.mult
+            )
+
+        def tw(g, first, count, name):
+            words = get("r_tok", g)[:].rearrange("n j c -> n (j c)").bitcast(F32)
+            rw = put(("rw", first), g, bank([P, count, 2, P], name))
+            for j in range(count):
+                for u in range(2):
+                    nc.tensor.transpose(rw[:, j, u, :], words[:, (first + j) * TOK + u : (first + j + 1) * TOK : 2], ident[:])
+
+        def cw(g, first, count):
+            words = r_cols(g, first, count).rearrange("p n s -> p (n s)").bitcast(F32)
+            nc.scalar.copy(out=words.rearrange("p (j n u) -> p j n u", j=count, u=2), in_=get(("rw", first), g)[:].rearrange("p j u n -> p j n u"))
 
         def r_cols(g, j, count=1):
             return once("r", g, [P, GT, PACK], BF16, bufs=3)[:, j * P : (j + count) * P, :]
 
         def tu(g, j, name, plain=0):
             ut = put(("ut", j), g, bank([P, PACK, P], name))
-            u = get("u" + str(j), g)
+            u = u_tile(g, j)
             for s in range(PACK):
                 turn(ut[:, s, :], u[:, s * P : (s + 1) * P], s >= PACK - plain)
 
@@ -240,6 +287,10 @@ def tile_ellipticalnormalizedrbfnet_t_kernel(tc, x, a, m, p_bytes, p_scale, lp, 
 
         def dg(g, j):
             gp_copy(once("diag" + str(j), g, [P, P], F32)[:], ident[:], get("rs", g)[:, j : j + 1])
+
+        def dg_scalar(g, j):
+            diag = once("diag" + str(j), g, [P, P], F32)
+            nc.scalar.activation(out=diag[:], in_=ident[:], func=ACT.Copy, scale=get("rs", g)[:, j : j + 1])
 
         def dm(g, j, name, first=0, last=PACK):
             if first == 0:
@@ -266,8 +317,8 @@ def tile_ellipticalnormalizedrbfnet_t_kernel(tc, x, a, m, p_bytes, p_scale, lp, 
         def qr(g, first=0, count=4):
             cols = slice(first * P, (first + count) * P)
             nc.vector.quantize_mx(
-                out=once("rcodes", g, [P, GT], U32)[:, cols].bitcast(FP8X4),
-                scales=once("rscales", g, [P, GT], U8)[:, cols],
+                out=once("rcodes", g, [P, GT], U32, bufs=3)[:, cols].bitcast(FP8X4),
+                scales=once("rscales", g, [P, GT], U8, bufs=3)[:, cols],
                 in_=get("r", g)[:, cols, :].rearrange("p n s -> p (n s)"),
             )
 
@@ -290,7 +341,7 @@ def tile_ellipticalnormalizedrbfnet_t_kernel(tc, x, a, m, p_bytes, p_scale, lp, 
                 last_product(o_ps[:, j * O : (j + 1) * O], g, 2 * b + j)
 
         def store(g, b, copy=nc.scalar.copy):
-            o_sb = work.tile([P, 2 * O], F32, name="o_sb", bufs=2 * GROUPS - 1)
+            o_sb = work.tile([P, 2 * O], F32, name="o_sb", bufs=2 * GROUPS - 4)
             copy(out=o_sb[:], in_=get(("o_ps", b), g)[:])
             nc.sync.dma_start(out=out_v[2 * g + b], in_=o_sb[:].rearrange("p (j o) -> p j o", j=2))
 
@@ -336,6 +387,8 @@ def tile_ellipticalnormalizedrbfnet_t_kernel(tc, x, a, m, p_bytes, p_scale, lp, 
                 nc.vector.tensor_scalar(
                     out=p_w[:, t, cols], in0=pb_sb[:, t, cols].bitcast(FP8), scalar1=signed[:, t : t + 1], scalar2=None, op0=ALU.mult
                 )
+        minus_mean = keep.tile([P, 1], F32, name="minus_mean")
+        nc.gpsimd.memset(minus_mean[:], -1.0 / C)
         tx(0, 0, "b0")
         const_ps = psum.tile([P, 2, PACK], F32, name="const_ps")
         abs_ps, mag_ps = const_ps[:, 0, :], const_ps[:, 1, :]
@@ -379,6 +432,7 @@ def tile_ellipticalnormalizedrbfnet_t_kernel(tc, x, a, m, p_bytes, p_scale, lp, 
         plane(0, 1, "b1")
         h(1, 0)
         h(1, 1)
+        sq(3, 0)
         plane(0, 2, "b2")
         plane(0, 3, "b3")
         k_ve(1, TOK, GT)
@@ -388,34 +442,169 @@ def tile_ellipticalnormalizedrbfnet_t_kernel(tc, x, a, m, p_bytes, p_scale, lp, 
         add_lp(0, 1)
         add_lp(0, 2)
         add_lp(0, 3)
-        tq(0, 0, "b0", 2)
-        tq(0, 1, "b1", 2)
+        plane(1, 0, "b0")
+        tq(0, 0, "b1")
+        tq(0, 1, "b2")
         sq(2, 1)
         k_gp(2, TOK, GT)
         h(2, 0)
         k_plain(2, 0)
-        plane(1, 0, "b2")
         plane(1, 1, "b3")
-        tq(0, 2, "b4", 2)
-        tq(0, 3, "b5", 2)
-        mx(0, 0)
-        mx(0, 1)
-        ex(0, 0)
+        tq(0, 2, "b4")
         add_lp(1, 0)
-        add_lp_ve(1, 1)
+        mx(0, 0)
+        h(3, 0)
         plane(1, 2, "b0")
-        plane(1, 3, "b2")
-        ex(0, 1)
+        tq(0, 3, "b5")
+        ex(0, 0)
+        mx(0, 1)
+        plane(1, 3, "b6")
+        add_lp(1, 1)
         mx(0, 2)
+        ex(0, 1)
         tx(3, 1, "b1")
+        add_lp_ve(1, 2)
+        tx(4, 0, "b0")
         mx(0, 3)
         ex(0, 2)
-        h(3, 0)
-        ex(0, 3)
-        add_lp_ve(1, 2)
         add_lp(1, 3)
-        sq(3, 0)
-        tq(1, 0, "b2", 1)
+        ex(0, 3)
+        tq(1, 0, "b2")
+        tq(1, 1, "b4")
+
+        qz(2)
+        sq(3, 1)
+        rc(0)
+        sq(4, 0)
+        plane(2, 0, "b3")
+        plane(2, 1, "b6")
+        mx(1, 0)
+        dg(0, 3)
+        us(0, 0)
+        us(0, 1)
+        k_gp(3)
+        us(0, 2)
+        tq(1, 2, "b5")
+        mx(1, 1)
+        h(3, 1)
+        plane(2, 2, "b1")
+        add_lp(2, 0)
+        k_ve(3)
+        tq(1, 3, "b3")
+        ex(1, 0)
+        h(4, 0)
+        tu(0, 0, "b2")
+        add_lp(2, 1)
+        plane(2, 3, "b0")
+        mx(1, 2)
+        ex(1, 1)
+        tu(0, 1, "b6")
+        mx(1, 3)
+        add_lp(2, 2)
+        tx(4, 1, "b4")
+        rr(0, 0)
+        ex(1, 2)
+        tx(5, 0, "b1")
+        rr(0, 1)
+        add_lp(2, 3)
+        dm(0, 3, "b2", 0, 1)
+        tq(2, 0, "b5")
+        ex(1, 3)
+        dm(0, 3, "b2", 1, 2)
+        tq(2, 1, "b6")
+
+        qz(3)
+        sq(4, 1)
+        rc(1)
+        sq(5, 0)
+        plane(3, 0, "b0")
+        plane(3, 1, "b3")
+        dm(0, 3, "b2", 2, 4)
+        mx(2, 0)
+        dg(1, 3)
+        us(1, 0)
+        us(1, 1)
+        k_gp(4)
+        us(1, 2)
+        mx(2, 1)
+        h(4, 1)
+        tq(2, 2, "b4")
+        k_ve(4)
+        add_lp(3, 0)
+        plane(3, 2, "b0")
+        h(5, 0)
+        ex(2, 0)
+        tu(0, 2, "b1")
+        tq(2, 3, "b5")
+        rd(0, 3)
+        add_lp(3, 1)
+        tu(1, 0, "b2")
+        tu(1, 1, "b3")
+        mx(2, 2)
+        ex(2, 1)
+        plane(3, 3, "b6")
+        rr(0, 2)
+        add_lp(3, 2)
+        mx(2, 3)
+        ex(2, 2)
+        tx(5, 1, "b0")
+        rr(1, 0)
+        tx(6, 0, "b1")
+        ex(2, 3)
+        rr(1, 1)
+        dm(1, 3, "b4", 0, 1)
+        add_lp(3, 3)
+        tq(3, 0, "b2")
+        dm(1, 3, "b4", 1, 2)
+        tq(3, 1, "b5")
+
+        gc_row = keep.tile([P, C], BF16, name="gc_row")
+        nc.sync.dma_start(out=gc_row[:], in_=gc.partition_broadcast(P))
+        qz(4)
+        sq(5, 1)
+        rc(2)
+        qr(0)
+        sq(6, 0)
+        plane(4, 0, "b3")
+        plane(4, 1, "b6")
+        dm(1, 3, "b4", 2, 4)
+        mx(3, 0)
+        dg(2, 3)
+        us(2, 0)
+        us(2, 1)
+        k_gp(5)
+        us(2, 2)
+        mx(3, 1)
+        h(5, 1)
+        add_lp(4, 0)
+        plane(4, 2, "b3")
+        tq(3, 2, "b0")
+        k_ve(5)
+        ex(3, 0)
+        tu(1, 2, "b2")
+        h(6, 0)
+        add_lp(4, 1)
+        plane(4, 3, "b1")
+        tq(3, 3, "b6")
+        rd(1, 3)
+        ex(3, 1)
+        tu(2, 0, "b5")
+        tu(2, 1, "b4")
+        mx(3, 2)
+        add_lp(4, 2)
+        ou(0, 0, "b3")
+        rr(1, 2)
+        ex(3, 2)
+        dm(2, 3, "b0", 0, 2)
+        mx(3, 3)
+        add_lp(4, 3)
+        tx(6, 1, "b1")
+        rr(2, 0)
+        ex(3, 3)
+        ou(0, 1, "b6")
+        dm(2, 3, "b0", 2, 4)
+        rr(2, 1)
+        tq(4, 0, "b2")
 
         order = [
             (1, qz, ()), (6, store, (0,)), (3, rc, ()), (6, store, (1,)), (5, qr, ()), (0, sq, (1,)),
@@ -428,112 +617,157 @@ def tile_ellipticalnormalizedrbfnet_t_kernel(tc, x, a, m, p_bytes, p_scale, lp, 
             (-1, sq, (0,)), (5, ou, (0, "b3")), (3, rr, (1,)), (5, ou, (1, "b4")), (3, dm, (3, "b0", 2, 3)),
             (-1, tx, (1, "b1")), (3, dm, (3, "b0", 3, 4)), (1, tq, (0, "b2")),
         ]
-        for step in range(3, GROUPS):
+        for step in range(6, GROUPS - 1):
             for lag, stage, args in order:
                 if 0 <= step - lag < GROUPS:
                     stage(step - lag, *args)
 
         z = GROUPS - 1
-        qz(z)
-        store(z - 5, 0)
-        rc(z - 2)
-        store(z - 5, 1)
+        qz(z - 1)
+        store(z - 6, 0)
+        rc(z - 3)
+        store(z - 6, 1)
+        qr(z - 5)
+        sq(z, 1)
+        plane(z - 1, 0, "b3")
+        mx(z - 2, 0)
+        dg(z - 3, 3)
+        plane(z - 1, 1, "b4")
+        us(z - 3, 0)
+        rd(z - 4, 3)
+        add_lp(z - 1, 0)
+        tq(z - 2, 1, "b5")
+        h(z, 1)
+        us(z - 3, 1)
+        tu(z - 4, 2, "b6")
+        ex(z - 2, 0)
+        tq(z - 2, 2, "b3")
+        mx(z - 2, 1)
+        k_gp(z)
+        add_lp(z - 1, 1)
+        plane(z - 1, 2, "b0")
+        rr(z - 4, 2)
+        ex(z - 2, 1)
+        plane(z - 1, 3, "b1")
+        mx(z - 2, 2)
+        add_lp(z - 1, 2)
+        tq(z - 2, 3, "b4")
+        tu(z - 3, 0, "b5")
+        tu(z - 3, 1, "b6")
+        k_ve(z)
+        add_lp(z - 1, 3)
+        dm(z - 3, 3, "b0", 0, 2)
+        ou(z - 5, 0, "b2")
+        mx(z - 2, 3)
+        ex(z - 2, 2)
+        tq(z - 1, 0, "b1")
+        rr(z - 3, 0)
+        ua(z - 3, 2)
+        ou(z - 5, 1, "b3")
+        ex(z - 2, 3)
+        dm(z - 3, 3, "b0", 2, 4)
+        rr(z - 3, 1)
         qr(z - 4)
-        plane(z, 0, "b3")
-        mx(z - 1, 0)
-        dg(z - 2, 3)
-        plane(z, 1, "b4")
-        us(z - 2, 0)
-        us(z - 2, 1)
+        tu(z - 3, 2, "b5")
+        store(z - 5, 0)
+        tq(z - 1, 1, "b6")
+        ou(z - 4, 0, "b4")
+        store(z - 5, 1)
+        ou(z - 4, 1, "b2")
+
+        qz(z)
+        rc(z - 2)
+        uw(z - 2)
         us(z - 2, 2)
-        plane(z, 2, "b1")
-        rd(z - 3, 3)
-        add_lp(z, 0)
-        tq(z - 1, 1, "b5")
-        tu(z - 3, 2, "b6")
-        plane(z, 3, "b0")
-        add_lp(z, 1)
-        tq(z - 1, 2, "b3")
-        mx(z - 1, 1)
-        ex(z - 1, 0)
-        add_lp(z, 2)
-        tq(z - 1, 3, "b4")
-        rr(z - 3, 2)
-        tu(z - 2, 0, "b2")
-        add_lp(z, 3)
-        mx(z - 1, 2)
-        ex(z - 1, 1)
-        ou(z - 4, 0, "b1")
-        tu(z - 2, 1, "b6")
-        mx(z - 1, 3)
-        ex(z - 1, 2)
-        tq(z, 0, "b0", 1)
-        rr(z - 2, 0)
-        tq(z, 1, "b5", 1)
-        ex(z - 1, 3)
-        qr(z - 3)
-        tq(z, 2, "b3", 1)
-        rr(z - 2, 1)
         store(z - 4, 0)
-        tq(z, 3, "b2", 1)
-        mx(z, 0)
-        rc(z - 1)
+        mx(z - 1, 0)
+        plane(z, 0, "b3")
+        store(z - 4, 1)
+        plane(z, 1, "b4")
+        rd(z - 3, 3)
+        ex(z - 1, 0)
+        plane(z, 2, "b0")
+        rr(z - 3, 2)
+        tq(z - 1, 2, "b2")
+        plane(z, 3, "b5")
+        add_lp(z, 0)
+        tq(z - 1, 3, "b1")
+        mx(z - 1, 1)
+        add_lp(z, 1)
+        qr(z - 3)
+        gt(z - 2)
+        add_lp(z, 2)
+        mx(z - 1, 2)
+        tu(z - 2, 2, "b3")
+        add_lp_ve(z, 3)
+        ex(z - 1, 1)
+        mx(z - 1, 3)
+        tq(z, 0, "b4")
+        tq(z, 1, "b0", 1)
+        rr(z - 2, 2)
+        ex(z - 1, 2)
+        tq(z, 2, "b5")
+        tq(z, 3, "b6", 1)
+        rc(z - 1, 0, 2)
         us(z - 1, 0)
-        dg(z - 1, 3)
         us(z - 1, 1)
-        us(z - 1, 2)
-        dm(z - 2, 3, "b4")
+        mx(z, 0)
+        dm(z - 2, 3, "b3")
+        ex(z - 1, 3)
         mx(z, 1)
+        ou(z - 3, 0, "b2")
+        rc(z - 1, 2, 4)
+        dg(z - 1, 3)
+        us(z - 1, 2)
         ex(z, 0)
-        tu(z - 2, 2, "b6")
         mx(z, 2)
+        tu(z - 1, 0, "b1")
         ex(z, 1)
-        ou(z - 4, 1, "b1")
-        tu(z - 1, 0, "b0", 1)
         mx(z, 3)
+        tw(z - 2, 0, 2, "b4")
+        rc(z, 0, 2)
+        us(z, 0)
+        us(z, 1)
         ex(z, 2)
         rd(z - 2, 3)
-        tu(z - 1, 1, "b5", 1)
+        tu(z - 1, 1, "b0")
         ex(z, 3)
-        rr(z - 2, 2)
-        store(z - 4, 1)
-        dm(z - 1, 3, "b4")
+        dm(z - 1, 3, "b5", 0, 2)
         rr(z - 1, 0)
-        rc(z)
-        qr(z - 2)
-        dg(z, 0)
-        us(z, 1)
-        us(z, 2)
-        us(z, 3)
-        ou(z - 3, 0, "b3")
-        ou(z - 3, 1, "b2")
-        tu(z - 1, 2, "b6")
+        cw(z - 2, 0, 2)
+        tu(z - 1, 2, "b3")
+        rc(z, 2, 4)
+        dm(z - 1, 3, "b5", 2, 4)
         rr(z - 1, 1)
-        store(z - 3, 0)
-        dm(z, 0, "b1")
-        rd(z - 1, 3)
-        store(z - 3, 1)
-        ou(z - 2, 0, "b0")
-        ou(z - 2, 1, "b5")
+        ua(z, 2)
+        ua(z, 3)
+        ou(z - 3, 1, "b6")
+        tu(z, 0, "b1")
         rr(z - 1, 2)
         tu(z, 1, "b4", 1)
+        qr(z - 2)
+        store(z - 3, 0)
+        tu(z, 2, "b0", 1)
+        store(z - 3, 1)
+        ou(z - 2, 0, "b3")
+        ou(z - 2, 1, "b2")
+        rd(z - 1, 3)
+        tu(z, 3, "b6", 1)
+        rr(z, 0)
         store(z - 2, 0)
-        tu(z, 2, "b3", 1)
-        rd(z, 0)
-        store(z - 2, 1)
-        tu(z, 3, "b2", 1)
         qr(z - 1)
+        store(z - 2, 1)
+        ou(z - 1, 0, "b5")
+        ou(z - 1, 1, "b1")
         rr(z, 1)
-        ou(z - 1, 0, "b6")
-        ou(z - 1, 1, "b0")
         rr(z, 2)
         store(z - 1, 0)
         qr(z, 0, 2)
-        ou(z, 0, "b5")
+        ou(z, 0, "b3")
         rr(z, 3)
         store(z - 1, 1)
         qr(z, 2, 1)
-        store(z, 0)
         qr(z, 3, 1)
-        out_tile(z, 2, "b1", nc.vector.tensor_copy, nc.sync)
+        store(z, 0)
+        out_tile(z, 2, "b2", nc.vector.tensor_copy, nc.sync)
         out_tile(z, 3, "b4", nc.scalar.copy, nc.scalar)

@@ -21,8 +21,9 @@ PACK = 4
 TOK = 2 * P
 GT = 4 * P
 GROUPS = N // GT
-K_SPLIT = 384
-EARLY_SPLIT = {3: 256, GROUPS - 1: 448}
+K_SPLIT = 400
+LP_SPLIT = 448
+EARLY_SPLIT = {3: 288, GROUPS - 1: 416}
 WORD_GROUP = GROUPS - 3
 AHEAD = 4
 
@@ -146,7 +147,7 @@ def tile_ellipticalnormalizedrbfnet_t_kernel(tc, x, a, m, p_bytes, p_scale, lp, 
             )
 
         def k_ve(g, first=None, last=GT):
-            first = first or k_split(g)
+            first = k_split(g) if first is None else first
             nc.vector.tensor_tensor(
                 out=hk_part(g, 1, first, last).rearrange("p (c i t) -> p c t i", i=4, t=PACK),
                 in0=get("y", g)[:, first // 4 : last // 4],
@@ -358,7 +359,9 @@ def tile_ellipticalnormalizedrbfnet_t_kernel(tc, x, a, m, p_bytes, p_scale, lp, 
         nc.sync.dma_start(out=ps_sb[:], in_=p_scale.rearrange("(p t) o -> p (t o)", t=PACK))
         pb_sb = keep.tile([P, PACK, C], U8, name="pb_sb")
         nc.sync.dma_start(out=pb_sb[:], in_=p_bytes.rearrange("(p t) c -> p t c", t=PACK))
-        load(0)
+        x_first = put("x", 0, xin.tile([P, 2, D], BF16, name="x_sb"))
+        for j in range(2):
+            nc.sync.dma_start(out=x_first[:, j, :], in_=x_v[0][:, j, :])
         load(1)
         m_sb = keep.tile([P, PACK, C], BF16, name="m_sb")
         nc.sync.dma_start(out=m_sb[:], in_=m.rearrange("(p t) c -> p t c", t=PACK))
@@ -382,14 +385,21 @@ def tile_ellipticalnormalizedrbfnet_t_kernel(tc, x, a, m, p_bytes, p_scale, lp, 
         nc.vector.scalar_tensor_tensor(out=signed[:], in0=twice_neg[:], scalar=-1.0, in1=ps_sb[:], op0=ALU.add, op1=ALU.mult)
         p_w = keep.tile([P, PACK, C], BF16, name="p_w")
         halves = (slice(0, C // 2), slice(C // 2, C))
-        for cols in halves:
-            for t in range(PACK):
-                nc.vector.tensor_scalar(
-                    out=p_w[:, t, cols], in0=pb_sb[:, t, cols].bitcast(FP8), scalar1=signed[:, t : t + 1], scalar2=None, op0=ALU.mult
-                )
+        for t in range(PACK):
+            nc.vector.tensor_scalar(
+                out=p_w[:, t, halves[0]], in0=pb_sb[:, t, halves[0]].bitcast(FP8), scalar1=signed[:, t : t + 1], scalar2=None, op0=ALU.mult
+            )
+            nc.scalar.activation(out=p_w[:, t, halves[1]], in_=pb_sb[:, t, halves[1]].bitcast(FP8), func=ACT.Copy, scale=signed[:, t : t + 1])
         minus_mean = keep.tile([P, 1], F32, name="minus_mean")
         nc.gpsimd.memset(minus_mean[:], -1.0 / C)
-        tx(0, 0, "b0")
+        load(AHEAD)
+        first_words = x_first[:].rearrange("p j d -> p (j d)").bitcast(F32)
+        first_turned = []
+        for j, name in enumerate(("b0", "b6")):
+            xt = bank([P, 2, P], name)
+            for u in range(2):
+                nc.tensor.transpose(xt[:, u, :], first_words[:, j * D // 2 + u : (j + 1) * D // 2 : 2], ident[:])
+            first_turned.append(xt[:].rearrange("p u r -> p (u r)").bitcast(BF16).rearrange("p (u r e) -> p r u e", u=2, e=2))
         const_ps = psum.tile([P, 2, PACK], F32, name="const_ps")
         abs_ps, mag_ps = const_ps[:, 0, :], const_ps[:, 1, :]
         nc.tensor.matmul(abs_ps, lhsT=ident[:], rhs=a_abs[:], start=True, stop=True)
@@ -401,8 +411,15 @@ def tile_ellipticalnormalizedrbfnet_t_kernel(tc, x, a, m, p_bytes, p_scale, lp, 
         tx(1, 1, "b3")
         tx(2, 0, "b4")
         tx(2, 1, "b5")
-        sq_plain(0, 0)
+        x2_first = put(("x2", 0), 0, work.tile([P, TOK * PACK], F32, name="x2", bufs=2))
+        for j in range(2):
+            nc.scalar.activation(
+                out=x2_first[:, j * D : (j + 1) * D].rearrange("p (r u e) -> p r u e", u=2, e=2), in_=first_turned[j], func=ACT.Square
+            )
+        m_g = interleaved("m", C, "m_g")
+        nc.scalar.copy(out=m_g[:, 0 : C // 8], in_=by_fours(m_sb[:, :, halves[0]]))
         sq_plain(0, 1)
+        nc.scalar.copy(out=m_g[:, C // 8 : C // 4], in_=by_fours(m_sb[:, :, halves[1]]))
         quantise("p", C, 0, C // 2)
         half = keep.tile([P, PACK], F32, name="half")
         nc.vector.memset(half[:], 0.5)
@@ -410,10 +427,15 @@ def tile_ellipticalnormalizedrbfnet_t_kernel(tc, x, a, m, p_bytes, p_scale, lp, 
         root = keep.tile([P, PACK], F32, name="root")
         nc.gpsimd.tensor_tensor(out=root[:], in0=a_abs[:], in1=half[:], op=ALU.pow)
         gp_copy(interleaved("w", O, "w_g"), by_fours(w_sb[:]))
-        nc.scalar.copy(out=interleaved("m", C, "m_g"), in_=by_fours(m_sb[:]))
         mag = keep.tile([P, PACK], F32, name="mag")
         nc.scalar.activation(out=mag[:], in_=root[:], func=ACT.Square)
-        h(0, 0)
+        for j in range(2):
+            nc.vector.tensor_tensor(
+                out=hk_part(0, 0, j * P, (j + 1) * P).rearrange("p (r u e) -> p r u e", u=2, e=2),
+                in0=first_turned[j],
+                in1=a_sb[:].rearrange("p (u e) -> p u e", e=2).unsqueeze(1).to_broadcast([P, P, 2, 2]),
+                op=ALU.mult,
+            )
         k_plain(0, 0)
         h(0, 1)
         k_plain(0, 1)
@@ -421,10 +443,9 @@ def tile_ellipticalnormalizedrbfnet_t_kernel(tc, x, a, m, p_bytes, p_scale, lp, 
         nc.tensor.matmul(mag_ps, lhsT=ident[:], rhs=mag[:], start=True, stop=True)
         sq(1, 0)
         quantise("m", C)
-        quantise("w", O)
         qz(0)
-        k_gp(1, 0, TOK)
         sq(1, 1)
+        k_gp(1, TOK, GT)
         sq_plain(2, 0)
         gc_f = keep.tile([P, PACK], F32, name="gc_f")
         nc.scalar.activation(out=gc_f[:], in_=gc_sb[:], func=ACT.Copy, scale=float(C))
@@ -432,13 +453,14 @@ def tile_ellipticalnormalizedrbfnet_t_kernel(tc, x, a, m, p_bytes, p_scale, lp, 
         plane(0, 1, "b1")
         h(1, 0)
         h(1, 1)
-        sq(3, 0)
         plane(0, 2, "b2")
         plane(0, 3, "b3")
-        k_ve(1, TOK, GT)
+        k_ve(1, 0, TOK)
+        sq(3, 0)
         add_lp(0, 0)
         h(2, 1)
         qz(1)
+        quantise("w", O)
         add_lp(0, 1)
         add_lp(0, 2)
         add_lp(0, 3)
@@ -469,8 +491,8 @@ def tile_ellipticalnormalizedrbfnet_t_kernel(tc, x, a, m, p_bytes, p_scale, lp, 
         ex(0, 2)
         add_lp(1, 3)
         ex(0, 3)
-        tq(1, 0, "b2")
-        tq(1, 1, "b4")
+        tq(1, 0, "b2", 2)
+        tq(1, 1, "b4", 1)
 
         qz(2)
         sq(3, 1)
@@ -508,7 +530,7 @@ def tile_ellipticalnormalizedrbfnet_t_kernel(tc, x, a, m, p_bytes, p_scale, lp, 
         rr(0, 1)
         add_lp(2, 3)
         dm(0, 3, "b2", 0, 1)
-        tq(2, 0, "b5")
+        tq(2, 0, "b5", 1)
         ex(1, 3)
         dm(0, 3, "b2", 1, 2)
         tq(2, 1, "b6")
@@ -601,45 +623,86 @@ def tile_ellipticalnormalizedrbfnet_t_kernel(tc, x, a, m, p_bytes, p_scale, lp, 
         tx(6, 1, "b1")
         rr(2, 0)
         ex(3, 3)
-        ou(0, 1, "b6")
+        ou(0, 1, "b5")
         dm(2, 3, "b0", 2, 4)
         rr(2, 1)
         tq(4, 0, "b2")
 
-        order = [
-            (1, qz, ()), (6, store, (0,)), (3, rc, ()), (6, store, (1,)), (5, qr, ()), (0, sq, (1,)),
-            (1, plane, (0, "b3")), (2, mx, (0,)), (3, dg, (3,)), (1, plane, (1, "b4")), (3, us, (0,)), (4, rd, (3,)),
-            (1, add_lp, (0,)), (2, tq, (1, "b5")), (0, h, (1,)), (3, us, (1,)), (4, tu, (2, "b6")), (2, ex, (0,)),
-            (2, tq, (2, "b3")), (2, mx, (1,)), (0, k_gp, ()), (1, add_lp, (1,)), (1, plane, (2, "b0")), (4, rr, (2,)),
-            (2, ex, (1,)), (1, plane, (3, "b1")), (2, mx, (2,)), (1, add_lp, (2,)), (2, tq, (3, "b4")), (0, k_ve, ()),
-            (-1, tx, (0, "b2")), (2, ex, (2,)), (2, mx, (3,)), (3, dm, (3, "b0", 0, 1)), (1, add_lp, (3,)), (3, tu, (0, "b5")),
-            (-1, h, (0,)), (3, dm, (3, "b0", 1, 2)), (2, ex, (3,)), (3, tu, (1, "b6")), (3, rr, (0,)), (3, us, (2,)),
-            (-1, sq, (0,)), (5, ou, (0, "b3")), (3, rr, (1,)), (5, ou, (1, "b4")), (3, dm, (3, "b0", 2, 3)),
-            (-1, tx, (1, "b1")), (3, dm, (3, "b0", 3, 4)), (1, tq, (0, "b2")),
-        ]
-        for step in range(6, GROUPS - 1):
-            for lag, stage, args in order:
-                if 0 <= step - lag < GROUPS:
-                    stage(step - lag, *args)
+        def steady(n):
+            free, held = ("b0", "b3") if n % 2 == 0 else ("b3", "b0")
+            qz(n - 1)
+            store(n - 6, 0)
+            rc(n - 3)
+            sq(n, 1)
+            qr(n - 5)
+            store(n - 6, 1)
+            plane(n - 1, 0, held)
+            mx(n - 2, 0)
+            dg(n - 3, 3)
+            plane(n - 1, 1, "b4")
+            us(n - 3, 0)
+            rd(n - 4, 3)
+            add_lp(n - 1, 0)
+            tq(n - 2, 1, "b6")
+            h(n, 1)
+            us(n - 3, 1)
+            tu(n - 4, 2, "b5")
+            ex(n - 2, 0)
+            tq(n - 2, 2, free)
+            mx(n - 2, 1)
+            k_gp(n)
+            add_lp(n - 1, 1)
+            plane(n - 1, 2, held)
+            rr(n - 4, 2)
+            ex(n - 2, 1)
+            plane(n - 1, 3, "b1")
+            mx(n - 2, 2)
+            add_lp(n - 1, 2)
+            tq(n - 2, 3, "b4")
+            k_ve(n)
+            add_lp_ve(n - 1, 3, LP_SPLIT)
+            tx(n + 1, 0, "b2")
+            ex(n - 2, 2)
+            mx(n - 2, 3)
+            dm(n - 3, 3, held, 0, 1)
+            tu(n - 3, 0, "b5")
+            add_lp(n - 1, 3, 0, LP_SPLIT)
+            h(n + 1, 0)
+            dm(n - 3, 3, held, 1, 2)
+            tu(n - 3, 1, "b6")
+            tx(n + 1, 1, "b1")
+            ex(n - 2, 3)
+            rr(n - 3, 0)
+            us(n - 3, 2)
+            sq(n + 1, 0)
+            ou(n - 5, 0, free)
+            rr(n - 3, 1)
+            ou(n - 5, 1, "b5")
+            dm(n - 3, 3, held, 2, 3)
+            dm(n - 3, 3, held, 3, 4)
+            tq(n - 1, 0, "b2")
+
+        for n in range(6, GROUPS - 1):
+            steady(n)
 
         z = GROUPS - 1
         qz(z - 1)
         store(z - 6, 0)
         rc(z - 3)
-        store(z - 6, 1)
-        qr(z - 5)
         sq(z, 1)
-        plane(z - 1, 0, "b3")
+        qr(z - 5)
+        store(z - 6, 1)
+        plane(z - 1, 0, "b0")
         mx(z - 2, 0)
         dg(z - 3, 3)
         plane(z - 1, 1, "b4")
         us(z - 3, 0)
         rd(z - 4, 3)
         add_lp(z - 1, 0)
-        tq(z - 2, 1, "b5")
+        tq(z - 2, 1, "b6")
         h(z, 1)
         us(z - 3, 1)
-        tu(z - 4, 2, "b6")
+        tu(z - 4, 2, "b5")
         ex(z - 2, 0)
         tq(z - 2, 2, "b3")
         mx(z - 2, 1)
@@ -691,7 +754,7 @@ def tile_ellipticalnormalizedrbfnet_t_kernel(tc, x, a, m, p_bytes, p_scale, lp, 
         tq(z - 1, 2, "b2")
         plane(z, 3, "b5")
         add_lp(z, 0)
-        tq(z - 1, 3, "b1")
+        tq(z - 1, 3, "b1", 2)
         mx(z - 1, 1)
         add_lp(z, 1)
         qr(z - 3)

@@ -21,9 +21,8 @@ PACK = 4
 TOK = 2 * P
 GT = 4 * P
 GROUPS = N // GT
-K_SPLIT = 400
-LP_SPLIT = 448
-EARLY_SPLIT = {3: 288, GROUPS - 1: 416}
+K_SPLIT = 384
+EARLY_SPLIT = {3: 256, GROUPS - 1: 448}
 WORD_GROUP = GROUPS - 3
 AHEAD = 4
 
@@ -660,13 +659,12 @@ def tile_ellipticalnormalizedrbfnet_t_kernel(tc, x, a, m, p_bytes, p_scale, lp, 
             add_lp(n - 1, 2)
             tq(n - 2, 3, "b4")
             k_ve(n)
-            add_lp_ve(n - 1, 3, LP_SPLIT)
             tx(n + 1, 0, "b2")
             ex(n - 2, 2)
             mx(n - 2, 3)
             dm(n - 3, 3, held, 0, 1)
             tu(n - 3, 0, "b5")
-            add_lp(n - 1, 3, 0, LP_SPLIT)
+            add_lp(n - 1, 3)
             h(n + 1, 0)
             dm(n - 3, 3, held, 1, 2)
             tu(n - 3, 1, "b6")

@@ -22,8 +22,9 @@ TOK = 2 * P
 GT = 4 * P
 GROUPS = N // GT
 K_SPLIT = 384
-EARLY_SPLIT = {3: 256, GROUPS - 1: 448}
+EARLY_SPLIT = {2: 464, 3: 288, GROUPS - 1: 416}
 WORD_GROUP = GROUPS - 3
+TURNS = ("b3", "b0", "b6")
 AHEAD = 4
 
 
@@ -123,7 +124,10 @@ def tile_ellipticalnormalizedrbfnet_t_kernel(tc, x, a, m, p_bytes, p_scale, lp, 
             )
 
         def hk_part(g, which, first, last):
-            return once("hk", g, [P, 2, GT * PACK], BF16)[:, which, first * PACK : last * PACK]
+            if ("hk", g) not in tiles:
+                slot = g % 2 if g < 2 else (g + 1) % 2
+                put("hk", g, work.tile([P, 2, GT * PACK], BF16, name="hk" + str(slot), align_bytes=64, bufs=1))
+            return get("hk", g)[:, which, first * PACK : last * PACK]
 
         def h(g, b):
             nc.vector.tensor_tensor(
@@ -445,7 +449,8 @@ def tile_ellipticalnormalizedrbfnet_t_kernel(tc, x, a, m, p_bytes, p_scale, lp, 
         qz(0)
         sq(1, 1)
         k_gp(1, TOK, GT)
-        sq_plain(2, 0)
+        sq(2, 0)
+        sq(2, 1)
         gc_f = keep.tile([P, PACK], F32, name="gc_f")
         nc.scalar.activation(out=gc_f[:], in_=gc_sb[:], func=ACT.Copy, scale=float(C))
         plane(0, 0, "b0")
@@ -455,40 +460,39 @@ def tile_ellipticalnormalizedrbfnet_t_kernel(tc, x, a, m, p_bytes, p_scale, lp, 
         plane(0, 2, "b2")
         plane(0, 3, "b3")
         k_ve(1, 0, TOK)
-        sq(3, 0)
         add_lp(0, 0)
-        h(2, 1)
+        h(3, 0)
         qz(1)
         quantise("w", O)
+        k_gp(2)
         add_lp(0, 1)
         add_lp(0, 2)
         add_lp(0, 3)
         plane(1, 0, "b0")
         tq(0, 0, "b1")
         tq(0, 1, "b2")
-        sq(2, 1)
-        k_gp(2, TOK, GT)
+        sq(3, 0)
         h(2, 0)
-        k_plain(2, 0)
+        h(2, 1)
+        k_ve(2)
         plane(1, 1, "b3")
         tq(0, 2, "b4")
         add_lp(1, 0)
         mx(0, 0)
-        h(3, 0)
-        plane(1, 2, "b0")
-        tq(0, 3, "b5")
+        plane(1, 2, "b5")
+        tq(0, 3, "b6", 1)
         ex(0, 0)
         mx(0, 1)
-        plane(1, 3, "b6")
-        add_lp(1, 1)
-        mx(0, 2)
+        plane(1, 3, "b0")
+        add_lp_ve(1, 1)
         ex(0, 1)
+        mx(0, 2)
         tx(3, 1, "b1")
         add_lp_ve(1, 2)
-        tx(4, 0, "b0")
-        mx(0, 3)
         ex(0, 2)
         add_lp(1, 3)
+        tx(4, 0, "b3")
+        mx(0, 3)
         ex(0, 3)
         tq(1, 0, "b2", 2)
         tq(1, 1, "b4", 1)
@@ -497,7 +501,7 @@ def tile_ellipticalnormalizedrbfnet_t_kernel(tc, x, a, m, p_bytes, p_scale, lp, 
         sq(3, 1)
         rc(0)
         sq(4, 0)
-        plane(2, 0, "b3")
+        plane(2, 0, "b0")
         plane(2, 1, "b6")
         mx(1, 0)
         dg(0, 3)
@@ -505,42 +509,42 @@ def tile_ellipticalnormalizedrbfnet_t_kernel(tc, x, a, m, p_bytes, p_scale, lp, 
         us(0, 1)
         k_gp(3)
         us(0, 2)
-        tq(1, 2, "b5")
+        tq(1, 2, "b5", 1)
         mx(1, 1)
         h(3, 1)
         plane(2, 2, "b1")
         add_lp(2, 0)
         k_ve(3)
-        tq(1, 3, "b3")
+        tq(1, 3, "b0", 1)
         ex(1, 0)
         h(4, 0)
-        tu(0, 0, "b2")
+        tu(0, 0, "b2", 1)
         add_lp(2, 1)
-        plane(2, 3, "b0")
+        tu(0, 1, "b6")
+        plane(2, 3, "b3")
         mx(1, 2)
         ex(1, 1)
-        tu(0, 1, "b6")
         mx(1, 3)
         add_lp(2, 2)
         tx(4, 1, "b4")
         rr(0, 0)
+        dm(0, 3, "b2", 0, 1)
         ex(1, 2)
         tx(5, 0, "b1")
         rr(0, 1)
         add_lp(2, 3)
-        dm(0, 3, "b2", 0, 1)
-        tq(2, 0, "b5", 1)
+        tq(2, 0, "b5")
         ex(1, 3)
-        dm(0, 3, "b2", 1, 2)
+        dm(0, 3, "b2", 1, 3)
         tq(2, 1, "b6")
 
         qz(3)
         sq(4, 1)
         rc(1)
         sq(5, 0)
-        plane(3, 0, "b0")
-        plane(3, 1, "b3")
-        dm(0, 3, "b2", 2, 4)
+        plane(3, 0, "b3")
+        plane(3, 1, "b0")
+        dm(0, 3, "b2", 3, 4)
         mx(2, 0)
         dg(1, 3)
         us(1, 0)
@@ -549,18 +553,18 @@ def tile_ellipticalnormalizedrbfnet_t_kernel(tc, x, a, m, p_bytes, p_scale, lp, 
         us(1, 2)
         mx(2, 1)
         h(4, 1)
-        tq(2, 2, "b4")
+        tq(2, 2, "b4", 1)
         k_ve(4)
         add_lp(3, 0)
-        plane(3, 2, "b0")
+        plane(3, 2, "b3")
         h(5, 0)
         ex(2, 0)
         tu(0, 2, "b1")
         tq(2, 3, "b5")
         rd(0, 3)
         add_lp(3, 1)
-        tu(1, 0, "b2")
-        tu(1, 1, "b3")
+        tu(1, 0, "b2", 1)
+        tu(1, 1, "b0")
         mx(2, 2)
         ex(2, 1)
         plane(3, 3, "b6")
@@ -568,15 +572,16 @@ def tile_ellipticalnormalizedrbfnet_t_kernel(tc, x, a, m, p_bytes, p_scale, lp, 
         add_lp(3, 2)
         mx(2, 3)
         ex(2, 2)
-        tx(5, 1, "b0")
+        tx(5, 1, "b3")
         rr(1, 0)
+        dm(1, 3, "b4", 0, 1)
         tx(6, 0, "b1")
         ex(2, 3)
         rr(1, 1)
-        dm(1, 3, "b4", 0, 1)
         add_lp(3, 3)
-        tq(3, 0, "b2")
         dm(1, 3, "b4", 1, 2)
+        tq(3, 0, "b2")
+        dm(1, 3, "b4", 2, 3)
         tq(3, 1, "b5")
 
         gc_row = keep.tile([P, C], BF16, name="gc_row")
@@ -586,9 +591,9 @@ def tile_ellipticalnormalizedrbfnet_t_kernel(tc, x, a, m, p_bytes, p_scale, lp, 
         rc(2)
         qr(0)
         sq(6, 0)
-        plane(4, 0, "b3")
+        plane(4, 0, "b0")
         plane(4, 1, "b6")
-        dm(1, 3, "b4", 2, 4)
+        dm(1, 3, "b4", 3, 4)
         mx(3, 0)
         dg(2, 3)
         us(2, 0)
@@ -598,11 +603,11 @@ def tile_ellipticalnormalizedrbfnet_t_kernel(tc, x, a, m, p_bytes, p_scale, lp, 
         mx(3, 1)
         h(5, 1)
         add_lp(4, 0)
-        plane(4, 2, "b3")
-        tq(3, 2, "b0")
+        tq(3, 2, "b3")
+        plane(4, 2, "b0")
         k_ve(5)
         ex(3, 0)
-        tu(1, 2, "b2")
+        tu(1, 2, "b2", 1)
         h(6, 0)
         add_lp(4, 1)
         plane(4, 3, "b1")
@@ -613,45 +618,45 @@ def tile_ellipticalnormalizedrbfnet_t_kernel(tc, x, a, m, p_bytes, p_scale, lp, 
         tu(2, 1, "b4")
         mx(3, 2)
         add_lp(4, 2)
-        ou(0, 0, "b3")
+        ou(0, 0, "b0")
         rr(1, 2)
         ex(3, 2)
-        dm(2, 3, "b0", 0, 2)
+        dm(2, 3, "b3", 0, 2)
         mx(3, 3)
         add_lp(4, 3)
         tx(6, 1, "b1")
         rr(2, 0)
         ex(3, 3)
-        ou(0, 1, "b5")
-        dm(2, 3, "b0", 2, 4)
+        ou(0, 1, "b6")
+        dm(2, 3, "b3", 2, 4)
         rr(2, 1)
         tq(4, 0, "b2")
 
         def steady(n):
-            free, held = ("b0", "b3") if n % 2 == 0 else ("b3", "b0")
+            first, second, third = (TURNS[(i - n) % 3] for i in range(3))
             qz(n - 1)
             store(n - 6, 0)
             rc(n - 3)
-            sq(n, 1)
-            qr(n - 5)
             store(n - 6, 1)
-            plane(n - 1, 0, held)
+            qr(n - 5)
+            sq(n, 1)
+            plane(n - 1, 0, second)
             mx(n - 2, 0)
             dg(n - 3, 3)
             plane(n - 1, 1, "b4")
             us(n - 3, 0)
             rd(n - 4, 3)
             add_lp(n - 1, 0)
-            tq(n - 2, 1, "b6")
+            tq(n - 2, 1, "b5")
             h(n, 1)
             us(n - 3, 1)
-            tu(n - 4, 2, "b5")
+            tu(n - 4, 2, third)
             ex(n - 2, 0)
-            tq(n - 2, 2, free)
+            tq(n - 2, 2, first)
             mx(n - 2, 1)
             k_gp(n)
             add_lp(n - 1, 1)
-            plane(n - 1, 2, held)
+            plane(n - 1, 2, second)
             rr(n - 4, 2)
             ex(n - 2, 1)
             plane(n - 1, 3, "b1")
@@ -659,26 +664,26 @@ def tile_ellipticalnormalizedrbfnet_t_kernel(tc, x, a, m, p_bytes, p_scale, lp, 
             add_lp(n - 1, 2)
             tq(n - 2, 3, "b4")
             k_ve(n)
+            dm(n - 3, 3, third, 0, 1)
             tx(n + 1, 0, "b2")
             ex(n - 2, 2)
             mx(n - 2, 3)
-            dm(n - 3, 3, held, 0, 1)
+            dm(n - 3, 3, third, 1, 2)
             tu(n - 3, 0, "b5")
             add_lp(n - 1, 3)
             h(n + 1, 0)
-            dm(n - 3, 3, held, 1, 2)
-            tu(n - 3, 1, "b6")
-            tx(n + 1, 1, "b1")
+            dm(n - 3, 3, third, 2, 3)
+            tu(n - 3, 1, second)
             ex(n - 2, 3)
             rr(n - 3, 0)
             us(n - 3, 2)
             sq(n + 1, 0)
-            ou(n - 5, 0, free)
+            ou(n - 5, 0, first)
             rr(n - 3, 1)
-            ou(n - 5, 1, "b5")
-            dm(n - 3, 3, held, 2, 3)
-            dm(n - 3, 3, held, 3, 4)
-            tq(n - 1, 0, "b2")
+            ou(n - 5, 1, "b4")
+            tx(n + 1, 1, "b1")
+            dm(n - 3, 3, third, 3, 4)
+            tq(n - 1, 0, "b2", 1)
 
         for n in range(6, GROUPS - 1):
             steady(n)
@@ -687,9 +692,9 @@ def tile_ellipticalnormalizedrbfnet_t_kernel(tc, x, a, m, p_bytes, p_scale, lp, 
         qz(z - 1)
         store(z - 6, 0)
         rc(z - 3)
-        sq(z, 1)
-        qr(z - 5)
         store(z - 6, 1)
+        qr(z - 5)
+        sq(z, 1)
         plane(z - 1, 0, "b0")
         mx(z - 2, 0)
         dg(z - 3, 3)
@@ -697,10 +702,10 @@ def tile_ellipticalnormalizedrbfnet_t_kernel(tc, x, a, m, p_bytes, p_scale, lp, 
         us(z - 3, 0)
         rd(z - 4, 3)
         add_lp(z - 1, 0)
-        tq(z - 2, 1, "b6")
+        tq(z - 2, 1, "b5")
         h(z, 1)
         us(z - 3, 1)
-        tu(z - 4, 2, "b5")
+        tu(z - 4, 2, "b6")
         ex(z - 2, 0)
         tq(z - 2, 2, "b3")
         mx(z - 2, 1)
@@ -752,7 +757,7 @@ def tile_ellipticalnormalizedrbfnet_t_kernel(tc, x, a, m, p_bytes, p_scale, lp, 
         tq(z - 1, 2, "b2")
         plane(z, 3, "b5")
         add_lp(z, 0)
-        tq(z - 1, 3, "b1", 2)
+        tq(z - 1, 3, "b1", 1)
         mx(z - 1, 1)
         add_lp(z, 1)
         qr(z - 3)
@@ -763,7 +768,7 @@ def tile_ellipticalnormalizedrbfnet_t_kernel(tc, x, a, m, p_bytes, p_scale, lp, 
         add_lp_ve(z, 3)
         ex(z - 1, 1)
         mx(z - 1, 3)
-        tq(z, 0, "b4")
+        tq(z, 0, "b4", 1)
         tq(z, 1, "b0", 1)
         rr(z - 2, 2)
         ex(z - 1, 2)
@@ -791,9 +796,10 @@ def tile_ellipticalnormalizedrbfnet_t_kernel(tc, x, a, m, p_bytes, p_scale, lp, 
         us(z, 1)
         ex(z, 2)
         rd(z - 2, 3)
-        tu(z - 1, 1, "b0")
         ex(z, 3)
-        dm(z - 1, 3, "b5", 0, 2)
+        dm(z - 1, 3, "b5", 0, 1)
+        tu(z - 1, 1, "b0")
+        dm(z - 1, 3, "b5", 1, 2)
         rr(z - 1, 0)
         cw(z - 2, 0, 2)
         tu(z - 1, 2, "b3")

@@ -362,9 +362,7 @@ def tile_ellipticalnormalizedrbfnet_t_kernel(tc, x, a, m, p_bytes, p_scale, lp, 
         nc.sync.dma_start(out=ps_sb[:], in_=p_scale.rearrange("(p t) o -> p (t o)", t=PACK))
         pb_sb = keep.tile([P, PACK, C], U8, name="pb_sb")
         nc.sync.dma_start(out=pb_sb[:], in_=p_bytes.rearrange("(p t) c -> p t c", t=PACK))
-        x_first = put("x", 0, xin.tile([P, 2, D], BF16, name="x_sb"))
-        for j in range(2):
-            nc.sync.dma_start(out=x_first[:, j, :], in_=x_v[0][:, j, :])
+        load(0)
         load(1)
         m_sb = keep.tile([P, PACK, C], BF16, name="m_sb")
         nc.sync.dma_start(out=m_sb[:], in_=m.rearrange("(p t) c -> p t c", t=PACK))
@@ -388,21 +386,14 @@ def tile_ellipticalnormalizedrbfnet_t_kernel(tc, x, a, m, p_bytes, p_scale, lp, 
         nc.vector.scalar_tensor_tensor(out=signed[:], in0=twice_neg[:], scalar=-1.0, in1=ps_sb[:], op0=ALU.add, op1=ALU.mult)
         p_w = keep.tile([P, PACK, C], BF16, name="p_w")
         halves = (slice(0, C // 2), slice(C // 2, C))
-        for t in range(PACK):
-            nc.vector.tensor_scalar(
-                out=p_w[:, t, halves[0]], in0=pb_sb[:, t, halves[0]].bitcast(FP8), scalar1=signed[:, t : t + 1], scalar2=None, op0=ALU.mult
-            )
-            nc.scalar.activation(out=p_w[:, t, halves[1]], in_=pb_sb[:, t, halves[1]].bitcast(FP8), func=ACT.Copy, scale=signed[:, t : t + 1])
+        for cols in halves:
+            for t in range(PACK):
+                nc.vector.tensor_scalar(
+                    out=p_w[:, t, cols], in0=pb_sb[:, t, cols].bitcast(FP8), scalar1=signed[:, t : t + 1], scalar2=None, op0=ALU.mult
+                )
         minus_mean = keep.tile([P, 1], F32, name="minus_mean")
         nc.gpsimd.memset(minus_mean[:], -1.0 / C)
-        load(AHEAD)
-        first_words = x_first[:].rearrange("p j d -> p (j d)").bitcast(F32)
-        first_turned = []
-        for j, name in enumerate(("b0", "b6")):
-            xt = bank([P, 2, P], name)
-            for u in range(2):
-                nc.tensor.transpose(xt[:, u, :], first_words[:, j * D // 2 + u : (j + 1) * D // 2 : 2], ident[:])
-            first_turned.append(xt[:].rearrange("p u r -> p (u r)").bitcast(BF16).rearrange("p (u r e) -> p r u e", u=2, e=2))
+        tx(0, 0, "b0")
         const_ps = psum.tile([P, 2, PACK], F32, name="const_ps")
         abs_ps, mag_ps = const_ps[:, 0, :], const_ps[:, 1, :]
         nc.tensor.matmul(abs_ps, lhsT=ident[:], rhs=a_abs[:], start=True, stop=True)
@@ -414,15 +405,8 @@ def tile_ellipticalnormalizedrbfnet_t_kernel(tc, x, a, m, p_bytes, p_scale, lp, 
         tx(1, 1, "b3")
         tx(2, 0, "b4")
         tx(2, 1, "b5")
-        x2_first = put(("x2", 0), 0, work.tile([P, TOK * PACK], F32, name="x2", bufs=2))
-        for j in range(2):
-            nc.scalar.activation(
-                out=x2_first[:, j * D : (j + 1) * D].rearrange("p (r u e) -> p r u e", u=2, e=2), in_=first_turned[j], func=ACT.Square
-            )
-        m_g = interleaved("m", C, "m_g")
-        nc.scalar.copy(out=m_g[:, 0 : C // 8], in_=by_fours(m_sb[:, :, halves[0]]))
+        sq_plain(0, 0)
         sq_plain(0, 1)
-        nc.scalar.copy(out=m_g[:, C // 8 : C // 4], in_=by_fours(m_sb[:, :, halves[1]]))
         quantise("p", C, 0, C // 2)
         half = keep.tile([P, PACK], F32, name="half")
         nc.vector.memset(half[:], 0.5)
@@ -430,15 +414,10 @@ def tile_ellipticalnormalizedrbfnet_t_kernel(tc, x, a, m, p_bytes, p_scale, lp, 
         root = keep.tile([P, PACK], F32, name="root")
         nc.gpsimd.tensor_tensor(out=root[:], in0=a_abs[:], in1=half[:], op=ALU.pow)
         gp_copy(interleaved("w", O, "w_g"), by_fours(w_sb[:]))
+        nc.scalar.copy(out=interleaved("m", C, "m_g"), in_=by_fours(m_sb[:]))
         mag = keep.tile([P, PACK], F32, name="mag")
         nc.scalar.activation(out=mag[:], in_=root[:], func=ACT.Square)
-        for j in range(2):
-            nc.vector.tensor_tensor(
-                out=hk_part(0, 0, j * P, (j + 1) * P).rearrange("p (r u e) -> p r u e", u=2, e=2),
-                in0=first_turned[j],
-                in1=a_sb[:].rearrange("p (u e) -> p u e", e=2).unsqueeze(1).to_broadcast([P, P, 2, 2]),
-                op=ALU.mult,
-            )
+        h(0, 0)
         k_plain(0, 0)
         h(0, 1)
         k_plain(0, 1)
@@ -447,8 +426,8 @@ def tile_ellipticalnormalizedrbfnet_t_kernel(tc, x, a, m, p_bytes, p_scale, lp, 
         sq(1, 0)
         quantise("m", C)
         qz(0)
+        k_gp(1, 0, TOK)
         sq(1, 1)
-        k_gp(1, TOK, GT)
         sq(2, 0)
         sq(2, 1)
         gc_f = keep.tile([P, PACK], F32, name="gc_f")
@@ -459,7 +438,7 @@ def tile_ellipticalnormalizedrbfnet_t_kernel(tc, x, a, m, p_bytes, p_scale, lp, 
         h(1, 1)
         plane(0, 2, "b2")
         plane(0, 3, "b3")
-        k_ve(1, 0, TOK)
+        k_ve(1, TOK, GT)
         add_lp(0, 0)
         h(3, 0)
         qz(1)

@@ -22,7 +22,7 @@ TOK = 2 * P
 GT = 4 * P
 GROUPS = N // GT
 K_SPLIT = 384
-EARLY_SPLIT = {2: 464, 3: 288, GROUPS - 1: 416}
+EARLY_SPLIT = {0: 0, 1: 256, 2: 464, 3: 288, GROUPS - 1: 416}
 WORD_GROUP = GROUPS - 3
 TURNS = ("b3", "b0", "b6")
 AHEAD = 4
@@ -97,28 +97,32 @@ def tile_ellipticalnormalizedrbfnet_t_kernel(tc, x, a, m, p_bytes, p_scale, lp, 
             halves = get(("xt", b), g)[:].rearrange("p u r -> p (u r)").bitcast(BF16)
             return halves.rearrange("p (u r e) -> p u e r", u=2, e=2)
 
+        def k_split(g):
+            return EARLY_SPLIT.get(g, K_SPLIT)
+
         def sq(g, b):
-            y = once("y", g, [P, GT // 4, PACK, 4], F32, bufs=3)
-            for t in range(PACK):
-                nc.scalar.activation(
-                    out=y[:, b * TOK // 4 : (b + 1) * TOK // 4, t, :],
-                    in_=x_turned(g, b)[:, t // 2, t % 2, :].rearrange("p (c i) -> p c i", i=4),
-                    func=ACT.Square,
-                    scale=root[:, t : t + 1],
-                )
+            split = min(max(k_split(g) - b * TOK, 0), TOK)
+            turned = x_turned(g, b)
+            if split > 0:
+                y = once("y", g, [P, GT // 4, PACK, 4], F32, bufs=3)
+                for t in range(PACK):
+                    nc.scalar.activation(
+                        out=y[:, b * TOK // 4 : (b * TOK + split) // 4, t, :],
+                        in_=turned[:, t // 2, t % 2, 0:split].rearrange("p (c i) -> p c i", i=4),
+                        func=ACT.Square,
+                        scale=root[:, t : t + 1],
+                    )
+            if split < TOK:
+                x2 = put(("x2", b), g, work.tile([P, TOK - split, 2, 2], F32, name="x2"))
+                nc.scalar.activation(out=x2[:], in_=turned[:, :, :, split:TOK].rearrange("p u e r -> p r u e"), func=ACT.Square)
 
-        def sq_plain(g, b):
-            x2 = put(("x2", b), g, work.tile([P, TOK * PACK], F32, name="x2", bufs=2))
-            nc.scalar.activation(
-                out=x2[:].rearrange("p (r u e) -> p r u e", u=2, e=2), in_=x_turned(g, b).rearrange("p u e r -> p r u e"), func=ACT.Square
-            )
-
-        def k_plain(g, b):
+        def k_ve(g, b=1):
+            first = max(k_split(g), b * TOK)
             nc.vector.scalar_tensor_tensor(
-                out=hk_part(g, 1, b * TOK, (b + 1) * TOK).rearrange("p (r t) -> p r t", t=PACK),
-                in0=get(("x2", b), g)[:].rearrange("p (r t) -> p r t", t=PACK),
+                out=hk_part(g, 1, first, (b + 1) * TOK).rearrange("p (r t) -> p r t", t=PACK),
+                in0=get(("x2", b), g)[:].rearrange("p r u e -> p r (u e)"),
                 scalar=-1.0,
-                in1=abs_ps.unsqueeze(1).to_broadcast([P, TOK, PACK]),
+                in1=abs_ps[:].unsqueeze(1).to_broadcast([P, (b + 1) * TOK - first, PACK]),
                 op0=ALU.add,
                 op1=ALU.mult,
             )
@@ -137,24 +141,12 @@ def tile_ellipticalnormalizedrbfnet_t_kernel(tc, x, a, m, p_bytes, p_scale, lp, 
                 op=ALU.mult,
             )
 
-        def k_split(g):
-            return EARLY_SPLIT.get(g, K_SPLIT)
-
-        def k_gp(g, first=0, last=None):
-            last = last or k_split(g)
+        def k_gp(g):
+            first, last = 0, k_split(g)
             nc.gpsimd.tensor_tensor(
                 out=hk_part(g, 1, first, last).rearrange("p (c i t) -> p c i t", i=4, t=PACK),
                 in0=get("y", g)[:, first // 4 : last // 4].rearrange("p c t i -> p c i t"),
                 in1=mag[:].unsqueeze(1).unsqueeze(2).to_broadcast([P, (last - first) // 4, 4, PACK]),
-                op=ALU.subtract,
-            )
-
-        def k_ve(g, first=None, last=GT):
-            first = k_split(g) if first is None else first
-            nc.vector.tensor_tensor(
-                out=hk_part(g, 1, first, last).rearrange("p (c i t) -> p c t i", i=4, t=PACK),
-                in0=get("y", g)[:, first // 4 : last // 4],
-                in1=mag_ps.unsqueeze(1).unsqueeze(3).to_broadcast([P, (last - first) // 4, PACK, 4]),
                 op=ALU.subtract,
             )
 
@@ -394,9 +386,8 @@ def tile_ellipticalnormalizedrbfnet_t_kernel(tc, x, a, m, p_bytes, p_scale, lp, 
         minus_mean = keep.tile([P, 1], F32, name="minus_mean")
         nc.gpsimd.memset(minus_mean[:], -1.0 / C)
         tx(0, 0, "b0")
-        const_ps = psum.tile([P, 2, PACK], F32, name="const_ps")
-        abs_ps, mag_ps = const_ps[:, 0, :], const_ps[:, 1, :]
-        nc.tensor.matmul(abs_ps, lhsT=ident[:], rhs=a_abs[:], start=True, stop=True)
+        abs_ps = psum.tile([P, PACK], F32, name="abs_ps")
+        nc.tensor.matmul(abs_ps[:], lhsT=ident[:], rhs=a_abs[:], start=True, stop=True)
         tx(0, 1, "b1")
         p_g = interleaved("p", C, "p_g")
         for b, cols in enumerate(halves):
@@ -405,8 +396,8 @@ def tile_ellipticalnormalizedrbfnet_t_kernel(tc, x, a, m, p_bytes, p_scale, lp, 
         tx(1, 1, "b3")
         tx(2, 0, "b4")
         tx(2, 1, "b5")
-        sq_plain(0, 0)
-        sq_plain(0, 1)
+        sq(0, 0)
+        sq(0, 1)
         quantise("p", C, 0, C // 2)
         half = keep.tile([P, PACK], F32, name="half")
         nc.vector.memset(half[:], 0.5)
@@ -418,15 +409,14 @@ def tile_ellipticalnormalizedrbfnet_t_kernel(tc, x, a, m, p_bytes, p_scale, lp, 
         mag = keep.tile([P, PACK], F32, name="mag")
         nc.scalar.activation(out=mag[:], in_=root[:], func=ACT.Square)
         h(0, 0)
-        k_plain(0, 0)
+        k_ve(0, 0)
         h(0, 1)
-        k_plain(0, 1)
+        k_ve(0, 1)
         tx(3, 0, "b6")
-        nc.tensor.matmul(mag_ps, lhsT=ident[:], rhs=mag[:], start=True, stop=True)
         sq(1, 0)
         quantise("m", C)
         qz(0)
-        k_gp(1, 0, TOK)
+        k_gp(1)
         sq(1, 1)
         sq(2, 0)
         sq(2, 1)
@@ -438,7 +428,7 @@ def tile_ellipticalnormalizedrbfnet_t_kernel(tc, x, a, m, p_bytes, p_scale, lp, 
         h(1, 1)
         plane(0, 2, "b2")
         plane(0, 3, "b3")
-        k_ve(1, TOK, GT)
+        k_ve(1)
         add_lp(0, 0)
         h(3, 0)
         qz(1)

@@ -21,7 +21,7 @@ PACK = 4
 TOK = 2 * P
 GT = 4 * P
 GROUPS = N // GT
-K_SPLIT = 384
+K_SPLIT = 360
 EARLY_SPLIT = {0: 0, 1: 256, 2: 464, 3: 288, GROUPS - 1: 416}
 WORD_GROUP = GROUPS - 3
 TURNS = ("b3", "b0", "b6")

from contextlib import ExitStack

import concourse.mybir as mybir
from concourse.masks import make_identity

N, D, C, O = 8192, 512, 512, 256
FLOPS = 2 * N * D * C * 2 + 2 * N * C * O

F32 = mybir.dt.float32
BF16 = mybir.dt.bfloat16
U32 = mybir.dt.uint32
U8 = mybir.dt.uint8
FP8 = mybir.dt.float8_e4m3fn
FP8X4 = mybir.dt.float8_e4m3fn_x4
ACT = mybir.ActivationFunctionType
ALU = mybir.AluOpType
AX = mybir.AxisListType

P = 128
PACK = 4
TOK = 2 * P
GT = 4 * P
GROUPS = N // GT
K_SPLIT = 360
EARLY_SPLIT = {0: 0, 1: 256, 2: 464, 3: 288, GROUPS - 1: 416}
WORD_GROUP = GROUPS - 3
TURNS = ("b3", "b0", "b6")
AHEAD = 4


def tile_ellipticalnormalizedrbfnet_t_kernel(tc, x, a, m, p_bytes, p_scale, lp, gc, w, out):
    nc = tc.nc
    x_v = x.rearrange("(g p j) d -> g p j d", p=P, j=2)
    out_v = out.rearrange("(g p j) o -> g p j o", p=P, j=2)

    with ExitStack() as ctx:
        keep = ctx.enter_context(tc.tile_pool(name="keep", bufs=1))
        xin = ctx.enter_context(tc.tile_pool(name="xin", bufs=AHEAD + 2))
        work = ctx.enter_context(tc.tile_pool(name="work", bufs=2))
        psum = ctx.enter_context(tc.psum_pool(name="psum", bufs=1))
        ctx.enter_context(tc.manual_schedule())

        tiles = {}

        def put(kind, g, t):
            tiles[(kind, g)] = t
            return t

        def get(kind, g):
            return tiles[(kind, g)]

        def once(kind, g, shape, dtype, bufs=2):
            if (kind, g) not in tiles:
                put(kind, g, work.tile(shape, dtype, name=kind, align_bytes=64, bufs=bufs))
            return get(kind, g)

        def bank(shape, name):
            return psum.tile(shape, F32, name=name)

        def load(i):
            x_sb = put("x", i, xin.tile([P, 2, D], BF16, name="x_sb"))
            nc.sync.dma_start(out=x_sb[:], in_=x_v[i])

        def gp_copy(dst, src, factor=1.0):
            nc.gpsimd.tensor_scalar(out=dst, in0=src, scalar1=factor, scalar2=0.0, op0=ALU.mult, op1=ALU.add)

        def quantise(name, width, first=0, last=None):
            if first == 0:
                codes = keep.tile([P, width], U32, name=name + "_codes", align_bytes=64)
                scales = keep.tile([P, width], U8, name=name + "_scales", align_bytes=64)
                put(name, 0, (codes, scales))
            codes, scales = get(name, 0)
            last = last or width
            nc.vector.quantize_mx(
                out=codes[:, first:last].bitcast(FP8X4), scales=scales[:, first:last], in_=get(name + "_g", 0)[:, PACK * first : PACK * last]
            )

        def interleaved(name, width, tag):
            g = put(name + "_g", 0, keep.tile([P, PACK * width], BF16, name=tag, align_bytes=64))
            return g[:].rearrange("p (c i t) -> p c t i", i=4, t=PACK)

        def by_fours(rows):
            return rows.rearrange("p t (c i) -> p c t i", i=4)

        def tx(g, b, name):
            i = 2 * g + b
            if i + AHEAD < 2 * GROUPS:
                load(i + AHEAD)
            words = get("x", i)[:].rearrange("p j d -> p (j d)").bitcast(F32)
            xt = put(("xt", b), g, bank([P, 2, TOK], name))
            half = D // 2
            for j in range(2):
                for u in range(2):
                    nc.tensor.transpose(xt[:, u, j * P : (j + 1) * P], words[:, j * half + u : (j + 1) * half : 2], ident[:])

        def x_turned(g, b):
            halves = get(("xt", b), g)[:].rearrange("p u r -> p (u r)").bitcast(BF16)
            return halves.rearrange("p (u r e) -> p u e r", u=2, e=2)

        def k_split(g):
            return EARLY_SPLIT.get(g, K_SPLIT)

        def sq(g, b):
            split = min(max(k_split(g) - b * TOK, 0), TOK)
            turned = x_turned(g, b)
            if split > 0:
                y = once("y", g, [P, GT // 4, PACK, 4], F32, bufs=3)
                for t in range(PACK):
                    nc.scalar.activation(
                        out=y[:, b * TOK // 4 : (b * TOK + split) // 4, t, :],
                        in_=turned[:, t // 2, t % 2, 0:split].rearrange("p (c i) -> p c i", i=4),
                        func=ACT.Square,
                        scale=root[:, t : t + 1],
                    )
            if split < TOK:
                x2 = put(("x2", b), g, work.tile([P, TOK - split, 2, 2], F32, name="x2"))
                nc.scalar.activation(out=x2[:], in_=turned[:, :, :, split:TOK].rearrange("p u e r -> p r u e"), func=ACT.Square)

        def k_ve(g, b=1):
            first = max(k_split(g), b * TOK)
            nc.vector.scalar_tensor_tensor(
                out=hk_part(g, 1, first, (b + 1) * TOK).rearrange("p (r t) -> p r t", t=PACK),
                in0=get(("x2", b), g)[:].rearrange("p r u e -> p r (u e)"),
                scalar=-1.0,
                in1=abs_ps[:].unsqueeze(1).to_broadcast([P, (b + 1) * TOK - first, PACK]),
                op0=ALU.add,
                op1=ALU.mult,
            )

        def hk_part(g, which, first, last):
            if ("hk", g) not in tiles:
                slot = g % 2 if g < 2 else (g + 1) % 2
                put("hk", g, work.tile([P, 2, GT * PACK], BF16, name="hk" + str(slot), align_bytes=64, bufs=1))
            return get("hk", g)[:, which, first * PACK : last * PACK]

        def h(g, b):
            nc.vector.tensor_tensor(
                out=hk_part(g, 0, b * TOK, (b + 1) * TOK).rearrange("p (r u e) -> p r u e", u=2, e=2),
                in0=x_turned(g, b).rearrange("p u e r -> p r u e"),
                in1=a_sb[:].rearrange("p (u e) -> p u e", e=2).unsqueeze(1).to_broadcast([P, TOK, 2, 2]),
                op=ALU.mult,
            )

        def k_gp(g):
            first, last = 0, k_split(g)
            nc.gpsimd.tensor_tensor(
                out=hk_part(g, 1, first, last).rearrange("p (c i t) -> p c i t", i=4, t=PACK),
                in0=get("y", g)[:, first // 4 : last // 4].rearrange("p c t i -> p c i t"),
                in1=mag[:].unsqueeze(1).unsqueeze(2).to_broadcast([P, (last - first) // 4, 4, PACK]),
                op=ALU.subtract,
            )

        def qz(g):
            codes = once("codes", g, [P, 2, GT], U32)
            scales = once("scales", g, [P, 2, GT], U8)
            nc.vector.quantize_mx(
                out=codes[:].rearrange("p b r -> p (b r)").bitcast(FP8X4),
                scales=scales[:].rearrange("p b r -> p (b r)"),
                in_=get("hk", g)[:].rearrange("p b r -> p (b r)"),
            )

        def plane(g, s, name):
            qt = put(("qt", s), g, bank([P, GT], name))
            codes, scales = get("codes", g), get("scales", g)
            cols = slice(s * P, (s + 1) * P)
            for b, weight in enumerate(("m", "p")):
                wc, ws = get(weight, 0)
                nc.tensor.matmul_mx(
                    out=qt[:],
                    lhsT=wc[:, cols].bitcast(FP8X4),
                    lhsT_scale=ws[:, cols],
                    rhs=codes[:, b, :].bitcast(FP8X4),
                    rhs_scale=scales[:, b, :],
                    start=(b == 0),
                    stop=(b == 1),
                )

        def add_lp(g, s, first=0, last=GT):
            ql = once("ql" + str(s), g, [P, GT], F32)
            nc.scalar.activation(
                out=ql[:, first:last], in_=get(("qt", s), g)[:, first:last], func=ACT.Identity, bias=lp_sb[:, s, 0:1], scale=1.0
            )

        def add_lp_ve(g, s, first=0, last=GT):
            ql = once("ql" + str(s), g, [P, GT], F32)
            nc.vector.tensor_scalar(
                out=ql[:, first:last], in0=get(("qt", s), g)[:, first:last], scalar1=lp_sb[:, s, 0:1], scalar2=None, op0=ALU.add
            )

        def turn(dst, src, plain):
            if plain:
                nc.tensor.matmul(dst, lhsT=src, rhs=ident[:], start=True, stop=True)
            else:
                nc.tensor.transpose(dst, src, ident[:])

        def tq(g, j, name, plain=0):
            q = put(("q", j), g, bank([P, C], name))
            for s in range(PACK):
                turn(q[:, s * P : (s + 1) * P], get("ql" + str(s), g)[:, j * P : (j + 1) * P], s >= PACK - plain)

        def mx(g, j):
            nm = once("nm" + str(j), g, [P, 1], F32)
            nc.vector.tensor_reduce(out=nm[:], in_=get(("q", j), g)[:], axis=AX.X, op=ALU.max, negate=True)

        def ex(g, j):
            e = once("e" + str(j), g, [P, C], F32)
            total = once("total", g, [P, 4], F32)
            if g == WORD_GROUP and j < 2:
                e_v, q_v = e[:], get(("q", j), g)[:]
            else:
                e_v = e[:].rearrange("n (t p) -> n t p", t=PACK)
                q_v = get(("q", j), g)[:].rearrange("n (p t) -> n t p", t=PACK)
            nc.scalar.activation(
                out=e_v,
                in_=q_v,
                func=ACT.Exp,
                bias=get("nm" + str(j), g)[:],
                scale=1.0,
                accum_out=total[:, j : j + 1],
            )

        def rc(g, first=0, last=4):
            rs = once("rs", g, [P, 4], F32)
            nc.vector.reciprocal(out=rs[:, first:last], in_=get("total", g)[:, first:last])

        def u_tile(g, j):
            if g == WORD_GROUP and j < 2:
                return once("u_words", g, [P, 2, C], F32, bufs=1)[:, j, :]
            return once("u" + str(j), g, [P, C], F32)[:]

        def us(g, j):
            nc.gpsimd.tensor_scalar(
                out=u_tile(g, j), in0=get("e" + str(j), g)[:], scalar1=get("rs", g)[:, j : j + 1], scalar2=-1.0 / C, op0=ALU.mult, op1=ALU.add
            )

        def uw(g):
            big = once("big", g, [P, 2], F32, bufs=1)
            gp_copy(big[:], get("rs", g)[:, 0:2], float(C))
            dg(g, 3)
            for j in range(2):
                nc.gpsimd.tensor_scalar(
                    out=u_tile(g, j), in0=get("e" + str(j), g)[:], scalar1=big[:, j : j + 1], scalar2=-1.0, op0=ALU.mult, op1=ALU.add
                )

        def ua(g, j):
            nc.scalar.activation(
                out=u_tile(g, j), in_=get("e" + str(j), g)[:], func=ACT.Identity, scale=get("rs", g)[:, j : j + 1], bias=minus_mean[:]
            )

        def gt(g):
            r_tok = once("r_tok", g, [P, 2, C], BF16, bufs=1)
            nc.gpsimd.tensor_tensor(
                out=r_tok[:], in0=get("u_words", g)[:], in1=gc_row[:].unsqueeze(1).to_broadcast([P, 2, C]), op=ALU.mult
            )

        def tw(g, first, count, name):
            words = get("r_tok", g)[:].rearrange("n j c -> n (j c)").bitcast(F32)
            rw = put(("rw", first), g, bank([P, count, 2, P], name))
            for j in range(count):
                for u in range(2):
                    nc.tensor.transpose(rw[:, j, u, :], words[:, (first + j) * TOK + u : (first + j + 1) * TOK : 2], ident[:])

        def cw(g, first, count):
            words = r_cols(g, first, count).rearrange("p n s -> p (n s)").bitcast(F32)
            nc.scalar.copy(out=words.rearrange("p (j n u) -> p j n u", j=count, u=2), in_=get(("rw", first), g)[:].rearrange("p j u n -> p j n u"))

        def r_cols(g, j, count=1):
            return once("r", g, [P, GT, PACK], BF16, bufs=3)[:, j * P : (j + count) * P, :]

        def tu(g, j, name, plain=0):
            ut = put(("ut", j), g, bank([P, PACK, P], name))
            u = u_tile(g, j)
            for s in range(PACK):
                turn(ut[:, s, :], u[:, s * P : (s + 1) * P], s >= PACK - plain)

        def rr(g, j):
            nc.vector.tensor_tensor(
                out=r_cols(g, j),
                in0=get(("ut", j), g)[:].rearrange("p s n -> p n s"),
                in1=gc_f[:].unsqueeze(1).to_broadcast([P, P, PACK]),
                op=ALU.mult,
            )

        def dg(g, j):
            gp_copy(once("diag" + str(j), g, [P, P], F32)[:], ident[:], get("rs", g)[:, j : j + 1])

        def dg_scalar(g, j):
            diag = once("diag" + str(j), g, [P, P], F32)
            nc.scalar.activation(out=diag[:], in_=ident[:], func=ACT.Copy, scale=get("rs", g)[:, j : j + 1])

        def dm(g, j, name, first=0, last=PACK):
            if first == 0:
                put(("ut", j), g, bank([P, PACK, P], name))
            for s in range(first, last):
                nc.tensor.matmul(
                    get(("ut", j), g)[:, s, :],
                    lhsT=get("e" + str(j), g)[:, s * P : (s + 1) * P],
                    rhs=get("diag" + str(j), g)[:],
                    start=True,
                    stop=True,
                )

        def rd(g, j):
            nc.vector.scalar_tensor_tensor(
                out=r_cols(g, j),
                in0=get(("ut", j), g)[:].rearrange("p s n -> p n s"),
                scalar=-1.0 / C,
                in1=gc_f[:].unsqueeze(1).to_broadcast([P, P, PACK]),
                op0=ALU.add,
                op1=ALU.mult,
            )

        def qr(g, first=0, count=4):
            cols = slice(first * P, (first + count) * P)
            nc.vector.quantize_mx(
                out=once("rcodes", g, [P, GT], U32, bufs=3)[:, cols].bitcast(FP8X4),
                scales=once("rscales", g, [P, GT], U8, bufs=3)[:, cols],
                in_=get("r", g)[:, cols, :].rearrange("p n s -> p (n s)"),
            )

        def last_product(dst, g, j):
            w_codes, w_scales = get("w", 0)
            cols = slice(j * P, (j + 1) * P)
            nc.tensor.matmul_mx(
                out=dst,
                lhsT=get("rcodes", g)[:, cols].bitcast(FP8X4),
                lhsT_scale=get("rscales", g)[:, cols],
                rhs=w_codes[:].bitcast(FP8X4),
                rhs_scale=w_scales[:],
                start=True,
                stop=True,
            )

        def ou(g, b, name):
            o_ps = put(("o_ps", b), g, bank([P, 2 * O], name))
            for j in range(2):
                last_product(o_ps[:, j * O : (j + 1) * O], g, 2 * b + j)

        def store(g, b, copy=nc.scalar.copy):
            o_sb = work.tile([P, 2 * O], F32, name="o_sb", bufs=2 * GROUPS - 4)
            copy(out=o_sb[:], in_=get(("o_ps", b), g)[:])
            nc.sync.dma_start(out=out_v[2 * g + b], in_=o_sb[:].rearrange("p (j o) -> p j o", j=2))

        def out_tile(g, j, name, copy, queue):
            o_ps = bank([P, O], name)
            last_product(o_ps[:], g, j)
            o_sb = work.tile([P, O], F32, name="o_last")
            copy(out=o_sb[:], in_=o_ps[:])
            queue.dma_start(out=out_v[2 * g + j // 2][:, j % 2, :], in_=o_sb[:])

        a_sb = keep.tile([P, PACK], BF16, name="a_sb")
        nc.sync.dma_start(out=a_sb[:], in_=a.rearrange("(p t) -> p t", t=PACK))
        ps_sb = keep.tile([P, PACK], F32, name="ps_sb")
        nc.sync.dma_start(out=ps_sb[:], in_=p_scale.rearrange("(p t) o -> p (t o)", t=PACK))
        pb_sb = keep.tile([P, PACK, C], U8, name="pb_sb")
        nc.sync.dma_start(out=pb_sb[:], in_=p_bytes.rearrange("(p t) c -> p t c", t=PACK))
        load(0)
        load(1)
        m_sb = keep.tile([P, PACK, C], BF16, name="m_sb")
        nc.sync.dma_start(out=m_sb[:], in_=m.rearrange("(p t) c -> p t c", t=PACK))
        load(2)
        load(3)
        lp_sb = keep.tile([P, PACK, 2], BF16, name="lp_sb")
        with nc.allow_non_contiguous_dma("512 values, one to a partition and slice"):
            nc.sync.dma_start(out=lp_sb[:, :, 0:1], in_=lp.rearrange("(s p o) -> p s o", p=P, o=1))
        gc_sb = keep.tile([P, PACK], BF16, name="gc_sb")
        nc.sync.dma_start(out=gc_sb[:], in_=gc.rearrange("(p t) -> p t", t=PACK))
        w_sb = keep.tile([P, PACK, O], BF16, name="w_sb")
        nc.sync.dma_start(out=w_sb[:], in_=w.rearrange("(p t) o -> p t o", t=PACK))

        ident = keep.tile([P, P], F32, name="ident")
        make_identity(nc, ident[:])
        a_abs = keep.tile([P, PACK], F32, name="a_abs")
        nc.scalar.activation(out=a_abs[:], in_=a_sb[:], func=ACT.Abs)
        twice_neg = keep.tile([P, PACK], F32, name="twice_neg")
        nc.vector.tensor_scalar(out=twice_neg[:], in0=a_sb[:], scalar1=0.0, scalar2=2.0, op0=ALU.is_lt, op1=ALU.mult)
        signed = keep.tile([P, PACK], F32, name="signed")
        nc.vector.scalar_tensor_tensor(out=signed[:], in0=twice_neg[:], scalar=-1.0, in1=ps_sb[:], op0=ALU.add, op1=ALU.mult)
        p_w = keep.tile([P, PACK, C], BF16, name="p_w")
        halves = (slice(0, C // 2), slice(C // 2, C))
        for cols in halves:
            for t in range(PACK):
                nc.vector.tensor_scalar(
                    out=p_w[:, t, cols], in0=pb_sb[:, t, cols].bitcast(FP8), scalar1=signed[:, t : t + 1], scalar2=None, op0=ALU.mult
                )
        minus_mean = keep.tile([P, 1], F32, name="minus_mean")
        nc.gpsimd.memset(minus_mean[:], -1.0 / C)
        tx(0, 0, "b0")
        abs_ps = psum.tile([P, PACK], F32, name="abs_ps")
        nc.tensor.matmul(abs_ps[:], lhsT=ident[:], rhs=a_abs[:], start=True, stop=True)
        tx(0, 1, "b1")
        p_g = interleaved("p", C, "p_g")
        for b, cols in enumerate(halves):
            nc.vector.tensor_copy(out=p_g[:, b * C // 8 : (b + 1) * C // 8], in_=by_fours(p_w[:, :, cols]))
        tx(1, 0, "b2")
        tx(1, 1, "b3")
        tx(2, 0, "b4")
        tx(2, 1, "b5")
        sq(0, 0)
        sq(0, 1)
        quantise("p", C, 0, C // 2)
        half = keep.tile([P, PACK], F32, name="half")
        nc.vector.memset(half[:], 0.5)
        quantise("p", C, C // 2, C)
        root = keep.tile([P, PACK], F32, name="root")
        nc.gpsimd.tensor_tensor(out=root[:], in0=a_abs[:], in1=half[:], op=ALU.pow)
        gp_copy(interleaved("w", O, "w_g"), by_fours(w_sb[:]))
        nc.scalar.copy(out=interleaved("m", C, "m_g"), in_=by_fours(m_sb[:]))
        mag = keep.tile([P, PACK], F32, name="mag")
        nc.scalar.activation(out=mag[:], in_=root[:], func=ACT.Square)
        h(0, 0)
        k_ve(0, 0)
        h(0, 1)
        k_ve(0, 1)
        tx(3, 0, "b6")
        sq(1, 0)
        quantise("m", C)
        qz(0)
        k_gp(1)
        sq(1, 1)
        sq(2, 0)
        sq(2, 1)
        gc_f = keep.tile([P, PACK], F32, name="gc_f")
        nc.scalar.activation(out=gc_f[:], in_=gc_sb[:], func=ACT.Copy, scale=float(C))
        plane(0, 0, "b0")
        plane(0, 1, "b1")
        h(1, 0)
        h(1, 1)
        plane(0, 2, "b2")
        plane(0, 3, "b3")
        k_ve(1)
        add_lp(0, 0)
        h(3, 0)
        qz(1)
        quantise("w", O)
        k_gp(2)
        add_lp(0, 1)
        add_lp(0, 2)
        add_lp(0, 3)
        plane(1, 0, "b0")
        tq(0, 0, "b1")
        tq(0, 1, "b2")
        sq(3, 0)
        h(2, 0)
        h(2, 1)
        k_ve(2)
        plane(1, 1, "b3")
        tq(0, 2, "b4")
        add_lp(1, 0)
        mx(0, 0)
        plane(1, 2, "b5")
        tq(0, 3, "b6", 1)
        ex(0, 0)
        mx(0, 1)
        plane(1, 3, "b0")
        add_lp_ve(1, 1)
        ex(0, 1)
        mx(0, 2)
        tx(3, 1, "b1")
        add_lp_ve(1, 2)
        ex(0, 2)
        add_lp(1, 3)
        tx(4, 0, "b3")
        mx(0, 3)
        ex(0, 3)
        tq(1, 0, "b2", 2)
        tq(1, 1, "b4", 1)

        qz(2)
        sq(3, 1)
        rc(0)
        sq(4, 0)
        plane(2, 0, "b0")
        plane(2, 1, "b6")
        mx(1, 0)
        dg(0, 3)
        us(0, 0)
        us(0, 1)
        k_gp(3)
        us(0, 2)
        tq(1, 2, "b5", 1)
        mx(1, 1)
        h(3, 1)
        plane(2, 2, "b1")
        add_lp(2, 0)
        k_ve(3)
        tq(1, 3, "b0", 1)
        ex(1, 0)
        h(4, 0)
        tu(0, 0, "b2", 1)
        add_lp(2, 1)
        tu(0, 1, "b6")
        plane(2, 3, "b3")
        mx(1, 2)
        ex(1, 1)
        mx(1, 3)
        add_lp(2, 2)
        tx(4, 1, "b4")
        rr(0, 0)
        dm(0, 3, "b2", 0, 1)
        ex(1, 2)
        tx(5, 0, "b1")
        rr(0, 1)
        add_lp(2, 3)
        tq(2, 0, "b5")
        ex(1, 3)
        dm(0, 3, "b2", 1, 3)
        tq(2, 1, "b6")

        qz(3)
        sq(4, 1)
        rc(1)
        sq(5, 0)
        plane(3, 0, "b3")
        plane(3, 1, "b0")
        dm(0, 3, "b2", 3, 4)
        mx(2, 0)
        dg(1, 3)
        us(1, 0)
        us(1, 1)
        k_gp(4)
        us(1, 2)
        mx(2, 1)
        h(4, 1)
        tq(2, 2, "b4", 1)
        k_ve(4)
        add_lp(3, 0)
        plane(3, 2, "b3")
        h(5, 0)
        ex(2, 0)
        tu(0, 2, "b1")
        tq(2, 3, "b5")
        rd(0, 3)
        add_lp(3, 1)
        tu(1, 0, "b2", 1)
        tu(1, 1, "b0")
        mx(2, 2)
        ex(2, 1)
        plane(3, 3, "b6")
        rr(0, 2)
        add_lp(3, 2)
        mx(2, 3)
        ex(2, 2)
        tx(5, 1, "b3")
        rr(1, 0)
        dm(1, 3, "b4", 0, 1)
        tx(6, 0, "b1")
        ex(2, 3)
        rr(1, 1)
        add_lp(3, 3)
        dm(1, 3, "b4", 1, 2)
        tq(3, 0, "b2")
        dm(1, 3, "b4", 2, 3)
        tq(3, 1, "b5")

        gc_row = keep.tile([P, C], BF16, name="gc_row")
        nc.sync.dma_start(out=gc_row[:], in_=gc.partition_broadcast(P))
        qz(4)
        sq(5, 1)
        rc(2)
        qr(0)
        sq(6, 0)
        plane(4, 0, "b0")
        plane(4, 1, "b6")
        dm(1, 3, "b4", 3, 4)
        mx(3, 0)
        dg(2, 3)
        us(2, 0)
        us(2, 1)
        k_gp(5)
        us(2, 2)
        mx(3, 1)
        h(5, 1)
        add_lp(4, 0)
        tq(3, 2, "b3")
        plane(4, 2, "b0")
        k_ve(5)
        ex(3, 0)
        tu(1, 2, "b2", 1)
        h(6, 0)
        add_lp(4, 1)
        plane(4, 3, "b1")
        tq(3, 3, "b6")
        rd(1, 3)
        ex(3, 1)
        tu(2, 0, "b5")
        tu(2, 1, "b4")
        mx(3, 2)
        add_lp(4, 2)
        ou(0, 0, "b0")
        rr(1, 2)
        ex(3, 2)
        dm(2, 3, "b3", 0, 2)
        mx(3, 3)
        add_lp(4, 3)
        tx(6, 1, "b1")
        rr(2, 0)
        ex(3, 3)
        ou(0, 1, "b6")
        dm(2, 3, "b3", 2, 4)
        rr(2, 1)
        tq(4, 0, "b2")

        def steady(n):
            first, second, third = (TURNS[(i - n) % 3] for i in range(3))
            qz(n - 1)
            store(n - 6, 0)
            rc(n - 3)
            store(n - 6, 1)
            qr(n - 5)
            sq(n, 1)
            plane(n - 1, 0, second)
            mx(n - 2, 0)
            dg(n - 3, 3)
            plane(n - 1, 1, "b4")
            us(n - 3, 0)
            rd(n - 4, 3)
            add_lp(n - 1, 0)
            tq(n - 2, 1, "b5")
            h(n, 1)
            us(n - 3, 1)
            tu(n - 4, 2, third)
            ex(n - 2, 0)
            tq(n - 2, 2, first)
            mx(n - 2, 1)
            k_gp(n)
            add_lp(n - 1, 1)
            plane(n - 1, 2, second)
            rr(n - 4, 2)
            ex(n - 2, 1)
            plane(n - 1, 3, "b1")
            mx(n - 2, 2)
            add_lp(n - 1, 2)
            tq(n - 2, 3, "b4")
            k_ve(n)
            dm(n - 3, 3, third, 0, 1)
            tx(n + 1, 0, "b2")
            ex(n - 2, 2)
            mx(n - 2, 3)
            dm(n - 3, 3, third, 1, 2)
            tu(n - 3, 0, "b5")
            add_lp(n - 1, 3)
            h(n + 1, 0)
            dm(n - 3, 3, third, 2, 3)
            tu(n - 3, 1, second)
            ex(n - 2, 3)
            rr(n - 3, 0)
            us(n - 3, 2)
            sq(n + 1, 0)
            ou(n - 5, 0, first)
            rr(n - 3, 1)
            ou(n - 5, 1, "b4")
            tx(n + 1, 1, "b1")
            dm(n - 3, 3, third, 3, 4)
            tq(n - 1, 0, "b2", 1)

        for n in range(6, GROUPS - 1):
            steady(n)

        z = GROUPS - 1
        qz(z - 1)
        store(z - 6, 0)
        rc(z - 3)
        store(z - 6, 1)
        qr(z - 5)
        sq(z, 1)
        plane(z - 1, 0, "b0")
        mx(z - 2, 0)
        dg(z - 3, 3)
        plane(z - 1, 1, "b4")
        us(z - 3, 0)
        rd(z - 4, 3)
        add_lp(z - 1, 0)
        tq(z - 2, 1, "b5")
        h(z, 1)
        us(z - 3, 1)
        tu(z - 4, 2, "b6")
        ex(z - 2, 0)
        tq(z - 2, 2, "b3")
        mx(z - 2, 1)
        k_gp(z)
        add_lp(z - 1, 1)
        plane(z - 1, 2, "b0")
        rr(z - 4, 2)
        ex(z - 2, 1)
        plane(z - 1, 3, "b1")
        mx(z - 2, 2)
        add_lp(z - 1, 2)
        tq(z - 2, 3, "b4")
        tu(z - 3, 0, "b5")
        tu(z - 3, 1, "b6")
        k_ve(z)
        add_lp(z - 1, 3)
        dm(z - 3, 3, "b0", 0, 2)
        ou(z - 5, 0, "b2")
        mx(z - 2, 3)
        ex(z - 2, 2)
        tq(z - 1, 0, "b1")
        rr(z - 3, 0)
        ua(z - 3, 2)
        ou(z - 5, 1, "b3")
        ex(z - 2, 3)
        dm(z - 3, 3, "b0", 2, 4)
        rr(z - 3, 1)
        qr(z - 4)
        tu(z - 3, 2, "b5")
        store(z - 5, 0)
        tq(z - 1, 1, "b6")
        ou(z - 4, 0, "b4")
        store(z - 5, 1)
        ou(z - 4, 1, "b2")

        qz(z)
        rc(z - 2)
        uw(z - 2)
        us(z - 2, 2)
        store(z - 4, 0)
        mx(z - 1, 0)
        plane(z, 0, "b3")
        store(z - 4, 1)
        plane(z, 1, "b4")
        rd(z - 3, 3)
        ex(z - 1, 0)
        plane(z, 2, "b0")
        rr(z - 3, 2)
        tq(z - 1, 2, "b2")
        plane(z, 3, "b5")
        add_lp(z, 0)
        tq(z - 1, 3, "b1", 1)
        mx(z - 1, 1)
        add_lp(z, 1)
        qr(z - 3)
        gt(z - 2)
        add_lp(z, 2)
        mx(z - 1, 2)
        tu(z - 2, 2, "b3")
        add_lp_ve(z, 3)
        ex(z - 1, 1)
        mx(z - 1, 3)
        tq(z, 0, "b4", 1)
        tq(z, 1, "b0", 1)
        rr(z - 2, 2)
        ex(z - 1, 2)
        tq(z, 2, "b5")
        tq(z, 3, "b6", 1)
        rc(z - 1, 0, 2)
        us(z - 1, 0)
        us(z - 1, 1)
        mx(z, 0)
        dm(z - 2, 3, "b3")
        ex(z - 1, 3)
        mx(z, 1)
        ou(z - 3, 0, "b2")
        rc(z - 1, 2, 4)
        dg(z - 1, 3)
        us(z - 1, 2)
        ex(z, 0)
        mx(z, 2)
        tu(z - 1, 0, "b1")
        ex(z, 1)
        mx(z, 3)
        tw(z - 2, 0, 2, "b4")
        rc(z, 0, 2)
        us(z, 0)
        us(z, 1)
        ex(z, 2)
        rd(z - 2, 3)
        ex(z, 3)
        dm(z - 1, 3, "b5", 0, 1)
        tu(z - 1, 1, "b0")
        dm(z - 1, 3, "b5", 1, 2)
        rr(z - 1, 0)
        cw(z - 2, 0, 2)
        tu(z - 1, 2, "b3")
        rc(z, 2, 4)
        dm(z - 1, 3, "b5", 2, 4)
        rr(z - 1, 1)
        ua(z, 2)
        ua(z, 3)
        ou(z - 3, 1, "b6")
        tu(z, 0, "b1")
        rr(z - 1, 2)
        tu(z, 1, "b4", 1)
        qr(z - 2)
        store(z - 3, 0)
        tu(z, 2, "b0", 1)
        store(z - 3, 1)
        ou(z - 2, 0, "b3")
        ou(z - 2, 1, "b2")
        rd(z - 1, 3)
        tu(z, 3, "b6", 1)
        rr(z, 0)
        store(z - 2, 0)
        qr(z - 1)
        store(z - 2, 1)
        ou(z - 1, 0, "b5")
        ou(z - 1, 1, "b1")
        rr(z, 1)
        rr(z, 2)
        store(z - 1, 0)
        qr(z, 0, 2)
        ou(z, 0, "b3")
        rr(z, 3)
        store(z - 1, 1)
        qr(z, 2, 1)
        qr(z, 3, 1)
        store(z, 0)
        out_tile(z, 2, "b2", nc.vector.tensor_copy, nc.sync)
        out_tile(z, 3, "b4", nc.scalar.copy, nc.scalar)
